import numpy as np, ml_dtypes
CORES = [3,7,11,15,131,135,139,143]
N = 8
BF = ml_dtypes.bfloat16
W, P, R, M0, M, S, RO, TH = 2048, 128, 128, 384, 896, 3, 2, 620
def even(rng, *shape):
    return rng.integers(0, W - 1, shape)
def uneven(rng, *shape):
    return np.minimum(np.exp2(11 * rng.random(shape)).astype(np.int64) - 1, W - 2)
def edgy(rng, *shape):
    return (rng.random(shape) < 0.4) * (W - 2)
def across(t):
    y = t ^ (W // 2)
    return np.where(y == W - 1, W - 2, y)
def look(rng):
    x = rng.integers(0, 256, (16, W)); h = W // 2; m = rng.choice(np.array([0, 8, 40, 90, 120]), h)
    x[:, h:] = np.clip(x[:, :h] + rng.integers(-m, m + 1, (16, h)), 0, 255)
    return x
def rough(rng):
    return np.minimum((np.exp2(8 * rng.random((1, W))) * rng.random((16, W))).astype(np.int64), 255)
def grow(rng, tok, stem, slots, keep=0):
    k = np.arange(16)[:, None]; o = R + keep + rng.permutation(M0 - R - 2 * keep); h = len(o) // 2
    L = np.full((16, M0), W - 1); ch = np.zeros((16, M0), np.int64); F = tok(rng, 16, M0); e = np.zeros(M0, np.int64)
    levels = [np.arange(R), o[:h], o[h:h + h // 2], o[h + h // 2:]]
    for z in range(3):
        up, dn = levels[z], levels[z + 1]; n = len(dn)
        x = rng.permutation(slots)[:n] if z == 0 else rng.permutation(16 * len(up))[:n]
        p, t = up[x >> 4], x & 15; T = tok(rng, 16, n)
        if z == 0:
            T = np.where(rng.random((16, n)) < 0.8, stem[:, x], T); T[0] = x
        s = e[p]; e[dn] = np.minimum(16, s + rng.choice(np.array([1, 1, 2, 3, 5, 8, 16]), n))
        y = (T & -16) + t; T = np.where(k == s, np.where(y == W - 1, W - 17, y), T)
        F[:, dn] = np.where(k < s, F[:, p], T)
        stray = (rng.random(n) < 0.125) & (rng.random((16, n)) < 0.5) & (k != e[dn])
        L[:, dn] = np.where((k >= s) & (k < e[dn]), T, np.where(stray, tok(rng, 16, n), W - 1)); ch[t, p] = dn
        if z == 0: L[0, dn] = np.where(rng.random(n) < 0.1, tok(rng, n), L[0, dn])
    return L, ch, F
def ask(rng, tok, F):
    k = np.arange(16)[:, None]; q = F[:, rng.integers(R, M0, P)]; z = rng.integers(1, 17, P); near = q ^ (W // 2)
    q = np.where((k > 0) & (rng.random((16, P)) < 0.3) & (near != W - 1), near, q)
    y = tok(rng, 16, P); y = np.where(rng.random((16, P)) < 0.5, (y & -16) + (q & 15), y); y = np.where(y == W - 1, W - 17, y)
    return np.where((k >= z) | (rng.random(P) < 0.125), y, q)
def draw(rng, tok, shape):
    h = (M0 - R) // 2; stem = [tok(rng, 16, W) for g in range(8)]; slots = [rng.permutation(W - 1)[:h + h // 4] for g in range(8)]; d = []
    for r in range(N):
        for g in range(8):
            L, ch, F = grow(rng, tok, stem[g], slots[g]); d.append([shape(rng), L, ch, ask(rng, tok, F)])
    return d
def apart(rng):
    return 16 * rng.permutation(R)[:P] + rng.integers(0, 15, P)
def pack(d):
    a = [np.stack([x[z] for x in d]).reshape(N, 128, -1) for z in range(4)]
    return {"desc": a[0].astype(np.float32).astype(BF), "edge": a[1].astype(np.int32), "child": a[2].astype(np.int32), "req": a[3].astype(np.int32)}
def setup_inputs(rng):
    return pack(draw(rng, even, look))
def setup_inputs_spread(rng):
    return pack(draw(rng, uneven, rough))
def setup_inputs_ends(rng):
    k = np.arange(16)[:, None]; h = (M0 - R) // 2; d = []
    stem = [edgy(rng, 16, W) for g in range(8)]; slots = [2 + rng.permutation(W - 18)[:h + h // 4] for g in range(8)]
    for r in range(N):
        for g in range(8):
            L, ch, F = grow(rng, edgy, stem[g], slots[g], 1)
            x = rng.integers(0, 2, (16, W)) * 255; x[:, 0] = 0; x[:, W - 2] = 255; x[:8, W // 2] = 0; x[8:, W // 2] = 255
            q = np.where(k >= rng.integers(1, 17, P), edgy(rng, 16, P), F[:, rng.integers(R + 1, M0 - 1, P)])
            ch[0, 0] = R; ch[1, 0] = 1; ch[14, R - 1] = M0 - 1
            L[:, R] = 0; L[15, R] = W // 2; L[:, M0 - 1] = 0; L[0, M0 - 1] = W - 2
            q[:, 0] = 0; q[15, 0] = W - 2; q[0, 1] = 1
            q[:, P - 1] = 0; q[0, P - 1] = W - 2; q[15, P - 1] = W - 2
            if g % 2: q[14, P - 1] = W - 2
            d.append([x, L, ch, q])
    return pack(d)
def setup_inputs_corners(rng):
    k = np.arange(16)[:, None]; i = np.arange(P); d = draw(rng, even, look)
    for j in range(8 * N):
        x, L, ch, q = d[j]; z = j % 11; q0 = apart(rng)
        if z in (2, 3, 4, 6, 8, 9, 10):
            ch[:] = 0; L[:] = W - 1
        if z in (9, 10):
            x = np.concatenate([rng.integers(0, 100, (16, W // 2)), rng.integers(156, 256, (16, W // 2))], axis=1)
        if z == 0:
            ch[:] = 0; q[0] = rng.choice(np.array([0, 1, 15, 16, W - 17, W - 2]), P)
            L[:, 0] = np.where(k < 8, q[:, :1], W - 1)[:, 0]
        if z == 1:
            y = int(rng.choice(np.flatnonzero(ch[:, :R].T.reshape(-1)))); e = L[:, ch[y & 15, y >> 4]][:, None]
            q = np.where((rng.random(P) < 0.5) & (k > 0) & (e < W - 1), e, q); q[0] = y
        if z in (2, 3):
            q = even(rng, 16, P); q[0] = q0; u = R + i if z == 2 else q0 >> 4; ch[q0 & 15, q0 >> 4] = u; m = rng.integers(0, 5, P)
            e = np.where(((m == 1) & (k == 15)) | ((m == 2) & (k == 0)) | ((m == 3) & (k == 1)), even(rng, 16, P), q)
            L[:, u] = np.where((m == 4) & (k >= (8 if z == 2 else np.maximum(rng.integers(-5, 16, P), 0))), W - 1, e)
        if z == 4:
            nc = (M0 - R) // 4; T = even(rng, 16, nc); T[0] = rng.permutation(W - 1)[:nc]
            for m in range(4):
                u = R + 4 * np.arange(nc) + m; L[m, u] = T[m]; ch[T[m] & 15, T[0] >> 4 if m == 0 else u - 1] = u
            q = T[:, i % nc]
        if z == 5: L[:] = W - 1
        if z == 6:
            q = even(rng, 16, P); q[0] = q0; w = q0 >> 4; a = np.flatnonzero(w % 2 == 0); ch[q0[a] & 15, w[a]] = w[a] + 1
            L[:, w[a] + 1] = np.where(k < rng.integers(1, 16, len(a)), q[:, a], even(rng, 16, len(a))); q[0] = np.where(w % 4 == 3, q0 - 32, q0)
        if z == 7: q[1:] = rng.choice(np.array([0, 1, W - 3, W - 2]), (15, 1))
        if z == 8:
            nb = P // N; nc = min((M0 - R) // 17, nb); a = rng.permutation(nb)[:nc]; o = nb + rng.permutation(P - nb)[:nc]
            m = rng.integers(2, 16, nc); p = rng.integers(1, m); u = R + 17 * np.arange(nc)
            q = even(rng, 16, P); q[0] = q0; q[:, o] = np.where(k < p, q[:, a], q[:, o]); T = q[:, a]
            h = ((T[1:] * T[:-1]) >> 5) & (W - 1); h = np.concatenate([T[:1], np.where(h == W - 1, 0, h)])
            ch[T[0] & 15, T[0] >> 4] = u; L[:, u] = np.where(k < m, T, W - 1)
            for t in range(16):
                e = m + rng.integers(0, 17 - m); ch[t, u] = u + 1 + t
                L[:, u + 1 + t] = np.where((k >= m) & (k < e), np.where(rng.random((16, nc)) < 0.1, even(rng, 16, nc), h), W - 1)
        if z == 9:
            q = even(rng, 16, P); q[0] = q0; nc = P // 16; n = np.arange(nc); c = R + n; m = rng.integers(1, 8, nc)
            s = np.sort(rng.permutation(np.flatnonzero(q0 > 15))[:9 * nc].reshape(9, nc), axis=0)
            u, o, uu, oo = [q0[s[t]] >> 4 for t in (0, 2, 8, 5)]; T = q[:, s[0]]; y = q[:, s[8]]
            q[:, s[1]] = np.where(k < m, T, np.where(k == m, np.where((T ^ 1) == W - 1, 0, T ^ 1), q[:, s[1]]))
            q[0, s[2:5]] = 16 * o + (rng.integers(0, 15, nc) + 5 * np.arange(3)[:, None]) % 15
            q[0, s[5:8]] = 16 * oo + (rng.integers(0, 15, nc) + 5 * np.arange(3)[:, None]) % 15
            ch[T[0] & 15, u] = c; ch[T[m, n] & 15, c] = o; ch[y[0] & 15, uu] = oo
            L[:, c] = np.where(k < m, T, W - 1); L[:, o] = np.where(k <= m, T, across(T))
            L[:, oo] = np.where(k < rng.integers(1, 16, nc), y, W - 1)
        if z == 10:
            q = even(rng, 16, P); q[0] = q0; ch[q0 & 15, q0 >> 4] = R + i; p = rng.integers(1, 16, P); y = across(q)
            y = np.where(rng.random(P) < 0.25, y, (y & -16) + rng.integers(0, 15, P))
            L[:, R + i] = np.where(k == p, y, q)
        d[j] = [x, L, ch, q]
    return pack(d)
def setup_inputs_ties(rng):
    k = np.arange(16)[:, None]; i = np.arange(P); h = 3 * P // 4; s = np.where(i < h, i, i - P // 2); d = []
    for j in range(8 * N):
        x = look(rng); b = 16 * rng.integers(0, R - 1, 16) + np.arange(16)
        A = rng.permutation(W - 1); A = A[~np.isin(A, b)][:P]; B = b[np.where(rng.random(P) < 0.25, A & 15, rng.integers(0, 16, P))]; p = rng.integers(1, 16, P)
        x[:, b] = rng.integers(100, 121, (16, 16)); y = TH + rng.integers(-1, 2, P); v = rng.integers(-20, 21, (8, P))
        D = (y >> 4) + (k < (y & 15)) + np.concatenate([v, -v])
        f1 = rng.integers(0, 16, P); f2 = f1 ^ (1 << rng.integers(0, 4, P)); w = np.where(y > TH, 257, 259); z = y - w; o = k - (k > f1) - (k > f2)
        D = np.where(rng.random(P) < 0.5, D, np.where(k == f1, w >> 1, np.where(k == f2, w - (w >> 1), z // 14 + (o < z % 14))))
        x[:, A] = x[:, B] + D * np.where(D > 100, 1, rng.choice(np.array([-1, 1]), (16, P)))
        T = even(rng, 16, P); T[0] = apart(rng); T = T[:, s]
        L = np.full((16, M0), W - 1); ch = np.zeros((16, M0), np.int64)
        L[:, R:R + h] = np.where(k == p, A, T)[:, :h]; ch[T[0] & 15, T[0] >> 4] = R + s
        d.append([x, L, ch, np.where(k == p, B, T)])
    return pack(d)
def check_inputs(d):
    bad = []
    for a, lo, hi in (("desc", 0, 255), ("edge", 0, W - 1), ("child", 0, M0 - 1), ("req", 0, W - 2)):
        x = np.asarray(d[a]).astype(np.float64)
        if not (np.min(x) >= lo and np.max(x) <= hi): bad.append("range of " + a)
        if np.any(x != np.floor(x)): bad.append("whole numbers in " + a)
    c = np.sort(np.asarray(d["child"]).reshape(N, 8, 16 * M0), axis=-1)
    if np.any((c[..., 1:] == c[..., :-1]) & (c[..., 1:] > 0)): bad.append("a node stands twice in child")
    return bad
def walk(X, L, C, Q, rnd):
    i = np.arange(P); k = np.arange(16)[:, None]; n = M0 + 2 * P * rnd + 2 * i
    v = Q[0] >> 4; a = np.zeros(P, np.int64); on = np.ones(P, bool)
    for step in range(S):
        low = np.full(M, P); np.minimum.at(low, v[on], i[on])
        act = on & (low[v] == i)
        t = Q[np.minimum(a, 15), i] & 15; c = C[t, v]; E = L[:, c]; none = E == W - 1
        dist = np.add.reduce(np.abs(X[:, E] - X[:, Q]), axis=0)
        b = np.min(np.where((k >= a) & none, k, 16), axis=0)
        l = np.min(np.where((k >= a) & (none | (dist > TH)), k, 16), axis=0)
        leaf = act & ((c == 0) | ((l == a) & (l < b)))
        down = act & (c > 0) & (l == b)
        cut = act & (c > 0) & (l > a) & (l < b) & (low[c] == P)
        j = np.flatnonzero(cut); lj = l[j]; cj = c[j]; ej = E[lj, j]; qj = Q[lj, j]
        f = np.unique(qj, return_index=True)[1]
        X[:, qj[f]] = (X[:, qj[f]] + X[:, ej[f]]) >> 1
        L[:, n[j]] = np.where(k >= lj, E[:, j], W - 1); C[:, n[j]] = C[:, cj]
        L[:, cj] = np.where(k < lj, E[:, j], W - 1); C[:, cj] = 0; C[ej & 15, cj] = n[j]
        two = (ej & 15) != (qj & 15); o = j[two]
        C[qj[two] & 15, cj[two]] = n[o] + 1; L[:, n[o] + 1] = np.where(k >= l[o], Q[:, o], W - 1)
        j = np.flatnonzero(leaf)
        L[:, n[j]] = np.where(k >= a[j], Q[:, j], W - 1); C[t[j], v[j]] = n[j]
        v = np.where(down, c, v); a = np.where(down, b, a); on = on & ~leaf & ~cut & (a < 16)
    return a
def reference(desc, edge, child, req):
    X = desc.astype(np.float32).astype(np.int64).reshape(N, 8, 16, W); Q = req.astype(np.int64).reshape(N, 8, 16, P)
    L = np.full((N, 8, 16, M), W - 1); L[..., :M0] = edge.reshape(N, 8, 16, M0)
    C = np.zeros((N, 8, 16, M), np.int64); C[..., :M0] = child.reshape(N, 8, 16, M0)
    k = np.arange(1, 16)[:, None]; B = P // N
    for rnd in range(RO):
        new = np.zeros_like(Q)
        for r in range(N):
            for g in range(8):
                q = Q[r, g]; a = walk(X[r, g], L[r, g], C[r, g], q, rnd)
                h = ((q[1:] * q[:-1]) >> 5) & (W - 1); h = np.where(h == W - 1, 0, h)
                q = np.concatenate([q[:1], np.where(k >= a, h, q[1:])])
                for e in range(N): new[(r + e) % N, g, :, e * B:(e + 1) * B] = q[:, e * B:(e + 1) * B]
        Q = new
    return {"yd": X.reshape(N, 128, W).astype(np.float32).astype(BF), "ye": L.reshape(N, 128, M).astype(np.float32), "yr": Q.reshape(N, 128, P).astype(np.float32)}

@@ -1,0 +1,723 @@
+from concourse.bass import DstId, RemoteDMATransfer
+from concourse.mybir import AluOpType as A, ActivationFunctionType as F
+
+S_, RO_ = 3, 2
+F32, BF, H16, I32, U16 = "float32", "bfloat16", "float16", "int32", "uint16"
+SCRATCH = {}
+
+
+PLACE = {}
+
+
+def _b(name, n, d, where="sbuf"):
+    pool = {F32: "poolf", U16: "poolu", I32: "pooli"}.get(d)
+    if name.startswith("QE"):
+        pool = "poolq"
+    elif n > 16 or where != "sbuf":
+        pool = None
+    if pool is None:
+        SCRATCH[name] = (where, [128, n], d)
+        PLACE[name] = (name, 0, n)
+    else:
+        at = SCRATCH[pool][1][1] if pool in SCRATCH else 0
+        SCRATCH[pool] = ("sbuf", [128, at + n + n % 2], d)
+        PLACE[name] = (pool, at, n)
+
+
+_b("X", 2192, BF); _b("L", 1152, F32); _b("C", 1152, F32); _b("BT", 2048, BF)
+_b("Ei", 384, I32); _b("Ci", 384, I32); _b("Qi", 128, I32); _b("xsave", 16, BF); _b("lsave", 4, F32)
+_b("IQ", 128, I32); _b("IP", 1, I32); _b("IC", 4, I32); _b("R4i", 256, I32); _b("Qb", 128, BF); _b("Q4b", 256, BF)
+_b("cols", 16, F32); _b("flip", 16, F32); _b("BO", 128, BF); _b("R", 128, BF); _b("CONV", 2048, BF)
+for _n in ("I", "TRI", "STRI", "SHD", "SHU", "D64", "Dm64", "DQ", "I64", "Im128", "IB", "ImB", "TRI64", "BO64", "BOm16", "BOm1",
+           "MSK", "B0", "ONES", "tmpc", "tmpd", "tmpe"):
+    _b(_n, 128, BF)
+_b("I32", 128, F32); _b("SEL", 8, BF); _b("SELB", 8, BF); _b("MASKN", 512, BF); _b("BAND", 240, BF); _b("Y0", 384, BF)
+_b("W8", 8, F32); _b("DUM", 16, F32); _b("DD", 16, F32); _b("DTOK", 8, F32); _b("N01", 512, F32)
+_b("Qi2", 128, I32); _b("QF", 128, F32); _b("Ql", 128, U16); _b("Q4i", 128, I32); _b("Q4m", 128, H16); _b("QMi", 128, I32)
+_b("QM", 128, H16); _b("uQ", 128, H16); _b("Q16", 128, H16); _b("HP", 128, I32); _b("HI", 128, I32); _b("HM", 128, F32)
+_b("HMQ", 128, F32); _b("HK", 128, F32); _b("SND", 128, F32); _b("LQ", 128, F32); _b("LK", 128, BF); _b("LAND1", 128, F32)
+_b("vl", 8, U16); _b("cl", 8, U16); _b("VC", 16, F32); _b("OH", 128, F32); _b("P", 128, BF); _b("KGE", 128, BF)
+_b("M1", 128, H16); _b("mk", 128, H16); _b("mkq", 256, H16); _b("El", 128, U16); _b("XQ", 2048, BF); _b("DF", 2048, BF)
+_b("AB", 2048, BF); _b("VB", 128, BF); _b("VBo", 128, BF); _b("CB", 128, BF); _b("CV", 128, F32); _b("Cc", 128, F32)
+_b("uE", 128, F32); _b("EA", 1024, BF); _b("ED", 1024, BF); _b("ES", 1024, BF); _b("NA", 128, BF); _b("STD", 128, BF)
+_b("NN", 128, BF); _b("T1", 128, F32); _b("T2", 128, F32); _b("BUF", 512, H16)
+for _n in range(6):
+    _b("QE%d" % _n, 256, H16)
+_b("CMV", 8, F32); _b("DMC", 8, F32); _b("VCD", 16, F32); _b("WF", 16, F32); _b("x1", 8, F32); _b("x2", 8, F32)
+_b("x3", 8, F32); _b("x4", 8, F32); _b("w6", 16, F32); _b("y1", 8, F32); _b("l1", 16, F32); _b("l2", 16, F32)
+_b("lc", 16, U16); _b("qel", 16, U16); _b("QLF", 8, F32); _b("QB", 128, BF); _b("QBo", 128, BF)
+_b("XLg", 128, BF); _b("XQg", 128, BF); _b("DS", 128, F32); _b("DH", 128, F32); _b("mk2", 128, H16); _b("d1", 8, F32); _b("d2", 8, F32)
+_b("didx", 8, U16); _b("X1", 128, H16); _b("X2", 128, F32); _b("X3", 128, H16); _b("X5", 128, F32)
+_b("RI", 128, I32); _b("RA", 128, I32); _b("RW", 16, I32); _b("RL", 16, U16); _b("IDT", 32, F32); _b("OHc", 256, F32); _b("OHN", 256, F32); _b("YE", 896, F32)
+PS = ["pg0", "pg1", "pc", "pm", "pd", "py", "ps", "pw"]
+for _n in PS:
+    _b(_n, 512, F32, "psum")
+SEMAPHORES = ["sV", "sT", "sS", "sG", "locE", "loc0", "loc1", "arrE", "arr0", "arr1"] + ["d%d" % _i for _i in range(12)]
+NDUM, NDUMP, TDUMP, BIG = 896, 1024, 2064, float(2 ** 17)
+
+
+def make(g, T):
+    eng = {"V": g.vector, "S": g.scalar, "T": g.tensor, "G": g, "Y": g.sync}
+    tick = {"V": 0, "S": 0, "T": 0, "G": 0}
+    known = {q: {} for q in eng}
+    snap, acc, final, ndma = {}, {}, {}, [0]
+
+    def ap(x):
+        if x[0] == "@":
+            return ap(x[1]).indirect(ap(x[2]))
+        t = T[x[0]]
+        st = x[3] if len(x) > 3 else 1
+        p0, p1 = (x[4], x[5]) if len(x) > 4 else (0, 128)
+        return t[p0:p1, x[1]:x[2]:st] if st != 1 else t[p0:p1, x[1]:x[2]]
+
+    def flat(xs):
+        out = []
+        for x in xs:
+            if x is None or isinstance(x, (int, float)):
+                continue
+            if x[0] == "@":
+                out += [x[1], x[2]]
+            else:
+                out.append(x)
+        return out
+
+    def wait(q, sem, val):
+        k = known[q]
+        if k.get(sem, 0) >= val:
+            return
+        eng[q].wait_ge(T.sem[sem], val)
+        k[sem] = val
+        for s, v in snap.get((sem, val), {}).items():
+            if k.get(s, 0) < v:
+                k[s] = v
+
+    def deps(q, reads, writes, sem, val, dma=False):
+        need = {}
+        for isw, xs in ((0, reads), (1, writes)):
+            for x in xs:
+                n, lo, hi = x[0], x[1], x[2]
+                ps = n in PS
+                for e in acc.get(n, []):
+                    elo, ehi, ew, eq, es, ev, ed = e
+                    if ps:
+                        if eq == q and (q == "T" or not (isw or ew) or ehi <= lo or hi <= elo):
+                            continue
+                    else:
+                        if ehi <= lo or hi <= elo or not (isw or ew):
+                            continue
+                    need[es] = max(need.get(es, 0), ev)
+        for s in sorted(need, key=lambda z: z == "s" + q):
+            wait(q, s, need[s])
+        for isw, xs in ((0, reads), (1, writes)):
+            for x in xs:
+                n, lo, hi = x[0], x[1], x[2]
+                full = len(x) < 5
+                l = acc.setdefault(n, [])
+                if isw and full and n not in PS and (len(x) < 4 or x[3] == 1):
+                    l[:] = [e for e in l if not (lo <= e[0] and e[1] <= hi)]
+                else:
+                    l[:] = [e for e in l if not (e[3] == q and not e[6] and not dma and e[0] == lo and e[1] == hi and e[2] == isw)]
+                l.append((lo, hi, isw, q, sem, val, dma))
+
+    def fin(q, ins):
+        sem = "s" + q
+        tick[q] += 1
+        snap[(sem, tick[q])] = dict(known[q])
+        final[sem] = tick[q]
+        ins.then_inc(T.sem[sem], 1)
+
+    def pre(q, reads, writes):
+        deps(q, flat(reads), flat(writes), "s" + q, tick[q] + 1)
+
+    def wr(out):
+        return ([out[1]], [out[2]]) if out[0] == "@" else ([out], [])
+
+    def tt(out, a, b, op):
+        w, r = wr(out)
+        pre("V", [a, b] + r, w)
+        fin("V", g.vector.tensor_tensor(ap(out), ap(a), ap(b), op))
+
+    def ts(out, a, s1, op0, s2=None, op1=None):
+        pre("V", [a, s1, s2], [out])
+        f = lambda s: ap(s) if isinstance(s, tuple) else s
+        if op1 is None:
+            fin("V", g.vector.tensor_scalar(ap(out), ap(a), f(s1), None, op0))
+        else:
+            fin("V", g.vector.tensor_scalar(ap(out), ap(a), f(s1), f(s2), op0, op1))
+
+    def cp(out, a):
+        w, r = wr(out)
+        pre("V", [a] + r, w)
+        fin("V", g.vector.tensor_copy(ap(out), ap(a)))
+
+    def ms(out, c):
+        pre("V", [], [out])
+        fin("V", g.vector.memset(ap(out), c))
+
+    def act(out, a, func, bias=0.0, scale=1.0):
+        pre("S", [a, scale], [out])
+        sc = ap(scale) if isinstance(scale, tuple) else scale
+        fin("S", g.scalar.activation(ap(out), ap(a), func, bias=bias, scale=sc))
+
+    def iota(out, pattern, base, cm, fl=False):
+        pre("G", [], [out])
+        if fl:
+            fin("G", g.iota(ap(out), pattern, base, cm, allow_small_or_imprecise_dtypes=True))
+        else:
+            fin("G", g.iota(ap(out), pattern, base, cm))
+
+    def sel(out, a, pattern, op, base, cm):
+        pre("G", [a], [out])
+        fin("G", g.affine_select(ap(out), ap(a), pattern, op, 0.0, base, cm))
+
+    def mm(lst):
+        pre("T", [x[1] for x in lst] + [x[2] for x in lst], [x[0] for x in lst])
+        for i, (o, l, r, st, sp) in enumerate(lst):
+            ins = g.tensor.matmul(ap(o), ap(l), ap(r), st, sp)
+            if i == len(lst) - 1:
+                fin("T", ins)
+        return tick["T"]
+
+    def dma(q, out, in_, r=(), w=()):
+        sem = "d%d" % ndma[0]
+        ndma[0] += 1
+        deps(q, list(r), list(w), sem, 16, True)
+        snap[(sem, 16)] = dict(known[q])
+        final[sem] = 16
+        eng[q].dma_start(out, in_).then_inc(T.sem[sem], 16)
+
+    return dict(tt=tt, ts=ts, cp=cp, ms=ms, act=act, iota=iota, sel=sel, mm=mm, dma=dma, wait=wait, deps=deps, known=known,
+                final=final, acc=acc)
+
+
+def plan(src, cores, topo):
+    far = [d for d in cores if d != src and d not in topo.cores_of(src)]
+    near = [d for d in cores if d != src and d in topo.cores_of(src)]
+    eng = topo.engines(src, far[0])
+    rest = [e for e in topo.engines(src, near[0]) if e not in eng]
+    h = len(eng) // 2
+    a = [(d, eng[2 * i:2 * i + 2]) for i, d in enumerate(far[:h])]
+    b = [(d, eng[h * i:h * i + h]) for i, d in enumerate(far[h:])] + [(d, rest) for d in near]
+    return [a, b]
+
+
+def rank_program(g, core, T, topo):
+    rank = T.rank_of(core)
+    if rank is None:
+        return
+    K = make(g, T)
+    tt, ts, cp, ms, act, iota, sel, mm, dma, wait, deps = (K[x] for x in ("tt", "ts", "cp", "ms", "act", "iota", "sel", "mm", "dma", "wait", "deps"))
+
+    def b(n, lo=0, hi=None, st=1):
+        n, at, size = PLACE[n]
+        lo, hi = at + lo, at + (size if hi is None else hi)
+        return (n, lo, hi, st) if st != 1 else (n, lo, hi)
+
+    def col(j):
+        return b("cols", j, j + 1)
+
+    def ind(w, hi, o, lo=0, oh=None):
+        return ("@", (w, 0, hi), b(o, lo, oh))
+
+    def part(x, p0, p1):
+        return (x[0], x[1], x[2], 1, p0, p1)
+
+    fills = []
+
+    def fill(n=1):
+        for _ in range(n):
+            if fills:
+                fills.pop(0)()
+
+    dma("Y", T.Qi[:], T.req[:], w=[b("Qi")])
+    dma("S", T.Ci[:], T.child[:], w=[b("Ci")])
+    dma("Y", T.Ei[:], T.edge[:], w=[b("Ei")])
+    dma("S", T.X[:, 0:1024], T.desc[:, 0:1024], w=[b("X", 0, 1024)])
+    dma("Y", T.X[:, 1024:2048], T.desc[:, 1024:2048], w=[b("X", 1024, 2048)])
+    iota(b("IP"), [[1, 1]], 0, 1)
+    iota(b("IQ"), [[1, 128]], 0, 0)
+    iota(b("C", NDUM, NDUMP), [[1, 128]], NDUM, 0, True)
+    ms(b("L", 384, 1024), 0.0)
+    ts(b("IC", 0, 1), b("IP"), 4, A.arith_shift_right)
+    ts(b("IC", 1, 2), b("IP"), 15, A.bitwise_and)
+    ts(b("IC", 2, 3), b("IP"), 4, A.arith_shift_right, 1, A.bitwise_and)
+    ts(b("R4i", 0, 128), b("IQ"), 4, A.arith_shift_right)
+    ts(b("R4i", 128, 256), b("IQ"), 15, A.bitwise_and)
+    cp(col(0), b("IP"))
+    cp(b("cols", 1, 4), b("IC", 0, 3))
+    cp(b("Qb"), b("IQ"))
+    cp(b("Q4b"), b("R4i"))
+    QMb = b("Q4b", 128, 256)
+    ts(col(5), col(2), 0.0, A.is_equal)
+    ts(col(8), col(0), -1.0, A.add)
+    ts(b("BO"), b("Q4b", 0, 128), col(1), A.is_equal)
+    ts(b("I"), b("Qb"), col(0), A.is_equal)
+    ts(b("MSK"), QMb, col(2), A.is_equal)
+    ts(b("SEL"), b("Qb", 0, 8), col(1), A.is_equal)
+    ts(b("B0"), b("BO"), col(5), A.mult)
+    for n, op, base in (("SHU", A.is_equal, 1), ("TRI", A.is_ge, 0), ("STRI", A.is_gt, 0), ("SHD", A.is_equal, -1)):
+        sel(b(n), b("BO"), [[1, 128]], op, base, -1)
+    for m in range(16):
+        sel(b("CONV", 128 * m, 128 * m + 128), b("BO"), [[0, 8], [1, 16]], A.is_equal, -m, 0)
+    iota(b("N01", 0, 256), [[1, 256]], 384, 0, True)
+    iota(b("N01", 256, 512), [[1, 256]], 640, 0, True)
+    for n, src, c in (("I64", "I", 64.0), ("Im128", "I", -128.0), ("IB", "I", BIG), ("ImB", "I", -BIG), ("I32", "I", 1.0),
+                      ("BO64", "BO", 64.0), ("BOm16", "BO", -16.0), ("BOm1", "BO", -1.0), ("SELB", "SEL", 4096.0)):
+        act(b(n), b(src), F.Copy, scale=c)
+    ms(b("C", 384, NDUM), 0.0)
+
+    def consts_b():
+        ms(b("KGE"), 1.0)
+        ms(b("BT", 0, 1), -1.0)
+        ts(b("flip"), b("Qb", 0, 16), col(2), A.is_equal, -2.0, A.mult)
+        ts(b("flip"), b("flip"), 1.0, A.add)
+        n = 1
+        for i in range(11):
+            ts(b("BT", n, 2 * n), b("BT", 0, n), b("flip", i, i + 1), A.mult)
+            n *= 2
+        tt(b("tmpe"), b("I"), b("SHD"), A.subtract)
+        for n, src, c in (("TRI64", "TRI", 64.0), ("D64", "tmpe", 64.0), ("Dm64", "tmpe", -64.0)):
+            act(b(n), b(src), F.Copy, scale=c)
+        for i in range(4):
+            ts(b("MASKN", 128 * i, 128 * i + 128), b("Qb"), col(0), A.is_le, -64.0, A.mult)
+        ms(b("BAND"), 0.0)
+        ms(b("BAND", 112, 128), 1.0)
+
+    def consts_c():
+        ms(b("ONES"), 1.0)
+        ms(b("Y0"), 1.0)
+        ms(b("Y0", 128, 256), 65.0)
+        ts(b("W8"), b("Qb", 0, 8), 16.0, A.mult, col(2), A.add)
+        for h in (0, 8):
+            ts(b("DUM", h, h + 8), b("W8"), float(NDUM), A.add)
+            ts(b("DD", h, h + 8), b("W8"), float(NDUMP), A.add)
+        ts(b("DTOK"), b("W8"), float(TDUMP), A.add)
+        ts(col(4), col(2), -1.0, A.mult, 15.0, A.add)
+        ts(col(6), col(2), 0.0, A.is_gt)
+        ts(b("IDT", 0, 16), b("Qb", 0, 16), col(4), A.is_equal)
+
+    def round_start(r):
+        src = b("Qi") if r == 0 else b("QF")
+        if r:
+            tt(b("HK"), b("LK"), b("HMQ"), A.mult)
+            tt(b("QF"), b("HK"), b("LQ"), A.add)
+        cp(b("Ql"), src)
+        qi = src
+        if r:
+            xq(0)
+            xq(1)
+            qi = b("Qi2")
+            cp(qi, src)
+        ts(b("Q4i"), qi, 4, A.arith_shift_right)
+        ts(b("Q4m"), b("Q4i"), col(5), A.mult)
+        mm([(b("pm", 0, 128), b("Q4m"), b("BO"), True, True)])
+        ts(b("QMi"), qi, 15, A.bitwise_and)
+        cp(b("QM"), b("QMi"))
+        if r == 0:
+            tt(b("DQ"), b("I"), b("SHU"), A.subtract)
+        tt(b("mk"), b("pm", 0, 128), b("MSK"), A.mult)
+        mm([(b("pm", 128, 136), b("mk"), b("SEL"), True, True)])
+        mm([(b("ps", 128, 256), b("B0"), b("QM"), True, True)])
+        mm([(b("pw", 0, 128), b("DQ"), b("QM"), True, True)])
+        cp(b("vl"), b("pm", 128, 136))
+        act(b("VC", 0, 8), b("pm", 128, 136), F.Copy)
+        ts(b("OH"), b("ps", 128, 256), col(2), A.is_equal)
+
+    def round_rest(r):
+        ts(b("P"), b("pw", 0, 128), 16.0, A.add)
+        if r:
+            ms(b("KGE"), 1.0)
+        else:
+            cp(b("QF"), b("Qi"))
+            travel("QF", "LQ", "E")
+        ts(b("uQ"), b("QF"), -1.0, A.mult, 2047.0, A.add)
+
+    hsrc = lambda r: b("QF" if r else "LQ")
+
+    def hash_a(r):
+        cp(b("Q16"), hsrc(r))
+        mm([(b("pw", 0, 128), b("SHD"), b("Q16"), True, True)])
+
+    def hash_b(r):
+        tt(b("HP"), b("pw", 0, 128), hsrc(r), A.mult)
+        ts(b("HI"), b("HP"), 5, A.arith_shift_right, 2047, A.bitwise_and)
+        ts(b("HM"), b("HI"), 2046.5, A.is_lt)
+
+    def hash_c(r):
+        tt(b("HMQ"), b("HI"), b("HM"), A.mult)
+        tt(b("HMQ"), b("HMQ"), hsrc(r), A.subtract)
+        ts(b("HMQ"), b("HMQ"), col(6), A.mult)
+
+    def gram_mask(h):
+        mm([(b("pg%d" % h), b("I"), b("MASKN"), True, False)])
+
+    def gram(left, lefto, right, masked):
+        done = {}
+        for y in range(2):
+            for h in range(2):
+                l = []
+                for x in (2 * y, 2 * y + 1):
+                    gr = 4 * h + x
+                    p0 = 32 * (gr // 2)
+                    p1 = p0 + (32 if gr % 2 else 16)
+                    l.append((b("pg%d" % h, 128 * x, 128 * x + 128), part(b(lefto if gr % 2 else left), p0, p1), part(b(right), p0, p1),
+                              not masked, not masked or x == 3))
+                if y:
+                    wait("T", "sT", done[h])
+                done[h] = mm(l)
+
+    def band(gr):
+        return b("BAND", 112 - 16 * gr, 240 - 16 * gr)
+
+    def def_m(r, s):
+        if r == 0:
+            mm([(b("pg1", 384, 512), b("BO"), b("BUF", 384, 512), True, True)])
+
+    def def_a(r, s):
+        cp(b("RW"), b("pm", 384, 400))
+        ts(b("RW"), b("RW"), 15, A.bitwise_and)
+        cp(b("RL"), b("RW"))
+        for h in range(2):
+            act(b("OHc", 128 * h, 128 * h + 128), ind("IDT", 16, "RL", 8 * h, 8 * h + 8), F.Copy)
+
+    def def_b(r, s):
+        if r == 0:
+            n0 = 384 + 256 * r + 128
+            tt(b("X5"), b("pg1", 384, 512), b("Cc"), A.mult)
+            tt(b("C", n0, n0 + 128), b("C", n0, n0 + 128), b("X5"), A.add)
+        tt(b("OHN"), b("OHc"), b("N01", 256 * r, 256 * r + 256), A.mult)
+
+    def def_c(r, s):
+        tt(ind("C", 1152, "lc", 8, 16), b("OHN", 0, 128), b("OHN", 128, 256), A.max)
+
+    def unmade_m(r):
+        l = []
+        for s in range(S_):
+            q = "QE%d" % (3 * r + s)
+            l += [(b("pg0", 256, 384), b("BO"), b(q, 0, 128), s == 0, False), (b("pg0", 256, 384), b("BOm1"), b(q, 128, 256), False, s == S_ - 1)]
+        mm(l)
+
+    def unmade(r):
+        n1 = 384 + 256 * r
+        cp(b("RI", 0, 128), b("pg0", 256, 384))
+        ts(b("RA", 0, 128), b("RI", 0, 128), 15, A.bitwise_and)
+        ts(b("X5"), b("RA", 0, 128), 0.5, A.is_gt)
+        tt(b("L", n1, n1 + 128), b("L", n1, n1 + 128), b("X5"), A.mult)
+
+    def step_a1():
+        tt(b("M1"), ind("C", 1024, "vl"), b("OH"), A.mult)
+        mm([(b("pm", 0, 128), b("M1"), b("BO"), True, True)])
+
+    def step_a2():
+        tt(b("mk"), b("pm", 0, 128), b("MSK"), A.mult)
+        mm([(b("pm", 128, 136), b("mk"), b("SEL"), True, True), (b("pm", 256, 384), b("BO"), b("M1"), True, True)])
+
+    def step_a3(late=False):
+        cp(b("cl"), b("pm", 128, 136))
+        act(b("VC", 8, 16), b("pm", 128, 136), F.Copy)
+        if not late:
+            act(b("CB"), ind("BT", 1024, "cl"), F.Copy)
+
+    def step_a4():
+        ts(b("El"), ind("L", 1024, "cl"), -1.0, A.mult, 2047.0, A.add)
+
+    def act_1():
+        act(b("VB"), ind("BT", 1024, "vl"), F.Copy)
+        act(b("VBo"), b("VB"), F.Copy, scale=col(3))
+        gram("VB", "VBo", "VB", True)
+
+    def act_2(stand=False):
+        act(b("EA", 0, 512), b("pg0"), F.Relu, bias=-15.0)
+        ts(b("EA", 512, 1024), b("pg1"), 15.5, A.is_gt)
+        if stand:
+            gram("VB", "VBo", "CB", False)
+        mm([(b("pc", 0, 128), band(x), b("EA", 128 * x, 128 * x + 128), x == 0, x == 7) for x in range(8)])
+
+    last = (RO_ - 1, S_ - 1)
+
+    def stood():
+        act(b("CB"), ind("BT", 1024, "cl"), F.Copy)
+        gram("VB", "VBo", "CB", False)
+
+    def xq(q):
+        act(b("XQ", 512 * q, 512 * q + 512), ind("X", 2064, "Ql", 32 * q, 32 * q + 32), F.Copy)
+
+    def df(q):
+        tt(b("DF", 512 * q, 512 * q + 512), ind("X", 2064, "El", 32 * q, 32 * q + 32), b("XQ", 512 * q, 512 * q + 512), A.subtract)
+
+    def ab(q):
+        act(b("AB", 512 * q, 512 * q + 512), b("DF", 512 * q, 512 * q + 512), F.Abs)
+
+    def es(h):
+        ts(b("ES", 512 * h, 512 * h + 512), b("pg%d" % h), 15.5, A.is_gt)
+
+    def words():
+        tt(b("CMV"), b("VC", 8, 16), b("VC", 0, 8), A.subtract)
+        tt(b("DMC"), b("DUM", 0, 8), b("VC", 8, 16), A.subtract)
+        tt(b("VCD"), b("VC"), b("DD"), A.subtract)
+
+    def step(r, s):
+        leafc = (r, s) != last
+        first = r == 0 and s == 0
+        QE = "QE%d" % (3 * r + s)
+        yF, yL, yC = b("py", 0, 128), b("py", 128, 256), b("pm", 256, 384)
+
+        def dist(h):
+            mm([(b("pd", 0, 128), b("ImB"), b("NA"), False, False) if h else (b("pd", 0, 128), b("IB"), b("KGE"), True, False)] + [(b("pd", 64 * h, 64 * h + 64), b("CONV", 128 * k, 128 * k + 128), b("AB", 1024 * h + k, 1024 * h + 1024, 16), False,
+                   h == 1 and k == 15) for k in range(16)])
+
+        def y_pre():
+            mm([(b("py", 0, 256), b("I"), b("Y0", 0, 256), True, False),
+                (yF, b("Im128"), b("NA"), False, False), (yL, b("Dm64"), b("KGE"), False, False),
+                (yF, b("I64"), b("NN"), False, False), (yL, b("I64"), b("NN"), False, False)])
+            mm([(yC, b("I"), b("Y0", 0, 128), True, False), (yC, b("D64"), b("KGE"), False, False), (yC, b("I64"), b("NN"), False, False)])
+
+        if s == 0:
+            step_a4()
+            round_rest(r)
+            xq(2)
+            df(0)
+            ab(0)
+            if first:
+                xq(3)
+                consts_b()
+                for h in range(2):
+                    gram_mask(h)
+                act_1()
+                df(1)
+                ab(1)
+                df(2)
+                act_2()
+                stood()
+                consts_c()
+                ab(2)
+                df(3)
+                ab(3)
+                dist(0)
+                act(b("NA"), b("pc", 0, 128), F.Sign)
+                es(0)
+                es(1)
+            else:
+                act_2()
+                df(1)
+                xq(3)
+                ab(1)
+                stood()
+                df(2)
+                dist(0)
+                ab(2)
+                df(3)
+                es(0)
+                act(b("NA"), b("pc", 0, 128), F.Sign)
+                es(1)
+                ab(3)
+        else:
+            xq(0)
+            df(0)
+            act_2(True)
+            xq(1)
+            ab(0)
+            df(1)
+            xq(2)
+            ab(1)
+            es(0)
+            df(2)
+            es(1)
+            dist(0)
+            xq(3)
+            act(b("NA"), b("pc", 0, 128), F.Sign)
+            ab(2)
+            if len(fills) == 4:
+                fill(2)
+        if (r, s) == last:
+            fills.extend([lambda: hash_a(r), lambda: hash_b(r), lambda: hash_c(r)])
+        elif s == 0 and r:
+            fills.extend([lambda: unmade_m(r - 1), lambda: unmade(r - 1)])
+        if len(fills) > 2 or s == 0:
+            fill()
+        mm([(b("pc", 128, 256), band(x), b("ES", 128 * x, 128 * x + 128), x == 0, x == 7) for x in range(8)])
+        ts(b("NN"), b("El"), 2047.0, A.is_equal)
+        if leafc:
+            tt(b("T1"), b("pm", 256, 384), b("N01", 256 * r + 128, 256 * r + 256), A.subtract)
+        y_pre()
+        if s:
+            df(3)
+            ab(3)
+        ts(b("STD"), b("pc", 128, 256), 0.5, A.is_gt)
+        mm([(yC, b("I64"), b("STD"), False, False)])
+        dist(1)
+        late = len(fills) > 0
+        fill(9)
+        if not late:
+            for h in range(2):
+                gram_mask(h)
+        act(b("uE"), ind("L", 1024, "cl"), F.Copy)
+        if leafc:
+            act(b("CV"), ind("C", 1024, "vl"), F.Copy)
+        if r == 0:
+            act(b("Cc"), ind("C", 1024, "cl"), F.Copy)
+        ST, FS, LF, CU = (b("BUF", 128 * i, 128 * i + 128) for i in range(4))
+        ts(ST, b("pd", 0, 128), BIG + 620.5, A.is_gt)
+        mm([(yC, b("STRI"), ST, False, True)])
+        mm([(yF, b("STRI"), ST, False, False), (yL, b("STRI"), ST, False, True)])
+        mm([(b("ps", 0, 128), b("TRI64"), ST, True, False)])
+        if late:
+            gram_mask(0)
+        words()
+        tt(CU, yC, ST, A.is_le)
+        tt(b(QE, 0, 128), CU, b("uQ"), A.mult)
+        mm([(b("pm", 0, 128), b(QE, 0, 128), b("BO"), True, True)])
+        tt(FS, yF, ST, A.is_le)
+        mm([(b("ps", 0, 128), b("BO64"), FS, False, True)])
+        if late:
+            gram_mask(1)
+        tt(LF, yL, ST, A.is_le)
+        tt(b("mkq", 0, 128), b("pm", 0, 128), b("MSK"), A.mult)
+        mm([(b("pm", 384, 392), b("mkq", 0, 128), b("SEL"), True, True)])
+        mm([(b("pd", 128, 384), b("TRI"), b("BUF", 256, 512), True, True)])
+        tt(b(QE, 128, 256), CU, b("uE"), A.mult)
+        mm([(b("pm", 128, 256), b(QE, 128, 256), b("BO"), True, True)])
+        mm([(b("pw", 0, 32), b("CONV", 128 * m, 128 * m + 128), b("BUF", m, 512, 16), m == 0, m == 15) for m in range(16)])
+        if (r, s) != last:
+            tt(b("P"), b("ps", 0, 128), b("P"), A.min)
+            act(b("KGE"), b("P"), F.Sign)
+        if (r, s) == last:
+            tt(b("KGE"), b("ps", 0, 128), b("KGE"), A.min)
+        ts(b("qel", 0, 8), b("pm", 384, 392), -1.0, A.mult, 2047.0, A.add)
+        if (r, s) == last:
+            tt(b("HK"), b("KGE"), b("HMQ"), A.mult)
+            tt(b("SND"), b("HK"), b("QF"), A.add)
+            travel("SND", "LAND1", "1")
+        elif s == S_ - 1:
+            travel("KGE", "LK", "0")
+        if leafc:
+            tt(b("T2"), b("T1"), b("OH"), A.mult)
+        tt(b("X2"), b("pd", 256, 384), b("uE"), A.mult)
+        tt(b("X1"), b("pd", 128, 256), b("uQ"), A.mult)
+        act(b("QB"), ind("BT", 2048, "qel", 0, 8), F.Copy)
+        act(b("QBo"), b("QB"), F.Copy, scale=col(3))
+        act(b("QLF"), b("pm", 384, 392), F.Copy, bias=2047.0, scale=-1.0)
+        act(b("XQg"), ind("X", 2064, "qel", 0, 8), F.Copy)
+        gram("QB", "QBo", "QB", True)
+        if s < S_ - 1:
+            mm([(b("ps", 128, 256), b("BO"), b("P"), True, False), (b("ps", 128, 256), b("BOm16"), b("KGE"), False, True)])
+        tt(b("mkq", 128, 256), b("pm", 128, 256), b("MSK"), A.mult)
+        mm([(b("pm", 392, 400), b("mkq", 128, 256), b("SEL"), True, True)])
+        act(b("ED", 0, 512), b("pg0"), F.Relu, bias=-15.0)
+        act(b("ED", 512, 1024), b("pg1"), F.Relu, bias=-15.0)
+        if s < S_ - 1:
+            for h in range(2):
+                gram_mask(h)
+        tt(b("l1"), b("pw", 16, 32), b("VCD"), A.mult)
+        tt(b("l2"), b("l1"), b("DD"), A.add)
+        cp(b("lc"), b("l2"))
+        if s < S_ - 1:
+            ts(b("WF"), b("pw", 0, 16), 0.5, A.is_lt)
+            tt(b("w6"), b("pw", 16, 32), b("DUM"), A.mult)
+            tt(b("x1"), b("WF", 0, 8), b("DMC"), A.mult)
+            tt(b("x2"), b("x1"), b("CMV"), A.add)
+            tt(b("x3"), b("WF", 8, 16), b("x2"), A.mult)
+            tt(b("x4"), b("x3"), b("VC", 0, 8), A.add)
+            tt(b("y1"), b("x4"), b("w6", 0, 8), A.max)
+            tt(b("VC", 0, 8), b("y1"), b("w6", 8, 16), A.max)
+            cp(b("vl"), b("VC", 0, 8))
+        ts(b("qel", 8, 16), b("pm", 392, 400), -1.0, A.mult, 2047.0, A.add)
+        act(b("XLg"), ind("X", 2064, "qel", 8, 16), F.Copy)
+        n1 = 384 + 256 * r
+        mm([(b("pc", 256 + 16 * x, 272 + 16 * x), b("ED", 128 * x, 128 * x + 128), b("ONES", 0, 16), True, True) for x in range(8)])
+        if leafc:
+            tt(ind("C", 1152, "lc", 0, 8), b("CV"), b("T2"), A.subtract)
+        if s < S_ - 1:
+            ts(b("OH"), b("ps", 128, 256), col(2), A.is_equal)
+            step_a1()
+        mm([(b("ps", 128, 256), b("I"), b("XQg"), True, False), (b("ps", 128, 256), b("I"), b("XLg"), False, True)])
+        act(b("DS"), b("ps", 128, 256), F.Copy, bias=2.0 ** 23, scale=0.5 - 2.0 ** -12)
+        act(b("DH"), b("DS"), F.Copy, bias=-2.0 ** 23)
+        if s < S_ - 1:
+            step_a2()
+        tt(b("X3"), b("pd", 256, 384), b("uQ"), A.mult)
+        if s == S_ - 1 and r == 0:
+            hash_a(r)
+            hash_b(r)
+        tt(b("mk2"), b("pc", 256, 384), b("MSK"), A.mult)
+        mm([(b("pw", 64, 72), b("mk2"), b("SELB"), True, True)])
+        mm([(b("ps", 256, 384), b("I"), b("X3"), True, True), (b("ps", 384, 512), b("I"), b("X1"), True, False),
+            (b("ps", 384, 512), b("I32"), b("X2"), False, True)])
+        if s < S_ - 1:
+            step_a3()
+            act_1()
+        if s == S_ - 1 and r == 0:
+            hash_c(r)
+        tt(b("d1"), b("pw", 64, 72), b("QLF"), A.max)
+        tt(b("d2"), b("d1"), b("DTOK"), A.min)
+        cp(b("didx"), b("d2"))
+        cp(ind("X", 2192, "didx"), b("DH"))
+        if (r, s) == last:
+            cp(b("X", 2047, 2048), b("xsave", 0, 1))
+            dma("Y", T.yd[:], T.X[:, 0:2048], r=[b("X", 0, 2048)])
+        tt(ind("L", 1152, "lc", 8, 16), b("uE"), b("X2"), A.subtract)
+        tt(b("L", n1, n1 + 256), b("ps", 256, 512), b("L", n1, n1 + 256), A.add)
+        if s < S_ - 1:
+            step_a4()
+        if r == 0 or s == 0:
+            fills.extend([lambda: def_m(r, s), lambda: def_a(r, s), lambda: def_b(r, s), lambda: def_c(r, s)])
+        if s == S_ - 1:
+            fill(9)
+        if (r, s) == last:
+            unmade_m(r)
+            unmade(r)
+
+    def travel(src, land, tag):
+        sent = [0]
+        deps("G", [b(src)], [], "loc" + tag, 0)
+        for call in plan(core, T.cores, topo):
+            tr = []
+            for d, en in call:
+                e = (T.rank_of(d) - rank) % 8
+                rid, pid = topo.addr(d, core)
+                tr.append(RemoteDMATransfer(dst_ids=[DstId(rid=rid, pnc=pid)], dma_engine_mask=sum(1 << x for x in en),
+                                            remote_sem=T.sem["arr" + tag], src=T[src][:, 16 * e:16 * e + 16],
+                                            dst=T[land][:, 16 * e:16 * e + 16]))
+                sent[0] += len(en)
+            g.remote_dma_fused(tr, local_sem=T.sem["loc" + tag])
+        cp(b(land, 0, 16), b(src, 0, 16))
+        n = sum(len(en) for s in T.cores if s != core for call in plan(s, T.cores, topo) for d, en in call if d == core)
+        K["acc"].setdefault(land, []).append((16, 128, 1, "R", "arr" + tag, n, True))
+        K["acc"].setdefault(src, []).append((0, 128, 0, "R", "loc" + tag, sent[0], True))
+        K["final"]["arr" + tag] = n
+        K["final"]["loc" + tag] = sent[0]
+
+    for r in range(RO_):
+        round_start(r)
+        if r == 0:
+            cp(b("C", 0, 384), b("Ci"))
+        step_a1()
+        if r == 0:
+            ts(b("L", 0, 384), b("Ei"), -1.0, A.mult, 2047.0, A.add)
+            cp(b("lsave", 0, 1), b("L", 0, 1))
+            ms(b("L", 0, 1), -1.0)
+            ms(b("X", 2048, 2192), 512.0)
+            cp(b("xsave", 0, 1), b("X", 2047, 2048))
+            ms(b("X", 2047, 2048), 4096.0)
+            xq(0)
+        step_a2()
+        step_a3(True)
+        if r == 0:
+            xq(1)
+        else:
+            for h in range(2):
+                gram_mask(h)
+            act_1()
+        for s in range(S_):
+            step(r, s)
+    act(b("YE", 0, 384), b("L", 0, 384), F.Copy, bias=2047.0, scale=-1.0)
+    act(b("YE", 0, 1), b("lsave", 0, 1), F.Copy, bias=2047.0, scale=-1.0)
+    for r in range(RO_):
+        n1 = 384 + 256 * r
+        for j, o in ((128, 0), (0, 1)):
+            act(b("YE", n1 + o, n1 + 256, 2), b("L", n1 + j, n1 + j + 128), F.Copy, bias=2047.0, scale=-1.0)
+    dma("S", T.ye[:], T.YE[:], r=[b("YE")])
+    dma("Y", T.yr[:], T.LAND1[:], r=[b("LAND1")])
+    for s, v in K["final"].items():
+        K["known"]["G"].pop(s, None)
+        wait("G", s, v)

@@ -4,18 +4,14 @@ from concourse.mybir import AluOpType as A, ActivationFunctionType as F
 S_, RO_ = 3, 2
 F32, BF, H16, I32, U16 = "float32", "bfloat16", "float16", "int32", "uint16"
 SCRATCH = {}
-
-
 PLACE = {}
 
 
 def _b(name, n, d, where="sbuf"):
     pool = {F32: "poolf", U16: "poolu", I32: "pooli"}.get(d)
-    if name.startswith("QE"):
-        pool = "poolq"
-    elif n > 16 or where != "sbuf":
-        pool = None
-    if pool is None:
+    if isinstance(n, list):
+        SCRATCH[name] = (where, [128] + n, d)
+    elif n > 40 or where != "sbuf" or pool is None:
         SCRATCH[name] = (where, [128, n], d)
         PLACE[name] = (name, 0, n)
     else:
@@ -24,61 +20,50 @@ def _b(name, n, d, where="sbuf"):
         PLACE[name] = (pool, at, n)
 
 
-_b("X", 2192, BF); _b("L", 1152, F32); _b("C", 1152, F32); _b("BT", 2048, BF)
-_b("Ei", 384, I32); _b("Ci", 384, I32); _b("Qi", 128, I32); _b("xsave", 16, BF); _b("lsave", 4, F32)
-_b("IQ", 128, I32); _b("IP", 1, I32); _b("IC", 4, I32); _b("R4i", 256, I32); _b("Qb", 128, BF); _b("Q4b", 256, BF)
-_b("cols", 16, F32); _b("flip", 16, F32); _b("BO", 128, BF); _b("R", 128, BF); _b("CONV", 2048, BF)
-for _n in ("I", "TRI", "STRI", "SHD", "SHU", "D64", "Dm64", "DQ", "I64", "Im128", "IB", "ImB", "TRI64", "BO64", "BOm16", "BOm1",
-           "MSK", "B0", "ONES", "tmpc", "tmpd", "tmpe"):
-    _b(_n, 128, BF)
-_b("I32", 128, F32); _b("SEL", 8, BF); _b("SELB", 8, BF); _b("MASKN", 512, BF); _b("BAND", 240, BF); _b("Y0", 384, BF)
-_b("W8", 8, F32); _b("DUM", 16, F32); _b("DD", 16, F32); _b("DTOK", 8, F32); _b("N01", 512, F32)
-_b("Qi2", 128, I32); _b("QF", 128, F32); _b("Ql", 128, U16); _b("Q4i", 128, I32); _b("Q4m", 128, H16); _b("QMi", 128, I32)
-_b("QM", 128, H16); _b("uQ", 128, H16); _b("Q16", 128, H16); _b("HP", 128, I32); _b("HI", 128, I32); _b("HM", 128, F32)
-_b("HMQ", 128, F32); _b("HK", 128, F32); _b("SND", 128, F32); _b("LQ", 128, F32); _b("LK", 128, BF); _b("LAND1", 128, F32)
-_b("vl", 8, U16); _b("cl", 8, U16); _b("VC", 16, F32); _b("OH", 128, F32); _b("P", 128, BF); _b("KGE", 128, BF)
-_b("M1", 128, H16); _b("mk", 128, H16); _b("mkq", 256, H16); _b("El", 128, U16); _b("XQ", 2048, BF); _b("DF", 2048, BF)
-_b("AB", 2048, BF); _b("VB", 128, BF); _b("VBo", 128, BF); _b("CB", 128, BF); _b("CV", 128, F32); _b("Cc", 128, F32)
-_b("uE", 128, F32); _b("EA", 1024, BF); _b("ED", 1024, BF); _b("ES", 1024, BF); _b("NA", 128, BF); _b("STD", 128, BF)
-_b("NN", 128, BF); _b("T1", 128, F32); _b("T2", 128, F32); _b("BUF", 512, H16)
-for _n in range(6):
-    _b("QE%d" % _n, 256, H16)
-_b("CMV", 8, F32); _b("DMC", 8, F32); _b("VCD", 16, F32); _b("WF", 16, F32); _b("x1", 8, F32); _b("x2", 8, F32)
-_b("x3", 8, F32); _b("x4", 8, F32); _b("w6", 16, F32); _b("y1", 8, F32); _b("l1", 16, F32); _b("l2", 16, F32)
-_b("lc", 16, U16); _b("qel", 16, U16); _b("QLF", 8, F32); _b("QB", 128, BF); _b("QBo", 128, BF)
-_b("XLg", 128, BF); _b("XQg", 128, BF); _b("DS", 128, F32); _b("DH", 128, F32); _b("mk2", 128, H16); _b("d1", 8, F32); _b("d2", 8, F32)
-_b("didx", 8, U16); _b("X1", 128, H16); _b("X2", 128, F32); _b("X3", 128, H16); _b("X5", 128, F32)
-_b("RI", 128, I32); _b("RA", 128, I32); _b("RW", 16, I32); _b("RL", 16, U16); _b("IDT", 32, F32); _b("OHc", 256, F32); _b("OHN", 256, F32); _b("YE", 896, F32)
-PS = ["pg0", "pg1", "pc", "pm", "pd", "py", "ps", "pw"]
+XW, LL = 2320, 137
+for _d, _l in (
+    (BF, "X:2320 XQ:2048 DF:2064 BO:128 BOH:128 I:128 I2:128 Im:128 IH:128 IR:128 B0:128 SHD:128 CONV:2048 ZH:272 ZL:272 OHZ:272 TRZ:272 "
+         "IDZ:272 OHB:272 KD:128 KT:128 KE:576 KA:576 KB:18 K3:137 M16:137 RD:137 RMP:137 OH:128 AD:576 RA:576 SG:128 SS:128 XQg:128 "
+         "DFg:128 DH:128 KGE:128 LK:128 xsave:16"),
+    (F32, "L:1152 C:1152 STD:1152 IOT:2064 W1:137 W2:137 W3:137 W4:137 W3n:137 S1:137 S2:137 S3:137 S4:137 QF:128 uQ0:128 uQ1:128 LQ:128 "
+          "LAND1:128 SND:128 HM:128 HMQ:128 HK:128 uE:128 CV:128 T2:128 SC:128 SE:128 SQ:128 tcol:128 vcol:128 DS:128 WN:384 WC:384 "
+          "OHN:256 X5:128 YE:896 cols:12 THR:6 LC:40 lsave:2 v0:8 v1:8 zs0:8 zs1:8 zacc:8 cf:8 cmv:8 athr:8 aleaf:8 acut:8 nf:8 x1:8 x2:8 "
+          "x3:8 zp:8 T0:8 T1:8 TL:8 Ap:8 G:8 M0:8 M:32 U:32 zcf:8 dn:8 y1:8 y2:8 y3:8 y4:8 y5:8 y6:8 q2:16 q1:8 q0:8 dd:8"),
+    (H16, "Q16:128 Q1:128 N16:256 B620:137 M1:128 EQ:576 RE:576 EL:128 Y:128"),
+    (I32, "Qi:128 Ci:384 Ei:384 QI:137 QA:137 HP:128 HI:128 RI:128 RJ:128 IP:2 IC:2 qi:8 qj:16 RW:8"),
+    (U16, "Ql:128 El:128 vz0:16 vz1:16 cl:8 tq:8 pos:8 UU0:32 UU1:32 sl:8 se0:8 se1:8 za:8 didx:8"),
+):
+    for _x in _l.split():
+        _b(_x.split(":")[0], int(_x.split(":")[1]), _d)
+_b("AB", [128, 17], BF); _b("QX", [8, 8, 16], H16); _b("XS", [3, 8], F32)
+PS = ["pd", "pm", "pt", "ps", "pq", "pe", "pw"]
 for _n in PS:
     _b(_n, 512, F32, "psum")
 SEMAPHORES = ["sV", "sT", "sS", "sG", "locE", "loc0", "loc1", "arrE", "arr0", "arr1"] + ["d%d" % _i for _i in range(12)]
-NDUM, NDUMP, TDUMP, BIG = 896, 1024, 2064, float(2 ** 17)
+NDUM, NDUMP, TDUMP, BIG, HH = 896, 1024, 2050, float(2 ** 22), float(2 ** 22)
+FAR, NONE = 294.0, 560.0
+HOP, FLY = 240, 3000
+ORDER = []
 
 
 def make(g, T):
     eng = {"V": g.vector, "S": g.scalar, "T": g.tensor, "G": g, "Y": g.sync}
     tick = {"V": 0, "S": 0, "T": 0, "G": 0}
     known = {q: {} for q in eng}
-    snap, acc, final, ndma = {}, {}, {}, [0]
+    snap, acc, final, ndma, ops = {}, {}, {}, [0], []
 
     def ap(x):
+        if not isinstance(x, tuple):
+            return x
         if x[0] == "@":
             return ap(x[1]).indirect(ap(x[2]))
-        t = T[x[0]]
-        st = x[3] if len(x) > 3 else 1
-        p0, p1 = (x[4], x[5]) if len(x) > 4 else (0, 128)
-        return t[p0:p1, x[1]:x[2]:st] if st != 1 else t[p0:p1, x[1]:x[2]]
+        return T[x[0]][x[3]]
 
     def flat(xs):
         out = []
         for x in xs:
-            if x is None or isinstance(x, (int, float)):
-                continue
-            if x[0] == "@":
-                out += [x[1], x[2]]
-            else:
-                out.append(x)
+            if isinstance(x, tuple):
+                out += [x[1], x[2]] if x[0] == "@" else [x]
         return out
 
     def wait(q, sem, val):
@@ -102,22 +87,86 @@ def make(g, T):
                     if ps:
                         if eq == q and (q == "T" or not (isw or ew) or ehi <= lo or hi <= elo):
                             continue
-                    else:
-                        if ehi <= lo or hi <= elo or not (isw or ew):
-                            continue
+                    elif ehi <= lo or hi <= elo or not (isw or ew):
+                        continue
                     need[es] = max(need.get(es, 0), ev)
         for s in sorted(need, key=lambda z: z == "s" + q):
             wait(q, s, need[s])
         for isw, xs in ((0, reads), (1, writes)):
             for x in xs:
                 n, lo, hi = x[0], x[1], x[2]
-                full = len(x) < 5
                 l = acc.setdefault(n, [])
-                if isw and full and n not in PS and (len(x) < 4 or x[3] == 1):
+                if isw and x[4] and n not in PS:
                     l[:] = [e for e in l if not (lo <= e[0] and e[1] <= hi)]
                 else:
                     l[:] = [e for e in l if not (e[3] == q and not e[6] and not dma and e[0] == lo and e[1] == hi and e[2] == isw)]
                 l.append((lo, hi, isw, q, sem, val, dma))
+
+    def size(x):
+        if x[0] == "@":
+            return 16 * size(x[2])
+        n = 1
+        for i, d in zip(x[3][1:], SCRATCH[x[0]][1][1:]):
+            n *= 1 if isinstance(i, int) else len(range(*i.indices(d)))
+        return n
+
+    def cycles(q, out, ins, both):
+        full = [x for x in ins if isinstance(x, tuple) and size(x) == size(out)]
+        if out[0] == "@" or any(x[0] == "@" for x in full):
+            return 70 + size(out) * (3.8 if out[0] == "@" else 1.56)
+        if q == "G":
+            return 180 + 2 * size(out)
+        f = 2 if both and all(x[0] not in PS for x in full) else 1
+        if q == "V" and not both and all(SCRATCH[x[0]][2] in (BF, H16, U16) for x in full + [out]):
+            f = 0.5
+        return max(64, f * size(out))
+
+    def call(q, out, ins, f, both=False):
+        w, r = ([out[1]], [out[2]]) if out[0] == "@" else ([out], [])
+        r = flat(ins) + r
+
+        def emit():
+            deps(q, r, w, "s" + q, tick[q] + 1)
+            fin(q, f())
+        ops.append((q, r, w, cycles(q, out, ins, both), HOP, emit))
+
+    def order():
+        seen, pred = {}, []
+        for i, (q, r, w, c, lat, emit) in enumerate(ops):
+            p = set()
+            for isw, xs in ((0, r), (1, w)):
+                for x in xs:
+                    for lo, hi, ew, j in seen.get(x[0], []):
+                        if x[0] in PS or (lo < x[2] and x[1] < hi and (isw or ew)):
+                            p.add(j)
+            for isw, xs in ((0, r), (1, w)):
+                for x in xs:
+                    l = seen.setdefault(x[0], [])
+                    if x[0] in PS or (isw and x[4]):
+                        l[:] = [e for e in l if x[0] not in PS and not (x[1] <= e[0] and e[1] <= x[2])]
+                    l.append((x[1], x[2], isw, i))
+            pred.append(p - {i})
+        gap = lambda j, i: 0 if ops[j][0] == ops[i][0] == "T" else ops[j][4]
+        level = [op[3] + op[4] for op in ops]
+        for i in reversed(range(len(ops))):
+            for j in pred[i]:
+                level[j] = max(level[j], ops[j][3] + gap(j, i) + level[i])
+        start, busy = {}, {q: [] for q in eng}
+        for i in sorted(range(len(ops)), key=lambda i: (-level[i], i)):
+            t, c, l = max([start[j] + ops[j][3] + gap(j, i) for j in pred[i]] + [0]), ops[i][3], busy[ops[i][0]]
+            at = 0
+            while at < len(l) and l[at][0] < t + c:
+                t = max(t, l[at][1])
+                at += 1
+            l.insert(at, (t, t + c))
+            start[i] = t
+        return sorted(range(len(ops)), key=lambda i: (start[i], i))
+
+    def flush():
+        if not ORDER:
+            ORDER.extend(order())
+        for i in ORDER:
+            ops[i][5]()
 
     def fin(q, ins):
         sem = "s" + q
@@ -126,68 +175,58 @@ def make(g, T):
         final[sem] = tick[q]
         ins.then_inc(T.sem[sem], 1)
 
-    def pre(q, reads, writes):
-        deps(q, flat(reads), flat(writes), "s" + q, tick[q] + 1)
-
-    def wr(out):
-        return ([out[1]], [out[2]]) if out[0] == "@" else ([out], [])
-
     def tt(out, a, b, op):
-        w, r = wr(out)
-        pre("V", [a, b] + r, w)
-        fin("V", g.vector.tensor_tensor(ap(out), ap(a), ap(b), op))
+        call("V", out, [a, b], lambda: g.vector.tensor_tensor(ap(out), ap(a), ap(b), op), True)
 
     def ts(out, a, s1, op0, s2=None, op1=None):
-        pre("V", [a, s1, s2], [out])
-        f = lambda s: ap(s) if isinstance(s, tuple) else s
-        if op1 is None:
-            fin("V", g.vector.tensor_scalar(ap(out), ap(a), f(s1), None, op0))
-        else:
-            fin("V", g.vector.tensor_scalar(ap(out), ap(a), f(s1), f(s2), op0, op1))
+        more = () if op1 is None else (op1,)
+        call("V", out, [a, s1, s2], lambda: g.vector.tensor_scalar(ap(out), ap(a), ap(s1), ap(s2), op0, *more))
 
     def cp(out, a):
-        w, r = wr(out)
-        pre("V", [a] + r, w)
-        fin("V", g.vector.tensor_copy(ap(out), ap(a)))
+        call("V", out, [a], lambda: g.vector.tensor_copy(ap(out), ap(a)))
 
     def ms(out, c):
-        pre("V", [], [out])
-        fin("V", g.vector.memset(ap(out), c))
+        call("V", out, [], lambda: g.vector.memset(ap(out), c))
 
-    def act(out, a, func, bias=0.0, scale=1.0):
-        pre("S", [a, scale], [out])
-        sc = ap(scale) if isinstance(scale, tuple) else scale
-        fin("S", g.scalar.activation(ap(out), ap(a), func, bias=bias, scale=sc))
+    def scan(out, d0, d1, init, op0, op1):
+        call("V", out, [d0, d1], lambda: g.vector.tensor_tensor_scan(ap(out), ap(d0), ap(d1), init, op0, op1))
 
-    def iota(out, pattern, base, cm, fl=False):
-        pre("G", [], [out])
-        if fl:
-            fin("G", g.iota(ap(out), pattern, base, cm, allow_small_or_imprecise_dtypes=True))
+    def act(out, a, func=F.Copy, bias=0.0, scale=1.0):
+        if out[0] == "@":
+            call("S", out, [a], lambda: g.scalar.activation(ap(out), ap(a), func))
         else:
-            fin("G", g.iota(ap(out), pattern, base, cm))
+            call("S", out, [a, bias, scale], lambda: g.scalar.activation(ap(out), ap(a), func, bias=ap(bias), scale=ap(scale)))
+
+    def iota(out, pattern, base, cm, fl=True):
+        kw = dict(allow_small_or_imprecise_dtypes=True) if fl else {}
+        call("G", out, [], lambda: g.iota(ap(out), pattern, base, cm, **kw))
 
     def sel(out, a, pattern, op, base, cm):
-        pre("G", [a], [out])
-        fin("G", g.affine_select(ap(out), ap(a), pattern, op, 0.0, base, cm))
+        call("G", out, [a], lambda: g.affine_select(ap(out), ap(a), pattern, op, 0.0, base, cm))
 
-    def mm(lst):
-        pre("T", [x[1] for x in lst] + [x[2] for x in lst], [x[0] for x in lst])
-        for i, (o, l, r, st, sp) in enumerate(lst):
-            ins = g.tensor.matmul(ap(o), ap(l), ap(r), st, sp)
-            if i == len(lst) - 1:
-                fin("T", ins)
-        return tick["T"]
+    def mm(*lst):
+        r, w = [x[1] for x in lst] + [x[2] for x in lst], [x[0] for x in lst]
+
+        def emit():
+            deps("T", r, w, "sT", tick["T"] + 1)
+            for o, lt, rh, st, sp in lst:
+                ins = g.tensor.matmul(ap(o), ap(lt), ap(rh), st, sp)
+            fin("T", ins)
+        ops.append(("T", r, w, sum(max(64, size(x[0])) for x in lst) / 2, HOP, emit))
 
     def dma(q, out, in_, r=(), w=()):
         sem = "d%d" % ndma[0]
         ndma[0] += 1
-        deps(q, list(r), list(w), sem, 16, True)
-        snap[(sem, 16)] = dict(known[q])
-        final[sem] = 16
-        eng[q].dma_start(out, in_).then_inc(T.sem[sem], 16)
 
-    return dict(tt=tt, ts=ts, cp=cp, ms=ms, act=act, iota=iota, sel=sel, mm=mm, dma=dma, wait=wait, deps=deps, known=known,
-                final=final, acc=acc)
+        def emit():
+            deps(q, list(r), list(w), sem, 16, True)
+            snap[(sem, 16)] = dict(known[q])
+            final[sem] = 16
+            eng[q].dma_start(out, in_).then_inc(T.sem[sem], 16)
+        ops.append((q, list(r), list(w), 120, FLY + size((list(r) + list(w))[0]), emit))
+
+    return dict(tt=tt, ts=ts, cp=cp, ms=ms, scan=scan, act=act, iota=iota, sel=sel, mm=mm, dma=dma, wait=wait, deps=deps,
+                known=known, final=final, acc=acc, ops=ops, flush=flush)
 
 
 def plan(src, cores, topo):
@@ -206,473 +245,281 @@ def rank_program(g, core, T, topo):
     if rank is None:
         return
     K = make(g, T)
-    tt, ts, cp, ms, act, iota, sel, mm, dma, wait, deps = (K[x] for x in ("tt", "ts", "cp", "ms", "act", "iota", "sel", "mm", "dma", "wait", "deps"))
+    tt, ts, cp, ms, scan, act, iota, sel, mm, dma, wait, deps = (
+        K[x] for x in ("tt", "ts", "cp", "ms", "scan", "act", "iota", "sel", "mm", "dma", "wait", "deps"))
+    al = slice(None)
 
     def b(n, lo=0, hi=None, st=1):
         n, at, size = PLACE[n]
         lo, hi = at + lo, at + (size if hi is None else hi)
-        return (n, lo, hi, st) if st != 1 else (n, lo, hi)
+        return (n, lo, hi, (al, slice(lo, hi, st) if st > 0 else slice(hi - 1, lo - 1, st)), abs(st) == 1)
+
+    def nd(n, lo, hi, *idx):
+        return (n, lo, hi, (al,) + idx, False)
 
     def col(j):
         return b("cols", j, j + 1)
 
     def ind(w, hi, o, lo=0, oh=None):
-        return ("@", (w, 0, hi), b(o, lo, oh))
+        return ("@", b(w, 0, hi), b(o, lo, oh))
 
-    def part(x, p0, p1):
-        return (x[0], x[1], x[2], 1, p0, p1)
+    def rev(n):
+        return b(n, 1, LL, -1)
 
-    fills = []
+    def at0(n):
+        return b(n, 1, LL, 17)
 
-    def fill(n=1):
-        for _ in range(n):
-            if fills:
-                fills.pop(0)()
+    def diag(out, src):
+        scan(b(out), b("KD"), src, 0.0, A.mult, A.max)
+        return b(out, 15, 128, 16)
+
+    def seg(c):
+        return (144 * c if c < 4 else 144 * (7 - c) + 16 * (8 - c)), 16 * c + 16
+
+    ends = lambda n: (b(n, 14, 576, 160), b(n, 142, 575, -144))
+    CS = col(4)
+    DT, DD, DUM = b("LC", 0, 8), b("LC", 8, 16), b("LC", 32, 40)
 
     dma("Y", T.Qi[:], T.req[:], w=[b("Qi")])
     dma("S", T.Ci[:], T.child[:], w=[b("Ci")])
     dma("Y", T.Ei[:], T.edge[:], w=[b("Ei")])
     dma("S", T.X[:, 0:1024], T.desc[:, 0:1024], w=[b("X", 0, 1024)])
     dma("Y", T.X[:, 1024:2048], T.desc[:, 1024:2048], w=[b("X", 1024, 2048)])
-    iota(b("IP"), [[1, 1]], 0, 1)
-    iota(b("IQ"), [[1, 128]], 0, 0)
-    iota(b("C", NDUM, NDUMP), [[1, 128]], NDUM, 0, True)
-    ms(b("L", 384, 1024), 0.0)
-    ts(b("IC", 0, 1), b("IP"), 4, A.arith_shift_right)
-    ts(b("IC", 1, 2), b("IP"), 15, A.bitwise_and)
-    ts(b("IC", 2, 3), b("IP"), 4, A.arith_shift_right, 1, A.bitwise_and)
-    ts(b("R4i", 0, 128), b("IQ"), 4, A.arith_shift_right)
-    ts(b("R4i", 128, 256), b("IQ"), 15, A.bitwise_and)
-    cp(col(0), b("IP"))
-    cp(b("cols", 1, 4), b("IC", 0, 3))
-    cp(b("Qb"), b("IQ"))
-    cp(b("Q4b"), b("R4i"))
-    QMb = b("Q4b", 128, 256)
-    ts(col(5), col(2), 0.0, A.is_equal)
-    ts(col(8), col(0), -1.0, A.add)
-    ts(b("BO"), b("Q4b", 0, 128), col(1), A.is_equal)
-    ts(b("I"), b("Qb"), col(0), A.is_equal)
-    ts(b("MSK"), QMb, col(2), A.is_equal)
-    ts(b("SEL"), b("Qb", 0, 8), col(1), A.is_equal)
-    ts(b("B0"), b("BO"), col(5), A.mult)
-    for n, op, base in (("SHU", A.is_equal, 1), ("TRI", A.is_ge, 0), ("STRI", A.is_gt, 0), ("SHD", A.is_equal, -1)):
-        sel(b(n), b("BO"), [[1, 128]], op, base, -1)
-    for m in range(16):
-        sel(b("CONV", 128 * m, 128 * m + 128), b("BO"), [[0, 8], [1, 16]], A.is_equal, -m, 0)
-    iota(b("N01", 0, 256), [[1, 256]], 384, 0, True)
-    iota(b("N01", 256, 512), [[1, 256]], 640, 0, True)
-    for n, src, c in (("I64", "I", 64.0), ("Im128", "I", -128.0), ("IB", "I", BIG), ("ImB", "I", -BIG), ("I32", "I", 1.0),
-                      ("BO64", "BO", 64.0), ("BOm16", "BO", -16.0), ("BOm1", "BO", -1.0), ("SELB", "SEL", 4096.0)):
-        act(b(n), b(src), F.Copy, scale=c)
-    ms(b("C", 384, NDUM), 0.0)
+
+    def consts_a():
+        iota(b("IP", 0, 1), [[1, 1]], 0, 1, False)
+        iota(b("ZH"), [[1, 17], [0, 16]], 0, 0)
+        iota(b("ZL"), [[0, 17], [1, 16]], 0, 0)
+        iota(b("IOT", 0, 256), [[1, 256]], 0, 0)
+        iota(b("C", NDUM, NDUMP), [[1, 128]], NDUM + 1, 0)
+        ts(b("IC", 0, 1), b("IP", 0, 1), 4, A.arith_shift_right)
+        ts(b("IC", 1, 2), b("IP", 0, 1), 15, A.bitwise_and)
+        cp(col(0), b("IP", 0, 1))
+        cp(b("cols", 1, 3), b("IC"))
+        ms(b("C", 384, NDUM), 1.0)
+        ms(b("L", 384, 1152), 0.0)
+        ts(col(3), col(2), 1.0, A.add)
+        ts(col(5), col(2), 0.0, A.is_equal)
+        ts(col(7), col(2), 14.5, A.is_lt, 4095.0, A.mult)
+        ts(b("BO"), b("ZH", 0, 128), col(1), A.is_equal)
+        ts(col(7), col(7), 1.0, A.add)
+        ts(col(4), col(2), 14.5, A.is_gt, 1.0 - 2.0 ** -12, A.mult)
+        ts(b("B0"), b("BO"), col(5), A.mult)
+        ts(col(4), col(4), 2.0 ** -12, A.add)
+        ts(b("KD"), b("ZL", 0, 128), col(2), A.is_gt)
+        ts(b("KT"), b("ZL", 0, 128), col(3), A.is_equal, 4095.0, A.mult)
+        ts(b("OHZ"), b("ZL"), col(2), A.is_equal)
+        tt(b("KD"), b("KD"), b("KT"), A.add)
+        act(b("BOH"), b("BO"), scale=-HH)
 
     def consts_b():
-        ms(b("KGE"), 1.0)
-        ms(b("BT", 0, 1), -1.0)
-        ts(b("flip"), b("Qb", 0, 16), col(2), A.is_equal, -2.0, A.mult)
-        ts(b("flip"), b("flip"), 1.0, A.add)
-        n = 1
-        for i in range(11):
-            ts(b("BT", n, 2 * n), b("BT", 0, n), b("flip", i, i + 1), A.mult)
-            n *= 2
-        tt(b("tmpe"), b("I"), b("SHD"), A.subtract)
-        for n, src, c in (("TRI64", "TRI", 64.0), ("D64", "tmpe", 64.0), ("Dm64", "tmpe", -64.0)):
-            act(b(n), b(src), F.Copy, scale=c)
-        for i in range(4):
-            ts(b("MASKN", 128 * i, 128 * i + 128), b("Qb"), col(0), A.is_le, -64.0, A.mult)
-        ms(b("BAND"), 0.0)
-        ms(b("BAND", 112, 128), 1.0)
+        iota(b("LC", 0, 8), [[32, 8]], TDUMP, 2)
+        iota(b("LC", 8, 24), [[0, 2], [16, 8]], NDUMP, 1)
+        iota(b("LC", 32, 40), [[16, 8]], NDUM, 1)
+        iota(b("IOT", 256, 1152), [[1, 896]], 256, 0)
+        for m in range(16):
+            sel(b("CONV", 128 * m, 128 * m + 128), b("BOH"), [[0, 8], [1, 16]], A.is_equal, -m, 0)
+            if m == 7:
+                iota(b("K3", 1, LL), [[0, 8], [16, 17]], 0, 0)
+                iota(b("W4", 1, LL), [[256, 8], [1, 17]], 0, 16)
+                iota(b("THR"), [[256, 6]], 192, 0)
+        iota(b("IOT", 1152, 2064), [[1, 912]], 1152, 0)
+        iota(nd("XS", 0, 24, al, al), [[128, 3], [16, 8]], 1152, 1)
+        sel(b("SHD"), b("BO"), [[1, 128]], A.is_equal, -1, -1)
 
     def consts_c():
-        ms(b("ONES"), 1.0)
-        ms(b("Y0"), 1.0)
-        ms(b("Y0", 128, 256), 65.0)
-        ts(b("W8"), b("Qb", 0, 8), 16.0, A.mult, col(2), A.add)
-        for h in (0, 8):
-            ts(b("DUM", h, h + 8), b("W8"), float(NDUM), A.add)
-            ts(b("DD", h, h + 8), b("W8"), float(NDUMP), A.add)
-        ts(b("DTOK"), b("W8"), float(TDUMP), A.add)
-        ts(col(4), col(2), -1.0, A.mult, 15.0, A.add)
+        ts(b("cols", 8, 9), col(1), -16.0, A.mult)
+        ts(b("cols", 9, 10), col(1), -32.0, A.mult)
+        ts(b("cols", 10, 11), col(1), -256.0, A.mult)
         ts(col(6), col(2), 0.0, A.is_gt)
-        ts(b("IDT", 0, 16), b("Qb", 0, 16), col(4), A.is_equal)
+        ts(b("I"), b("IOT", 0, 128), col(0), A.is_equal)
+        ts(b("IDZ"), b("ZH"), col(2), A.is_equal)
+        ts(b("TRZ"), b("ZH"), col(2), A.is_le)
+        ts(b("LC", 0, 8), b("LC", 0, 8), col(9), A.add)
+        ts(b("LC", 8, 24), b("LC", 8, 24), col(8), A.add)
+        ts(b("LC", 32, 40), b("LC", 32, 40), col(8), A.add)
+        ms(b("LC", 24, 32), 256.0)
+        ms(b("KE"), 0.0)
+        ts(b("KB", 0, 16), b("OHZ", 0, 16), 4096.0, A.mult)
+        ms(b("KB", 16, 17), -8192.0)
+        ts(b("KB", 15, 16), b("KB", 15, 16), -4096.0, A.add)
+        for c in range(8):
+            o, n = seg(c)
+            cp(b("KE", o + n - 16 - (c > 0), o + n), b("KB", 1 - (c > 0), 17))
+        ts(b("KA"), b("KE"), -1.0, A.mult)
 
-    def round_start(r):
-        src = b("Qi") if r == 0 else b("QF")
-        if r:
-            tt(b("HK"), b("LK"), b("HMQ"), A.mult)
-            tt(b("QF"), b("HK"), b("LQ"), A.add)
-        cp(b("Ql"), src)
-        qi = src
-        if r:
-            xq(0)
-            xq(1)
-            qi = b("Qi2")
-            cp(qi, src)
-        ts(b("Q4i"), qi, 4, A.arith_shift_right)
-        ts(b("Q4m"), b("Q4i"), col(5), A.mult)
-        mm([(b("pm", 0, 128), b("Q4m"), b("BO"), True, True)])
-        ts(b("QMi"), qi, 15, A.bitwise_and)
-        cp(b("QM"), b("QMi"))
-        if r == 0:
-            tt(b("DQ"), b("I"), b("SHU"), A.subtract)
-        tt(b("mk"), b("pm", 0, 128), b("MSK"), A.mult)
-        mm([(b("pm", 128, 136), b("mk"), b("SEL"), True, True)])
-        mm([(b("ps", 128, 256), b("B0"), b("QM"), True, True)])
-        mm([(b("pw", 0, 128), b("DQ"), b("QM"), True, True)])
-        cp(b("vl"), b("pm", 128, 136))
-        act(b("VC", 0, 8), b("pm", 128, 136), F.Copy)
-        ts(b("OH"), b("ps", 128, 256), col(2), A.is_equal)
+    def consts_d():
+        for n, c in (("IH", HH / 2), ("IR", 2.0 ** 37), ("I2", 2.0), ("Im", -1.0)):
+            ts(b(n), b("I"), c, A.mult)
+        ms(b("M16"), -16.0)
+        ms(b("RD"), 0.0)
+        ms(b("DF", 2048, 2064), 0.0)
+        ms(nd("AB", 0, 2176, al, slice(16, 17)), NONE)
+        ts(b("B620"), b("M16"), 0.0, A.mult, 1241.0, A.add)
+        ts(b("W4", 1, LL), b("W4", 1, LL), col(10), A.add)
+        ts(b("THR"), b("THR"), col(7), A.mult)
 
-    def round_rest(r):
-        ts(b("P"), b("pw", 0, 128), 16.0, A.add)
-        if r:
-            ms(b("KGE"), 1.0)
-        else:
-            cp(b("QF"), b("Qi"))
-            travel("QF", "LQ", "E")
-        ts(b("uQ"), b("QF"), -1.0, A.mult, 2047.0, A.add)
+    def consts_e():
+        ts(b("N16", 0, 128), b("IOT", 0, 128), 513.0, A.add)
+        ts(b("N16", 128, 256), b("IOT", 0, 128), 769.0, A.add)
+        ms(b("IOT", 2048, 2049), -1.0)
+        ts(nd("XS", 0, 24, al, al), nd("XS", 0, 24, al, al), col(8), A.add)
+        ts(b("OHB"), b("OHZ"), 4095.0, A.mult, 1.0, A.add)
+        ms(b("WC", 128, 256), 1.0)
 
-    hsrc = lambda r: b("QF" if r else "LQ")
+    def roots(r, src):
+        vz = "vz%d" % r
+        ts(b("Q1"), src, 1.0, A.add)
+        mm((b("pw", 0, 128), b("B0"), b("Q1"), True, True))
+        ts(b("qi"), diag("SQ", b("pw", 0, 128)), CS, A.mult, -1.0, A.add)
+        ts(b("qj", 0, 8), b("qi"), 4, A.arith_shift_right)
+        ts(b("qj", 8, 16), b("qi"), 15, A.bitwise_and)
+        cp(b(vz), b("qj"))
+        cp(b("v%d" % r), b("qj", 0, 8))
+        ts(b("zs%d" % r), b("qj", 8, 16), 4096.0, A.mult)
 
-    def hash_a(r):
-        cp(b("Q16"), hsrc(r))
-        mm([(b("pw", 0, 128), b("SHD"), b("Q16"), True, True)])
+    def row(r):
+        act(b("OH"), ind("OHZ", 272, "vz%d" % r, 8, 16))
 
-    def hash_b(r):
-        tt(b("HP"), b("pw", 0, 128), hsrc(r), A.mult)
-        ts(b("HI"), b("HP"), 5, A.arith_shift_right, 2047, A.bitwise_and)
-        ts(b("HM"), b("HI"), 2046.5, A.is_lt)
+    def child_1(r):
+        tt(b("M1"), ind("C", 1024, "vz%d" % r, 0, 8), b("OH"), A.mult)
+        mm((b("pm", 0, 128), b("BO"), b("M1"), True, True))
 
-    def hash_c(r):
-        tt(b("HMQ"), b("HI"), b("HM"), A.mult)
-        tt(b("HMQ"), b("HMQ"), hsrc(r), A.subtract)
-        ts(b("HMQ"), b("HMQ"), col(6), A.mult)
+    def child_2():
+        ts(b("cl"), diag("SC", b("pm", 0, 128)), CS, A.mult, -1.0, A.add)
 
-    def gram_mask(h):
-        mm([(b("pg%d" % h), b("I"), b("MASKN"), True, False)])
-
-    def gram(left, lefto, right, masked):
-        done = {}
-        for y in range(2):
-            for h in range(2):
-                l = []
-                for x in (2 * y, 2 * y + 1):
-                    gr = 4 * h + x
-                    p0 = 32 * (gr // 2)
-                    p1 = p0 + (32 if gr % 2 else 16)
-                    l.append((b("pg%d" % h, 128 * x, 128 * x + 128), part(b(lefto if gr % 2 else left), p0, p1), part(b(right), p0, p1),
-                              not masked, not masked or x == 3))
-                if y:
-                    wait("T", "sT", done[h])
-                done[h] = mm(l)
-
-    def band(gr):
-        return b("BAND", 112 - 16 * gr, 240 - 16 * gr)
-
-    def def_m(r, s):
-        if r == 0:
-            mm([(b("pg1", 384, 512), b("BO"), b("BUF", 384, 512), True, True)])
-
-    def def_a(r, s):
-        cp(b("RW"), b("pm", 384, 400))
-        ts(b("RW"), b("RW"), 15, A.bitwise_and)
-        cp(b("RL"), b("RW"))
-        for h in range(2):
-            act(b("OHc", 128 * h, 128 * h + 128), ind("IDT", 16, "RL", 8 * h, 8 * h + 8), F.Copy)
-
-    def def_b(r, s):
-        if r == 0:
-            n0 = 384 + 256 * r + 128
-            tt(b("X5"), b("pg1", 384, 512), b("Cc"), A.mult)
-            tt(b("C", n0, n0 + 128), b("C", n0, n0 + 128), b("X5"), A.add)
-        tt(b("OHN"), b("OHc"), b("N01", 256 * r, 256 * r + 256), A.mult)
-
-    def def_c(r, s):
-        tt(ind("C", 1152, "lc", 8, 16), b("OHN", 0, 128), b("OHN", 128, 256), A.max)
-
-    def unmade_m(r):
-        l = []
-        for s in range(S_):
-            q = "QE%d" % (3 * r + s)
-            l += [(b("pg0", 256, 384), b("BO"), b(q, 0, 128), s == 0, False), (b("pg0", 256, 384), b("BOm1"), b(q, 128, 256), False, s == S_ - 1)]
-        mm(l)
-
-    def unmade(r):
-        n1 = 384 + 256 * r
-        cp(b("RI", 0, 128), b("pg0", 256, 384))
-        ts(b("RA", 0, 128), b("RI", 0, 128), 15, A.bitwise_and)
-        ts(b("X5"), b("RA", 0, 128), 0.5, A.is_gt)
-        tt(b("L", n1, n1 + 128), b("L", n1, n1 + 128), b("X5"), A.mult)
-
-    def step_a1():
-        tt(b("M1"), ind("C", 1024, "vl"), b("OH"), A.mult)
-        mm([(b("pm", 0, 128), b("M1"), b("BO"), True, True)])
-
-    def step_a2():
-        tt(b("mk"), b("pm", 0, 128), b("MSK"), A.mult)
-        mm([(b("pm", 128, 136), b("mk"), b("SEL"), True, True), (b("pm", 256, 384), b("BO"), b("M1"), True, True)])
-
-    def step_a3(late=False):
-        cp(b("cl"), b("pm", 128, 136))
-        act(b("VC", 8, 16), b("pm", 128, 136), F.Copy)
-        if not late:
-            act(b("CB"), ind("BT", 1024, "cl"), F.Copy)
-
-    def step_a4():
+    def child_3():
         ts(b("El"), ind("L", 1024, "cl"), -1.0, A.mult, 2047.0, A.add)
 
-    def act_1():
-        act(b("VB"), ind("BT", 1024, "vl"), F.Copy)
-        act(b("VBo"), b("VB"), F.Copy, scale=col(3))
-        gram("VB", "VBo", "VB", True)
+    def child_4(r, leaf):
+        ts(b("cf"), b("SC", 15, 128, 16), CS, A.mult, -1.0, A.add)
+        tt(b("cmv"), b("cf"), b("v%d" % r), A.subtract)
+        if leaf:
+            mm((b("pt", 0, 128), b("BO"), b("M1"), True, False), (b("pt", 0, 128), b("Im"), b("N16", 128 * r, 128 * r + 128), False, True))
+            tt(b("T2"), b("pt", 0, 128), b("OH"), A.mult)
 
-    def act_2(stand=False):
-        act(b("EA", 0, 512), b("pg0"), F.Relu, bias=-15.0)
-        ts(b("EA", 512, 1024), b("pg1"), 15.5, A.is_gt)
-        if stand:
-            gram("VB", "VBo", "CB", False)
-        mm([(b("pc", 0, 128), band(x), b("EA", 128 * x, 128 * x + 128), x == 0, x == 7) for x in range(8)])
+    def acts_1(r):
+        act(b("vcol"), ind("IOT", 1024, "vz%d" % r, 0, 8))
+        for c in range(8):
+            o, n = seg(c)
+            act(b("AD", o, o + n), b("vcol", 0, n), F.Abs, bias=b("v%d" % r, c, c + 1), scale=-1.0)
 
-    last = (RO_ - 1, S_ - 1)
+    def acts_2(r, s):
+        v, zs = b("v%d" % r), b("zs%d" % r)
+        scan(b("RA"), b("AD"), b("KA"), 8192.0, A.min, A.add)
+        tt(b("x1"), zs, v, A.subtract)
+        for h, e in enumerate(ends("RA")):
+            ts(b("athr", 4 * h, 4 * h + 4), e, 0.5, A.is_lt, BIG, A.mult)
+        ts(b("x3"), zs, 4096.0, A.add)
+        tt(b("x2"), b("athr"), v, A.max)
+        tt(b("aleaf"), b("x1"), b("athr"), A.subtract)
+        tt(b("x2"), b("x2"), DD, A.min)
+        tt(b("x3"), b("x3"), b("athr"), A.add)
+        cp(b("sl"), b("x2"))
 
-    def stood():
-        act(b("CB"), ind("BT", 1024, "cl"), F.Copy)
-        gram("VB", "VBo", "CB", False)
+    def stood_1(r, s):
+        o = 256 * (3 * r + s + 1)
+        act(ind("STD", 1152, "sl"), b("IOT", o, o + 128), F.Silu)
+        act(b("SG"), ind("STD", 1024, "cl"))
+
+    def stood_2(r, s):
+        ts(b("nf"), diag("SS", b("SG")), b("THR", 3 * r + s, 3 * r + s + 1), A.is_gt, BIG, A.mult)
+        tt(b("acut"), b("x3"), b("nf"), A.add)
+
+    def payload_1():
+        for x in range(8):
+            ts(nd("QX", 0, 1024, al, x, al), b("Q16"), b("BO", 16 * x, 16 * x + 1), A.mult)
+        mm(*[(b("pq", 1 + 17 * c, 18 + 17 * c), nd("QX", 0, 1024, c, al, al), b("IDZ", 0, 272, 16), True, True) for c in range(8)])
+
+    def payload_2():
+        cp(b("QI", 1, LL), b("pq", 1, LL))
+        ts(b("QA", 1, LL), b("QI", 1, LL), 15, A.bitwise_and)
+        tt(b("W3n", 1, LL), b("QA", 1, LL), b("K3", 1, LL), A.add)
+        act(b("W3", 1, LL), b("W3n", 1, LL), scale=4096.0)
+        act(b("W2", 1, LL), b("W3n", 1, LL), scale=4096.0, bias=-4096.0 * HH)
+
+    def payload_3():
+        tt(b("W1", 1, LL), b("pq", 1, LL), b("W3", 1, LL), A.add)
+
+    def hash_a(r):
+        if r == 0:
+            cp(b("Q16"), b("LQ"))
+        mm((b("pw", 0, 128), b("SHD"), b("Q16"), True, True))
+
+    def hash_b(r):
+        src = b("QF" if r else "LQ")
+        tt(b("HP"), b("pw", 0, 128), src, A.mult)
+        ts(b("HI"), b("HP"), 5, A.arith_shift_right, 2047, A.bitwise_and)
+        ts(b("HM"), b("HI"), 2046.5, A.is_lt)
+        tt(b("HMQ"), b("HI"), b("HM"), A.mult)
+        tt(b("HMQ"), b("HMQ"), src, A.subtract)
+        if r:
+            act(b("HMQ"), b("HMQ"), scale=col(6))
+
+    def ramp(r):
+        act(at0("RD"), b("zs%d" % r), F.Relu, bias=-15.0, scale=2.0 ** -12)
+        scan(b("RMP", 1, LL), b("M16", 1, LL), b("RD", 1, LL), 0.0, A.add, A.max)
+
+    def dist_0(s):
+        mm((b("pd", 1, LL), b("IH"), b("B620", 1, LL), True, False), *([(b("pd", 1, LL), b("IR"), b("RMP", 1, LL), False, False)] if s else []))
+
+    def dist(h):
+        mm(*[(b("pd", 1 + 68 * h, 69 + 68 * h), b("CONV", 128 * p, 128 * p + 128),
+              nd("AB", 1088 * h, 1088 * h + 1088, slice(64 * h + p, 64 * h + 64, 16), al), False, h == 1 and p == 15) for p in range(16)])
 
     def xq(q):
-        act(b("XQ", 512 * q, 512 * q + 512), ind("X", 2064, "Ql", 32 * q, 32 * q + 32), F.Copy)
+        act(b("XQ", 512 * q, 512 * q + 512), ind("X", 2064, "Ql", 32 * q, 32 * q + 32))
 
     def df(q):
         tt(b("DF", 512 * q, 512 * q + 512), ind("X", 2064, "El", 32 * q, 32 * q + 32), b("XQ", 512 * q, 512 * q + 512), A.subtract)
 
     def ab(q):
-        act(b("AB", 512 * q, 512 * q + 512), b("DF", 512 * q, 512 * q + 512), F.Abs)
+        act(nd("AB", 544 * q, 544 * q + 544, slice(32 * q, 32 * q + 32), slice(0, 16)), b("DF", 512 * q, 512 * q + 512), F.Abs)
 
-    def es(h):
-        ts(b("ES", 512 * h, 512 * h + 512), b("pg%d" % h), 15.5, A.is_gt)
-
-    def words():
-        tt(b("CMV"), b("VC", 8, 16), b("VC", 0, 8), A.subtract)
-        tt(b("DMC"), b("DUM", 0, 8), b("VC", 8, 16), A.subtract)
-        tt(b("VCD"), b("VC"), b("DD"), A.subtract)
-
-    def step(r, s):
-        leafc = (r, s) != last
-        first = r == 0 and s == 0
-        QE = "QE%d" % (3 * r + s)
-        yF, yL, yC = b("py", 0, 128), b("py", 128, 256), b("pm", 256, 384)
-
-        def dist(h):
-            mm([(b("pd", 0, 128), b("ImB"), b("NA"), False, False) if h else (b("pd", 0, 128), b("IB"), b("KGE"), True, False)] + [(b("pd", 64 * h, 64 * h + 64), b("CONV", 128 * k, 128 * k + 128), b("AB", 1024 * h + k, 1024 * h + 1024, 16), False,
-                   h == 1 and k == 15) for k in range(16)])
-
-        def y_pre():
-            mm([(b("py", 0, 256), b("I"), b("Y0", 0, 256), True, False),
-                (yF, b("Im128"), b("NA"), False, False), (yL, b("Dm64"), b("KGE"), False, False),
-                (yF, b("I64"), b("NN"), False, False), (yL, b("I64"), b("NN"), False, False)])
-            mm([(yC, b("I"), b("Y0", 0, 128), True, False), (yC, b("D64"), b("KGE"), False, False), (yC, b("I64"), b("NN"), False, False)])
-
-        if s == 0:
-            step_a4()
-            round_rest(r)
-            xq(2)
-            df(0)
-            ab(0)
-            if first:
-                xq(3)
-                consts_b()
-                for h in range(2):
-                    gram_mask(h)
-                act_1()
-                df(1)
-                ab(1)
-                df(2)
-                act_2()
-                stood()
-                consts_c()
-                ab(2)
-                df(3)
-                ab(3)
-                dist(0)
-                act(b("NA"), b("pc", 0, 128), F.Sign)
-                es(0)
-                es(1)
-            else:
-                act_2()
-                df(1)
-                xq(3)
-                ab(1)
-                stood()
-                df(2)
-                dist(0)
-                ab(2)
-                df(3)
-                es(0)
-                act(b("NA"), b("pc", 0, 128), F.Sign)
-                es(1)
-                ab(3)
-        else:
-            xq(0)
-            df(0)
-            act_2(True)
-            xq(1)
-            ab(0)
-            df(1)
-            xq(2)
-            ab(1)
-            es(0)
-            df(2)
-            es(1)
-            dist(0)
-            xq(3)
-            act(b("NA"), b("pc", 0, 128), F.Sign)
-            ab(2)
-            if len(fills) == 4:
-                fill(2)
-        if (r, s) == last:
-            fills.extend([lambda: hash_a(r), lambda: hash_b(r), lambda: hash_c(r)])
-        elif s == 0 and r:
-            fills.extend([lambda: unmade_m(r - 1), lambda: unmade(r - 1)])
-        if len(fills) > 2 or s == 0:
-            fill()
-        mm([(b("pc", 128, 256), band(x), b("ES", 128 * x, 128 * x + 128), x == 0, x == 7) for x in range(8)])
-        ts(b("NN"), b("El"), 2047.0, A.is_equal)
-        if leafc:
-            tt(b("T1"), b("pm", 256, 384), b("N01", 256 * r + 128, 256 * r + 256), A.subtract)
-        y_pre()
-        if s:
-            df(3)
-            ab(3)
-        ts(b("STD"), b("pc", 128, 256), 0.5, A.is_gt)
-        mm([(yC, b("I64"), b("STD"), False, False)])
-        dist(1)
-        late = len(fills) > 0
-        fill(9)
-        if not late:
-            for h in range(2):
-                gram_mask(h)
-        act(b("uE"), ind("L", 1024, "cl"), F.Copy)
-        if leafc:
-            act(b("CV"), ind("C", 1024, "vl"), F.Copy)
+    def cut_1(r, s):
+        uu, n0 = "UU%d" % (s % 2), 512 + 256 * r
+        tt(b("EL"), ind("IDZ", 272, uu, 16, 24), b("WN", 0, 128), A.mult)
+        mm((b("pe", 0, 128), b("BO"), b("EL"), True, True))
         if r == 0:
-            act(b("Cc"), ind("C", 1024, "cl"), F.Copy)
-        ST, FS, LF, CU = (b("BUF", 128 * i, 128 * i + 128) for i in range(4))
-        ts(ST, b("pd", 0, 128), BIG + 620.5, A.is_gt)
-        mm([(yC, b("STRI"), ST, False, True)])
-        mm([(yF, b("STRI"), ST, False, False), (yL, b("STRI"), ST, False, True)])
-        mm([(b("ps", 0, 128), b("TRI64"), ST, True, False)])
-        if late:
-            gram_mask(0)
-        words()
-        tt(CU, yC, ST, A.is_le)
-        tt(b(QE, 0, 128), CU, b("uQ"), A.mult)
-        mm([(b("pm", 0, 128), b(QE, 0, 128), b("BO"), True, True)])
-        tt(FS, yF, ST, A.is_le)
-        mm([(b("ps", 0, 128), b("BO64"), FS, False, True)])
-        if late:
-            gram_mask(1)
-        tt(LF, yL, ST, A.is_le)
-        tt(b("mkq", 0, 128), b("pm", 0, 128), b("MSK"), A.mult)
-        mm([(b("pm", 384, 392), b("mkq", 0, 128), b("SEL"), True, True)])
-        mm([(b("pd", 128, 384), b("TRI"), b("BUF", 256, 512), True, True)])
-        tt(b(QE, 128, 256), CU, b("uE"), A.mult)
-        mm([(b("pm", 128, 256), b(QE, 128, 256), b("BO"), True, True)])
-        mm([(b("pw", 0, 32), b("CONV", 128 * m, 128 * m + 128), b("BUF", m, 512, 16), m == 0, m == 15) for m in range(16)])
-        if (r, s) != last:
-            tt(b("P"), b("ps", 0, 128), b("P"), A.min)
-            act(b("KGE"), b("P"), F.Sign)
-        if (r, s) == last:
-            tt(b("KGE"), b("ps", 0, 128), b("KGE"), A.min)
-        ts(b("qel", 0, 8), b("pm", 384, 392), -1.0, A.mult, 2047.0, A.add)
-        if (r, s) == last:
-            tt(b("HK"), b("KGE"), b("HMQ"), A.mult)
-            tt(b("SND"), b("HK"), b("QF"), A.add)
-            travel("SND", "LAND1", "1")
-        elif s == S_ - 1:
-            travel("KGE", "LK", "0")
-        if leafc:
-            tt(b("T2"), b("T1"), b("OH"), A.mult)
-        tt(b("X2"), b("pd", 256, 384), b("uE"), A.mult)
-        tt(b("X1"), b("pd", 128, 256), b("uQ"), A.mult)
-        act(b("QB"), ind("BT", 2048, "qel", 0, 8), F.Copy)
-        act(b("QBo"), b("QB"), F.Copy, scale=col(3))
-        act(b("QLF"), b("pm", 384, 392), F.Copy, bias=2047.0, scale=-1.0)
-        act(b("XQg"), ind("X", 2064, "qel", 0, 8), F.Copy)
-        gram("QB", "QBo", "QB", True)
-        if s < S_ - 1:
-            mm([(b("ps", 128, 256), b("BO"), b("P"), True, False), (b("ps", 128, 256), b("BOm16"), b("KGE"), False, True)])
-        tt(b("mkq", 128, 256), b("pm", 128, 256), b("MSK"), A.mult)
-        mm([(b("pm", 392, 400), b("mkq", 128, 256), b("SEL"), True, True)])
-        act(b("ED", 0, 512), b("pg0"), F.Relu, bias=-15.0)
-        act(b("ED", 512, 1024), b("pg1"), F.Relu, bias=-15.0)
-        if s < S_ - 1:
-            for h in range(2):
-                gram_mask(h)
-        tt(b("l1"), b("pw", 16, 32), b("VCD"), A.mult)
-        tt(b("l2"), b("l1"), b("DD"), A.add)
-        cp(b("lc"), b("l2"))
-        if s < S_ - 1:
-            ts(b("WF"), b("pw", 0, 16), 0.5, A.is_lt)
-            tt(b("w6"), b("pw", 16, 32), b("DUM"), A.mult)
-            tt(b("x1"), b("WF", 0, 8), b("DMC"), A.mult)
-            tt(b("x2"), b("x1"), b("CMV"), A.add)
-            tt(b("x3"), b("WF", 8, 16), b("x2"), A.mult)
-            tt(b("x4"), b("x3"), b("VC", 0, 8), A.add)
-            tt(b("y1"), b("x4"), b("w6", 0, 8), A.max)
-            tt(b("VC", 0, 8), b("y1"), b("w6", 8, 16), A.max)
-            cp(b("vl"), b("VC", 0, 8))
-        ts(b("qel", 8, 16), b("pm", 392, 400), -1.0, A.mult, 2047.0, A.add)
-        act(b("XLg"), ind("X", 2064, "qel", 8, 16), F.Copy)
+            act(b("WC", 256, 384), b("C", n0, n0 + 128))
+            act(b("C", n0, n0 + 128), ind("WC", 384, "se%d" % (s % 2)))
+
+    def cut_2(r, s):
+        uu = "UU%d" % (s % 2)
+        ts(b("RW"), diag("SE", b("pe", 0, 128)), CS, A.mult)
+        ts(b("RW"), b("RW"), 15, A.bitwise_and)
+        ts(b(uu, 24, 32), b("RW"), -1.0, A.mult, 15.0, A.add)
+
+    def cut_3(r, s):
+        uu, n1 = "UU%d" % (s % 2), 384 + 256 * r
+        tt(b("OHN"), ind("OHB", 272, uu, 16, 32), b("IOT", n1 + 1, n1 + 257), A.min)
+        tt(ind("C", 1152, uu, 0, 8), b("OHN", 0, 128), b("OHN", 128, 256), A.max)
+
+    def second(r, lst):
+        tt(b("L", 384 + 256 * r, 512 + 256 * r), ("@", b("TRZ"), lst), b("uQ%d" % r), A.mult)
+
+    def unmade_1(r):
+        tt(b("Y"), b("L", 512 + 256 * r, 640 + 256 * r), b("uQ%d" % r), A.subtract)
+        tt(b("EL"), ind("IDZ", 272, "za"), b("Y"), A.mult)
+        mm((b("pe", 0, 128), b("BO"), b("EL"), True, True))
+
+    def unmade_2(r):
         n1 = 384 + 256 * r
-        mm([(b("pc", 256 + 16 * x, 272 + 16 * x), b("ED", 128 * x, 128 * x + 128), b("ONES", 0, 16), True, True) for x in range(8)])
-        if leafc:
-            tt(ind("C", 1152, "lc", 0, 8), b("CV"), b("T2"), A.subtract)
-        if s < S_ - 1:
-            ts(b("OH"), b("ps", 128, 256), col(2), A.is_equal)
-            step_a1()
-        mm([(b("ps", 128, 256), b("I"), b("XQg"), True, False), (b("ps", 128, 256), b("I"), b("XLg"), False, True)])
-        act(b("DS"), b("ps", 128, 256), F.Copy, bias=2.0 ** 23, scale=0.5 - 2.0 ** -12)
-        act(b("DH"), b("DS"), F.Copy, bias=-2.0 ** 23)
-        if s < S_ - 1:
-            step_a2()
-        tt(b("X3"), b("pd", 256, 384), b("uQ"), A.mult)
-        if s == S_ - 1 and r == 0:
-            hash_a(r)
-            hash_b(r)
-        tt(b("mk2"), b("pc", 256, 384), b("MSK"), A.mult)
-        mm([(b("pw", 64, 72), b("mk2"), b("SELB"), True, True)])
-        mm([(b("ps", 256, 384), b("I"), b("X3"), True, True), (b("ps", 384, 512), b("I"), b("X1"), True, False),
-            (b("ps", 384, 512), b("I32"), b("X2"), False, True)])
-        if s < S_ - 1:
-            step_a3()
-            act_1()
-        if s == S_ - 1 and r == 0:
-            hash_c(r)
-        tt(b("d1"), b("pw", 64, 72), b("QLF"), A.max)
-        tt(b("d2"), b("d1"), b("DTOK"), A.min)
-        cp(b("didx"), b("d2"))
-        cp(ind("X", 2192, "didx"), b("DH"))
-        if (r, s) == last:
-            cp(b("X", 2047, 2048), b("xsave", 0, 1))
-            dma("Y", T.yd[:], T.X[:, 0:2048], r=[b("X", 0, 2048)])
-        tt(ind("L", 1152, "lc", 8, 16), b("uE"), b("X2"), A.subtract)
-        tt(b("L", n1, n1 + 256), b("ps", 256, 512), b("L", n1, n1 + 256), A.add)
-        if s < S_ - 1:
-            step_a4()
-        if r == 0 or s == 0:
-            fills.extend([lambda: def_m(r, s), lambda: def_a(r, s), lambda: def_b(r, s), lambda: def_c(r, s)])
-        if s == S_ - 1:
-            fill(9)
-        if (r, s) == last:
-            unmade_m(r)
-            unmade(r)
+        cp(b("RI"), b("pe", 0, 128))
+        ts(b("RJ"), b("RI"), 15, A.bitwise_and)
+        ts(b("X5"), b("RJ"), 4096.0, A.mult)
+        tt(b("L", n1, n1 + 128), b("L", n1, n1 + 128), b("X5"), A.min)
 
     def travel(src, land, tag):
+        act(b(land, 0, 16), b(src, 0, 16))
+        K["ops"].append(("G", [b(src)], [b(land, 16, 128)], 1400, FLY, lambda: send(src, land, tag)))
+
+    def send(src, land, tag):
         sent = [0]
         deps("G", [b(src)], [], "loc" + tag, 0)
-        for call in plan(core, T.cores, topo):
+        for calls in plan(core, T.cores, topo):
             tr = []
-            for d, en in call:
+            for d, en in calls:
                 e = (T.rank_of(d) - rank) % 8
                 rid, pid = topo.addr(d, core)
                 tr.append(RemoteDMATransfer(dst_ids=[DstId(rid=rid, pnc=pid)], dma_engine_mask=sum(1 << x for x in en),
@@ -680,44 +527,219 @@ def rank_program(g, core, T, topo):
                                             dst=T[land][:, 16 * e:16 * e + 16]))
                 sent[0] += len(en)
             g.remote_dma_fused(tr, local_sem=T.sem["loc" + tag])
-        cp(b(land, 0, 16), b(src, 0, 16))
-        n = sum(len(en) for s in T.cores if s != core for call in plan(s, T.cores, topo) for d, en in call if d == core)
+        n = sum(len(en) for s in T.cores if s != core for calls in plan(s, T.cores, topo) for d, en in calls if d == core)
         K["acc"].setdefault(land, []).append((16, 128, 1, "R", "arr" + tag, n, True))
         K["acc"].setdefault(src, []).append((0, 128, 0, "R", "loc" + tag, sent[0], True))
         K["final"]["arr" + tag] = n
         K["final"]["loc" + tag] = sent[0]
 
-    for r in range(RO_):
-        round_start(r)
-        if r == 0:
-            cp(b("C", 0, 384), b("Ci"))
-        step_a1()
-        if r == 0:
-            ts(b("L", 0, 384), b("Ei"), -1.0, A.mult, 2047.0, A.add)
-            cp(b("lsave", 0, 1), b("L", 0, 1))
-            ms(b("L", 0, 1), -1.0)
-            ms(b("X", 2048, 2192), 512.0)
-            cp(b("xsave", 0, 1), b("X", 2047, 2048))
-            ms(b("X", 2047, 2048), 4096.0)
+    def step(r, s):
+        first, end, last = (r, s) == (0, 0), s == S_ - 1, (r, s) == (RO_ - 1, S_ - 1)
+        prev = (r, s - 1) if s and (r == 0 or s == 1) else None
+        v, zs, vz, uu, se = b("v%d" % r), b("zs%d" % r), "vz%d" % r, "UU%d" % (s % 2), "se%d" % (s % 2)
+        n0 = 512 + 256 * r
+        if not first:
             xq(0)
-        step_a2()
-        step_a3(True)
-        if r == 0:
-            xq(1)
+        xq(1)
+        if s:
+            ramp(r)
+        df(0)
+        if first:
+            consts_d()
+        if s:
+            acts_1(r)
+        dist_0(s)
+        child_4(r, not last) if not first else None
+        ab(0)
+        if s == 0:
+            if r:
+                cp(b("Q16"), b("QF"))
+            payload_1()
+        df(1)
+        xq(2)
+        if s or first:
+            acts_2(r, s)
+        if prev:
+            cut_1(*prev)
+        ab(1)
+        df(2)
+        xq(3)
+        dist(0)
+        stood_1(r, s)
+        if s == 0:
+            payload_2()
+        if first:
+            consts_e()
+            child_4(r, True)
+        if prev:
+            cut_2(*prev)
+        ab(2)
+        df(3)
+        stood_2(r, s)
+        ab(3)
+        dist(1)
+        if last:
+            cp(b("X", 2047, 2048), b("xsave", 0, 1))
+        if s == 0:
+            payload_3()
+            ts(b("uQ%d" % r), b("QF"), -1.0, A.mult, 2047.0, A.add)
+            act(b("WN", 128, 256), b("uQ%d" % r))
         else:
-            for h in range(2):
-                gram_mask(h)
-            act_1()
-        for s in range(S_):
-            step(r, s)
-    act(b("YE", 0, 384), b("L", 0, 384), F.Copy, bias=2047.0, scale=-1.0)
-    act(b("YE", 0, 1), b("lsave", 0, 1), F.Copy, bias=2047.0, scale=-1.0)
+            tt(b("WN", 128, 256), ind("TRZ", 272, vz, 8, 16), b("uQ%d" % r), A.mult)
+        if prev:
+            cut_3(*prev)
+        if s == 1:
+            second(r, b("UU0", 16, 24))
+        if (r, s) == (1, 0):
+            unmade_1(0)
+            unmade_2(0)
+        if (r, s) == (0, 1):
+            hash_a(0)
+            roots_late()
+        if (r, s) == (1, 1):
+            hash_a(1)
+            hash_b(1)
+        act(b("uE"), ind("L", 1024, "cl"))
+        act(b("WN", 256, 384), b("L", n0, n0 + 128))
+        if not last:
+            act(b("CV"), ind("C", 1024, vz, 0, 8))
+        if r == 0:
+            act(b("WC", 0, 128), ind("C", 1024, "cl"))
+        for n in "2314":
+            scan(rev("S" + n), rev("pd"), rev("W" + n), 0.0, A.min, A.max)
+        s3 = at0("S3")
+        Mx, Mc, Mv, Mz = (b("M", 8 * i, 8 * i + 8) for i in range(4))
+        ts(b("zp"), at0("S2"), 4096.0 * HH - 4096.0, A.add)
+        tt(b("T0"), b("acut"), s3, A.subtract)
+        tt(b("TL"), at0("S1"), s3, A.subtract)
+        tt(b("Ap"), s3, b("zp"), A.subtract)
+        tt(b("M0"), b("TL"), b("T0"), A.max)
+        cp(b("pos"), at0("S4"))
+        tt(Mx, b("M0"), b("Ap"), A.max)
+        tt(b("dn"), b("Ap"), b("athr"), A.is_gt)
+        tt(b("G"), b("T0"), b("Ap"), A.max)
+        ts(b("tq"), Mx, 2048.0, A.min)
+        act(b("tcol"), ind("IOT", 2064, "tq"))
+        act(b("DFg"), ind("DF", 2064, "pos"))
+        act(b("XQg"), ind("X", 2064, "tq"))
+        mm((b("ps", 0, 128), b("I"), b("DFg"), True, False), (b("ps", 0, 128), b("I2"), b("XQg"), False, True))
+        tt(b("y1"), b("dn"), s3, A.mult)
+        tt(b("T1"), s3, b("aleaf"), A.subtract)
+        ts(b("zcf"), s3, 2.0 ** -12, A.mult)
+        tt(zs, zs, b("y1"), A.max)
+        tt(Mc, b("cf"), b("G"), A.max)
+        tt(Mv, b("T1"), b("Ap"), A.max)
+        ts(b(vz, 8, 16), zs, 2.0 ** -12, A.mult)
+        tt(Mz, b("zcf"), b("G"), A.max)
+        if last:
+            tt(b("HK"), ind("TRZ", 272, vz, 8, 16), b("HMQ"), A.mult)
+            tt(b("SND"), b("HK"), b("QF"), A.add)
+            travel("SND", "LAND1", "1")
+        elif end:
+            act(b("KGE"), ind("TRZ", 272, vz, 8, 16), scale=col(6))
+            travel("KGE", "LK", "0")
+        act(b("DS"), b("ps", 0, 128), bias=2.0 ** 23, scale=0.5 - 2.0 ** -12)
+        act(b("DH"), b("DS"), bias=-2.0 ** 23)
+        if not end:
+            row(r)
+        for c in range(8):
+            o, n = seg(c)
+            ts(b("EQ", o, o + n), b("tcol", 0, n), b("TL", c, c + 1), A.is_equal, b("LC", c, c + 1), A.mult)
+        tt(b("U"), b("M"), b("LC", 0, 32), A.min)
+        scan(b("RE"), b("EQ"), b("KE"), -8192.0, A.max, A.add)
+        tt(b("q2"), nd("XS", 0, 24, slice(0, 2), al), b("M", 8, 24), A.max)
+        cp(b(uu, 0, 24), b("U", 8, 32))
+        for h, e in enumerate(ends("RE")):
+            tt(b("dd", 4 * h, 4 * h + 4), e, b("U", 4 * h, 4 * h + 4), A.max)
+        tt(b("q1"), b("q2", 0, 8), b("q2", 8, 16), A.min)
+        cp(b("didx"), b("dd"))
+        if not end:
+            tt(b("y2"), b("dn"), b("cmv"), A.mult)
+        tt(b("q0"), b("q1"), nd("XS", 0, 24, 2, al), A.min)
+        cp(ind("X", XW, "didx"), b("DH"))
+        if last:
+            dma("Y", T.yd[:], T.X[:, 0:2048], r=[b("X", 0, 2048)])
+        ts(b(se), b("q0"), -1152.0, A.add)
+        if not end:
+            ts(b("y3"), zs, -4096.0 * 255.5, A.add)
+            tt(b("y2"), b("y2"), v, A.add)
+            ts(b("y4"), b("q1"), -1.0, A.mult, 4096.0, A.add)
+        tt(b("WN", 0, 128), ind("TRZ", 272, uu, 16, 24), b("uE"), A.mult)
+        act(b("L", n0, n0 + 128), ind("WN", 384, se))
+        if not end:
+            tt(b("y5"), b("y2"), b("y3"), A.max)
+        if not last:
+            tt(ind("C", 1152, uu, 8, 16), b("CV"), b("T2"), A.subtract)
+        if not end:
+            tt(b("y6"), b("y5"), b("y4"), A.max)
+            tt(v, b("y6"), DUM, A.min)
+            cp(b(vz, 0, 8), v)
+            child_1(r)
+        if s == 0:
+            cp(b("zacc"), b("U", 24, 32))
+        else:
+            tt(b("zacc"), b("zacc"), b("U", 24, 32), A.min)
+        if end:
+            cp(b("za"), b("zacc"))
+            second(r, b("za"))
+        tt(ind("L", 1152, uu, 0, 8), b("uE"), b("WN", 0, 128), A.subtract)
+        if not end:
+            child_2()
+            child_3()
+
+    def roots_late():
+        hash_b(0)
+        roots(1, b("LQ"))
+
+    consts_a()
+    consts_b()
+    roots(0, b("Qi"))
+    cp(b("Ql"), b("Qi"))
+    row(0)
+    ts(b("C", 0, 384), b("Ci"), 1.0, A.add)
+    child_1(0)
+    ts(b("L", 0, 384), b("Ei"), -1.0, A.mult, 2047.0, A.add)
+    cp(b("lsave", 0, 1), b("L", 0, 1))
+    ms(b("L", 0, 1), -1.0)
+    child_2()
+    cp(b("QF"), b("Qi"))
+    ms(b("X", 2048, XW), FAR)
+    cp(b("xsave", 0, 1), b("X", 2047, 2048))
+    ms(b("X", 2047, 2048), NONE)
+    child_3()
+    travel("QF", "LQ", "E")
+    act(b("STD"), b("IOT", 0, 1152), F.Silu, scale=0.0)
+    acts_1(0)
+    xq(0)
+    cp(b("Q16"), b("Qi"))
+    consts_c()
+    for s in range(S_):
+        step(0, s)
+    row(1)
+    acts_1(1)
+    cut_1(0, 2)
+    acts_2(1, 0)
+    cut_2(0, 2)
+    cut_3(0, 2)
+    child_1(1)
+    child_2()
+    tt(b("HK"), b("LK"), b("HMQ"), A.mult)
+    child_3()
+    tt(b("QF"), b("HK"), b("LQ"), A.add)
+    cp(b("Ql"), b("QF"))
+    for s in range(S_):
+        step(1, s)
+    unmade_1(1)
+    unmade_2(1)
+    act(b("YE", 0, 384), b("L", 0, 384), bias=2047.0, scale=-1.0)
+    act(b("YE", 0, 1), b("lsave", 0, 1), bias=2047.0, scale=-1.0)
     for r in range(RO_):
         n1 = 384 + 256 * r
         for j, o in ((128, 0), (0, 1)):
-            act(b("YE", n1 + o, n1 + 256, 2), b("L", n1 + j, n1 + j + 128), F.Copy, bias=2047.0, scale=-1.0)
+            act(b("YE", n1 + o, n1 + 256, 2), b("L", n1 + j, n1 + j + 128), bias=2047.0, scale=-1.0)
     dma("S", T.ye[:], T.YE[:], r=[b("YE")])
     dma("Y", T.yr[:], T.LAND1[:], r=[b("LAND1")])
-    for s, v in K["final"].items():
+    K["flush"]()
+    for s, n in K["final"].items():
         K["known"]["G"].pop(s, None)
-        wait("G", s, v)
+        wait("G", s, n)

@@ -22,27 +22,28 @@ def _b(name, n, d, where="sbuf"):
 
 XW, LL = 2320, 137
 for _d, _l in (
-    (BF, "X:2320 XQ:2048 DF:2064 BO:128 BOH:128 I:128 I2:128 Im:128 IH:128 IR:128 B0:128 SHD:128 CONV:2048 ZH:272 ZL:272 OHZ:272 TRZ:272 "
-         "IDZ:272 OHB:272 KD:128 KT:128 KE:576 KA:576 KB:18 K3:137 M16:137 RD:137 RMP:137 OH:128 AD:576 RA:576 SG:128 SS:128 XQg:128 "
-         "DFg:128 DH:128 KGE:128 LK:128 xsave:16"),
-    (F32, "L:1152 C:1152 STD:1152 IOT:2064 W1:137 W2:137 W3:137 W4:137 W3n:137 S1:137 S2:137 S3:137 S4:137 QF:128 uQ0:128 uQ1:128 LQ:128 "
-          "LAND1:128 SND:128 HM:128 HMQ:128 HK:128 uE:128 CV:128 T2:128 SC:128 SE:128 SQ:128 tcol:128 vcol:128 DS:128 WN:384 WC:384 "
-          "OHN:256 X5:128 YE:896 cols:12 THR:6 LC:40 lsave:2 v0:8 v1:8 zs0:8 zs1:8 zacc:8 cf:8 cmv:8 athr:8 aleaf:8 acut:8 nf:8 x1:8 x2:8 "
-          "x3:8 zp:8 T0:8 T1:8 TL:8 Ap:8 G:8 M0:8 M:32 U:32 zcf:8 dn:8 y1:8 y2:8 y3:8 y4:8 y5:8 y6:8 q2:16 q1:8 q0:8 dd:8"),
-    (H16, "Q16:128 Q1:128 N16:256 B620:137 M1:128 EQ:576 RE:576 EL:128 Y:128"),
-    (I32, "Qi:128 Ci:384 Ei:384 QI:137 QA:137 HP:128 HI:128 RI:128 RJ:128 IP:2 IC:2 qi:8 qj:16 RW:8"),
-    (U16, "Ql:128 El:128 vz0:16 vz1:16 cl:8 tq:8 pos:8 UU0:32 UU1:32 sl:8 se0:8 se1:8 za:8 didx:8"),
+    (BF, "X:2320 XQ:2048 DF:2064 BO:128 I:128 I2:128 Im:128 IH:128 IR:128 B0:128 SHD:128 ZH:272 ZL:272 OHZ:272 TRZ:272 "
+         "IDZ:272 OHB:272 KD:128 KT:128 KA:576 KB:18 K3:137 M16:137 RD:137 RMP:137 OH:128 AD:576 RA:576 NE:576 RE:576 SG:128 SS:128 "
+         "XQg:128 DFg:128 DH:128 KGE:128 LK:128 xsave:16"),
+    (F32, "L:1152 C:1152 STD:1152 IOT:2320 W1:137 W2:137 W3:137 W4:137 W3n:137 S1:137 S2:137 S3:137 S4:137 QF:128 uQ0:128 uQ1:128 LQ:128 "
+          "LAND1:128 SND:128 HMQ:128 HK:128 uE:128 CV:128 T2:128 SC:128 SE:128 SQ:128 tcol:128 vcol:128 DS:128 WN:384 WC:384 "
+          "OHN:256 OHM:128 X5:128 X6:128 YE:896 cols:14 THR:6 THS:6 LC:40 lsave:2 v0:8 v1:8 zs0:8 zs1:8 zacc:8 cf:8 cmv:8 athr:8 aleaf:8 "
+          "acut:8 nf:8 x1:8 x2:8 x3:8 x4:8 x5:8 zp:8 T0:8 T1:8 TL:8 TS:8 Ap:8 G:8 M:32 U:32 zcf:8 dn:8 y1:8 y2:8 y3:8 y4:8 y5:8 y6:8 y7:8 "
+          "q2:16 q1:8 q0:8 d0:8 dd:8"),
+    (H16, "Q16:128 Q1:128 N16:256 B620:137 M1:128 EL:128 Y:128 Hf:128 Hm:128"),
+    (I32, "Qi:128 Ci:384 Ei:384 QI:137 QA:137 HP:128 HI:128 IP:2 IC:2 qi:8 qj:16 RW:8"),
+    (U16, "Ql:128 El:128 vz0:16 vz1:16 cl:8 pos:8 UU0:40 UU1:40 sl:8 se0:8 se1:8 za:8 didx:8"),
 ):
     for _x in _l.split():
         _b(_x.split(":")[0], int(_x.split(":")[1]), _d)
-_b("AB", [128, 17], BF); _b("QX", [8, 8, 16], H16); _b("XS", [3, 8], F32)
-PS = ["pd", "pm", "pt", "ps", "pq", "pe", "pw"]
+_b("AB", [128, 17], BF); _b("QX", [8, 8, 16], H16); _b("XS", [3, 8], F32); _b("CZ", 144, BF)
+PS = ["pd", "pm", "pt", "ps", "pq", "pe", "pw", "ph"]
 for _n in PS:
     _b(_n, 512, F32, "psum")
 SEMAPHORES = ["sV", "sT", "sS", "sG", "locE", "loc0", "loc1", "arrE", "arr0", "arr1"] + ["d%d" % _i for _i in range(12)]
-NDUM, NDUMP, TDUMP, BIG, HH = 896, 1024, 2050, float(2 ** 22), float(2 ** 22)
+NDUM, NDUMP, TDUMP, BIG, HH, FRZ, CO = 896, 1024, 2050, float(2 ** 22), float(2 ** 22), float(2 ** 24), 32
 FAR, NONE = 294.0, 560.0
-HOP, FLY = 240, 3000
+HOP, FLY, LEAN = 300, 3000, 300
 ORDER = []
 
 
@@ -130,43 +131,54 @@ def make(g, T):
             fin(q, f())
         ops.append((q, r, w, cycles(q, out, ins, both), HOP, emit))
 
+    def either(fs, fv):
+        fs()
+        fv()
+        v, s = ops.pop(), ops.pop()
+        ops.append((s[0], s[1] + v[1], s[2], s[3], s[4], s[5], v))
+
     def order():
         seen, pred = {}, []
-        for i, (q, r, w, c, lat, emit) in enumerate(ops):
-            p = set()
-            for isw, xs in ((0, r), (1, w)):
+        for i, op in enumerate(ops):
+            p = {}
+            for isw, xs in ((0, op[1]), (1, op[2])):
                 for x in xs:
                     for lo, hi, ew, j in seen.get(x[0], []):
-                        if x[0] in PS or (lo < x[2] and x[1] < hi and (isw or ew)):
-                            p.add(j)
-            for isw, xs in ((0, r), (1, w)):
+                        hit = lo < x[2] and x[1] < hi and (isw or ew)
+                        if hit or x[0] in PS:
+                            p[j] = p.get(j, False) or hit
+            for isw, xs in ((0, op[1]), (1, op[2])):
                 for x in xs:
                     l = seen.setdefault(x[0], [])
-                    if x[0] in PS or (isw and x[4]):
-                        l[:] = [e for e in l if x[0] not in PS and not (x[1] <= e[0] and e[1] <= x[2])]
+                    if isw and x[4]:
+                        l[:] = [e for e in l if not (x[1] <= e[0] and e[1] <= x[2])]
                     l.append((x[1], x[2], isw, i))
-            pred.append(p - {i})
-        gap = lambda j, i: 0 if ops[j][0] == ops[i][0] == "T" else ops[j][4]
+            p.pop(i, None)
+            pred.append(p)
         level = [op[3] + op[4] for op in ops]
+        gap = lambda j, i, qj, qi: 0 if qj == qi and (qi == "T" or not pred[i][j]) else ops[j][4]
         for i in reversed(range(len(ops))):
             for j in pred[i]:
-                level[j] = max(level[j], ops[j][3] + gap(j, i) + level[i])
-        start, busy = {}, {q: [] for q in eng}
+                level[j] = max(level[j], ops[j][3] + gap(j, i, ops[j][0], ops[i][0]) + level[i] + 1)
+        place, busy = {}, {q: [] for q in eng}
         for i in sorted(range(len(ops)), key=lambda i: (-level[i], i)):
-            t, c, l = max([start[j] + ops[j][3] + gap(j, i) for j in pred[i]] + [0]), ops[i][3], busy[ops[i][0]]
-            at = 0
-            while at < len(l) and l[at][0] < t + c:
-                t = max(t, l[at][1])
-                at += 1
-            l.insert(at, (t, t + c))
-            start[i] = t
-        return sorted(range(len(ops)), key=lambda i: (start[i], i))
+            best = None
+            for k, op in enumerate([ops[i]] + list(ops[i][6:])):
+                t, l, at = max([place[j][1] + gap(j, i, place[j][2], op[0]) for j in pred[i]] + [0]), busy[op[0]], 0
+                while at < len(l) and l[at][0] < t + op[3]:
+                    t = max(t, l[at][1])
+                    at += 1
+                if best is None or t + op[3] + LEAN < best[1]:
+                    best = (t, t + op[3], op[0], k, at)
+            busy[best[2]].insert(best[4], best[:2])
+            place[i] = best
+        return [(i, place[i][3]) for i in sorted(range(len(ops)), key=lambda i: (place[i][0], -level[i]))]
 
     def flush():
         if not ORDER:
             ORDER.extend(order())
-        for i in ORDER:
-            ops[i][5]()
+        for i, k in ORDER:
+            (ops[i][6] if k else ops[i])[5]()
 
     def fin(q, ins):
         sem = "s" + q
@@ -197,6 +209,10 @@ def make(g, T):
         else:
             call("S", out, [a, bias, scale], lambda: g.scalar.activation(ap(out), ap(a), func, bias=ap(bias), scale=ap(scale)))
 
+    def lin(out, a, scale=1.0, bias=0.0):
+        either(lambda: act(out, a, F.Identity if isinstance(bias, tuple) else F.Copy, bias, scale),
+               lambda: ts(out, a, scale, A.mult, bias, A.add))
+
     def iota(out, pattern, base, cm, fl=True):
         kw = dict(allow_small_or_imprecise_dtypes=True) if fl else {}
         call("G", out, [], lambda: g.iota(ap(out), pattern, base, cm, **kw))
@@ -226,7 +242,7 @@ def make(g, T):
         ops.append((q, list(r), list(w), 120, FLY + size((list(r) + list(w))[0]), emit))
 
     return dict(tt=tt, ts=ts, cp=cp, ms=ms, scan=scan, act=act, iota=iota, sel=sel, mm=mm, dma=dma, wait=wait, deps=deps,
-                known=known, final=final, acc=acc, ops=ops, flush=flush)
+                known=known, final=final, acc=acc, ops=ops, flush=flush, lin=lin, either=either)
 
 
 def plan(src, cores, topo):
@@ -245,8 +261,8 @@ def rank_program(g, core, T, topo):
     if rank is None:
         return
     K = make(g, T)
-    tt, ts, cp, ms, scan, act, iota, sel, mm, dma, wait, deps = (
-        K[x] for x in ("tt", "ts", "cp", "ms", "scan", "act", "iota", "sel", "mm", "dma", "wait", "deps"))
+    tt, ts, cp, ms, scan, act, iota, sel, mm, dma, wait, deps, lin, either = (
+        K[x] for x in ("tt", "ts", "cp", "ms", "scan", "act", "iota", "sel", "mm", "dma", "wait", "deps", "lin", "either"))
     al = slice(None)
 
     def b(n, lo=0, hi=None, st=1):
@@ -276,9 +292,17 @@ def rank_program(g, core, T, topo):
     def seg(c):
         return (144 * c if c < 4 else 144 * (7 - c) + 16 * (8 - c)), 16 * c + 16
 
-    ends = lambda n: (b(n, 14, 576, 160), b(n, 142, 575, -144))
+    def lower(out, res, row, own, own4096):
+        for c in range(8):
+            o, n = seg(c)
+            either(lambda: act(b(out, o, o + n), b(row, 0, n), F.Abs, bias=b(own4096, c, c + 1), scale=-4096.0),
+                   lambda: ts(b(out, o, o + n), b(row, 0, n), b(own, c, c + 1), A.not_equal, 4096.0, A.mult))
+        scan(b(res), b(out), b("KA"), 2 * FRZ, A.min, A.add)
+        return b(res, 14, 576, 160), b(res, 142, 575, -144)
+
     CS = col(4)
     DT, DD, DUM = b("LC", 0, 8), b("LC", 8, 16), b("LC", 32, 40)
+    XS = lambda *i: nd("XS", 0, 24, *i)
 
     dma("Y", T.Qi[:], T.req[:], w=[b("Qi")])
     dma("S", T.Ci[:], T.child[:], w=[b("Ci")])
@@ -286,86 +310,72 @@ def rank_program(g, core, T, topo):
     dma("S", T.X[:, 0:1024], T.desc[:, 0:1024], w=[b("X", 0, 1024)])
     dma("Y", T.X[:, 1024:2048], T.desc[:, 1024:2048], w=[b("X", 1024, 2048)])
 
-    def consts_a():
-        iota(b("IP", 0, 1), [[1, 1]], 0, 1, False)
-        iota(b("ZH"), [[1, 17], [0, 16]], 0, 0)
-        iota(b("ZL"), [[0, 17], [1, 16]], 0, 0)
-        iota(b("IOT", 0, 256), [[1, 256]], 0, 0)
-        iota(b("C", NDUM, NDUMP), [[1, 128]], NDUM + 1, 0)
-        ts(b("IC", 0, 1), b("IP", 0, 1), 4, A.arith_shift_right)
-        ts(b("IC", 1, 2), b("IP", 0, 1), 15, A.bitwise_and)
-        cp(col(0), b("IP", 0, 1))
-        cp(b("cols", 1, 3), b("IC"))
-        ms(b("C", 384, NDUM), 1.0)
-        ms(b("L", 384, 1152), 0.0)
-        ts(col(3), col(2), 1.0, A.add)
-        ts(col(5), col(2), 0.0, A.is_equal)
-        ts(col(7), col(2), 14.5, A.is_lt, 4095.0, A.mult)
-        ts(b("BO"), b("ZH", 0, 128), col(1), A.is_equal)
-        ts(col(7), col(7), 1.0, A.add)
-        ts(col(4), col(2), 14.5, A.is_gt, 1.0 - 2.0 ** -12, A.mult)
-        ts(b("B0"), b("BO"), col(5), A.mult)
-        ts(col(4), col(4), 2.0 ** -12, A.add)
-        ts(b("KD"), b("ZL", 0, 128), col(2), A.is_gt)
-        ts(b("KT"), b("ZL", 0, 128), col(3), A.is_equal, 4095.0, A.mult)
-        ts(b("OHZ"), b("ZL"), col(2), A.is_equal)
-        tt(b("KD"), b("KD"), b("KT"), A.add)
-        act(b("BOH"), b("BO"), scale=-HH)
-
-    def consts_b():
-        iota(b("LC", 0, 8), [[32, 8]], TDUMP, 2)
-        iota(b("LC", 8, 24), [[0, 2], [16, 8]], NDUMP, 1)
-        iota(b("LC", 32, 40), [[16, 8]], NDUM, 1)
-        iota(b("IOT", 256, 1152), [[1, 896]], 256, 0)
-        for m in range(16):
-            sel(b("CONV", 128 * m, 128 * m + 128), b("BOH"), [[0, 8], [1, 16]], A.is_equal, -m, 0)
-            if m == 7:
-                iota(b("K3", 1, LL), [[0, 8], [16, 17]], 0, 0)
-                iota(b("W4", 1, LL), [[256, 8], [1, 17]], 0, 16)
-                iota(b("THR"), [[256, 6]], 192, 0)
-        iota(b("IOT", 1152, 2064), [[1, 912]], 1152, 0)
-        iota(nd("XS", 0, 24, al, al), [[128, 3], [16, 8]], 1152, 1)
-        sel(b("SHD"), b("BO"), [[1, 128]], A.is_equal, -1, -1)
-
-    def consts_c():
-        ts(b("cols", 8, 9), col(1), -16.0, A.mult)
-        ts(b("cols", 9, 10), col(1), -32.0, A.mult)
-        ts(b("cols", 10, 11), col(1), -256.0, A.mult)
-        ts(col(6), col(2), 0.0, A.is_gt)
-        ts(b("I"), b("IOT", 0, 128), col(0), A.is_equal)
-        ts(b("IDZ"), b("ZH"), col(2), A.is_equal)
-        ts(b("TRZ"), b("ZH"), col(2), A.is_le)
-        ts(b("LC", 0, 8), b("LC", 0, 8), col(9), A.add)
-        ts(b("LC", 8, 24), b("LC", 8, 24), col(8), A.add)
-        ts(b("LC", 32, 40), b("LC", 32, 40), col(8), A.add)
-        ms(b("LC", 24, 32), 256.0)
-        ms(b("KE"), 0.0)
-        ts(b("KB", 0, 16), b("OHZ", 0, 16), 4096.0, A.mult)
-        ms(b("KB", 16, 17), -8192.0)
-        ts(b("KB", 15, 16), b("KB", 15, 16), -4096.0, A.add)
-        for c in range(8):
-            o, n = seg(c)
-            cp(b("KE", o + n - 16 - (c > 0), o + n), b("KB", 1 - (c > 0), 17))
-        ts(b("KA"), b("KE"), -1.0, A.mult)
-
-    def consts_d():
-        for n, c in (("IH", HH / 2), ("IR", 2.0 ** 37), ("I2", 2.0), ("Im", -1.0)):
-            ts(b(n), b("I"), c, A.mult)
-        ms(b("M16"), -16.0)
-        ms(b("RD"), 0.0)
-        ms(b("DF", 2048, 2064), 0.0)
-        ms(nd("AB", 0, 2176, al, slice(16, 17)), NONE)
-        ts(b("B620"), b("M16"), 0.0, A.mult, 1241.0, A.add)
-        ts(b("W4", 1, LL), b("W4", 1, LL), col(10), A.add)
-        ts(b("THR"), b("THR"), col(7), A.mult)
-
-    def consts_e():
-        ts(b("N16", 0, 128), b("IOT", 0, 128), 513.0, A.add)
-        ts(b("N16", 128, 256), b("IOT", 0, 128), 769.0, A.add)
-        ms(b("IOT", 2048, 2049), -1.0)
-        ts(nd("XS", 0, 24, al, al), nd("XS", 0, 24, al, al), col(8), A.add)
-        ts(b("OHB"), b("OHZ"), 4095.0, A.mult, 1.0, A.add)
-        ms(b("WC", 128, 256), 1.0)
+    iota(b("IP", 0, 1), [[1, 1]], 0, 1, False)
+    iota(b("ZH"), [[1, 17], [0, 16]], 0, 0)
+    iota(b("ZL"), [[0, 17], [1, 16]], 0, 0)
+    for lo, hi in ((0, 144), (144, 1024), (1024, 1664), (1664, XW)):
+        iota(b("IOT", lo, hi), [[1, hi - lo]], lo, 0)
+    iota(b("C", NDUM, NDUMP), [[1, 128]], NDUM + CO, 0)
+    iota(b("LC", 0, 8), [[32, 8]], TDUMP, 2)
+    iota(b("LC", 8, 24), [[0, 2], [16, 8]], NDUMP, 1)
+    iota(b("LC", 32, 40), [[16, 8]], NDUM, 1)
+    iota(b("K3", 1, LL), [[0, 8], [16, 17]], 0, 0)
+    iota(b("W4", 1, LL), [[256, 8], [1, 17]], 0, 16)
+    iota(b("THR"), [[256, 6]], 192, 0)
+    iota(XS(al, al), [[128, 3], [16, 8]], 1152, 1)
+    ts(b("IC", 0, 1), b("IP", 0, 1), 4, A.arith_shift_right)
+    ts(b("IC", 1, 2), b("IP", 0, 1), 15, A.bitwise_and)
+    cp(col(0), b("IP", 0, 1))
+    cp(b("cols", 1, 3), b("IC"))
+    ms(b("C", 384, NDUM), float(CO))
+    for n, lo, hi in (("L", 384, 896), ("L", 896, 1152), ("STD", 0, 512), ("STD", 512, 1024), ("STD", 1024, 1152)):
+        act(b(n, lo, hi), b("C", 384, 384 + hi - lo), F.Silu, scale=0.0)
+    lin(col(3), col(2), 1.0, 1.0)
+    ts(col(5), col(2), 0.0, A.is_equal)
+    ts(col(6), col(2), 0.0, A.is_gt)
+    ts(col(11), col(2), 14.5, A.is_gt)
+    lin(col(7), col(11), -4095.0, 4096.0)
+    lin(col(4), col(11), 1.0 - 2.0 ** -12, 2.0 ** -12)
+    for j, c in ((8, -16.0), (9, -32.0), (10, -256.0)):
+        lin(col(j), col(1), c)
+    ts(b("BO"), b("ZH", 0, 128), col(1), A.is_equal)
+    lin(b("B0"), b("BO"), col(5))
+    sel(b("SHD"), b("BO"), [[1, 128]], A.is_equal, -1, -1)
+    ts(b("KD"), b("ZL", 0, 128), col(2), A.is_gt)
+    ts(b("KT"), b("ZL", 0, 128), col(3), A.is_equal, 4095.0, A.mult)
+    tt(b("KD"), b("KD"), b("KT"), A.add)
+    ts(b("OHZ"), b("ZL"), col(2), A.is_equal)
+    ts(b("IDZ"), b("ZH"), col(2), A.is_equal)
+    ts(b("TRZ"), b("ZH"), col(2), A.is_le)
+    lin(b("OHB"), b("OHZ"), 4096.0 - CO, float(CO))
+    ts(b("I"), b("IOT", 0, 128), col(0), A.is_equal)
+    for n, c in (("IH", HH / 2), ("IR", 2.0 ** 37), ("I2", 2.0), ("Im", -1.0)):
+        lin(b(n), b("I"), c)
+    lin(col(12), col(1), 16.0, 15.0)
+    ts(b("CZ"), b("IOT", 0, 144), col(12), A.is_equal, -HH, A.mult)
+    lin(DT, DT, 1.0, col(9))
+    lin(b("LC", 8, 24), b("LC", 8, 24), 1.0, col(8))
+    lin(DUM, DUM, 1.0, col(8))
+    lin(XS(al, al), XS(al, al), 1.0, col(8))
+    lin(b("W4", 1, LL), b("W4", 1, LL), 1.0, col(10))
+    lin(b("THR"), b("THR"), col(7))
+    lin(b("THS"), b("THR"), -32768.0)
+    ms(b("LC", 24, 32), 256.0)
+    ms(b("KA"), 0.0)
+    lin(b("KB", 0, 16), b("OHZ", 0, 16), -FRZ)
+    ms(b("KB", 16, 17), 2 * FRZ)
+    lin(b("KB", 15, 16), b("KB", 15, 16), 1.0, FRZ)
+    for c in range(8):
+        o, n = seg(c)
+        lin(b("KA", o + n - 16 - (c > 0), o + n), b("KB", 1 - (c > 0), 17))
+    ms(b("M16"), -16.0)
+    ms(b("RD"), 0.0)
+    ms(b("DF", 2048, 2064), 0.0)
+    ms(nd("AB", 0, 2176, al, slice(16, 17)), NONE)
+    ts(b("B620"), b("M16"), 0.0, A.mult, 1241.0, A.add)
+    for r in range(RO_):
+        ts(b("N16", 128 * r, 128 * r + 128), b("IOT", 0, 128), 512.0 + 256 * r + CO, A.add)
+    lin(b("WC", 128, 256), b("C", 384, 512))
 
     def roots(r, src):
         vz = "vz%d" % r
@@ -378,140 +388,114 @@ def rank_program(g, core, T, topo):
         cp(b("v%d" % r), b("qj", 0, 8))
         ts(b("zs%d" % r), b("qj", 8, 16), 4096.0, A.mult)
 
-    def row(r):
-        act(b("OH"), ind("OHZ", 272, "vz%d" % r, 8, 16))
-
-    def child_1(r):
-        tt(b("M1"), ind("C", 1024, "vz%d" % r, 0, 8), b("OH"), A.mult)
+    def child(r):
+        vz = "vz%d" % r
+        lin(b("OH"), ind("OHZ", 272, vz, 8, 16))
+        tt(b("M1"), ind("C", 1024, vz, 0, 8), b("OH"), A.mult)
         mm((b("pm", 0, 128), b("BO"), b("M1"), True, True))
+        ts(b("cl"), diag("SC", b("pm", 0, 128)), CS, A.mult, -float(CO), A.add)
+        lin(b("cf"), b("SC", 15, 128, 16), CS, -float(CO))
+        tt(b("cmv"), b("cf"), b("v%d" % r), A.subtract)
 
-    def child_2():
-        ts(b("cl"), diag("SC", b("pm", 0, 128)), CS, A.mult, -1.0, A.add)
-
-    def child_3():
+    def edge():
         ts(b("El"), ind("L", 1024, "cl"), -1.0, A.mult, 2047.0, A.add)
 
-    def child_4(r, leaf):
-        ts(b("cf"), b("SC", 15, 128, 16), CS, A.mult, -1.0, A.add)
-        tt(b("cmv"), b("cf"), b("v%d" % r), A.subtract)
-        if leaf:
-            mm((b("pt", 0, 128), b("BO"), b("M1"), True, False), (b("pt", 0, 128), b("Im"), b("N16", 128 * r, 128 * r + 128), False, True))
-            tt(b("T2"), b("pt", 0, 128), b("OH"), A.mult)
+    def leaf(r):
+        mm((b("pt", 0, 128), b("BO"), b("M1"), True, False), (b("pt", 0, 128), b("Im"), b("N16", 128 * r, 128 * r + 128), False, True))
+        tt(b("T2"), b("pt", 0, 128), b("OH"), A.mult)
+        tt(b("CV"), ind("C", 1024, "vz%d" % r, 0, 8), b("T2"), A.subtract)
 
-    def acts_1(r):
-        act(b("vcol"), ind("IOT", 1024, "vz%d" % r, 0, 8))
-        for c in range(8):
-            o, n = seg(c)
-            act(b("AD", o, o + n), b("vcol", 0, n), F.Abs, bias=b("v%d" % r, c, c + 1), scale=-1.0)
-
-    def acts_2(r, s):
-        v, zs = b("v%d" % r), b("zs%d" % r)
-        scan(b("RA"), b("AD"), b("KA"), 8192.0, A.min, A.add)
+    def acts(r, s):
+        v, zs, o = b("v%d" % r), b("zs%d" % r), 256 * (3 * r + s + 1)
+        lin(b("vcol"), ind("IOT", 1024, "vz%d" % r, 0, 8))
+        lin(b("x5"), v, 4096.0)
+        for h, e in enumerate(lower("AD", "RA", "vcol", "v%d" % r, "x5")):
+            out = b("athr", 4 * h, 4 * h + 4)
+            either(lambda: act(out, e, F.Relu, bias=BIG, scale=-BIG / 2048), lambda: ts(out, e, 0.5, A.is_lt, BIG, A.mult))
         tt(b("x1"), zs, v, A.subtract)
-        for h, e in enumerate(ends("RA")):
-            ts(b("athr", 4 * h, 4 * h + 4), e, 0.5, A.is_lt, BIG, A.mult)
-        ts(b("x3"), zs, 4096.0, A.add)
-        tt(b("x2"), b("athr"), v, A.max)
         tt(b("aleaf"), b("x1"), b("athr"), A.subtract)
+        tt(b("x2"), b("athr"), v, A.max)
         tt(b("x2"), b("x2"), DD, A.min)
-        tt(b("x3"), b("x3"), b("athr"), A.add)
         cp(b("sl"), b("x2"))
-
-    def stood_1(r, s):
-        o = 256 * (3 * r + s + 1)
         act(ind("STD", 1152, "sl"), b("IOT", o, o + 128), F.Silu)
-        act(b("SG"), ind("STD", 1024, "cl"))
+        lin(b("x3"), zs, 1.0, 4096.0)
+        tt(b("x4"), b("x3"), b("athr"), A.add)
 
-    def stood_2(r, s):
-        ts(b("nf"), diag("SS", b("SG")), b("THR", 3 * r + s, 3 * r + s + 1), A.is_gt, BIG, A.mult)
-        tt(b("acut"), b("x3"), b("nf"), A.add)
+    def stood(r, s):
+        j = 3 * r + s
+        lin(b("SG"), ind("STD", 1024, "cl"))
+        e = diag("SS", b("SG"))
+        either(lambda: act(b("nf"), e, F.Relu, bias=b("THS", j, j + 1), scale=32768.0),
+               lambda: ts(b("nf"), e, b("THR", j, j + 1), A.is_gt, BIG, A.mult))
+        tt(b("acut"), b("x4"), b("nf"), A.add)
 
-    def payload_1():
+    def payload():
         for x in range(8):
             ts(nd("QX", 0, 1024, al, x, al), b("Q16"), b("BO", 16 * x, 16 * x + 1), A.mult)
         mm(*[(b("pq", 1 + 17 * c, 18 + 17 * c), nd("QX", 0, 1024, c, al, al), b("IDZ", 0, 272, 16), True, True) for c in range(8)])
-
-    def payload_2():
         cp(b("QI", 1, LL), b("pq", 1, LL))
         ts(b("QA", 1, LL), b("QI", 1, LL), 15, A.bitwise_and)
         tt(b("W3n", 1, LL), b("QA", 1, LL), b("K3", 1, LL), A.add)
-        act(b("W3", 1, LL), b("W3n", 1, LL), scale=4096.0)
-        act(b("W2", 1, LL), b("W3n", 1, LL), scale=4096.0, bias=-4096.0 * HH)
-
-    def payload_3():
+        lin(b("W3", 1, LL), b("W3n", 1, LL), 4096.0)
+        lin(b("W2", 1, LL), b("W3n", 1, LL), 4096.0, -4096.0 * HH)
         tt(b("W1", 1, LL), b("pq", 1, LL), b("W3", 1, LL), A.add)
 
-    def hash_a(r):
-        if r == 0:
-            cp(b("Q16"), b("LQ"))
-        mm((b("pw", 0, 128), b("SHD"), b("Q16"), True, True))
-
-    def hash_b(r):
+    def hashes(r):
         src = b("QF" if r else "LQ")
-        tt(b("HP"), b("pw", 0, 128), src, A.mult)
+        if r == 0:
+            cp(b("Q16"), src)
+        mm((b("ph", 0, 128), b("SHD"), b("Q16"), True, True))
+        tt(b("HP"), b("ph", 0, 128), src, A.mult)
         ts(b("HI"), b("HP"), 5, A.arith_shift_right, 2047, A.bitwise_and)
-        ts(b("HM"), b("HI"), 2046.5, A.is_lt)
-        tt(b("HMQ"), b("HI"), b("HM"), A.mult)
-        tt(b("HMQ"), b("HMQ"), src, A.subtract)
-        if r:
-            act(b("HMQ"), b("HMQ"), scale=col(6))
+        cp(b("Hf"), b("HI"))
+        ts(b("Hm"), b("HI"), 2046.5, A.is_gt, -2047.0, A.mult)
+        mm(*[(b("ph", 128, 256), b(w), b(x), x == "Hf", x == "Q16") for w, x in (("I", "Hf"), ("I", "Hm"), ("Im", "Q16"))])
+        lin(b("HMQ"), b("ph", 128, 256), col(6))
 
-    def ramp(r):
-        act(at0("RD"), b("zs%d" % r), F.Relu, bias=-15.0, scale=2.0 ** -12)
-        scan(b("RMP", 1, LL), b("M16", 1, LL), b("RD", 1, LL), 0.0, A.add, A.max)
+    def distances(r, s):
+        pd = b("pd", 1, LL)
+        if s:
+            act(at0("RD"), b("zs%d" % r), F.Relu, bias=-15.0, scale=2.0 ** -12)
+            scan(b("RMP", 1, LL), b("M16", 1, LL), b("RD", 1, LL), 0.0, A.add, A.max)
+        mm((pd, b("IH"), b("B620", 1, LL), True, False), *([(pd, b("IR"), b("RMP", 1, LL), False, False)] if s else []))
+        for q in range(4):
+            lo, hi = 512 * q, 512 * q + 512
+            act(b("XQ", lo, hi), ind("X", 2064, "Ql", 32 * q, 32 * q + 32))
+            tt(b("DF", lo, hi), ind("X", 2064, "El", 32 * q, 32 * q + 32), b("XQ", lo, hi), A.subtract)
+            act(nd("AB", 544 * q, 544 * q + 544, slice(32 * q, 32 * q + 32), slice(0, 16)), b("DF", lo, hi), F.Abs)
+        for h in range(2):
+            mm(*[(b("pd", 1 + 68 * h, 69 + 68 * h), b("CZ", 15 - p, 143 - p),
+                  nd("AB", 1088 * h, 1088 * h + 1088, slice(64 * h + p, 64 * h + 64, 16), al), False, h == 1 and p == 15) for p in range(16)])
 
-    def dist_0(s):
-        mm((b("pd", 1, LL), b("IH"), b("B620", 1, LL), True, False), *([(b("pd", 1, LL), b("IR"), b("RMP", 1, LL), False, False)] if s else []))
-
-    def dist(h):
-        mm(*[(b("pd", 1 + 68 * h, 69 + 68 * h), b("CONV", 128 * p, 128 * p + 128),
-              nd("AB", 1088 * h, 1088 * h + 1088, slice(64 * h + p, 64 * h + 64, 16), al), False, h == 1 and p == 15) for p in range(16)])
-
-    def xq(q):
-        act(b("XQ", 512 * q, 512 * q + 512), ind("X", 2064, "Ql", 32 * q, 32 * q + 32))
-
-    def df(q):
-        tt(b("DF", 512 * q, 512 * q + 512), ind("X", 2064, "El", 32 * q, 32 * q + 32), b("XQ", 512 * q, 512 * q + 512), A.subtract)
-
-    def ab(q):
-        act(nd("AB", 544 * q, 544 * q + 544, slice(32 * q, 32 * q + 32), slice(0, 16)), b("DF", 512 * q, 512 * q + 512), F.Abs)
-
-    def cut_1(r, s):
-        uu, n0 = "UU%d" % (s % 2), 512 + 256 * r
-        tt(b("EL"), ind("IDZ", 272, uu, 16, 24), b("WN", 0, 128), A.mult)
+    def cut_rows(r, s):
+        uu, n1, n0 = "UU%d" % (s % 2), 384 + 256 * r, 512 + 256 * r
+        tt(b("EL"), ind("IDZ", 272, uu, 24, 32), b("WN", 0, 128), A.mult)
         mm((b("pe", 0, 128), b("BO"), b("EL"), True, True))
         if r == 0:
-            act(b("WC", 256, 384), b("C", n0, n0 + 128))
-            act(b("C", n0, n0 + 128), ind("WC", 384, "se%d" % (s % 2)))
-
-    def cut_2(r, s):
-        uu = "UU%d" % (s % 2)
+            lin(b("WC", 256, 384), b("C", n0, n0 + 128))
+            lin(b("C", n0, n0 + 128), ind("WC", 384, "se%d" % (s % 2)))
         ts(b("RW"), diag("SE", b("pe", 0, 128)), CS, A.mult)
         ts(b("RW"), b("RW"), 15, A.bitwise_and)
-        ts(b(uu, 24, 32), b("RW"), -1.0, A.mult, 15.0, A.add)
-
-    def cut_3(r, s):
-        uu, n1 = "UU%d" % (s % 2), 384 + 256 * r
-        tt(b("OHN"), ind("OHB", 272, uu, 16, 32), b("IOT", n1 + 1, n1 + 257), A.min)
-        tt(ind("C", 1152, uu, 0, 8), b("OHN", 0, 128), b("OHN", 128, 256), A.max)
+        ts(b(uu, 32, 40), b("RW"), -1.0, A.mult, 15.0, A.add)
+        tt(b("OHN"), ind("OHB", 272, uu, 24, 40), b("IOT", n1 + CO, n1 + CO + 256), A.min)
+        tt(b("OHM"), b("OHN", 0, 128), b("OHN", 128, 256), A.max)
+        act(ind("C", 1152, uu, 8, 16), b("OHM"), F.Silu)
 
     def second(r, lst):
         tt(b("L", 384 + 256 * r, 512 + 256 * r), ("@", b("TRZ"), lst), b("uQ%d" % r), A.mult)
 
-    def unmade_1(r):
-        tt(b("Y"), b("L", 512 + 256 * r, 640 + 256 * r), b("uQ%d" % r), A.subtract)
+    def unmade(r):
+        n1 = 384 + 256 * r
+        tt(b("Y"), b("L", n1 + 128, n1 + 256), b("uQ%d" % r), A.subtract)
         tt(b("EL"), ind("IDZ", 272, "za"), b("Y"), A.mult)
         mm((b("pe", 0, 128), b("BO"), b("EL"), True, True))
-
-    def unmade_2(r):
-        n1 = 384 + 256 * r
-        cp(b("RI"), b("pe", 0, 128))
-        ts(b("RJ"), b("RI"), 15, A.bitwise_and)
-        ts(b("X5"), b("RJ"), 4096.0, A.mult)
-        tt(b("L", n1, n1 + 128), b("L", n1, n1 + 128), b("X5"), A.min)
+        lin(b("X5"), b("pe", 0, 128), 1.0, 1.5 * 2 ** 27)
+        lin(b("X5"), b("X5"), 1.0, -1.5 * 2 ** 27)
+        tt(b("X6"), b("pe", 0, 128), b("X5"), A.not_equal)
+        tt(b("L", n1, n1 + 128), b("L", n1, n1 + 128), b("X6"), A.mult)
 
     def travel(src, land, tag):
-        act(b(land, 0, 16), b(src, 0, 16))
+        lin(b(land, 0, 16), b(src, 0, 16))
         K["ops"].append(("G", [b(src)], [b(land, 16, 128)], 1400, FLY, lambda: send(src, land, tag)))
 
     def send(src, land, tag):
@@ -534,210 +518,141 @@ def rank_program(g, core, T, topo):
         K["final"]["loc" + tag] = sent[0]
 
     def step(r, s):
-        first, end, last = (r, s) == (0, 0), s == S_ - 1, (r, s) == (RO_ - 1, S_ - 1)
-        prev = (r, s - 1) if s and (r == 0 or s == 1) else None
+        end, last = s == S_ - 1, (r, s) == (RO_ - 1, S_ - 1)
         v, zs, vz, uu, se = b("v%d" % r), b("zs%d" % r), "vz%d" % r, "UU%d" % (s % 2), "se%d" % (s % 2)
         n0 = 512 + 256 * r
-        if not first:
-            xq(0)
-        xq(1)
-        if s:
-            ramp(r)
-        df(0)
-        if first:
-            consts_d()
-        if s:
-            acts_1(r)
-        dist_0(s)
-        child_4(r, not last) if not first else None
-        ab(0)
-        if s == 0:
-            if r:
-                cp(b("Q16"), b("QF"))
-            payload_1()
-        df(1)
-        xq(2)
-        if s or first:
-            acts_2(r, s)
-        if prev:
-            cut_1(*prev)
-        ab(1)
-        df(2)
-        xq(3)
-        dist(0)
-        stood_1(r, s)
-        if s == 0:
-            payload_2()
-        if first:
-            consts_e()
-            child_4(r, True)
-        if prev:
-            cut_2(*prev)
-        ab(2)
-        df(3)
-        stood_2(r, s)
-        ab(3)
-        dist(1)
+        distances(r, s)
+        acts(r, s)
+        stood(r, s)
         if last:
             cp(b("X", 2047, 2048), b("xsave", 0, 1))
         if s == 0:
-            payload_3()
-            ts(b("uQ%d" % r), b("QF"), -1.0, A.mult, 2047.0, A.add)
-            act(b("WN", 128, 256), b("uQ%d" % r))
+            payload()
+            lin(b("uQ%d" % r), b("QF"), -1.0, 2047.0)
+            lin(b("WN", 128, 256), b("QF"), -1.0, 2047.0)
         else:
             tt(b("WN", 128, 256), ind("TRZ", 272, vz, 8, 16), b("uQ%d" % r), A.mult)
-        if prev:
-            cut_3(*prev)
+        if s and (r == 0 or s == 1):
+            cut_rows(r, s - 1)
         if s == 1:
-            second(r, b("UU0", 16, 24))
+            second(r, b("UU0", 24, 32))
+            hashes(r)
         if (r, s) == (1, 0):
-            unmade_1(0)
-            unmade_2(0)
+            unmade(0)
         if (r, s) == (0, 1):
-            hash_a(0)
-            roots_late()
-        if (r, s) == (1, 1):
-            hash_a(1)
-            hash_b(1)
-        act(b("uE"), ind("L", 1024, "cl"))
-        act(b("WN", 256, 384), b("L", n0, n0 + 128))
+            roots(1, b("LQ"))
+        lin(b("uE"), ind("L", 1024, "cl"))
+        lin(b("WN", 256, 384), b("L", n0, n0 + 128))
         if not last:
-            act(b("CV"), ind("C", 1024, vz, 0, 8))
+            leaf(r)
         if r == 0:
-            act(b("WC", 0, 128), ind("C", 1024, "cl"))
+            lin(b("WC", 0, 128), ind("C", 1024, "cl"))
         for n in "2314":
             scan(rev("S" + n), rev("pd"), rev("W" + n), 0.0, A.min, A.max)
         s3 = at0("S3")
         Mx, Mc, Mv, Mz = (b("M", 8 * i, 8 * i + 8) for i in range(4))
-        ts(b("zp"), at0("S2"), 4096.0 * HH - 4096.0, A.add)
+        lin(b("zp"), at0("S2"), 1.0, 4096.0 * HH - 4096.0)
         tt(b("T0"), b("acut"), s3, A.subtract)
         tt(b("TL"), at0("S1"), s3, A.subtract)
         tt(b("Ap"), s3, b("zp"), A.subtract)
-        tt(b("M0"), b("TL"), b("T0"), A.max)
-        cp(b("pos"), at0("S4"))
-        tt(Mx, b("M0"), b("Ap"), A.max)
-        tt(b("dn"), b("Ap"), b("athr"), A.is_gt)
-        tt(b("G"), b("T0"), b("Ap"), A.max)
-        ts(b("tq"), Mx, 2048.0, A.min)
-        act(b("tcol"), ind("IOT", 2064, "tq"))
-        act(b("DFg"), ind("DF", 2064, "pos"))
-        act(b("XQg"), ind("X", 2064, "tq"))
-        mm((b("ps", 0, 128), b("I"), b("DFg"), True, False), (b("ps", 0, 128), b("I2"), b("XQg"), False, True))
-        tt(b("y1"), b("dn"), s3, A.mult)
         tt(b("T1"), s3, b("aleaf"), A.subtract)
-        ts(b("zcf"), s3, 2.0 ** -12, A.mult)
-        tt(zs, zs, b("y1"), A.max)
+        lin(b("zcf"), s3, 2.0 ** -12)
+        lin(b("TS"), b("TL"), 4096.0)
+        cp(b("pos"), at0("S4"))
+        tt(b("G"), b("T0"), b("Ap"), A.max)
+        tt(Mx, b("TL"), b("G"), A.max)
         tt(Mc, b("cf"), b("G"), A.max)
         tt(Mv, b("T1"), b("Ap"), A.max)
-        ts(b(vz, 8, 16), zs, 2.0 ** -12, A.mult)
         tt(Mz, b("zcf"), b("G"), A.max)
+        tt(b("U"), b("M"), b("LC", 0, 32), A.min)
+        cp(b(uu, 0, 32), b("U"))
+        tt(b("dn"), b("Ap"), b("athr"), A.is_gt)
+        tt(b("y1"), b("dn"), s3, A.mult)
+        tt(zs, zs, b("y1"), A.max)
+        ts(b(vz, 8, 16), zs, 2.0 ** -12, A.mult)
         if last:
             tt(b("HK"), ind("TRZ", 272, vz, 8, 16), b("HMQ"), A.mult)
             tt(b("SND"), b("HK"), b("QF"), A.add)
             travel("SND", "LAND1", "1")
         elif end:
-            act(b("KGE"), ind("TRZ", 272, vz, 8, 16), scale=col(6))
+            lin(b("KGE"), ind("TRZ", 272, vz, 8, 16))
             travel("KGE", "LK", "0")
-        act(b("DS"), b("ps", 0, 128), bias=2.0 ** 23, scale=0.5 - 2.0 ** -12)
-        act(b("DH"), b("DS"), bias=-2.0 ** 23)
-        if not end:
-            row(r)
-        for c in range(8):
-            o, n = seg(c)
-            ts(b("EQ", o, o + n), b("tcol", 0, n), b("TL", c, c + 1), A.is_equal, b("LC", c, c + 1), A.mult)
-        tt(b("U"), b("M"), b("LC", 0, 32), A.min)
-        scan(b("RE"), b("EQ"), b("KE"), -8192.0, A.max, A.add)
-        tt(b("q2"), nd("XS", 0, 24, slice(0, 2), al), b("M", 8, 24), A.max)
-        cp(b(uu, 0, 24), b("U", 8, 32))
-        for h, e in enumerate(ends("RE")):
-            tt(b("dd", 4 * h, 4 * h + 4), e, b("U", 4 * h, 4 * h + 4), A.max)
-        tt(b("q1"), b("q2", 0, 8), b("q2", 8, 16), A.min)
+        lin(b("DFg"), ind("DF", 2064, "pos"))
+        lin(b("XQg"), ind("X", XW, uu, 0, 8))
+        mm((b("ps", 0, 128), b("I"), b("DFg"), True, False), (b("ps", 0, 128), b("I2"), b("XQg"), False, True))
+        lin(b("DS"), b("ps", 0, 128), 0.5 - 2.0 ** -12, 2.0 ** 23)
+        lin(b("DH"), b("DS"), 1.0, -2.0 ** 23)
+        lin(b("tcol"), ind("IOT", XW, uu, 0, 8))
+        for h, e in enumerate(lower("NE", "RE", "tcol", "TL", "TS")):
+            tt(b("d0", 4 * h, 4 * h + 4), b("LC", 4 * h, 4 * h + 4), e, A.subtract)
+        tt(b("dd"), b("d0"), b("U", 0, 8), A.max)
         cp(b("didx"), b("dd"))
-        if not end:
-            tt(b("y2"), b("dn"), b("cmv"), A.mult)
-        tt(b("q0"), b("q1"), nd("XS", 0, 24, 2, al), A.min)
         cp(ind("X", XW, "didx"), b("DH"))
         if last:
             dma("Y", T.yd[:], T.X[:, 0:2048], r=[b("X", 0, 2048)])
+        tt(b("q2"), XS(slice(0, 2), al), b("M", 8, 24), A.max)
+        tt(b("q1"), b("q2", 0, 8), b("q2", 8, 16), A.min)
+        tt(b("q0"), b("q1"), XS(2, al), A.min)
         ts(b(se), b("q0"), -1152.0, A.add)
-        if not end:
-            ts(b("y3"), zs, -4096.0 * 255.5, A.add)
-            tt(b("y2"), b("y2"), v, A.add)
-            ts(b("y4"), b("q1"), -1.0, A.mult, 4096.0, A.add)
-        tt(b("WN", 0, 128), ind("TRZ", 272, uu, 16, 24), b("uE"), A.mult)
-        act(b("L", n0, n0 + 128), ind("WN", 384, se))
-        if not end:
-            tt(b("y5"), b("y2"), b("y3"), A.max)
+        tt(b("WN", 0, 128), ind("TRZ", 272, uu, 24, 32), b("uE"), A.mult)
+        lin(b("L", n0, n0 + 128), ind("WN", 384, se))
         if not last:
-            tt(ind("C", 1152, uu, 8, 16), b("CV"), b("T2"), A.subtract)
+            act(ind("C", 1152, uu, 16, 24), b("CV"), F.Silu)
         if not end:
+            tt(b("y2"), b("dn"), b("cmv"), A.mult)
+            tt(b("y7"), b("y2"), v, A.add)
+            lin(b("y3"), zs, 1.0, -4096.0 * 255.5)
+            lin(b("y4"), b("q1"), -1.0, 4096.0)
+            tt(b("y5"), b("y7"), b("y3"), A.max)
             tt(b("y6"), b("y5"), b("y4"), A.max)
             tt(v, b("y6"), DUM, A.min)
             cp(b(vz, 0, 8), v)
-            child_1(r)
+            child(r)
         if s == 0:
-            cp(b("zacc"), b("U", 24, 32))
+            lin(b("zacc"), b("U", 24, 32))
         else:
             tt(b("zacc"), b("zacc"), b("U", 24, 32), A.min)
         if end:
             cp(b("za"), b("zacc"))
             second(r, b("za"))
-        tt(ind("L", 1152, uu, 0, 8), b("uE"), b("WN", 0, 128), A.subtract)
+        tt(ind("L", 1152, uu, 8, 16), b("uE"), b("WN", 0, 128), A.subtract)
         if not end:
-            child_2()
-            child_3()
+            edge()
 
-    def roots_late():
-        hash_b(0)
-        roots(1, b("LQ"))
-
-    consts_a()
-    consts_b()
     roots(0, b("Qi"))
     cp(b("Ql"), b("Qi"))
-    row(0)
-    ts(b("C", 0, 384), b("Ci"), 1.0, A.add)
-    child_1(0)
+    ts(b("C", 0, 384), b("Ci"), float(CO), A.add)
     ts(b("L", 0, 384), b("Ei"), -1.0, A.mult, 2047.0, A.add)
-    cp(b("lsave", 0, 1), b("L", 0, 1))
+    lin(b("lsave", 0, 1), b("L", 0, 1))
     ms(b("L", 0, 1), -1.0)
-    child_2()
+    child(0)
     cp(b("QF"), b("Qi"))
     ms(b("X", 2048, XW), FAR)
     cp(b("xsave", 0, 1), b("X", 2047, 2048))
     ms(b("X", 2047, 2048), NONE)
-    child_3()
+    edge()
     travel("QF", "LQ", "E")
-    act(b("STD"), b("IOT", 0, 1152), F.Silu, scale=0.0)
-    acts_1(0)
-    xq(0)
     cp(b("Q16"), b("Qi"))
-    consts_c()
     for s in range(S_):
         step(0, s)
-    row(1)
-    acts_1(1)
-    cut_1(0, 2)
-    acts_2(1, 0)
-    cut_2(0, 2)
-    cut_3(0, 2)
-    child_1(1)
-    child_2()
+    cut_rows(0, 2)
+    child(1)
+    edge()
     tt(b("HK"), b("LK"), b("HMQ"), A.mult)
-    child_3()
     tt(b("QF"), b("HK"), b("LQ"), A.add)
     cp(b("Ql"), b("QF"))
+    cp(b("Q16"), b("QF"))
     for s in range(S_):
         step(1, s)
-    unmade_1(1)
-    unmade_2(1)
-    act(b("YE", 0, 384), b("L", 0, 384), bias=2047.0, scale=-1.0)
-    act(b("YE", 0, 1), b("lsave", 0, 1), bias=2047.0, scale=-1.0)
+    unmade(1)
+    lin(b("YE", 0, 384), b("L", 0, 384), -1.0, 2047.0)
+    lin(b("YE", 0, 1), b("lsave", 0, 1), -1.0, 2047.0)
     for r in range(RO_):
         n1 = 384 + 256 * r
         for j, o in ((128, 0), (0, 1)):
-            act(b("YE", n1 + o, n1 + 256, 2), b("L", n1 + j, n1 + j + 128), bias=2047.0, scale=-1.0)
-    dma("S", T.ye[:], T.YE[:], r=[b("YE")])
+            lin(b("YE", n1 + o, n1 + 256, 2), b("L", n1 + j, n1 + j + 128), -1.0, 2047.0)
+    dma("S", T.ye[:, 0:640], T.YE[:, 0:640], r=[b("YE", 0, 640)])
+    dma("S", T.ye[:, 640:896], T.YE[:, 640:896], r=[b("YE", 640, 896)])
     dma("Y", T.yr[:], T.LAND1[:], r=[b("LAND1")])
     K["flush"]()
     for s, n in K["final"].items():

@@ -8,7 +8,7 @@ PLACE = {}
 
 
 def _b(name, n, d, where="sbuf"):
-    pool = {F32: "poolf", U16: "poolu", I32: "pooli"}.get(d)
+    pool = {F32: "poolf", U16: "poolu", I32: "pooli", BF: "poolb"}.get(d)
     if isinstance(n, list):
         SCRATCH[name] = (where, [128] + n, d)
     elif n > 40 or where != "sbuf" or pool is None:
@@ -23,27 +23,28 @@ def _b(name, n, d, where="sbuf"):
 XW, LL = 2320, 137
 for _d, _l in (
     (BF, "X:2320 XQ:2048 DF:2064 BO:128 I:128 I2:128 Im:128 IH:128 IR:128 B0:128 SHD:128 ZH:272 ZL:272 OHZ:272 TRZ:272 "
-         "IDZ:272 OHB:272 KD:128 KT:128 KA:576 KB:18 K3:137 M16:137 RD:137 RMP:137 OH:128 AD:576 RA:576 NE:576 RE:576 SG:128 SS:128 "
-         "XQg:128 DFg:128 DH:128 KGE:128 LK:128 xsave:16"),
-    (F32, "L:1152 C:1152 STD:1152 IOT:2320 W1:137 W2:137 W3:137 W4:137 W3n:137 S1:137 S2:137 S3:137 S4:137 QF:128 uQ0:128 uQ1:128 LQ:128 "
+         "IDZ:272 OHB:256 OHC:256 KD:128 KT:128 KA:576 KB:18 K3:137 M16:137 RD:137 RMP:137 OH:128 AD:576 RA:576 NE:576 RE:576 SG:128 SS:128 "
+         "XQg:128 DFg:128 DH:128 xsave:16 I4:128 Im4:128 K32:32 athr:8 nf:8 E1:8 A1:8 zcf:8 y3:8 made:16"),
+    (F32, "L:1152 C:1152 STD:1152 IOT:2320 W1:137 W2:137 W3:137 W4:137 W3n:137 S1:137 S2:137 S3:137 S4:137 QF:128 uQ0:128 uQ1:128 "
           "LAND1:128 SND:128 HMQ:128 HK:128 uE:128 CV:128 T2:128 SC:128 SE:128 SQ:128 tcol:128 vcol:128 DS:128 WN:384 WC:384 "
-          "OHN:256 OHM:128 X5:128 X6:128 YE:896 cols:14 THR:6 THS:6 LC:40 lsave:2 v0:8 v1:8 zs0:8 zs1:8 zacc:8 cf:8 cmv:8 athr:8 aleaf:8 "
-          "acut:8 nf:8 x1:8 x2:8 x3:8 x4:8 x5:8 zp:8 T0:8 T1:8 TL:8 TS:8 Ap:8 G:8 M:32 U:32 zcf:8 dn:8 y1:8 y2:8 y3:8 y4:8 y5:8 y6:8 y7:8 "
-          "q2:16 q1:8 q0:8 d0:8 dd:8"),
+          "OHM:128 LK:48 LN:128 X5:128 X6:128 YE:896 cols:14 THR:6 THS:6 LC:40 lsave:2 v0:8 v1:8 zs0:8 zs1:8 zacc:8 cf:8 "
+          "I32:128 Im32:128 JC:8 x2:8 x5:8 zp:8 TL:8 TS:8 U:32 dn:8 y1:8 y2:8 D4:8 r1:8 d0:8 dd:8"),
     (H16, "Q16:128 Q1:128 N16:256 B620:137 M1:128 EL:128 Y:128 Hf:128 Hm:128"),
-    (I32, "Qi:128 Ci:384 Ei:384 QI:137 QA:137 HP:128 HI:128 IP:2 IC:2 qi:8 qj:16 RW:8"),
-    (U16, "Ql:128 El:128 vz0:16 vz1:16 cl:8 pos:8 UU0:40 UU1:40 sl:8 se0:8 se1:8 za:8 didx:8"),
+    (I32, "Qi:128 LQ:128 Ci:384 Ei:384 QI:137 QA:137 HP:128 HI:128 IP:2 IC:2 qi:8 qj:16 RW:8"),
+    (U16, "Ql:128 El:128 vz0:16 vz1:16 cl:8 pos:8 tq:8 lz:8 zo:8 UU0:40 UU1:40 sl:8 se0:8 se1:8 za:8 didx:8"),
 ):
     for _x in _l.split():
         _b(_x.split(":")[0], int(_x.split(":")[1]), _d)
-_b("AB", [128, 17], BF); _b("QX", [8, 8, 16], H16); _b("XS", [3, 8], F32); _b("CZ", 144, BF)
+_b("AB", [128, 17], BF); _b("QX", [8, 8, 16], H16); _b("CZ", 144, BF)
 PS = ["pd", "pm", "pt", "ps", "pq", "pe", "pw", "ph"]
 for _n in PS:
     _b(_n, 512, F32, "psum")
-SEMAPHORES = ["sV", "sT", "sS", "sG", "locE", "loc0", "loc1", "arrE", "arr0", "arr1"] + ["d%d" % _i for _i in range(12)]
+SEMAPHORES = ["sV", "sT", "sS", "sG", "locE", "loc0", "loc1", "arrE", "arr0", "arr1"] + ["d%d" % _i for _i in range(20)]
 NDUM, NDUMP, TDUMP, BIG, HH, FRZ, CO = 896, 1024, 2050, float(2 ** 22), float(2 ** 22), float(2 ** 24), 32
 FAR, NONE = 294.0, 560.0
-HOP, FLY, LEAN = 300, 3000, 300
+PLANS, PASSES = [(_h, _l) for _h in (280, 300, 320, 350) for _l in (100, 300, 600)], 4
+HOP, FLY = 240, 3000
+CHUNKS = (0, 16, 40, 64, 88, 112, 128)
 ORDER = []
 
 
@@ -155,24 +156,58 @@ def make(g, T):
                     l.append((x[1], x[2], isw, i))
             p.pop(i, None)
             pred.append(p)
-        level = [op[3] + op[4] for op in ops]
-        gap = lambda j, i, qj, qi: 0 if qj == qi and (qi == "T" or not pred[i][j]) else ops[j][4]
-        for i in reversed(range(len(ops))):
+        every = range(len(ops))
+        succ = [[] for op in ops]
+        for i in every:
             for j in pred[i]:
-                level[j] = max(level[j], ops[j][3] + gap(j, i, ops[j][0], ops[i][0]) + level[i] + 1)
-        place, busy = {}, {q: [] for q in eng}
-        for i in sorted(range(len(ops)), key=lambda i: (-level[i], i)):
-            best = None
-            for k, op in enumerate([ops[i]] + list(ops[i][6:])):
-                t, l, at = max([place[j][1] + gap(j, i, place[j][2], op[0]) for j in pred[i]] + [0]), busy[op[0]], 0
-                while at < len(l) and l[at][0] < t + op[3]:
-                    t = max(t, l[at][1])
-                    at += 1
-                if best is None or t + op[3] + LEAN < best[1]:
-                    best = (t, t + op[3], op[0], k, at)
-            busy[best[2]].insert(best[4], best[:2])
-            place[i] = best
-        return [(i, place[i][3]) for i in sorted(range(len(ops)), key=lambda i: (place[i][0], -level[i]))]
+                succ[j].append(i)
+
+        def gap(j, i, qj, qi, hop):
+            return 0 if qj == qi and (qi == "T" or not pred[i][j]) else hop if ops[j][4] == HOP else ops[j][4]
+
+        def sweep(seq, back, hop, lean):
+            place, busy = {}, {q: [] for q in eng}
+            for i in seq:
+                best = None
+                for k, op in enumerate([ops[i]] + list(ops[i][6:])):
+                    if back:
+                        t = max([place[j][1] + gap(i, j, op[0], place[j][2], hop) for j in succ[i]] + [op[4]])
+                    else:
+                        t = max([place[j][1] + gap(j, i, place[j][2], op[0], hop) for j in pred[i]] + [0])
+                    l, at = busy[op[0]], 0
+                    while at < len(l) and l[at][0] < t + op[3]:
+                        t = max(t, l[at][1])
+                        at += 1
+                    if best is None or t + op[3] + lean < best[1]:
+                        best = (t, t + op[3], op[0], k, at)
+                busy[best[2]].insert(best[4], best[:2])
+                place[i] = best
+            return place
+
+        def span(seq, hop, slow):
+            end, free = {}, {q: 0 for q in eng}
+            for i, k in seq:
+                op = ops[i][6] if k else ops[i]
+                t = max([end[j][0] + gap(j, i, end[j][1], op[0], hop) for j in pred[i]] + [free[op[0]]])
+                free[op[0]] = t + op[3] * (slow if op[0] in "VS" else 1)
+                end[i] = (free[op[0]], op[0])
+            return max(end[i][0] + ops[i][4] for i in every)
+
+        kept = None
+        for hop, lean in PLANS:
+            level = [op[3] + op[4] for op in ops]
+            for i in reversed(every):
+                for j in pred[i]:
+                    level[j] = max(level[j], ops[j][3] + gap(j, i, ops[j][0], ops[i][0], hop) + level[i] + 1)
+            place = sweep(sorted(every, key=lambda i: -level[i]), False, hop, lean)
+            for _ in range(PASSES):
+                place = sweep(sorted(every, key=lambda i: (-place[i][1], level[i])), True, hop, lean)
+                place = sweep(sorted(every, key=lambda i: (-place[i][1], -level[i])), False, hop, lean)
+                seq = [(i, place[i][3]) for i in sorted(every, key=lambda i: (place[i][0], -level[i]))]
+                t = span(seq, HOP, 1) + span(seq, 1.25 * HOP, 1.4) / 1.4
+                if kept is None or t < kept[0]:
+                    kept = (t, seq)
+        return kept[1]
 
     def flush():
         if not ORDER:
@@ -228,7 +263,7 @@ def make(g, T):
             for o, lt, rh, st, sp in lst:
                 ins = g.tensor.matmul(ap(o), ap(lt), ap(rh), st, sp)
             fin("T", ins)
-        ops.append(("T", r, w, sum(max(64, size(x[0])) for x in lst) / 2, HOP, emit))
+        ops.append(("T", r, w, sum(max(64, size(x[0])) * (2 if SCRATCH[x[1][0]][2] == F32 else 0.5) for x in lst), HOP, emit))
 
     def dma(q, out, in_, r=(), w=()):
         sem = "d%d" % ndma[0]
@@ -239,7 +274,8 @@ def make(g, T):
             snap[(sem, 16)] = dict(known[q])
             final[sem] = 16
             eng[q].dma_start(out, in_).then_inc(T.sem[sem], 16)
-        ops.append((q, list(r), list(w), 120, FLY + size((list(r) + list(w))[0]), emit))
+        x = (list(r) + list(w))[0]
+        ops.append((q, list(r), list(w), 120 + size(x) * (0.8 if SCRATCH[x[0]][2] == BF else 1.6), FLY - 600, emit))
 
     return dict(tt=tt, ts=ts, cp=cp, ms=ms, scan=scan, act=act, iota=iota, sel=sel, mm=mm, dma=dma, wait=wait, deps=deps,
                 known=known, final=final, acc=acc, ops=ops, flush=flush, lin=lin, either=either)
@@ -302,13 +338,11 @@ def rank_program(g, core, T, topo):
 
     CS = col(4)
     DT, DD, DUM = b("LC", 0, 8), b("LC", 8, 16), b("LC", 32, 40)
-    XS = lambda *i: nd("XS", 0, 24, *i)
 
     dma("Y", T.Qi[:], T.req[:], w=[b("Qi")])
-    dma("S", T.Ci[:], T.child[:], w=[b("Ci")])
+    dma("Y", T.Ci[:], T.child[:], w=[b("Ci")])
+    dma("Y", T.X[:, 0:2048], T.desc[:], w=[b("X", 0, 2048)])
     dma("Y", T.Ei[:], T.edge[:], w=[b("Ei")])
-    dma("S", T.X[:, 0:1024], T.desc[:, 0:1024], w=[b("X", 0, 1024)])
-    dma("Y", T.X[:, 1024:2048], T.desc[:, 1024:2048], w=[b("X", 1024, 2048)])
 
     iota(b("IP", 0, 1), [[1, 1]], 0, 1, False)
     iota(b("ZH"), [[1, 17], [0, 16]], 0, 0)
@@ -322,14 +356,16 @@ def rank_program(g, core, T, topo):
     iota(b("K3", 1, LL), [[0, 8], [16, 17]], 0, 0)
     iota(b("W4", 1, LL), [[256, 8], [1, 17]], 0, 16)
     iota(b("THR"), [[256, 6]], 192, 0)
-    iota(XS(al, al), [[128, 3], [16, 8]], 1152, 1)
+    iota(b("JC"), [[16, 8]], 256, 1)
     ts(b("IC", 0, 1), b("IP", 0, 1), 4, A.arith_shift_right)
     ts(b("IC", 1, 2), b("IP", 0, 1), 15, A.bitwise_and)
     cp(col(0), b("IP", 0, 1))
     cp(b("cols", 1, 3), b("IC"))
     ms(b("C", 384, NDUM), float(CO))
     for n, lo, hi in (("L", 384, 896), ("L", 896, 1152), ("STD", 0, 512), ("STD", 512, 1024), ("STD", 1024, 1152)):
-        act(b(n, lo, hi), b("C", 384, 384 + hi - lo), F.Silu, scale=0.0)
+        act(b(n, lo, hi), b("C", 384, 384 + hi - lo), F.Silu if lo == 384 else F.Copy, scale=0.0)
+        if lo == 384:
+            K["ops"][-1] = K["ops"][-1][:3] + (K["ops"][-1][3] + 1600,) + K["ops"][-1][4:]
     lin(col(3), col(2), 1.0, 1.0)
     ts(col(5), col(2), 0.0, A.is_equal)
     ts(col(6), col(2), 0.0, A.is_gt)
@@ -347,16 +383,23 @@ def rank_program(g, core, T, topo):
     ts(b("OHZ"), b("ZL"), col(2), A.is_equal)
     ts(b("IDZ"), b("ZH"), col(2), A.is_equal)
     ts(b("TRZ"), b("ZH"), col(2), A.is_le)
-    lin(b("OHB"), b("OHZ"), 4096.0 - CO, float(CO))
+    lin(col(13), col(2), -1.0, 15.0)
+    ts(b("OHC"), b("ZL", 0, 256), col(13), A.is_equal, 4224.0, A.mult)
+    ts(b("OHB"), b("ZH", 0, 256), col(2), A.is_equal, 4096.0, A.mult)
+    tt(b("OHB"), b("OHB"), b("OHC"), A.max)
+    lin(b("OHB"), b("OHB"), 1.0, -4096.0)
     ts(b("I"), b("IOT", 0, 128), col(0), A.is_equal)
-    for n, c in (("IH", HH / 2), ("IR", 2.0 ** 37), ("I2", 2.0), ("Im", -1.0)):
+    for n, c in (("IH", HH / 2), ("IR", 2.0 ** 37), ("I2", 2.0), ("Im", -1.0), ("I4", 4096.0), ("Im4", -4096.0),
+                 ("I32", 1.0), ("Im32", -1.0)):
         lin(b(n), b("I"), c)
     lin(col(12), col(1), 16.0, 15.0)
     ts(b("CZ"), b("IOT", 0, 144), col(12), A.is_equal, -HH, A.mult)
     lin(DT, DT, 1.0, col(9))
     lin(b("LC", 8, 24), b("LC", 8, 24), 1.0, col(8))
     lin(DUM, DUM, 1.0, col(8))
-    lin(XS(al, al), XS(al, al), 1.0, col(8))
+    lin(b("JC"), b("JC"), 1.0, col(8))
+    ms(b("K32"), 0.0)
+    ms(b("K32", 16, 24), 1.0)
     lin(b("W4", 1, LL), b("W4", 1, LL), 1.0, col(10))
     lin(b("THR"), b("THR"), col(7))
     lin(b("THS"), b("THR"), -32768.0)
@@ -388,14 +431,29 @@ def rank_program(g, core, T, topo):
         cp(b("v%d" % r), b("qj", 0, 8))
         ts(b("zs%d" % r), b("qj", 8, 16), 4096.0, A.mult)
 
-    def child(r):
+    def roots_first():
+        ts(b("HP"), b("Qi"), 4, A.arith_shift_right)
+        ts(b("HI"), b("Qi"), 15, A.bitwise_and)
+        ts(b("Q1"), b("HP"), 1.0, A.add)
+        ts(b("Hf"), b("HI"), 1.0, A.add)
+        ts(b("X5"), b("Hf"), 16.0, A.mult)
+        mm((b("pw", 0, 128), b("B0"), b("Q1"), True, True))
+        mm((b("pe", 0, 128), b("B0"), b("Hf"), True, True))
+        ts(b("vz0", 0, 8), diag("SQ", b("pw", 0, 128)), CS, A.mult, -1.0, A.add)
+        ts(b("OH"), b("pe", 0, 128), col(3), A.is_equal)
+        lin(b("v0"), b("SQ", 15, 128, 16), CS, -1.0)
+        lin(b("y1"), diag("SE", b("pe", 0, 128)), CS, -1.0)
+        lin(b("zs0"), b("y1"), 4096.0)
+
+    def child(r, row=True):
         vz = "vz%d" % r
-        lin(b("OH"), ind("OHZ", 272, vz, 8, 16))
+        if row:
+            lin(b("OH"), ind("OHZ", 272, vz, 8, 16))
         tt(b("M1"), ind("C", 1024, vz, 0, 8), b("OH"), A.mult)
         mm((b("pm", 0, 128), b("BO"), b("M1"), True, True))
         ts(b("cl"), diag("SC", b("pm", 0, 128)), CS, A.mult, -float(CO), A.add)
         lin(b("cf"), b("SC", 15, 128, 16), CS, -float(CO))
-        tt(b("cmv"), b("cf"), b("v%d" % r), A.subtract)
+        mm((b("pw", 272, 280), b("I32"), b("cf"), True, False), (b("pw", 272, 280), b("Im32"), b("v%d" % r), False, True))
 
     def edge():
         ts(b("El"), ind("L", 1024, "cl"), -1.0, A.mult, 2047.0, A.add)
@@ -412,14 +470,10 @@ def rank_program(g, core, T, topo):
         for h, e in enumerate(lower("AD", "RA", "vcol", "v%d" % r, "x5")):
             out = b("athr", 4 * h, 4 * h + 4)
             either(lambda: act(out, e, F.Relu, bias=BIG, scale=-BIG / 2048), lambda: ts(out, e, 0.5, A.is_lt, BIG, A.mult))
-        tt(b("x1"), zs, v, A.subtract)
-        tt(b("aleaf"), b("x1"), b("athr"), A.subtract)
-        tt(b("x2"), b("athr"), v, A.max)
-        tt(b("x2"), b("x2"), DD, A.min)
+            tt(b("D4", 4 * h, 4 * h + 4), b("LC", 8 + 4 * h, 12 + 4 * h), e, A.subtract)
+        tt(b("x2"), b("D4"), v, A.max)
         cp(b("sl"), b("x2"))
         act(ind("STD", 1152, "sl"), b("IOT", o, o + 128), F.Silu)
-        lin(b("x3"), zs, 1.0, 4096.0)
-        tt(b("x4"), b("x3"), b("athr"), A.add)
 
     def stood(r, s):
         j = 3 * r + s
@@ -427,11 +481,10 @@ def rank_program(g, core, T, topo):
         e = diag("SS", b("SG"))
         either(lambda: act(b("nf"), e, F.Relu, bias=b("THS", j, j + 1), scale=32768.0),
                lambda: ts(b("nf"), e, b("THR", j, j + 1), A.is_gt, BIG, A.mult))
-        tt(b("acut"), b("x4"), b("nf"), A.add)
 
     def payload():
         for x in range(8):
-            ts(nd("QX", 0, 1024, al, x, al), b("Q16"), b("BO", 16 * x, 16 * x + 1), A.mult)
+            ts(nd("QX", 128 * x, 128 * x + 128, al, x, al), b("Q16"), b("BO", 16 * x, 16 * x + 1), A.mult)
         mm(*[(b("pq", 1 + 17 * c, 18 + 17 * c), nd("QX", 0, 1024, c, al, al), b("IDZ", 0, 272, 16), True, True) for c in range(8)])
         cp(b("QI", 1, LL), b("pq", 1, LL))
         ts(b("QA", 1, LL), b("QI", 1, LL), 15, A.bitwise_and)
@@ -444,13 +497,13 @@ def rank_program(g, core, T, topo):
         src = b("QF" if r else "LQ")
         if r == 0:
             cp(b("Q16"), src)
-        mm((b("ph", 0, 128), b("SHD"), b("Q16"), True, True))
-        tt(b("HP"), b("ph", 0, 128), src, A.mult)
+        mm((b("pq", 256, 384), b("SHD"), b("Q16"), True, True))
+        tt(b("HP"), b("pq", 256, 384), src, A.mult)
         ts(b("HI"), b("HP"), 5, A.arith_shift_right, 2047, A.bitwise_and)
         cp(b("Hf"), b("HI"))
         ts(b("Hm"), b("HI"), 2046.5, A.is_gt, -2047.0, A.mult)
-        mm(*[(b("ph", 128, 256), b(w), b(x), x == "Hf", x == "Q16") for w, x in (("I", "Hf"), ("I", "Hm"), ("Im", "Q16"))])
-        lin(b("HMQ"), b("ph", 128, 256), col(6))
+        mm(*[(b("pq", 384, 512), b(w), b(x), x == "Hf", x == "Q16") for w, x in (("I", "Hf"), ("I", "Hm"), ("Im", "Q16"))])
+        lin(b("HMQ"), b("pq", 384, 512), col(6))
 
     def distances(r, s):
         pd = b("pd", 1, LL)
@@ -458,27 +511,31 @@ def rank_program(g, core, T, topo):
             act(at0("RD"), b("zs%d" % r), F.Relu, bias=-15.0, scale=2.0 ** -12)
             scan(b("RMP", 1, LL), b("M16", 1, LL), b("RD", 1, LL), 0.0, A.add, A.max)
         mm((pd, b("IH"), b("B620", 1, LL), True, False), *([(pd, b("IR"), b("RMP", 1, LL), False, False)] if s else []))
-        for q in range(4):
-            lo, hi = 512 * q, 512 * q + 512
-            act(b("XQ", lo, hi), ind("X", 2064, "Ql", 32 * q, 32 * q + 32))
-            tt(b("DF", lo, hi), ind("X", 2064, "El", 32 * q, 32 * q + 32), b("XQ", lo, hi), A.subtract)
-            act(nd("AB", 544 * q, 544 * q + 544, slice(32 * q, 32 * q + 32), slice(0, 16)), b("DF", lo, hi), F.Abs)
+        for lo, hi in zip(CHUNKS, CHUNKS[1:]):
+            lin(b("XQ", 16 * lo, 16 * hi), ind("X", 2064, "Ql", lo, hi))
+            tt(b("DF", 16 * lo, 16 * hi), ind("X", 2064, "El", lo, hi), b("XQ", 16 * lo, 16 * hi), A.subtract)
+            act(nd("AB", 17 * lo, 17 * hi, slice(lo, hi), slice(0, 16)), b("DF", 16 * lo, 16 * hi), F.Abs)
         for h in range(2):
             mm(*[(b("pd", 1 + 68 * h, 69 + 68 * h), b("CZ", 15 - p, 143 - p),
                   nd("AB", 1088 * h, 1088 * h + 1088, slice(64 * h + p, 64 * h + 64, 16), al), False, h == 1 and p == 15) for p in range(16)])
 
     def cut_rows(r, s):
         uu, n1, n0 = "UU%d" % (s % 2), 384 + 256 * r, 512 + 256 * r
-        tt(b("EL"), ind("IDZ", 272, uu, 24, 32), b("WN", 0, 128), A.mult)
+        end = s == S_ - 1
+        tt(b("EL"), ind("IDZ", 272, uu, 24, 32), b("X6") if end else b("WN", 0, 128), A.mult)
         mm((b("pe", 0, 128), b("BO"), b("EL"), True, True))
         if r == 0:
             lin(b("WC", 256, 384), b("C", n0, n0 + 128))
             lin(b("C", n0, n0 + 128), ind("WC", 384, "se%d" % (s % 2)))
-        ts(b("RW"), diag("SE", b("pe", 0, 128)), CS, A.mult)
-        ts(b("RW"), b("RW"), 15, A.bitwise_and)
-        ts(b(uu, 32, 40), b("RW"), -1.0, A.mult, 15.0, A.add)
-        tt(b("OHN"), ind("OHB", 272, uu, 24, 40), b("IOT", n1 + CO, n1 + CO + 256), A.min)
-        tt(b("OHM"), b("OHN", 0, 128), b("OHN", 128, 256), A.max)
+        if end:
+            ts(b(uu, 32, 40), diag("SE", b("pe", 0, 128)), CS, A.mult, -1.0, A.add)
+        else:
+            ts(b("RW"), diag("SE", b("pe", 0, 128)), CS, A.mult)
+            ts(b("RW"), b("RW"), 15, A.bitwise_and)
+            tt(b("RW"), b("RW"), b("r1"), A.add)
+            ts(b("RW"), b("RW"), 255, A.bitwise_and)
+            cp(b(uu, 32, 40), b("RW"))
+        tt(b("OHM"), ind("OHB", 256, uu, 32, 40), b("IOT", n1 + CO, n1 + CO + 128), A.add)
         act(ind("C", 1152, uu, 8, 16), b("OHM"), F.Silu)
 
     def second(r, lst):
@@ -486,20 +543,23 @@ def rank_program(g, core, T, topo):
 
     def unmade(r):
         n1 = 384 + 256 * r
-        tt(b("Y"), b("L", n1 + 128, n1 + 256), b("uQ%d" % r), A.subtract)
-        tt(b("EL"), ind("IDZ", 272, "za"), b("Y"), A.mult)
-        mm((b("pe", 0, 128), b("BO"), b("EL"), True, True))
         lin(b("X5"), b("pe", 0, 128), 1.0, 1.5 * 2 ** 27)
         lin(b("X5"), b("X5"), 1.0, -1.5 * 2 ** 27)
         tt(b("X6"), b("pe", 0, 128), b("X5"), A.not_equal)
-        tt(b("L", n1, n1 + 128), b("L", n1, n1 + 128), b("X6"), A.mult)
+        tt(b("LN") if r else b("L", n1, n1 + 128), b("L", n1, n1 + 128), b("X6"), A.mult)
 
-    def travel(src, land, tag):
-        lin(b(land, 0, 16), b(src, 0, 16))
-        K["ops"].append(("G", [b(src)], [b(land, 16, 128)], 1400, FLY, lambda: send(src, land, tag)))
+    def at_cut(r, src, lst, start, stop):
+        tt(b("Y"), src, b("uQ%d" % r), A.subtract)
+        tt(b("EL"), ("@", b("IDZ"), lst), b("Y"), A.mult)
+        mm((b("pe", 0, 128), b("BO"), b("EL"), start, stop))
 
-    def send(src, land, tag):
+    def travel(src, land, tag, n=16, at=16):
+        (cp if tag == "E" else lin)(b(land, 0, n), b(src, 0, n))
+        K["ops"].append(("G", [b(src)], [b(land, at)], 1400, FLY * (3 if tag == "E" else 1), lambda: send(src, land, tag, n, at)))
+
+    def send(src, land, tag, w, at):
         sent = [0]
+        part = lambda x: T[x[0]][x[3]]
         deps("G", [b(src)], [], "loc" + tag, 0)
         for calls in plan(core, T.cores, topo):
             tr = []
@@ -507,13 +567,13 @@ def rank_program(g, core, T, topo):
                 e = (T.rank_of(d) - rank) % 8
                 rid, pid = topo.addr(d, core)
                 tr.append(RemoteDMATransfer(dst_ids=[DstId(rid=rid, pnc=pid)], dma_engine_mask=sum(1 << x for x in en),
-                                            remote_sem=T.sem["arr" + tag], src=T[src][:, 16 * e:16 * e + 16],
-                                            dst=T[land][:, 16 * e:16 * e + 16]))
+                                            remote_sem=T.sem["arr" + tag], src=part(b(src, w * e, w * e + w)),
+                                            dst=part(b(land, at * e, at * e + w))))
                 sent[0] += len(en)
             g.remote_dma_fused(tr, local_sem=T.sem["loc" + tag])
         n = sum(len(en) for s in T.cores if s != core for calls in plan(s, T.cores, topo) for d, en in calls if d == core)
-        K["acc"].setdefault(land, []).append((16, 128, 1, "R", "arr" + tag, n, True))
-        K["acc"].setdefault(src, []).append((0, 128, 0, "R", "loc" + tag, sent[0], True))
+        K["acc"].setdefault(land, []).append((at, 8 * at, 1, "R", "arr" + tag, n, True))
+        K["acc"].setdefault(b(src)[0], []).append((b(src)[1], b(src)[2], 0, "R", "loc" + tag, sent[0], True))
         K["final"]["arr" + tag] = n
         K["final"]["loc" + tag] = sent[0]
 
@@ -538,11 +598,19 @@ def rank_program(g, core, T, topo):
             second(r, b("UU0", 24, 32))
             hashes(r)
         if (r, s) == (1, 0):
+            at_cut(0, b("L", 512, 640), b("za"), True, True)
             unmade(0)
+        if last:
+            cp(b("zo"), b("zacc"))
+            at_cut(r, b("L", n0, n0 + 128), b("zo"), True, False)
         if (r, s) == (0, 1):
             roots(1, b("LQ"))
+        if (r, s) == (0, 2):
+            cp(b("HP"), b("El"))
+            ts(b("HP"), b("HP"), 15, A.bitwise_and)
+            tt(b("X6"), b("X5"), b("HP"), A.subtract)
         lin(b("uE"), ind("L", 1024, "cl"))
-        lin(b("WN", 256, 384), b("L", n0, n0 + 128))
+        dma("Y", T.WN[:, 256:384], T.L[:, n0:n0 + 128], r=[b("L", n0, n0 + 128)], w=[b("WN", 256, 384)])
         if not last:
             leaf(r)
         if r == 0:
@@ -550,39 +618,46 @@ def rank_program(g, core, T, topo):
         for n in "2314":
             scan(rev("S" + n), rev("pd"), rev("W" + n), 0.0, A.min, A.max)
         s3 = at0("S3")
-        Mx, Mc, Mv, Mz = (b("M", 8 * i, 8 * i + 8) for i in range(4))
-        lin(b("zp"), at0("S2"), 1.0, 4096.0 * HH - 4096.0)
-        tt(b("T0"), b("acut"), s3, A.subtract)
+        M = [b("ph", 8 * i, 8 * i + 8) for i in range(4)]
+        mm((b("ph", 0, 32), b("I4"), b("K32"), True, False), (M[1], b("I32"), b("cf"), False, False), (M[2], b("I32"), v, False, False),
+           *[(M[i], b("I"), b("athr"), False, False) for i in range(4)])
+        mm(*[(M[i], b("I"), b("nf"), False, False) for i in (0, 1, 3)])
+        lin(b("zp"), at0("S2"), 1.0, 4096.0 * HH)
+        tt(b("E1"), s3, zs, A.is_le)
         tt(b("TL"), at0("S1"), s3, A.subtract)
-        tt(b("Ap"), s3, b("zp"), A.subtract)
-        tt(b("T1"), s3, b("aleaf"), A.subtract)
+        tt(b("A1"), s3, b("zp"), A.is_ge)
         lin(b("zcf"), s3, 2.0 ** -12)
         lin(b("TS"), b("TL"), 4096.0)
         cp(b("pos"), at0("S4"))
-        tt(b("G"), b("T0"), b("Ap"), A.max)
-        tt(Mx, b("TL"), b("G"), A.max)
-        tt(Mc, b("cf"), b("G"), A.max)
-        tt(Mv, b("T1"), b("Ap"), A.max)
-        tt(Mz, b("zcf"), b("G"), A.max)
-        tt(b("U"), b("M"), b("LC", 0, 32), A.min)
+        mm(*[(b("pt", 256, 264), b(w), b(x), x == "athr", x == "A1")
+             for w, x in (("I", "athr"), ("I", "nf"), ("I4", "E1"), ("I32", "TL"), ("I4", "A1"))])
+        ts(b("tq"), b("pt", 256, 264), 2048.0, A.min)
+        mm(*[(M[i], b("Im4" if i == 2 else "I4"), b("E1"), False, False) for i in range(4)], (M[0], b("I32"), b("TL"), False, False),
+           (M[3], b("I"), b("zcf"), False, False), *[(M[i], b("I4"), b("A1"), False, i == 3) for i in range(4)])
+        tt(b("U"), b("ph", 0, 32), b("LC", 0, 32), A.min)
         cp(b(uu, 0, 32), b("U"))
-        tt(b("dn"), b("Ap"), b("athr"), A.is_gt)
+        if (r == 0 or s == 0) and not end:
+            lin(b("r1"), b("U", 24, 32), 16.0)
+        tt(b("dn"), b("A1"), b("athr"), A.is_gt)
         tt(b("y1"), b("dn"), s3, A.mult)
-        tt(zs, zs, b("y1"), A.max)
-        ts(b(vz, 8, 16), zs, 2.0 ** -12, A.mult)
         if last:
-            tt(b("HK"), ind("TRZ", 272, vz, 8, 16), b("HMQ"), A.mult)
+            tt(b("CV"), ind("TRZ", 272, vz, 8, 16), b("HMQ"), A.mult)
+            ts(b("lz"), b("y1"), 2.0 ** -12, A.mult)
+            tt(b("HK"), ind("TRZ", 272, "lz"), b("CV"), A.mult)
             tt(b("SND"), b("HK"), b("QF"), A.add)
             travel("SND", "LAND1", "1")
-        elif end:
-            lin(b("KGE"), ind("TRZ", 272, vz, 8, 16))
-            travel("KGE", "LK", "0")
+        else:
+            tt(zs, zs, b("y1"), A.max)
+        if not end:
+            ts(b(vz, 8, 16), zs, 2.0 ** -12, A.mult)
+        elif r == 0:
+            travel("zs0", "LK", "0", 1, 4)
         lin(b("DFg"), ind("DF", 2064, "pos"))
-        lin(b("XQg"), ind("X", XW, uu, 0, 8))
+        lin(b("XQg"), ind("X", XW, "tq"))
         mm((b("ps", 0, 128), b("I"), b("DFg"), True, False), (b("ps", 0, 128), b("I2"), b("XQg"), False, True))
         lin(b("DS"), b("ps", 0, 128), 0.5 - 2.0 ** -12, 2.0 ** 23)
         lin(b("DH"), b("DS"), 1.0, -2.0 ** 23)
-        lin(b("tcol"), ind("IOT", XW, uu, 0, 8))
+        lin(b("tcol"), ind("IOT", XW, "tq"))
         for h, e in enumerate(lower("NE", "RE", "tcol", "TL", "TS")):
             tt(b("d0", 4 * h, 4 * h + 4), b("LC", 4 * h, 4 * h + 4), e, A.subtract)
         tt(b("dd"), b("d0"), b("U", 0, 8), A.max)
@@ -590,22 +665,20 @@ def rank_program(g, core, T, topo):
         cp(ind("X", XW, "didx"), b("DH"))
         if last:
             dma("Y", T.yd[:], T.X[:, 0:2048], r=[b("X", 0, 2048)])
-        tt(b("q2"), XS(slice(0, 2), al), b("M", 8, 24), A.max)
-        tt(b("q1"), b("q2", 0, 8), b("q2", 8, 16), A.min)
-        tt(b("q0"), b("q1"), XS(2, al), A.min)
-        ts(b(se), b("q0"), -1152.0, A.add)
+        ts(b("made"), b("U", 8, 24), NDUMP - 0.5, A.is_lt, -128.0, A.mult)
+        mm(*[(b("pt", 272, 280), b(w), x, i == 0, i == 2)
+             for i, (w, x) in enumerate((("I32", b("JC")), ("I2", b("made", 0, 8)), ("I", b("made", 8, 16))))])
+        cp(b(se), b("pt", 272, 280))
         tt(b("WN", 0, 128), ind("TRZ", 272, uu, 24, 32), b("uE"), A.mult)
         lin(b("L", n0, n0 + 128), ind("WN", 384, se))
         if not last:
             act(ind("C", 1152, uu, 16, 24), b("CV"), F.Silu)
         if not end:
-            tt(b("y2"), b("dn"), b("cmv"), A.mult)
-            tt(b("y7"), b("y2"), v, A.add)
-            lin(b("y3"), zs, 1.0, -4096.0 * 255.5)
-            lin(b("y4"), b("q1"), -1.0, 4096.0)
-            tt(b("y5"), b("y7"), b("y3"), A.max)
-            tt(b("y6"), b("y5"), b("y4"), A.max)
-            tt(v, b("y6"), DUM, A.min)
+            tt(b("y2"), b("dn"), b("pw", 272, 280), A.mult)
+            act(b("y3"), zs, F.Relu, bias=-4096.0 * 255.5)
+            mm(*[(b("pw", 256, 264), b(w), x, i == 0, i == 4) for i, (w, x) in enumerate(
+                (("I32", v), ("I32", b("y2")), ("I", b("y3")), ("Im4", b("made", 0, 8)), ("Im4", b("made", 8, 16))))])
+            tt(v, b("pw", 256, 264), DUM, A.min)
             cp(b(vz, 0, 8), v)
             child(r)
         if s == 0:
@@ -616,43 +689,46 @@ def rank_program(g, core, T, topo):
             cp(b("za"), b("zacc"))
             second(r, b("za"))
         tt(ind("L", 1152, uu, 8, 16), b("uE"), b("WN", 0, 128), A.subtract)
+        if last:
+            at_cut(r, b("uE"), b(uu, 24, 32), False, True)
+            unmade(r)
         if not end:
             edge()
 
-    roots(0, b("Qi"))
+    roots_first()
     cp(b("Ql"), b("Qi"))
     ts(b("C", 0, 384), b("Ci"), float(CO), A.add)
     ts(b("L", 0, 384), b("Ei"), -1.0, A.mult, 2047.0, A.add)
     lin(b("lsave", 0, 1), b("L", 0, 1))
     ms(b("L", 0, 1), -1.0)
-    child(0)
+    child(0, False)
     cp(b("QF"), b("Qi"))
     ms(b("X", 2048, XW), FAR)
     cp(b("xsave", 0, 1), b("X", 2047, 2048))
     ms(b("X", 2047, 2048), NONE)
     edge()
-    travel("QF", "LQ", "E")
+    travel("Qi", "LQ", "E")
     cp(b("Q16"), b("Qi"))
     for s in range(S_):
         step(0, s)
     cut_rows(0, 2)
     child(1)
     edge()
-    tt(b("HK"), b("LK"), b("HMQ"), A.mult)
+    ts(b("lz"), b("LK", 0, 32, 4), 2.0 ** -12, A.mult)
+    tt(b("HK"), ind("TRZ", 272, "lz"), b("HMQ"), A.mult)
     tt(b("QF"), b("HK"), b("LQ"), A.add)
     cp(b("Ql"), b("QF"))
     cp(b("Q16"), b("QF"))
     for s in range(S_):
         step(1, s)
-    unmade(1)
     lin(b("YE", 0, 384), b("L", 0, 384), -1.0, 2047.0)
     lin(b("YE", 0, 1), b("lsave", 0, 1), -1.0, 2047.0)
     for r in range(RO_):
         n1 = 384 + 256 * r
         for j, o in ((128, 0), (0, 1)):
-            lin(b("YE", n1 + o, n1 + 256, 2), b("L", n1 + j, n1 + j + 128), -1.0, 2047.0)
-    dma("S", T.ye[:, 0:640], T.YE[:, 0:640], r=[b("YE", 0, 640)])
-    dma("S", T.ye[:, 640:896], T.YE[:, 640:896], r=[b("YE", 640, 896)])
+            lin(b("YE", n1 + o, n1 + 256, 2), b("LN") if r and o else b("L", n1 + j, n1 + j + 128), -1.0, 2047.0)
+    dma("Y", T.ye[:, 0:640], T.YE[:, 0:640], r=[b("YE", 0, 640)])
+    dma("Y", T.ye[:, 640:896], T.YE[:, 640:896], r=[b("YE", 640, 896)])
     dma("Y", T.yr[:], T.LAND1[:], r=[b("LAND1")])
     K["flush"]()
     for s, n in K["final"].items():

@@ -8,10 +8,10 @@ PLACE = {}
 
 
 def _b(name, n, d, where="sbuf"):
-    pool = {F32: "poolf", U16: "poolu", I32: "pooli", BF: "poolb"}.get(d)
+    pool = {F32: "poolf", U16: "poolu", I32: "pooli", BF: "poolb", H16: "poolh"}.get(d)
     if isinstance(n, list):
         SCRATCH[name] = (where, [128] + n, d)
-    elif n > 40 or where != "sbuf" or pool is None:
+    elif n > (88 if d == BF else 40) or where != "sbuf" or pool is None:
         SCRATCH[name] = (where, [128, n], d)
         PLACE[name] = (name, 0, n)
     else:
@@ -22,29 +22,45 @@ def _b(name, n, d, where="sbuf"):
 
 XW, LL = 2320, 137
 for _d, _l in (
-    (BF, "X:2320 XQ:2048 DF:2064 BO:128 I:128 I2:128 Im:128 IH:128 IR:128 B0:128 SHD:128 ZH:272 ZL:272 OHZ:272 TRZ:272 "
-         "IDZ:272 OHB:256 OHC:256 KD:128 KT:128 KA:576 KB:18 K3:137 M16:137 RD:137 RMP:137 OH:128 AD:576 RA:576 NE:576 RE:576 SG:128 SS:128 "
-         "XQg:128 DFg:128 DH:128 xsave:16 I4:128 Im4:128 K32:32 athr:8 nf:8 E1:8 A1:8 zcf:8 y3:8 made:16"),
-    (F32, "L:1152 C:1152 STD:1152 IOT:2320 W1:137 W2:137 W3:137 W4:137 W3n:137 S1:137 S2:137 S3:137 S4:137 QF:128 uQ0:128 uQ1:128 "
-          "LAND1:128 SND:128 HMQ:128 HK:128 uE:128 CV:128 T2:128 SC:128 SE:128 SQ:128 tcol:128 vcol:128 DS:128 WN:384 WC:384 "
-          "OHM:128 LK:48 LN:128 X5:128 X6:128 YE:896 cols:14 THR:6 THS:6 LC:40 lsave:2 v0:8 v1:8 zs0:8 zs1:8 zacc:8 cf:8 "
-          "I32:128 Im32:128 JC:8 x2:8 x5:8 zp:8 TL:8 TS:8 U:32 dn:8 y1:8 y2:8 D4:8 r1:8 d0:8 dd:8"),
-    (H16, "Q16:128 Q1:128 N16:256 B620:137 M1:128 EL:128 Y:128 Hf:128 Hm:128"),
-    (I32, "Qi:128 LQ:128 Ci:384 Ei:384 QI:137 QA:137 HP:128 HI:128 IP:2 IC:2 qi:8 qj:16 RW:8"),
-    (U16, "Ql:128 El:128 vz0:16 vz1:16 cl:8 pos:8 tq:8 lz:8 zo:8 UU0:40 UU1:40 sl:8 se0:8 se1:8 za:8 didx:8"),
+    (BF, "X:2320 XQ:2048 BO:128 I:128 I2:128 Im:128 IH:128 IR:128 B0:128 SHD:128 ZH:272 ZL:272 OHZ:272 TRZ:272 "
+         "IDZ:272 OHB:272 OHC:272 OH0:272 OH1:272 OH2:272 KD:128 KT:128 K3:137 M16:137 RD:137 RMP:137 OH:128 "
+         "BA:128 TA:128 ONE:128 SA:128 I7:128 XQg:128 DFg:128 DH:128 xsave:16 I4:128 Im4:128 KC:88 athr:8 EA:16 "
+         "zcf:8 mk0:48 mk1:48 cut:8 CODE:1920 KD2:128 VC:256 SV:128 I16:128 I6:128 fz:8 fu:8 c24:2 CN:128 RMQ:144 B6:128 KD6:128 "
+         "IC6:128 JP:8 dn:8 y3:8 KA:576 KB:18 AD:576 RA:576 NE:576 RE:576 SG:128 nf:8 XA:128 XB:128"),
+    (F32, "L:2464 C:2192 IOT:2064 W1:137 W2:137 W3:137 W3n:137 S1:137 S2:137 SZ0:409 SZ1:409 SZ2:409 zt:8 QF:128 uQ0:128 uQ1:128 SN:128 "
+          "LAND1:128 SND:128 HMQ:128 HK:128 uE:128 CV:128 CG:128 SE:128 SQ:128 DS:128 WN:128 "
+          "OHM:128 LK:48 LN:128 X5:128 X6:128 YE:896 cols:18 LC:32 lsave:2 "
+          "I32:128 ICS:128 JC:8 U0:24 U1:24 U2:24 dd:8 STD:2192 I12:128 Ia:128 Ib:128 vcol:128 tcol:128 THR:6 THS:6 x50:8 x51:8 x2:8 TS:8 TU:8 d0:8"),
+    (H16, "Q16:128 Q1:128 B620:137 M1:128 EL:128 Y:128 Hf:128 Hm:128 VT:128 SC:128 v0:8 v1:8 y2:8"),
+    (I32, "Qi:128 LQ:128 Ci:384 Ei:384 QI:137 QA:137 HP:128 HI:128 IP:2 IC:2 qi:8 qj:16"),
+    (U16, "Ql:128 El:128 vz0:16 vz1:16 cl:8 tp:16 lz:8 zo:8 UU0:32 UU1:32 id0:8 id1:8 ido:8 za:8 didx:8 sl:8 zl0:8 zl1:8"),
 ):
     for _x in _l.split():
         _b(_x.split(":")[0], int(_x.split(":")[1]), _d)
-_b("AB", [128, 17], BF); _b("QX", [8, 8, 16], H16); _b("CZ", 144, BF)
-PS = ["pd", "pm", "pt", "ps", "pq", "pe", "pw", "ph"]
+_b("AB", [128, 17], BF); _b("QX", [8, 8, 16], H16); _b("CZ", 144, BF); _b("DF", 2064, BF)
+_b("NF", 584, H16); _b("RF", 584, H16); _b("KF", 584, BF); _b("KG", 18, BF)
+for _x in "SN NE RE tcol CODE KD2 VC SV BA TA ONE I7".split():
+    del SCRATCH[_x]
+TSCAN, ROW16, MDIR = True, True, True
+PS = ["pd", "pm", "pt", "ps", "pq", "pa", "pw", "ph"]
 for _n in PS:
     _b(_n, 512, F32, "psum")
 SEMAPHORES = ["sV", "sT", "sS", "sG", "locE", "loc0", "loc1", "arrE", "arr0", "arr1"] + ["d%d" % _i for _i in range(20)]
-NDUM, NDUMP, TDUMP, BIG, HH, FRZ, CO = 896, 1024, 2050, float(2 ** 22), float(2 ** 22), float(2 ** 24), 32
+TDUMP, BIG, HH, CO = 2050, float(2 ** 22), float(2 ** 22), 32
+Z, NEW = CO + 384, CO + 392
+NDUMP, TOP, BLANK = NEW + 136 * 12, NEW + 136 * 13, NEW + 136 * 14 + 128
+SB = [NEW, NEW + 136 * 7]
+LB = [[NEW + 136 * _j for _j in _l] for _l in ((1, 3, 5), (8, 10, 13))]
+KIDS = [[NEW, LB[0][0] + 128, LB[0][1] + 128], [LB[0][2] + 264, LB[1][0] + 128, LB[1][1] + 128]]
+REST = [[Z, Z + 1, KIDS[0][1]], [Z, KIDS[1][0], KIDS[1][1]]]
 FAR, NONE = 294.0, 560.0
 PLANS, PASSES = [(_h, _l) for _h in (280, 300, 320, 350) for _l in (100, 300, 600)], 4
 HOP, FLY = 240, 3000
 CHUNKS = (0, 16, 40, 64, 88, 112, 128)
+RELU = 0
+DIRECT, AOLD, TOLD, FRZ = True, True, True, float(2 ** 24)
+CASES, MOVES, SLACK, NOTE = [(330, 1, 0.65, 1.56, 3.8), (350, 1, 0.6, 1.2, 2.5), (270, 1.3, 0.8, 1.7, 4.4)], 20000, 400, []
+CELLS = {}
 ORDER = []
 
 
@@ -52,7 +68,7 @@ def make(g, T):
     eng = {"V": g.vector, "S": g.scalar, "T": g.tensor, "G": g, "Y": g.sync}
     tick = {"V": 0, "S": 0, "T": 0, "G": 0}
     known = {q: {} for q in eng}
-    snap, acc, final, ndma, ops = {}, {}, {}, [0], []
+    snap, acc, final, ndma, ops, INDIRECT = {}, {}, {}, [0], [], {}
 
     def ap(x):
         if not isinstance(x, tuple):
@@ -85,11 +101,11 @@ def make(g, T):
                 n, lo, hi = x[0], x[1], x[2]
                 ps = n in PS
                 for e in acc.get(n, []):
-                    elo, ehi, ew, eq, es, ev, ed = e
+                    elo, ehi, ew, eq, es, ev, ed, ex = e
                     if ps:
                         if eq == q and (q == "T" or not (isw or ew) or ehi <= lo or hi <= elo):
                             continue
-                    elif ehi <= lo or hi <= elo or not (isw or ew):
+                    elif ehi <= lo or hi <= elo or not (isw or ew) or (not dma and not ed and apart(x, ex)):
                         continue
                     need[es] = max(need.get(es, 0), ev)
         for s in sorted(need, key=lambda z: z == "s" + q):
@@ -101,8 +117,20 @@ def make(g, T):
                 if isw and x[4] and n not in PS:
                     l[:] = [e for e in l if not (lo <= e[0] and e[1] <= hi)]
                 else:
-                    l[:] = [e for e in l if not (e[3] == q and not e[6] and not dma and e[0] == lo and e[1] == hi and e[2] == isw)]
-                l.append((lo, hi, isw, q, sem, val, dma))
+                    l[:] = [e for e in l if not (e[3] == q and not e[6] and not dma and e[7][3] == x[3] and e[2] == isw)]
+                l.append((lo, hi, isw, q, sem, val, dma, x))
+
+    def cells(x):
+        key = (x[0], repr(x[3]))
+        if key not in CELLS:
+            at = [0]
+            for i, d in zip(x[3][1:], SCRATCH[x[0]][1][1:]):
+                at = [a * d + k for a in at for k in ([i] if isinstance(i, int) else range(*i.indices(d)))]
+            CELLS[key] = frozenset(at)
+        return CELLS[key]
+
+    def apart(x, y):
+        return not (x[4] and y[4]) and cells(x).isdisjoint(cells(y))
 
     def size(x):
         if x[0] == "@":
@@ -130,6 +158,8 @@ def make(g, T):
         def emit():
             deps(q, r, w, "s" + q, tick[q] + 1)
             fin(q, f())
+        if out[0] == "@" or any(isinstance(x, tuple) and x[0] == "@" for x in ins):
+            INDIRECT[emit] = ("s" if out[0] == "@" else "g", size(out))
         ops.append((q, r, w, cycles(q, out, ins, both), HOP, emit))
 
     def either(fs, fv):
@@ -144,16 +174,16 @@ def make(g, T):
             p = {}
             for isw, xs in ((0, op[1]), (1, op[2])):
                 for x in xs:
-                    for lo, hi, ew, j in seen.get(x[0], []):
-                        hit = lo < x[2] and x[1] < hi and (isw or ew)
-                        if hit or x[0] in PS:
+                    for lo, hi, ew, j, y in seen.get(x[0], []):
+                        hit = lo < x[2] and x[1] < hi and (isw or ew) and (op[4] != HOP or ops[j][4] != HOP or not apart(x, y))
+                        if hit or (x[0] in PS and not ops[j][0] == op[0] == "V" and not (len(op) == 6 == len(ops[j]) and ops[j][0] == op[0] == "S")):
                             p[j] = p.get(j, False) or hit
             for isw, xs in ((0, op[1]), (1, op[2])):
                 for x in xs:
                     l = seen.setdefault(x[0], [])
                     if isw and x[4]:
                         l[:] = [e for e in l if not (x[1] <= e[0] and e[1] <= x[2])]
-                    l.append((x[1], x[2], isw, i))
+                    l.append((x[1], x[2], isw, i, x))
             p.pop(i, None)
             pred.append(p)
         every = range(len(ops))
@@ -207,7 +237,109 @@ def make(g, T):
                 t = span(seq, HOP, 1) + span(seq, 1.25 * HOP, 1.4) / 1.4
                 if kept is None or t < kept[0]:
                     kept = (t, seq)
-        return kept[1]
+        return polish(kept[1], pred, succ)
+
+    def polish(seq, pred, succ):
+        n = len(ops)
+        below = [0] * n
+        for j in reversed(range(n)):
+            for i in succ[j]:
+                below[j] |= below[i] | 1 << i
+        need = [[] for _ in range(n)]
+        for j in range(n):
+            far = 0
+            for k in succ[j]:
+                if (pred[k][j] and ops[j][0] != "T") or ops[j][0] == ops[k][0] == "T" or (ops[j][0] == "T") != (ops[k][0] == "T"):
+                    far |= below[k]
+            hard = 0
+            for k in succ[j]:
+                if not ops[j][0] == ops[k][0] == "T":
+                    hard |= below[k] if pred[k][j] or "T" in (ops[j][0], ops[k][0]) else 0
+            for i in succ[j]:
+                tt_ = ops[j][0] == ops[i][0] == "T"
+                if not (far if tt_ else hard) >> i & 1:
+                    need[i].append((j, tt_ or not pred[i][j], ops[j][4]))
+        tail = [op[4] for op in ops]
+
+        def held(o, slow, pe, gather, scatter):
+            kind, m = INDIRECT.get(o[5], ("", 0))
+            d = o[3] + m * (gather - 1.56 if kind == "g" else scatter - 3.8)
+            return o[0], d * (pe if o[0] == "T" else 1 if o[0] == "Y" or o[4] != HOP else slow)
+        alts = [[[held(o, *x[1:]) for o in [op] + list(op[6:])] for op in ops] for x in CASES]
+        needs = [[[(j, soft, x[0] if lag == HOP else lag) for j, soft, lag in l] for l in need] for x in CASES]
+
+        def run(order, pick, alt, need, old, a):
+            end, que, why = (list(x) for x in old[2:])
+            free, last = {q: 0.0 for q in eng}, {q: None for q in eng}
+            left, k = set(eng), a - 1
+            while left and k >= 0:
+                i = order[k]
+                if que[i] in left:
+                    left.discard(que[i])
+                    free[que[i]], last[que[i]] = end[i], i
+                k -= 1
+            top, at = 0.0, None
+            for i in order[a:]:
+                q, d = alt[i][pick[i]]
+                t, w = free[q], last[q]
+                for j, soft, lag in need[i]:
+                    e = end[j] if soft and que[j] == q else end[j] + lag
+                    if e >= t:
+                        t, w = e, ~j
+                t += d
+                end[i], que[i], why[i], free[q], last[q] = t, q, w, t, i
+                if t + tail[i] > top:
+                    top, at = t + tail[i], i
+            return top, at, end, que, why
+
+        def judge(order, pick, old, a):
+            res = [run(order, pick, alts[k], needs[k], old[k], a) for k in range(len(CASES))]
+            return sum(r[0] / x[1] for r, x in zip(res, CASES)), res
+
+        order, pick = [i for i, k in seq], [0] * n
+        for i, k in seq:
+            pick[i] = k
+        alt = alts[0]
+        now, res = judge(order, pick, [(0, 0, [0.0] * n, [None] * n, [None] * n)] * len(CASES), 0)
+        best, state = (now, order, pick), 12345
+        for it in range(MOVES):
+            state = (state * 1103515245 + 12345) % 2 ** 31
+            top, i, _, _, why = res[(state >> 8) % len(res)]
+            pairs = []
+            while i is not None:
+                w = why[i]
+                if w is not None and w >= 0 and not below[w] >> i & 1:
+                    pairs.append((w, i))
+                i = w if w is None or w >= 0 else ~w
+            if not pairs:
+                break
+            state = (state * 1103515245 + 12345) % 2 ** 31
+            p, i = pairs[(state >> 8) % len(pairs)]
+            kind = (state >> 20) % 6
+            o2, p2 = order, pick
+            a = order.index(p)
+            if kind < 2 and len(alt[(p, i)[kind]]) > 1:
+                p2 = list(pick)
+                p2[(p, i)[kind]] ^= 1
+            else:
+                z = order.index(i)
+                mid = order[a:z + 1]
+                if kind % 2:
+                    up = [x for x in mid if x == i or below[x] >> i & 1]
+                    o2 = order[:a] + up + [x for x in mid if not (x == i or below[x] >> i & 1)] + order[z + 1:]
+                else:
+                    dn = [x for x in mid if x == p or below[p] >> x & 1]
+                    o2 = order[:a] + [x for x in mid if not (x == p or below[p] >> x & 1)] + dn + order[z + 1:]
+            t, r2 = judge(o2, p2, res, a)
+            if t <= now + SLACK * (1 - it / MOVES) * ((state >> 4) % 16) / 16:
+                now, res, order, pick = t, r2, o2, p2
+                if t < best[0]:
+                    best = (t, order, pick)
+        NOTE.extend([kept_first(best[0])])
+        return [(i, best[2][i]) for i in best[1]]
+
+    def kept_first(x):
+        return x
 
     def flush():
         if not ORDER:
@@ -263,7 +395,7 @@ def make(g, T):
             for o, lt, rh, st, sp in lst:
                 ins = g.tensor.matmul(ap(o), ap(lt), ap(rh), st, sp)
             fin("T", ins)
-        ops.append(("T", r, w, sum(max(64, size(x[0])) * (2 if SCRATCH[x[1][0]][2] == F32 else 0.5) for x in lst), HOP, emit))
+        ops.append(("T", r, w, sum(max(64, size(x[0])) * (3.2 if SCRATCH[x[1][0]][2] == F32 else 0.8) for x in lst), HOP, emit))
 
     def dma(q, out, in_, r=(), w=()):
         sem = "d%d" % ndma[0]
@@ -315,29 +447,46 @@ def rank_program(g, core, T, topo):
     def ind(w, hi, o, lo=0, oh=None):
         return ("@", b(w, 0, hi), b(o, lo, oh))
 
-    def rev(n):
-        return b(n, 1, LL, -1)
+    def rev(n, at=0):
+        return b(n, 1 + at, LL + at, -1)
 
-    def at0(n):
-        return b(n, 1, LL, 17)
+    def at0(n, k=0, m=1):
+        return b(n, 1 + 136 * k, 1 + 136 * (k + m), 17)
 
-    def diag(out, src):
-        scan(b(out), b("KD"), src, 0.0, A.mult, A.max)
+    def zs_(s):
+        return at0("SZ%d" % (s % 3))
+
+    def zl_(r, s):
+        return b("zl%d" % (s % 2)) if s else b("vz%d" % r, 8, 16)
+
+    def diag(out, src, kd="KD"):
+        scan(b(out), b(kd), src, 0.0, A.mult, A.max)
         return b(out, 15, 128, 16)
+
+    def lower(out, eq, row, width, own):
+        part = lambda c, lo, hi: nd(eq, width * c + lo, width * c + hi, c, slice(lo, hi))
+        for c in range(8):
+            n = width - 16 * c
+            own(part(c, 0, n), b(row, 16 * c, width), c)
+            if width > 128 or c < 7:
+                mm(*([(b("pa", out, out + 128), b("BO"), part(c, n - 128, n), False, False)] if width > 128 else []),
+                   *([(b("pa", out + 16 * c + 16, out + 128), b("BA"), part(c, 16, 128 - 16 * c), False, False)] if c < 7 else []))
+        mm((b("pa", out, out + 128), b("TA"), nd(eq, 0, 8 * width, al, slice(0, 16)), False, True))
 
     def seg(c):
         return (144 * c if c < 4 else 144 * (7 - c) + 16 * (8 - c)), 16 * c + 16
 
-    def lower(out, res, row, own, own4096):
+    def least(out, res, row, own):
         for c in range(8):
             o, n = seg(c)
-            either(lambda: act(b(out, o, o + n), b(row, 0, n), F.Abs, bias=b(own4096, c, c + 1), scale=-4096.0),
+            either(lambda: act(b(out, o, o + n), b(row, 0, n), F.Abs, bias=b(own, c, c + 1), scale=-1.0),
                    lambda: ts(b(out, o, o + n), b(row, 0, n), b(own, c, c + 1), A.not_equal, 4096.0, A.mult))
         scan(b(res), b(out), b("KA"), 2 * FRZ, A.min, A.add)
         return b(res, 14, 576, 160), b(res, 142, 575, -144)
 
     CS = col(4)
-    DT, DD, DUM = b("LC", 0, 8), b("LC", 8, 16), b("LC", 32, 40)
+    DT = b("LC", 24, 32)
+    pe = b("pa", 256, 384) if AOLD else b("ps", 128, 256)
 
     dma("Y", T.Qi[:], T.req[:], w=[b("Qi")])
     dma("Y", T.Ci[:], T.child[:], w=[b("Ci")])
@@ -347,35 +496,55 @@ def rank_program(g, core, T, topo):
     iota(b("IP", 0, 1), [[1, 1]], 0, 1, False)
     iota(b("ZH"), [[1, 17], [0, 16]], 0, 0)
     iota(b("ZL"), [[0, 17], [1, 16]], 0, 0)
-    for lo, hi in ((0, 144), (144, 1024), (1024, 1664), (1664, XW)):
+    for lo, hi in ((0, 144), (144, 704), (704, 1400), (1400, 2064)):
         iota(b("IOT", lo, hi), [[1, hi - lo]], lo, 0)
-    iota(b("C", NDUM, NDUMP), [[1, 128]], NDUM + CO, 0)
-    iota(b("LC", 0, 8), [[32, 8]], TDUMP, 2)
-    iota(b("LC", 8, 24), [[0, 2], [16, 8]], NDUMP, 1)
-    iota(b("LC", 32, 40), [[16, 8]], NDUM, 1)
+    if not TOLD:
+        ms(b("IOT", 2048, 2049), 4000.0)
+    if not AOLD:
+        lin(b("CODE", 0, 128), b("IOT", 0, 128), 1.0, 128.0)
+        for n in (128, 256, 512, 1024):
+            lin(b("CODE", n, min(2 * n, 1920)), b("CODE", 0, min(n, 896)), 2.0 ** (n // 128))
+    else:
+        for lo in range(0, KIDS[1][2], 272):
+            either(lambda: act(b("STD", lo, lo + 272), b("ZH"), scale=0.0), lambda: ms(b("STD", lo, lo + 272), 0.0))
+        iota(b("THR"), [[256, 6]], 192, 0)
+    lin(b("RMQ"), b("IOT", 0, 144))
+    for lo in [SB[0]] + LB[0] + LB[1][:1]:
+        iota(b("C", lo, lo + 128), [[0, 128]], CO, 0)
+    iota(DT, [[32, 8]], TDUMP + (0 if TOLD else 4096), 2)
+    iota(b("LC", 0, 16), [[0, 2], [16, 8]], NDUMP, 1)
     iota(b("K3", 1, LL), [[0, 8], [16, 17]], 0, 0)
-    iota(b("W4", 1, LL), [[256, 8], [1, 17]], 0, 16)
-    iota(b("THR"), [[256, 6]], 192, 0)
-    iota(b("JC"), [[16, 8]], 256, 1)
+    iota(b("JC"), [[16, 8]], BLANK + 16, 1)
+    iota(b("dd"), [[256, 8]], 0, 16)
     ts(b("IC", 0, 1), b("IP", 0, 1), 4, A.arith_shift_right)
     ts(b("IC", 1, 2), b("IP", 0, 1), 15, A.bitwise_and)
     cp(col(0), b("IP", 0, 1))
     cp(b("cols", 1, 3), b("IC"))
-    ms(b("C", 384, NDUM), float(CO))
-    for n, lo, hi in (("L", 384, 896), ("L", 896, 1152), ("STD", 0, 512), ("STD", 512, 1024), ("STD", 1024, 1152)):
-        act(b(n, lo, hi), b("C", 384, 384 + hi - lo), F.Silu if lo == 384 else F.Copy, scale=0.0)
-        if lo == 384:
-            K["ops"][-1] = K["ops"][-1][:3] + (K["ops"][-1][3] + 1600,) + K["ops"][-1][4:]
+    ms(b("C", Z, NEW), float(Z))
+    for x in (REST[0][2], REST[1][1], REST[1][2]):
+        ms(b("C", x, x + 1), float(Z))
+    act(b("L", Z, NEW), b("C", Z, NEW), F.Silu, scale=0.0)
+    K["ops"][-1] = K["ops"][-1][:3] + (K["ops"][-1][3] + 1600,) + K["ops"][-1][4:]
+    lin(b("L", BLANK, BLANK + 8), b("L", Z, NEW))
     lin(col(3), col(2), 1.0, 1.0)
     ts(col(5), col(2), 0.0, A.is_equal)
     ts(col(6), col(2), 0.0, A.is_gt)
     ts(col(11), col(2), 14.5, A.is_gt)
-    lin(col(7), col(11), -4095.0, 4096.0)
+    lin(col(7), col(11), 4095.0, 1.0)
     lin(col(4), col(11), 1.0 - 2.0 ** -12, 2.0 ** -12)
-    for j, c in ((8, -16.0), (9, -32.0), (10, -256.0)):
-        lin(col(j), col(1), c)
+    if not AOLD:
+        lin(col(14), col(11), -4095.0 * 271.5, 4096.0 * 271.5)
+        lin(col(15), col(7), 2048.0)
+        lin(b("c24", 0, 1), col(11), 1.0 - 2.0 ** 24, 2.0 ** 24)
+    lin(col(16), col(11), 63.0, 1.0)
+    for j, c, d in ((8, -16.0, 0.0), (9, -32.0, 0.0), (10, -256.0, 0.0)):
+        lin(col(j), col(1), c, d)
     ts(b("BO"), b("ZH", 0, 128), col(1), A.is_equal)
     lin(b("B0"), b("BO"), col(5))
+    if not AOLD:
+        lin(b("BA"), b("BO"), 256.0)
+        sel(b("TA"), b("BA"), [[1, 128]], A.is_gt, 0, -1)
+        ms(b("ONE"), 1.0)
     sel(b("SHD"), b("BO"), [[1, 128]], A.is_equal, -1, -1)
     ts(b("KD"), b("ZL", 0, 128), col(2), A.is_gt)
     ts(b("KT"), b("ZL", 0, 128), col(3), A.is_equal, 4095.0, A.mult)
@@ -383,104 +552,152 @@ def rank_program(g, core, T, topo):
     ts(b("OHZ"), b("ZL"), col(2), A.is_equal)
     ts(b("IDZ"), b("ZH"), col(2), A.is_equal)
     ts(b("TRZ"), b("ZH"), col(2), A.is_le)
-    lin(col(13), col(2), -1.0, 15.0)
-    ts(b("OHC"), b("ZL", 0, 256), col(13), A.is_equal, 4224.0, A.mult)
-    ts(b("OHB"), b("ZH", 0, 256), col(2), A.is_equal, 4096.0, A.mult)
+    if not AOLD:
+        act(b("KD2"), b("KD"), F.Square)
+    ts(b("KD6"), b("KD"), 64.0, A.min)
+    lin(b("B6"), b("BO"), 1.0 / 64)
+    ts(col(17), col(2), 7.5, A.is_gt, -16.0, A.mult)
+    ts(col(17), col(17), col(2), A.add, 8.0, A.add)
+    lin(col(13), col(17), -1.0, 15.0)
+    ts(b("OHC"), b("ZL"), col(13), A.is_equal, 17.0, A.mult)
+    ts(b("OHB"), b("ZH"), col(17), A.is_equal, 16.0, A.mult)
     tt(b("OHB"), b("OHB"), b("OHC"), A.max)
-    lin(b("OHB"), b("OHB"), 1.0, -4096.0)
+    for s in range(S_):
+        lin(b("OH%d" % s), b("OHB"), 272.0 * (s + 1), -16 * 272.0 * (s + 1))
     ts(b("I"), b("IOT", 0, 128), col(0), A.is_equal)
     for n, c in (("IH", HH / 2), ("IR", 2.0 ** 37), ("I2", 2.0), ("Im", -1.0), ("I4", 4096.0), ("Im4", -4096.0),
-                 ("I32", 1.0), ("Im32", -1.0)):
+                 ("I32", 1.0), ("I12", 2.0 ** -12) if AOLD else ("I7", col(7)), ("IC6", col(16)), ("ICS", CS), ("I16", 16.0), ("I6", 1.0 / 16)):
         lin(b(n), b("I"), c)
     lin(col(12), col(1), 16.0, 15.0)
     ts(b("CZ"), b("IOT", 0, 144), col(12), A.is_equal, -HH, A.mult)
-    lin(DT, DT, 1.0, col(9))
-    lin(b("LC", 8, 24), b("LC", 8, 24), 1.0, col(8))
-    lin(DUM, DUM, 1.0, col(8))
+    ts(col(17), col(11), -4095.0, A.mult, 4096.0, A.add)
+    if TOLD:
+        lin(DT, DT, 1.0, col(9))
+    else:
+        ts(DT, DT, col(9), A.add, col(17), A.mult)
+    if AOLD:
+        lin(b("THR"), b("THR"), col(17))
+        lin(b("THS"), b("THR"), -32768.0)
+    if TSCAN:
+        ms(b("KF"), 0.0)
+        lin(b("KG", 0, 16), b("OHZ", 0, 16), 4096.0)
+        ms(b("KG", 16, 17), -8192.0)
+        lin(b("KG", 15, 16), b("KG", 15, 16), 1.0, -4096.0)
+        for c in range(8):
+            o = 162 * c if c < 4 else 146 * (7 - c) + 129
+            lin(b("KF", o, o + 17), b("KG", 0, 17))
+    if AOLD:
+        ms(b("KA"), 0.0)
+        lin(b("KB", 0, 16), b("OHZ", 0, 16), -FRZ)
+        ms(b("KB", 16, 17), 2 * FRZ)
+        lin(b("KB", 15, 16), b("KB", 15, 16), 1.0, FRZ)
+        for c in range(8):
+            o, n = seg(c)
+            lin(b("KA", o + n - 16 - (c > 0), o + n), b("KB", 1 - (c > 0), 17))
+    lin(b("LC", 0, 16), b("LC", 0, 16), 1.0, col(8))
     lin(b("JC"), b("JC"), 1.0, col(8))
-    ms(b("K32"), 0.0)
-    ms(b("K32", 16, 24), 1.0)
-    lin(b("W4", 1, LL), b("W4", 1, LL), 1.0, col(10))
-    lin(b("THR"), b("THR"), col(7))
-    lin(b("THS"), b("THR"), -32768.0)
-    ms(b("LC", 24, 32), 256.0)
-    ms(b("KA"), 0.0)
-    lin(b("KB", 0, 16), b("OHZ", 0, 16), -FRZ)
-    ms(b("KB", 16, 17), 2 * FRZ)
-    lin(b("KB", 15, 16), b("KB", 15, 16), 1.0, FRZ)
-    for c in range(8):
-        o, n = seg(c)
-        lin(b("KA", o + n - 16 - (c > 0), o + n), b("KB", 1 - (c > 0), 17))
+    lin(b("JP"), b("dd"), 1.0, col(10))
+    if not AOLD:
+        ms(b("KC", 0, 24), -65536.0)
+    ms(b("KC", 0 if AOLD else 24, 40), 0.0)
+    ms(b("KC", 8, 16), 4096.0)
+    ms(b("KC", 80, 88), -256.0 * HH)
+    lin(b("Ia"), b("I"), -256.0)
+    lin(b("Ib"), b("I"), 257.0)
+    ms(b("LC", 16, 24), 256.0)
     ms(b("M16"), -16.0)
     ms(b("RD"), 0.0)
     ms(b("DF", 2048, 2064), 0.0)
     ms(nd("AB", 0, 2176, al, slice(16, 17)), NONE)
     ts(b("B620"), b("M16"), 0.0, A.mult, 1241.0, A.add)
-    for r in range(RO_):
-        ts(b("N16", 128 * r, 128 * r + 128), b("IOT", 0, 128), 512.0 + 256 * r + CO, A.add)
-    lin(b("WC", 128, 256), b("C", 384, 512))
 
     def roots(r, src):
         vz = "vz%d" % r
         ts(b("Q1"), src, 1.0, A.add)
         mm((b("pw", 0, 128), b("B0"), b("Q1"), True, True))
-        ts(b("qi"), diag("SQ", b("pw", 0, 128)), CS, A.mult, -1.0, A.add)
+        ts(b("qi"), diag("SQ", b("pw", 0, 128)), CS, A.mult, 16.0 * CO - 1, A.add)
         ts(b("qj", 0, 8), b("qi"), 4, A.arith_shift_right)
         ts(b("qj", 8, 16), b("qi"), 15, A.bitwise_and)
         cp(b(vz), b("qj"))
-        cp(b("v%d" % r), b("qj", 0, 8))
-        ts(b("zs%d" % r), b("qj", 8, 16), 4096.0, A.mult)
+        cp(b("v%d" % r, 0, 8), b("qj", 0, 8))
+        ts(zs_(0), b("qj", 8, 16), 4096.0, A.mult)
+        if AOLD:
+            ts(b("x5%d" % r), b("qj", 0, 8), 4096.0, A.mult)
 
     def roots_first():
         ts(b("HP"), b("Qi"), 4, A.arith_shift_right)
         ts(b("HI"), b("Qi"), 15, A.bitwise_and)
         ts(b("Q1"), b("HP"), 1.0, A.add)
         ts(b("Hf"), b("HI"), 1.0, A.add)
-        ts(b("X5"), b("Hf"), 16.0, A.mult)
         mm((b("pw", 0, 128), b("B0"), b("Q1"), True, True))
-        mm((b("pe", 0, 128), b("B0"), b("Hf"), True, True))
-        ts(b("vz0", 0, 8), diag("SQ", b("pw", 0, 128)), CS, A.mult, -1.0, A.add)
-        ts(b("OH"), b("pe", 0, 128), col(3), A.is_equal)
-        lin(b("v0"), b("SQ", 15, 128, 16), CS, -1.0)
-        lin(b("y1"), diag("SE", b("pe", 0, 128)), CS, -1.0)
-        lin(b("zs0"), b("y1"), 4096.0)
+        mm((pe, b("B0"), b("Hf"), True, True))
+        ts(b("vz0", 0, 8), diag("SQ", b("pw", 0, 128)), CS, A.mult, CO - 1.0, A.add)
+        ts(b("OH"), pe, col(3), A.is_equal)
+        ts(b("v0", 0, 8), b("SQ", 15, 128, 16), CS, A.mult, CO - 1.0, A.add)
+        lin(zs_(0), diag("SE", pe), col(7), -4096.0)
+        if AOLD:
+            lin(b("x50"), b("SQ", 15, 128, 16), col(7), 4096.0 * (CO - 1))
 
-    def child(r, row=True):
-        vz = "vz%d" % r
+    def child(r, s, row=True):
+        vz, n, last = "vz%d" % r, LB[r][s], (r, s) == (RO_ - 1, S_ - 1)
         if row:
-            lin(b("OH"), ind("OHZ", 272, vz, 8, 16))
-        tt(b("M1"), ind("C", 1024, vz, 0, 8), b("OH"), A.mult)
-        mm((b("pm", 0, 128), b("BO"), b("M1"), True, True))
-        ts(b("cl"), diag("SC", b("pm", 0, 128)), CS, A.mult, -float(CO), A.add)
-        lin(b("cf"), b("SC", 15, 128, 16), CS, -float(CO))
-        mm((b("pw", 272, 280), b("I32"), b("cf"), True, False), (b("pw", 272, 280), b("Im32"), b("v%d" % r), False, True))
+            lin(b("OH"), ("@", b("OHZ"), zl_(r, s)))
+        if last:
+            tt(b("M1"), ind("C", REST[r][s] + 1, vz, 0, 8), b("OH"), A.mult)
+        else:
+            iota(b("CN"), [[0, 128]], n - n % 16 - 4096, 0)
+            if MDIR:
+                tt(b("M1"), ind("C", REST[r][s] + 1, vz, 0, 8), b("OH"), A.mult)
+            else:
+                mm((b("ph", 128, 256), b("I"), b("OH"), True, True))
+            lin(b("CG"), ind("C", REST[r][s] + 1, vz, 0, 8))
+            if not MDIR:
+                tt(b("M1"), b("CG"), b("ph", 128, 256), A.mult)
+            mm((b("ph", 256, 384), b("I"), b("RMQ", n % 16, n % 16 + 128), True, False), (b("ph", 256, 384), b("I"), b("CN"), False, False),
+               (b("ph", 256, 384), b("I4"), b("OH"), False, True))
+            tt(b("CV"), b("CG"), b("ph", 256, 384), A.max)
+        mm((b("pm", 0, 128), b("B6"), b("M1"), True, True))
+        ts(b("cl"), diag("SC", b("pm", 0, 128), "KD6"), col(16), A.mult, float(CO), A.max)
 
-    def edge():
-        ts(b("El"), ind("L", 1024, "cl"), -1.0, A.mult, 2047.0, A.add)
+    def edge(r, s):
+        lin(b("uE"), ind("L", KIDS[r][s], "cl"))
+        ts(b("El"), ind("L", KIDS[r][s], "cl") if DIRECT else b("uE"), -1.0, A.mult, 2047.0, A.add)
 
-    def leaf(r):
-        mm((b("pt", 0, 128), b("BO"), b("M1"), True, False), (b("pt", 0, 128), b("Im"), b("N16", 128 * r, 128 * r + 128), False, True))
-        tt(b("T2"), b("pt", 0, 128), b("OH"), A.mult)
-        tt(b("CV"), ind("C", 1024, "vz%d" % r, 0, 8), b("T2"), A.subtract)
+    def made(r, out, zl, steps):
+        pz, pn = b("pw", 256, 264), b("pw", 264, 272)
+        mm((pn, b("I32"), b("JC"), True, False), *[(pn, b("I"), b("mk%d" % r, 8 * i, 8 * i + 8), False, False) for i in range(2 * steps - 2)])
+        mm(*[(pn, b("I"), b("mk%d" % r, 8 * i, 8 * i + 8), False, i % 2 == 1) for i in (2 * steps - 2, 2 * steps - 1)])
+        ts(b(out), pn, float(BLANK), A.min)
+        if zl:
+            mm(*[(pz, b("I32"), b("U%d" % i, 16, 24), i == 0, i == steps - 1) for i in range(steps)])
+            ts(b(zl), pz, 256.0 - 256 * steps, A.add)
 
     def acts(r, s):
-        v, zs, o = b("v%d" % r), b("zs%d" % r), 256 * (3 * r + s + 1)
-        lin(b("vcol"), ind("IOT", 1024, "vz%d" % r, 0, 8))
-        lin(b("x5"), v, 4096.0)
-        for h, e in enumerate(lower("AD", "RA", "vcol", "v%d" % r, "x5")):
-            out = b("athr", 4 * h, 4 * h + 4)
-            either(lambda: act(out, e, F.Relu, bias=BIG, scale=-BIG / 2048), lambda: ts(out, e, 0.5, A.is_lt, BIG, A.mult))
-            tt(b("D4", 4 * h, 4 * h + 4), b("LC", 8 + 4 * h, 12 + 4 * h), e, A.subtract)
-        tt(b("x2"), b("D4"), v, A.max)
-        cp(b("sl"), b("x2"))
-        act(ind("STD", 1152, "sl"), b("IOT", o, o + 128), F.Silu)
-
-    def stood(r, s):
-        j = 3 * r + s
-        lin(b("SG"), ind("STD", 1024, "cl"))
-        e = diag("SS", b("SG"))
-        either(lambda: act(b("nf"), e, F.Relu, bias=b("THS", j, j + 1), scale=32768.0),
-               lambda: ts(b("nf"), e, b("THR", j, j + 1), A.is_gt, BIG, A.mult))
+        if AOLD:
+            j, pa = 3 * r + s, b("pa", 0, 8)
+            lin(b("vcol"), ind("IOT", REST[r][s] + 1, "vz%d" % r, 0, 8), 4096.0)
+            mm((pa, b("I12"), b("x5%d" % r), True, False))
+            for h, e in enumerate(least("AD", "RA", "vcol", "x5%d" % r)):
+                out = b("athr", 4 * h, 4 * h + 4)
+                either(lambda: act(out, e, F.Relu, bias=BIG, scale=-BIG / 2048), lambda: ts(out, e, 0.5, A.is_lt, BIG, A.mult))
+            mm((pa, b("I"), b("athr"), False, True))
+            tt(b("x2"), pa, b("LC", 0, 8), A.min)
+            cp(b("sl"), b("x2"))
+            act(ind("STD", TOP, "sl"), b("IOT", 256 * j + 256, 256 * j + 384), F.Silu)
+            lin(b("SG"), ind("STD", KIDS[r][s], "cl"))
+            e = diag("SA", b("SG"))
+            either(lambda: act(b("nf"), e, F.Relu, bias=b("THS", j, j + 1), scale=32768.0),
+                   lambda: ts(b("nf"), e, b("THR", j, j + 1), A.is_gt, BIG, A.mult))
+            return b("nf")
+        lin(b("VC", 0, 128), ind("CODE", REST[r][s] + 1, "vz%d" % r, 0, 8))
+        lin(b("VC", 128, 256), ind("CODE", KIDS[r][s], "cl"))
+        diag("SV", b("VC", 0, 128), "KD2")
+        mm((b("pa", 0, 128), b("BO"), b("ONE"), True, False))
+        lower(0, "EQ", "VC", 256, lambda o, x, c: ts(o, x, b("c24", 0, 1), A.mult, b("SV", 16 * c + 15, 16 * c + 16), A.is_equal))
+        e = diag("SA", b("pa", 0, 128))
+        either(lambda: act(b("athr"), e, F.Relu, bias=-271.5 * 2 ** 23, scale=col(15)),
+               lambda: ts(b("athr"), e, col(14), A.is_gt, BIG, A.mult))
+        return e
 
     def payload():
         for x in range(8):
@@ -508,7 +725,7 @@ def rank_program(g, core, T, topo):
     def distances(r, s):
         pd = b("pd", 1, LL)
         if s:
-            act(at0("RD"), b("zs%d" % r), F.Relu, bias=-15.0, scale=2.0 ** -12)
+            act(at0("RD"), zs_(s), F.Relu, bias=-15.0, scale=2.0 ** -12)
             scan(b("RMP", 1, LL), b("M16", 1, LL), b("RD", 1, LL), 0.0, A.add, A.max)
         mm((pd, b("IH"), b("B620", 1, LL), True, False), *([(pd, b("IR"), b("RMP", 1, LL), False, False)] if s else []))
         for lo, hi in zip(CHUNKS, CHUNKS[1:]):
@@ -520,200 +737,241 @@ def rank_program(g, core, T, topo):
                   nd("AB", 1088 * h, 1088 * h + 1088, slice(64 * h + p, 64 * h + 64, 16), al), False, h == 1 and p == 15) for p in range(16)])
 
     def cut_rows(r, s):
-        uu, n1, n0 = "UU%d" % (s % 2), 384 + 256 * r, 512 + 256 * r
-        end = s == S_ - 1
-        tt(b("EL"), ind("IDZ", 272, uu, 24, 32), b("X6") if end else b("WN", 0, 128), A.mult)
-        mm((b("pe", 0, 128), b("BO"), b("EL"), True, True))
-        if r == 0:
-            lin(b("WC", 256, 384), b("C", n0, n0 + 128))
-            lin(b("C", n0, n0 + 128), ind("WC", 384, "se%d" % (s % 2)))
-        if end:
-            ts(b(uu, 32, 40), diag("SE", b("pe", 0, 128)), CS, A.mult, -1.0, A.add)
+        uu, n1 = "UU%d" % (s % 2), SB[r]
+        px = b(pe[0], 384, 392)
+        tt(b("EL"), ind("IDZ", 272, uu, 16, 24), b("X6" if s == S_ - 1 else "WN"), A.mult)
+        mm((pe, b("BO"), b("EL"), True, True))
+        e = diag("SE", pe)
+        if s == S_ - 1:
+            ts(b(uu, 24, 32), e, CS, A.mult, -1.0, A.add)
         else:
-            ts(b("RW"), diag("SE", b("pe", 0, 128)), CS, A.mult)
-            ts(b("RW"), b("RW"), 15, A.bitwise_and)
-            tt(b("RW"), b("RW"), b("r1"), A.add)
-            ts(b("RW"), b("RW"), 255, A.bitwise_and)
-            cp(b(uu, 32, 40), b("RW"))
-        tt(b("OHM"), ind("OHB", 256, uu, 32, 40), b("IOT", n1 + CO, n1 + CO + 128), A.add)
-        act(ind("C", 1152, uu, 8, 16), b("OHM"), F.Silu)
+            lin(b("fz"), b("zcf"), -1.0, -2048.5)
+            lin(b("fu"), e, CS, 2048.5)
+            mm((px, b("I16"), b("zcf"), True, False), (px, b("I16"), b("fz"), False, False), (px, b("ICS"), e, False, False))
+            mm((px, b("Im"), b("fu"), False, True))
+            ts(b(uu, 24, 32), px, 17 * 2048.0 + 136, A.add)
+        tt(b("OHM"), ind("OH%d" % s, 272, uu, 24, 32), b("IOT", n1, n1 + 128), A.add)
+        act(ind("C", TOP, uu, 0, 8), b("OHM"), F.Silu)
 
     def second(r, lst):
-        tt(b("L", 384 + 256 * r, 512 + 256 * r), ("@", b("TRZ"), lst), b("uQ%d" % r), A.mult)
+        tt(b("L", SB[r], SB[r] + 128), ("@", b("TRZ"), lst), b("uQ%d" % r), A.mult)
 
-    def unmade(r):
-        n1 = 384 + 256 * r
-        lin(b("X5"), b("pe", 0, 128), 1.0, 1.5 * 2 ** 27)
-        lin(b("X5"), b("X5"), 1.0, -1.5 * 2 ** 27)
-        tt(b("X6"), b("pe", 0, 128), b("X5"), A.not_equal)
-        tt(b("LN") if r else b("L", n1, n1 + 128), b("L", n1, n1 + 128), b("X6"), A.mult)
+    def unlike(out, x):
+        ts(b("X6"), x, 1.5 * 2 ** 27, A.add, -1.5 * 2 ** 27, A.add)
+        tt(out, x, b("X6"), A.not_equal)
 
-    def at_cut(r, src, lst, start, stop):
+    def at_cut(r, src, lst):
         tt(b("Y"), src, b("uQ%d" % r), A.subtract)
         tt(b("EL"), ("@", b("IDZ"), lst), b("Y"), A.mult)
-        mm((b("pe", 0, 128), b("BO"), b("EL"), start, stop))
+        mm((b("pq", 0, 128), b("BO"), b("EL"), True, True))
+        unlike(b("X5"), b("pq", 0, 128))
+        tt(b("L", SB[r], SB[r] + 128), b("L", SB[r], SB[r] + 128), b("X5"), A.mult)
 
-    def travel(src, land, tag, n=16, at=16):
-        (cp if tag == "E" else lin)(b(land, 0, n), b(src, 0, n))
-        K["ops"].append(("G", [b(src)], [b(land, at)], 1400, FLY * (3 if tag == "E" else 1), lambda: send(src, land, tag, n, at)))
+    def travel(src, land, tag, n=16, at=16, first=0, st=16):
+        (cp if tag == "E" else lin)(b(land, 0, n), b(src, first, first + n))
+        K["ops"].append(("G", [b(src, first, first + 8 * st)], [b(land, at)], 7500 if tag == "E" else 1400, FLY,
+                         lambda: send(src, land, tag, n, at, first, st)))
 
-    def send(src, land, tag, w, at):
+    def send(src, land, tag, w, at, first, st):
         sent = [0]
         part = lambda x: T[x[0]][x[3]]
-        deps("G", [b(src)], [], "loc" + tag, 0)
+        whole = b(src, first, first + 8 * st)
+        deps("G", [whole], [], "loc" + tag, 0)
         for calls in plan(core, T.cores, topo):
             tr = []
             for d, en in calls:
                 e = (T.rank_of(d) - rank) % 8
                 rid, pid = topo.addr(d, core)
                 tr.append(RemoteDMATransfer(dst_ids=[DstId(rid=rid, pnc=pid)], dma_engine_mask=sum(1 << x for x in en),
-                                            remote_sem=T.sem["arr" + tag], src=part(b(src, w * e, w * e + w)),
+                                            remote_sem=T.sem["arr" + tag], src=part(b(src, first + st * e, first + st * e + w)),
                                             dst=part(b(land, at * e, at * e + w))))
                 sent[0] += len(en)
             g.remote_dma_fused(tr, local_sem=T.sem["loc" + tag])
         n = sum(len(en) for s in T.cores if s != core for calls in plan(s, T.cores, topo) for d, en in calls if d == core)
-        K["acc"].setdefault(land, []).append((at, 8 * at, 1, "R", "arr" + tag, n, True))
-        K["acc"].setdefault(b(src)[0], []).append((b(src)[1], b(src)[2], 0, "R", "loc" + tag, sent[0], True))
+        K["acc"].setdefault(land, []).append((at, 8 * at, 1, "R", "arr" + tag, n, True, b(land, at, 8 * at)))
+        K["acc"].setdefault(whole[0], []).append((whole[1], whole[2], 0, "R", "loc" + tag, sent[0], True, whole))
         K["final"]["arr" + tag] = n
         K["final"]["loc" + tag] = sent[0]
 
     def step(r, s):
         end, last = s == S_ - 1, (r, s) == (RO_ - 1, S_ - 1)
-        v, zs, vz, uu, se = b("v%d" % r), b("zs%d" % r), "vz%d" % r, "UU%d" % (s % 2), "se%d" % (s % 2)
-        n0 = 512 + 256 * r
+        v, zs, vz, uu, sz = b("v%d" % r, 0, 8), zs_(s), "vz%d" % r, "UU%d" % (s % 2), "SZ%d" % s
+        lb, cb, mk = LB[r][s], LB[r][s] + 136, "mk%d" % r
+        low = b("L", cb, cb + 128) if last else b("WN")
         distances(r, s)
-        acts(r, s)
-        stood(r, s)
+        sa = acts(r, s)
         if last:
             cp(b("X", 2047, 2048), b("xsave", 0, 1))
         if s == 0:
             payload()
             lin(b("uQ%d" % r), b("QF"), -1.0, 2047.0)
-            lin(b("WN", 128, 256), b("QF"), -1.0, 2047.0)
+            lin(b("L", lb, lb + 128), b("QF"), -1.0, 2047.0)
         else:
-            tt(b("WN", 128, 256), ind("TRZ", 272, vz, 8, 16), b("uQ%d" % r), A.mult)
+            tt(b("L", lb, lb + 128), ("@", b("TRZ"), zl_(r, s)), b("uQ%d" % r), A.mult)
         if s and (r == 0 or s == 1):
             cut_rows(r, s - 1)
         if s == 1:
-            second(r, b("UU0", 24, 32))
+            second(r, b("UU0", 16, 24))
             hashes(r)
         if (r, s) == (1, 0):
-            at_cut(0, b("L", 512, 640), b("za"), True, True)
-            unmade(0)
+            at_cut(0, ind("L", BLANK + 1, "id0"), b("za"))
         if last:
-            cp(b("zo"), b("zacc"))
-            at_cut(r, b("L", n0, n0 + 128), b("zo"), True, False)
+            made(r, "ido", "zo", s)
+            second(r, b("zo"))
+            at_cut(r, ind("L", BLANK + 1, "ido"), b("zo"))
+            tt(b("X5"), b("uE"), b("uQ1"), A.subtract)
+            unlike(b("Y"), b("X5"))
         if (r, s) == (0, 1):
             roots(1, b("LQ"))
         if (r, s) == (0, 2):
-            cp(b("HP"), b("El"))
-            ts(b("HP"), b("HP"), 15, A.bitwise_and)
-            tt(b("X6"), b("X5"), b("HP"), A.subtract)
-        lin(b("uE"), ind("L", 1024, "cl"))
-        dma("Y", T.WN[:, 256:384], T.L[:, n0:n0 + 128], r=[b("L", n0, n0 + 128)], w=[b("WN", 256, 384)])
-        if not last:
-            leaf(r)
+            lin(b("XA"), b("uE"), 1.0, 2048.5)
+            mm((b("pq", 0, 128), b("I32"), b("uE"), True, False), (b("pq", 0, 128), b("Im"), b("XA"), False, False),
+               (b("pq", 0, 128), b("I16"), b("XB"), False, True))
+            lin(b("X6"), b("pq", 0, 128), 1.0, 2048.0 + 9)
+        if (r, s) == (0, 1):
+            lin(b("XA"), b("QF"), 1.0, 2048.5)
+            mm((b("pq", 0, 128), b("I32"), b("QF"), True, False), (b("pq", 0, 128), b("Im"), b("XA"), False, True))
+            lin(b("XB"), b("pq", 0, 128), 1.0, 2048.0 + 8)
         if r == 0:
-            lin(b("WC", 0, 128), ind("C", 1024, "cl"))
-        for n in "2314":
-            scan(rev("S" + n), rev("pd"), rev("W" + n), 0.0, A.min, A.max)
-        s3 = at0("S3")
-        M = [b("ph", 8 * i, 8 * i + 8) for i in range(4)]
-        mm((b("ph", 0, 32), b("I4"), b("K32"), True, False), (M[1], b("I32"), b("cf"), False, False), (M[2], b("I32"), v, False, False),
-           *[(M[i], b("I"), b("athr"), False, False) for i in range(4)])
-        mm(*[(M[i], b("I"), b("nf"), False, False) for i in (0, 1, 3)])
-        lin(b("zp"), at0("S2"), 1.0, 4096.0 * HH)
-        tt(b("E1"), s3, zs, A.is_le)
-        tt(b("TL"), at0("S1"), s3, A.subtract)
-        tt(b("A1"), s3, b("zp"), A.is_ge)
+            lin(b("C", cb, cb + 128), ind("C", KIDS[r][s], "cl"))
+        s3, E1, A1 = at0(sz, 1), b("EA", 0, 8), b("EA", 8, 16)
+        M, tk, pp, U = [b("ph", 8 * i, 8 * i + 8) for i in range(3)], b("pt", 0, 8), b("pt", 8, 16), "U%d" % s
+        pz, pc = b("pw", 288, 296), b("pm", 272, 280)
+        cf = b("SC", 15, 128, 16)
+        mm((b("ph", 0, 24), b("I"), b("KC", 0, 24), True, False), (M[0], b("IC6"), cf, False, False), (M[1], b("I"), v, False, False))
+        i7 = b("I" if AOLD else "I7")
+        mm(*[(x, b("I"), b("athr"), False, False) for x in (M if AOLD else M[1:2])])
+        mm((M[0], i7, sa, False, False), (M[2], i7, sa, False, False))
+        mm((b("pt", 0, 16), b("I"), b("KC", 16, 32), True, False), (pp, b("I"), b("JP"), False, False))
+        if AOLD:
+            mm((tk, b("I"), b("athr"), False, False))
+        mm((tk, i7, sa, False, False))
+        mm((pz, b("I4"), b("KC", 80, 88), True, False), (pz, b("Im"), b("athr"), False, False))
+        if not end:
+            mm((pc, b("IC6"), cf, True, False), (pc, b("Im"), v, False, True))
+        scan(rev("S2"), rev("pd"), rev("W2"), 0.0, A.min, A.max)
+        scan(rev(sz, 136), rev("pd"), rev("W3"), 0.0, A.min, A.max)
+        mm((pz, b("Ia"), at0("S2"), False, False))
+        mm((pz, b("Ib"), s3, False, True))
+        if not end:
+            zn = zs_(3 * r + s + 1)
+            tt(zn, zs, pz, A.max)
+            ts(b("dn"), pz, -0.5, A.is_ge)
+            either(lambda: act(b("y3"), pz, F.Relu, bias=-4096.0 * 255), lambda: ts(b("y3"), pz, -4096.0 * 255, A.add, 0.0, A.max))
+            ts(b("zl%d" % ((s + 1) % 2)), zn, 2.0 ** -12, A.mult)
+            tt(b("y2"), b("dn"), pc, A.mult)
+        scan(rev("S1"), rev("pd"), rev("W1"), 0.0, A.min, A.max)
+        lin(at0(sz, 2), at0("S2"), 1.0, 4096.0 * HH)
         lin(b("zcf"), s3, 2.0 ** -12)
-        lin(b("TS"), b("TL"), 4096.0)
-        cp(b("pos"), at0("S4"))
-        mm(*[(b("pt", 256, 264), b(w), b(x), x == "athr", x == "A1")
-             for w, x in (("I", "athr"), ("I", "nf"), ("I4", "E1"), ("I32", "TL"), ("I4", "A1"))])
-        ts(b("tq"), b("pt", 256, 264), 2048.0, A.min)
-        mm(*[(M[i], b("Im4" if i == 2 else "I4"), b("E1"), False, False) for i in range(4)], (M[0], b("I32"), b("TL"), False, False),
-           (M[3], b("I"), b("zcf"), False, False), *[(M[i], b("I4"), b("A1"), False, i == 3) for i in range(4)])
-        tt(b("U"), b("ph", 0, 32), b("LC", 0, 32), A.min)
-        cp(b(uu, 0, 32), b("U"))
-        if (r == 0 or s == 0) and not end:
-            lin(b("r1"), b("U", 24, 32), 16.0)
-        tt(b("dn"), b("A1"), b("athr"), A.is_gt)
-        tt(b("y1"), b("dn"), s3, A.mult)
+        tt(b("EA"), at0(sz, 0, 2), at0(sz, 1, 2), A.is_ge)
+        mm((tk, b("I32"), at0("S1"), False, False))
+        mm((tk, b("Im4"), b("zcf"), False, False), (pp, b("I6"), b("zcf"), False, False), (tk, b("I4"), E1, False, False),
+           (tk, b("I4"), A1, False, True))
+        ts(b("tp"), b("pt", 0, 16), -7.5 / 16, A.add, 2048.0, A.min)
+        if TOLD and not TSCAN:
+            lin(b("TS"), tk, 4096.0)
+            tt(b("TU"), tk, DT, A.min)
+        mm((M[2], b("I"), b("zcf"), False, False), *[(M[i], b("Im4" if i == 1 else "I4"), E1, False, False) for i in range(3)],
+           *[(M[i], b("I4"), A1, False, i == 2) for i in range(3)])
+        tt(b(U), b("ph", 0, 24), b("LC", 0, 24), A.min)
+        for i, x in enumerate((cb, lb)):
+            ts(b(mk, 16 * s + 8 * i, 16 * s + 8 * i + 8), M[i], NDUMP - 0.5, A.is_lt, x - BLANK - 16.0, A.mult)
+        cp(b(uu, 0, 24), b(U))
         if last:
-            tt(b("CV"), ind("TRZ", 272, vz, 8, 16), b("HMQ"), A.mult)
-            ts(b("lz"), b("y1"), 2.0 ** -12, A.mult)
+            tt(b("CV"), ("@", b("TRZ"), zl_(r, s)), b("HMQ"), A.mult)
+            ts(b("lz"), pz, 2.0 ** -12, A.mult)
             tt(b("HK"), ind("TRZ", 272, "lz"), b("CV"), A.mult)
             tt(b("SND"), b("HK"), b("QF"), A.add)
             travel("SND", "LAND1", "1")
-        else:
-            tt(zs, zs, b("y1"), A.max)
-        if not end:
-            ts(b(vz, 8, 16), zs, 2.0 ** -12, A.mult)
-        elif r == 0:
-            travel("zs0", "LK", "0", 1, 4)
-        lin(b("DFg"), ind("DF", 2064, "pos"))
-        lin(b("XQg"), ind("X", XW, "tq"))
+        elif end:
+            tt(b("zt"), zs, pz, A.max)
+            travel("zt", "LK", "0", 1, 4, 0, 1)
+        lin(b("DFg"), ind("DF", 2064, "tp", 8, 16))
+        lin(b("XQg"), ind("X", XW, "tp", 0, 8))
         mm((b("ps", 0, 128), b("I"), b("DFg"), True, False), (b("ps", 0, 128), b("I2"), b("XQg"), False, True))
         lin(b("DS"), b("ps", 0, 128), 0.5 - 2.0 ** -12, 2.0 ** 23)
         lin(b("DH"), b("DS"), 1.0, -2.0 ** 23)
-        lin(b("tcol"), ind("IOT", XW, "tq"))
-        for h, e in enumerate(lower("NE", "RE", "tcol", "TL", "TS")):
-            tt(b("d0", 4 * h, 4 * h + 4), b("LC", 4 * h, 4 * h + 4), e, A.subtract)
-        tt(b("dd"), b("d0"), b("U", 0, 8), A.max)
-        cp(b("didx"), b("dd"))
+        if TSCAN:
+            (cp if ROW16 else lin)(b("VT" if ROW16 else "tcol"), ind("IOT", 2064, "tp", 0, 8))
+            tt(b("NF", 0, 584, 146), b("pt", 0, 4), b("LC", 24, 28), A.min)
+            tt(b("NF", 17, 504, -162), b("pt", 4, 8), b("LC", 28, 32), A.min)
+            for c in range(8):
+                o = 146 * c + 1 if c < 4 else 162 * (7 - c) + 18
+                ts(b("NF", o, o + 16 * c + 16), b("VT" if ROW16 else "tcol", 0, 16 * c + 16), b("pt", c, c + 1), A.is_equal,
+                   b("LC", 24 + c, 25 + c), A.mult)
+            scan(b("RF"), b("NF"), b("KF"), 0.0, A.max, A.add)
+            cp(b("didx", 0, 4), b("RF", 15, 584, 162))
+            cp(b("didx", 4, 8), b("RF", 144, 583, -146))
+        elif TOLD:
+            lin(b("tcol"), ind("IOT", 2064, "tp", 0, 8), 4096.0)
+            for h, e in enumerate(least("NE", "RE", "tcol", "TS")):
+                tt(b("d0", 4 * h, 4 * h + 4), b("LC", 24 + 4 * h, 28 + 4 * h), e, A.subtract)
+            tt(b("dd"), b("d0"), b("TU"), A.max)
+            cp(b("didx"), b("dd"))
+        else:
+            cp(b("VT"), ind("IOT", 2064, "tp", 0, 8))
+            mm((b("pa", 128, 256), b("BA"), b("ONE"), True, False))
+            mm((b("pa", 128, 256), b("I"), b("VT"), False, False))
+            lower(128, "EN", "VT", 128, lambda o, x, c: ts(o, x, b("pt", c, c + 1), A.is_equal, 16.0, A.mult))
+            tt(b("dd"), diag("SN", b("pa", 128, 256)), DT, A.min)
+            ts(b("didx"), b("dd"), CS, A.mult, -4096.0, A.add)
         cp(ind("X", XW, "didx"), b("DH"))
         if last:
             dma("Y", T.yd[:], T.X[:, 0:2048], r=[b("X", 0, 2048)])
-        ts(b("made"), b("U", 8, 24), NDUMP - 0.5, A.is_lt, -128.0, A.mult)
-        mm(*[(b("pt", 272, 280), b(w), x, i == 0, i == 2)
-             for i, (w, x) in enumerate((("I32", b("JC")), ("I2", b("made", 0, 8)), ("I", b("made", 8, 16))))])
-        cp(b(se), b("pt", 272, 280))
-        tt(b("WN", 0, 128), ind("TRZ", 272, uu, 24, 32), b("uE"), A.mult)
-        lin(b("L", n0, n0 + 128), ind("WN", 384, se))
+        tt(low, ind("TRZ", 272, uu, 16, 24), b("uE"), A.mult)
         if not last:
-            act(ind("C", 1152, uu, 16, 24), b("CV"), F.Silu)
+            act(ind("C", TOP, uu, 8, 16), b("CV"), F.Silu)
         if not end:
-            tt(b("y2"), b("dn"), b("pw", 272, 280), A.mult)
-            act(b("y3"), zs, F.Relu, bias=-4096.0 * 255.5)
-            mm(*[(b("pw", 256, 264), b(w), x, i == 0, i == 4) for i, (w, x) in enumerate(
-                (("I32", v), ("I32", b("y2")), ("I", b("y3")), ("Im4", b("made", 0, 8)), ("Im4", b("made", 8, 16))))])
-            tt(v, b("pw", 256, 264), DUM, A.min)
-            cp(b(vz, 0, 8), v)
-            child(r)
-        if s == 0:
-            lin(b("zacc"), b("U", 24, 32))
-        else:
-            tt(b("zacc"), b("zacc"), b("U", 24, 32), A.min)
+            pv = b("pw", 272, 280)
+            mm((pv, b("I"), v, True, False), (pv, b("I"), b("y3"), False, False), (pv, b("I"), b("y2"), False, False))
+            mm((pv, b("Im4"), b(mk, 16 * s, 16 * s + 8), False, False), (pv, b("Im4"), b(mk, 16 * s + 8, 16 * s + 16), False, True))
+            ts(b(vz, 0, 8), pv, float(REST[r][s + 1]), A.min)
+            ts(v, pv, float(REST[r][s + 1]), A.min)
+            if AOLD:
+                lin(b("x5%d" % r), pv, 4096.0)
+            child(r, s + 1)
         if end:
-            cp(b("za"), b("zacc"))
-            second(r, b("za"))
-        tt(ind("L", 1152, uu, 8, 16), b("uE"), b("WN", 0, 128), A.subtract)
+            if r == 0:
+                cut_rows(0, 2)
+            if r == 0:
+                mm((b("pw", 272, 280), b("I32"), b("U1", 16, 24), True, False))
+                mm((b("pw", 272, 280), b("I32"), b("U2", 16, 24), False, True))
+                ts(b("zo"), b("pw", 272, 280), -256.0, A.add)
+                tt(b("X5"), ind("TRZ", 272, "zo"), b("uQ0"), A.mult)
+            made(r, "id%d" % r, None if r else "za", S_)
+        tt(ind("L", TOP, uu, 0, 8), b("uE"), low, A.subtract)
+        if end and r == 0:
+            tt(b("L", SB[0], SB[0] + 128), b("L", SB[0], SB[0] + 128), b("X5"), A.add)
         if last:
-            at_cut(r, b("uE"), b(uu, 24, 32), False, True)
-            unmade(r)
+            tt(b("EL"), ind("IDZ", 272, uu, 16, 24), b("Y"), A.mult)
+            tt(b("WN"), ind("TRZ", 272, uu, 16, 24), b("uQ1"), A.mult)
+            mm((b("pq", 0, 128), b("BO"), b("EL"), True, True))
+            tt(b("LN"), b("WN"), b("pq", 0, 128), A.mult)
+        elif end:
+            lin(b("L", cb, cb + 128), low)
+        else:
+            dma("Y", T.L[:, cb:cb + 128], T.WN[:], r=[low], w=[b("L", cb, cb + 128)])
         if not end:
-            edge()
+            edge(r, s + 1)
 
     roots_first()
     cp(b("Ql"), b("Qi"))
-    ts(b("C", 0, 384), b("Ci"), float(CO), A.add)
-    ts(b("L", 0, 384), b("Ei"), -1.0, A.mult, 2047.0, A.add)
-    lin(b("lsave", 0, 1), b("L", 0, 1))
-    ms(b("L", 0, 1), -1.0)
-    child(0, False)
+    ts(b("C", CO, Z), b("Ci"), float(CO), A.add)
+    ts(b("L", CO, Z), b("Ei"), -1.0, A.mult, 2047.0, A.add)
+    lin(b("lsave", 0, 1), b("L", CO, CO + 1))
+    ms(b("L", CO, CO + 1), -1.0)
+    child(0, 0, False)
     cp(b("QF"), b("Qi"))
     ms(b("X", 2048, XW), FAR)
     cp(b("xsave", 0, 1), b("X", 2047, 2048))
     ms(b("X", 2047, 2048), NONE)
-    edge()
+    edge(0, 0)
     travel("Qi", "LQ", "E")
     cp(b("Q16"), b("Qi"))
     for s in range(S_):
         step(0, s)
-    cut_rows(0, 2)
-    child(1)
-    edge()
+    child(1, 0)
+    edge(1, 0)
     ts(b("lz"), b("LK", 0, 32, 4), 2.0 ** -12, A.mult)
     tt(b("HK"), ind("TRZ", 272, "lz"), b("HMQ"), A.mult)
     tt(b("QF"), b("HK"), b("LQ"), A.add)
@@ -721,12 +979,13 @@ def rank_program(g, core, T, topo):
     cp(b("Q16"), b("QF"))
     for s in range(S_):
         step(1, s)
-    lin(b("YE", 0, 384), b("L", 0, 384), -1.0, 2047.0)
+    lin(b("YE", 0, 384), b("L", CO, Z), -1.0, 2047.0)
     lin(b("YE", 0, 1), b("lsave", 0, 1), -1.0, 2047.0)
     for r in range(RO_):
         n1 = 384 + 256 * r
-        for j, o in ((128, 0), (0, 1)):
-            lin(b("YE", n1 + o, n1 + 256, 2), b("LN") if r and o else b("L", n1 + j, n1 + j + 128), -1.0, 2047.0)
+        lin(b("YE", n1, n1 + 256, 2), ind("L", BLANK + 1, "id%d" % r), -1.0, 2047.0)
+        lin(b("X6") if r else b("YE", n1 + 1, n1 + 256, 2), b("L", SB[r], SB[r] + 128), -1.0, 2047.0)
+    tt(b("YE", 641, 896, 2), b("X6"), b("LN"), A.subtract)
     dma("Y", T.ye[:, 0:640], T.YE[:, 0:640], r=[b("YE", 0, 640)])
     dma("Y", T.ye[:, 640:896], T.YE[:, 640:896], r=[b("YE", 640, 896)])
     dma("Y", T.yr[:], T.LAND1[:], r=[b("LAND1")])

@@ -7,11 +7,11 @@ SCRATCH = {}
 PLACE = {}
 
 
-def _b(name, n, d, where="sbuf"):
-    pool = {F32: "poolf", U16: "poolu", I32: "pooli", BF: "poolb", H16: "poolh"}.get(d)
+def _b(name, n, d, where="sbuf", own=False):
+    pool = {F32: "poolf", U16: "poolu", I32: "pooli", BF: "poolb", H16: "poolh"}[d]
     if isinstance(n, list):
         SCRATCH[name] = (where, [128] + n, d)
-    elif n > (88 if d == BF else 40) or where != "sbuf" or pool is None:
+    elif n > (88 if d == BF else 40) or where != "sbuf" or own:
         SCRATCH[name] = (where, [128, n], d)
         PLACE[name] = (name, 0, n)
     else:
@@ -22,45 +22,38 @@ def _b(name, n, d, where="sbuf"):
 
 XW, LL = 2320, 137
 for _d, _l in (
-    (BF, "X:2320 XQ:2048 BO:128 I:128 I2:128 Im:128 IH:128 IR:128 B0:128 SHD:128 ZH:272 ZL:272 OHZ:272 TRZ:272 "
-         "IDZ:272 OHB:272 OHC:272 OH0:272 OH1:272 OH2:272 KD:128 KT:128 K3:137 M16:137 RD:137 RMP:137 OH:128 "
-         "BA:128 TA:128 ONE:128 SA:128 I7:128 XQg:128 DFg:128 DH:128 xsave:16 I4:128 Im4:128 KC:88 athr:8 EA:16 "
-         "zcf:8 mk0:48 mk1:48 cut:8 CODE:1920 KD2:128 VC:256 SV:128 I16:128 I6:128 fz:8 fu:8 c24:2 CN:128 RMQ:144 B6:128 KD6:128 "
-         "IC6:128 JP:8 dn:8 y3:8 KA:576 KB:18 AD:576 RA:576 NE:576 RE:576 SG:128 nf:8 XA:128 XB:128"),
-    (F32, "L:2464 C:2192 IOT:2064 W1:137 W2:137 W3:137 W3n:137 S1:137 S2:137 SZ0:409 SZ1:409 SZ2:409 zt:8 QF:128 uQ0:128 uQ1:128 SN:128 "
-          "LAND1:128 SND:128 HMQ:128 HK:128 uE:128 CV:128 CG:128 SE:128 SQ:128 DS:128 WN:128 "
-          "OHM:128 LK:48 LN:128 X5:128 X6:128 YE:896 cols:18 LC:32 lsave:2 "
-          "I32:128 ICS:128 JC:8 U0:24 U1:24 U2:24 dd:8 STD:2192 I12:128 Ia:128 Ib:128 vcol:128 tcol:128 THR:6 THS:6 x50:8 x51:8 x2:8 TS:8 TU:8 d0:8"),
-    (H16, "Q16:128 Q1:128 B620:137 M1:128 EL:128 Y:128 Hf:128 Hm:128 VT:128 SC:128 v0:8 v1:8 y2:8"),
-    (I32, "Qi:128 LQ:128 Ci:384 Ei:384 QI:137 QA:137 HP:128 HI:128 IP:2 IC:2 qi:8 qj:16"),
-    (U16, "Ql:128 El:128 vz0:16 vz1:16 cl:8 tp:16 lz:8 zo:8 UU0:32 UU1:32 id0:8 id1:8 ido:8 za:8 didx:8 sl:8 zl0:8 zl1:8"),
+    (BF, "X:2320 XQ:2048 DF:2064 BO:128 B0:128 B1:128 B6:128 SHD:128 I:128 I2:128 Im:128 IH:128 IR:128 I4:128 Im4:128 I16:128 I6:128 "
+         "IG:128 IC6:128 ZR:128 CZ:144 ZH:272 ZL:272 OHZ:272 TRZ:272 IDZ:272 ID4:18 OHB:272 OHC:272 OH2:528 WW:816 KD:128 KD6:128 "
+         "K3:137 M16:137 RD:137 RMP:137 FL:137 KA:584 KF:584 KG:18 KC:40 KP:32 KR:256 AD:584 RA:584 OH:128 SG:128 SA:128 XQg:128 "
+         "DFg:128 DH:128 CN:128 RMQ:144 Wg:128 XA:128 XB:128 XC:128 Hm:128 athr:8 nf:8 EA:16 zcf:8 mk0:48 mk1:48 fl:24 fz:8 fu:8 JP:8 dn:8 y3:8"),
+    (F32, "L:2464 C:2200 STD:2192 IOT:2200 W1:137 W2:137 W3:137 S1:137 S2:137 SZ0:409 SZ1:409 SZ2:409 QF:128 uQ0:128 uQ1:128 "
+          "LAND1:128 SND:128 HMQ:128 uE:128 CV:128 CG:128 SE:128 SQ:128 WN:128 OHM:128 LN:128 X5:128 X6:128 YE:896 vcol:128 "
+          "I32:128 ICS:128 Ia:128 Ib:128 cols:18 LC:32 lsave:2 JC:8 U0:40 U1:40 U2:24 THR:6 THS:6 x50:8 x51:8 x2:8 x3:8"),
+    (H16, "Q16:128 Q1:128 B620:137 M1:128 EL:128 HK:128 Y:128 VT:128 SC:128 NF:584 RF:584 v0:8 v1:8 y2:8"),
+    (I32, "Qi:128 LQ:128 Ci:384 Ei:384 HP:128 HI:128 IP:2 IC:2 qi:8 qj:16"),
+    (U16, "Ql0:128 Ql1:128 SQl:128 El:128 vz0:16 vz1:16 cl:8 tp:16 lz:8 zo:8 za:8 UU0:32 UU1:32 id0:8 id1:8 didx:8 sl:8 zl0:8 zl1:8"),
 ):
     for _x in _l.split():
         _b(_x.split(":")[0], int(_x.split(":")[1]), _d)
-_b("AB", [128, 17], BF); _b("QX", [8, 8, 16], H16); _b("CZ", 144, BF); _b("DF", 2064, BF)
-_b("NF", 584, H16); _b("RF", 584, H16); _b("KF", 584, BF); _b("KG", 18, BF)
-for _x in "SN NE RE tcol CODE KD2 VC SV BA TA ONE I7".split():
-    del SCRATCH[_x]
-TSCAN, ROW16, MDIR = True, True, True
+_b("AB", [128, 17], BF); _b("QX", [8, 8, 16], H16); _b("XT", 16, BF, own=True)
 PS = ["pd", "pm", "pt", "ps", "pq", "pa", "pw", "ph"]
 for _n in PS:
     _b(_n, 512, F32, "psum")
-SEMAPHORES = ["sV", "sT", "sS", "sG", "locE", "loc0", "loc1", "arrE", "arr0", "arr1"] + ["d%d" % _i for _i in range(20)]
-TDUMP, BIG, HH, CO = 2050, float(2 ** 22), float(2 ** 22), 32
-Z, NEW = CO + 384, CO + 392
+SEMAPHORES = ["sV", "sT", "sS", "sG", "locE", "loc0", "loc1", "arrE", "arr0", "arr1"] + ["d%d" % _i for _i in range(16)]
+TDUMP, BIG, HH, FRZ, CO = 2050, float(2 ** 22), float(2 ** 22), float(2 ** 24), 32
+FAR, NONE = 294.0, 560.0
+OLD, NEW = CO + 384, CO + 392
 NDUMP, TOP, BLANK = NEW + 136 * 12, NEW + 136 * 13, NEW + 136 * 14 + 128
 SB = [NEW, NEW + 136 * 7]
 LB = [[NEW + 136 * _j for _j in _l] for _l in ((1, 3, 5), (8, 10, 13))]
 KIDS = [[NEW, LB[0][0] + 128, LB[0][1] + 128], [LB[0][2] + 264, LB[1][0] + 128, LB[1][1] + 128]]
-REST = [[Z, Z + 1, KIDS[0][1]], [Z, KIDS[1][0], KIDS[1][1]]]
-FAR, NONE = 294.0, 560.0
-PLANS, PASSES = [(_h, _l) for _h in (280, 300, 320, 350) for _l in (100, 300, 600)], 4
+CHUNKS = (0, 24, 64, 100, 128)
+SPLIT, STDV = True, (1, 3, 4, 5)
 HOP, FLY = 240, 3000
-CHUNKS = (0, 16, 40, 64, 88, 112, 128)
-RELU = 0
-DIRECT, AOLD, TOLD, FRZ = True, True, True, float(2 ** 24)
-CASES, MOVES, SLACK, NOTE = [(330, 1, 0.65, 1.56, 3.8), (350, 1, 0.6, 1.2, 2.5), (270, 1.3, 0.8, 1.7, 4.4)], 20000, 400, []
-CELLS = {}
+PLANS, PASSES = [(_h, _l) for _h in (280, 300, 320, 350) for _l in (100, 300, 600)], 4
+CASES = [(250, 1, 0.65, 1.56, 3.8), (330, 1, 0.6, 1.3, 2.8), (220, 1.3, 0.8, 1.7, 4.4)]
+TURNS, WIDTH, MOVES, SLACK, EARLY, SEED = 55, 160, 150, 300, 0.1, 12345
+CELLS, NOTE, HINT = {}, [], True
 ORDER = []
 
 
@@ -68,7 +61,7 @@ def make(g, T):
     eng = {"V": g.vector, "S": g.scalar, "T": g.tensor, "G": g, "Y": g.sync}
     tick = {"V": 0, "S": 0, "T": 0, "G": 0}
     known = {q: {} for q in eng}
-    snap, acc, final, ndma, ops, INDIRECT = {}, {}, {}, [0], [], {}
+    snap, acc, final, ndma, ops, indirect = {}, {}, {}, [0], [], {}
 
     def ap(x):
         if not isinstance(x, tuple):
@@ -159,14 +152,17 @@ def make(g, T):
             deps(q, r, w, "s" + q, tick[q] + 1)
             fin(q, f())
         if out[0] == "@" or any(isinstance(x, tuple) and x[0] == "@" for x in ins):
-            INDIRECT[emit] = ("s" if out[0] == "@" else "g", size(out))
+            indirect[emit] = ("s" if out[0] == "@" else "g", size(out))
         ops.append((q, r, w, cycles(q, out, ins, both), HOP, emit))
 
-    def either(fs, fv):
-        fs()
-        fv()
-        v, s = ops.pop(), ops.pop()
-        ops.append((s[0], s[1] + v[1], s[2], s[3], s[4], s[5], v))
+    def either(*fs):
+        n = len(ops)
+        for f in fs:
+            f()
+        ways = [x for op in ops[n:] for x in [op[:6]] + list(op[6:])]
+        del ops[n:]
+        s = ways[0]
+        ops.append((s[0], [x for op in ways for x in op[1]], s[2], s[3], s[4], s[5], *ways[1:]))
 
     def order():
         seen, pred = {}, []
@@ -176,8 +172,9 @@ def make(g, T):
                 for x in xs:
                     for lo, hi, ew, j, y in seen.get(x[0], []):
                         hit = lo < x[2] and x[1] < hi and (isw or ew) and (op[4] != HOP or ops[j][4] != HOP or not apart(x, y))
-                        if hit or (x[0] in PS and not ops[j][0] == op[0] == "V" and not (len(op) == 6 == len(ops[j]) and ops[j][0] == op[0] == "S")):
-                            p[j] = p.get(j, False) or hit
+                        alike = len(op) == 6 == len(ops[j]) and ops[j][0] == op[0] != "T"
+                        if hit or (x[0] in PS and not alike):
+                            p[j] = p.get(j, False) or (hit and x[0][0] != "#")
             for isw, xs in ((0, op[1]), (1, op[2])):
                 for x in xs:
                     l = seen.setdefault(x[0], [])
@@ -217,7 +214,7 @@ def make(g, T):
         def span(seq, hop, slow):
             end, free = {}, {q: 0 for q in eng}
             for i, k in seq:
-                op = ops[i][6] if k else ops[i]
+                op = ops[i][5 + k] if k else ops[i]
                 t = max([end[j][0] + gap(j, i, end[j][1], op[0], hop) for j in pred[i]] + [free[op[0]]])
                 free[op[0]] = t + op[3] * (slow if op[0] in "VS" else 1)
                 end[i] = (free[op[0]], op[0])
@@ -240,112 +237,183 @@ def make(g, T):
         return polish(kept[1], pred, succ)
 
     def polish(seq, pred, succ):
-        n = len(ops)
+        n, cases = len(ops), range(len(CASES))
         below = [0] * n
         for j in reversed(range(n)):
             for i in succ[j]:
                 below[j] |= below[i] | 1 << i
         need = [[] for _ in range(n)]
         for j in range(n):
-            far = 0
-            for k in succ[j]:
-                if (pred[k][j] and ops[j][0] != "T") or ops[j][0] == ops[k][0] == "T" or (ops[j][0] == "T") != (ops[k][0] == "T"):
-                    far |= below[k]
             hard = 0
             for k in succ[j]:
-                if not ops[j][0] == ops[k][0] == "T":
+                if ops[j][0] != "T" or ops[k][0] != "T":
                     hard |= below[k] if pred[k][j] or "T" in (ops[j][0], ops[k][0]) else 0
             for i in succ[j]:
-                tt_ = ops[j][0] == ops[i][0] == "T"
-                if not (far if tt_ else hard) >> i & 1:
-                    need[i].append((j, tt_ or not pred[i][j], ops[j][4]))
+                both = ops[j][0] == ops[i][0] == "T"
+                if not (below[j] & ~(1 << i) and both and any(below[k] >> i & 1 for k in succ[j])) and not hard >> i & 1:
+                    need[i].append((j, both or not pred[i][j], ops[j][4]))
         tail = [op[4] for op in ops]
 
         def held(o, slow, pe, gather, scatter):
-            kind, m = INDIRECT.get(o[5], ("", 0))
+            kind, m = indirect.get(o[5], ("", 0))
             d = o[3] + m * (gather - 1.56 if kind == "g" else scatter - 3.8)
             return o[0], d * (pe if o[0] == "T" else 1 if o[0] == "Y" or o[4] != HOP else slow)
         alts = [[[held(o, *x[1:]) for o in [op] + list(op[6:])] for op in ops] for x in CASES]
         needs = [[[(j, soft, x[0] if lag == HOP else lag) for j, soft, lag in l] for l in need] for x in CASES]
-
-        def run(order, pick, alt, need, old, a):
-            end, que, why = (list(x) for x in old[2:])
-            free, last = {q: 0.0 for q in eng}, {q: None for q in eng}
-            left, k = set(eng), a - 1
-            while left and k >= 0:
-                i = order[k]
-                if que[i] in left:
-                    left.discard(que[i])
-                    free[que[i]], last[que[i]] = end[i], i
-                k -= 1
-            top, at = 0.0, None
-            for i in order[a:]:
-                q, d = alt[i][pick[i]]
-                t, w = free[q], last[q]
-                for j, soft, lag in need[i]:
-                    e = end[j] if soft and que[j] == q else end[j] + lag
-                    if e >= t:
-                        t, w = e, ~j
-                t += d
-                end[i], que[i], why[i], free[q], last[q] = t, q, w, t, i
-                if t + tail[i] > top:
-                    top, at = t + tail[i], i
-            return top, at, end, que, why
-
-        def judge(order, pick, old, a):
-            res = [run(order, pick, alts[k], needs[k], old[k], a) for k in range(len(CASES))]
-            return sum(r[0] / x[1] for r, x in zip(res, CASES)), res
-
+        gives = [[[] for _ in ops] for c in cases]
+        for c in cases:
+            for i in range(n):
+                for j, soft, lag in needs[c][i]:
+                    gives[c][j].append((i, soft, lag))
         order, pick = [i for i, k in seq], [0] * n
         for i, k in seq:
             pick[i] = k
-        alt = alts[0]
-        now, res = judge(order, pick, [(0, 0, [0.0] * n, [None] * n, [None] * n)] * len(CASES), 0)
-        best, state = (now, order, pick), 12345
-        for it in range(MOVES):
-            state = (state * 1103515245 + 12345) % 2 ** 31
-            top, i, _, _, why = res[(state >> 8) % len(res)]
-            pairs = []
-            while i is not None:
-                w = why[i]
+        ends, why, que = [[0.0] * n for c in cases], [[None] * n for c in cases], [alts[0][i][pick[i]][0] for i in range(n)]
+        state = [SEED]
+
+        def rnd(m):
+            state[0] = (state[0] * 1103515245 + 12345) % 2 ** 31
+            return (state[0] >> 8) % m
+
+        def rests(part, c, rest, beyond, behind):
+            nxt = dict(behind)
+            for x in reversed(part):
+                q = que[x]
+                t = max(beyond[x][pick[x]], nxt[q])
+                for y, soft, lag in gives[c][x]:
+                    e = rest[y] if soft and que[y] == q else rest[y] + lag
+                    if e > t:
+                        t = e
+                rest[x] = nxt[q] = t + alts[c][x][pick[x]][1]
+
+        def run(part, before, beyond, behind):
+            total, tops = 0.0, []
+            for c in cases:
+                end, wh, alt, need, out = ends[c], why[c], alts[c], needs[c], beyond[c]
+                free, last = dict(before[c]), {q: None for q in eng}
+                top, at, early = 0.0, None, 0.0
+                for i in part:
+                    k = pick[i]
+                    q, d = alt[i][k]
+                    t, w = free[q], last[q]
+                    for j, soft, lag in need[i]:
+                        e = end[j] if soft and que[j] == q else end[j] + lag
+                        if e >= t:
+                            t, w = e, ~j
+                    t += d
+                    end[i], wh[i], free[q], last[q] = t, w, t, i
+                    early += t
+                    if t + out[i][k] > top:
+                        top, at = t + out[i][k], i
+                for q in eng:
+                    if last[q] is not None and free[q] + behind[c][q] > top:
+                        top, at = free[q] + behind[c][q], last[q]
+                total += (top + EARLY * early / len(part)) / CASES[c][1]
+                tops.append(at)
+            return total, tops
+
+        def move(part, tops, inside, before, beyond, behind, rest, fresh):
+            c = rnd(len(CASES))
+            i, pairs = tops[c], []
+            while i is not None and i in inside:
+                w = why[c][i]
                 if w is not None and w >= 0 and not below[w] >> i & 1:
                     pairs.append((w, i))
                 i = w if w is None or w >= 0 else ~w
             if not pairs:
-                break
-            state = (state * 1103515245 + 12345) % 2 ** 31
-            p, i = pairs[(state >> 8) % len(pairs)]
-            kind = (state >> 20) % 6
-            o2, p2 = order, pick
-            a = order.index(p)
-            if kind < 2 and len(alt[(p, i)[kind]]) > 1:
-                p2 = list(pick)
-                p2[(p, i)[kind]] ^= 1
+                return None
+            p, i = pairs[rnd(len(pairs))]
+            kind, m, end = rnd(12), len(part), ends[c]
+            if kind < 7:
+                if c not in fresh:
+                    rests(part, c, rest[c], beyond[c], behind[c])
+                    fresh[c] = {x: k for k, x in enumerate(part)}
+                pos, rs, x = fresh[c], rest[c], p if kind % 3 else i
+                lo = max([pos.get(j, -1) for j in pred[x]] + [-1])
+                hi = min([pos.get(j, m) for j in succ[x]] + [m])
+                found = None
+                for k, (q, d) in enumerate(alts[c][x]):
+                    ready = max([end[j] + (0 if soft and que[j] == q else lag) for j, soft, lag in needs[c][x]] + [0])
+                    after = max([rs[y] + (0 if soft and que[y] == q else lag) for y, soft, lag in gives[c][x]] + [tail[x]])
+                    z = lo
+                    while z >= 0 and (que[part[z]] != q or part[z] == x):
+                        z -= 1
+                    u, at = end[part[z]] if z >= 0 else before[c][q], lo + 1
+                    for z in range(lo + 1, m + 1):
+                        w = part[z] if z < m else None
+                        if w is not None and (que[w] != q or w == x):
+                            continue
+                        t = max(ready, u) + d + max(after, rs[w] if w is not None else behind[c][q]) + rnd(128)
+                        if (found is None or t < found[0]) and (k != pick[x] or not at <= pos[x] <= z):
+                            found = (t, k, at)
+                        if z >= hi:
+                            break
+                        u, at = end[w], z + 1
+                if found is None:
+                    return None
+                a, z = pos[x], found[2]
+                return (part[:z] + [x] + part[z:a] + part[a + 1:] if z <= a else part[:a] + part[a + 1:z] + [x] + part[z:]), x, found[1]
+            if kind < 9 and len(alts[0][(p, i)[kind % 2]]) > 1:
+                x = (p, i)[kind % 2]
+                return part, x, (pick[x] + 1 + rnd(len(alts[0][x]) - 1)) % len(alts[0][x])
+            a, z = part.index(p), part.index(i)
+            if kind % 2:
+                first = lambda x: x == i or below[x] >> i & 1
             else:
-                z = order.index(i)
-                mid = order[a:z + 1]
-                if kind % 2:
-                    up = [x for x in mid if x == i or below[x] >> i & 1]
-                    o2 = order[:a] + up + [x for x in mid if not (x == i or below[x] >> i & 1)] + order[z + 1:]
-                else:
-                    dn = [x for x in mid if x == p or below[p] >> x & 1]
-                    o2 = order[:a] + [x for x in mid if not (x == p or below[p] >> x & 1)] + dn + order[z + 1:]
-            t, r2 = judge(o2, p2, res, a)
-            if t <= now + SLACK * (1 - it / MOVES) * ((state >> 4) % 16) / 16:
-                now, res, order, pick = t, r2, o2, p2
-                if t < best[0]:
-                    best = (t, order, pick)
-        NOTE.extend([kept_first(best[0])])
-        return [(i, best[2][i]) for i in best[1]]
+                first = lambda x: not (x == p or below[p] >> x & 1)
+            mid = part[a:z + 1]
+            return part[:a] + [x for x in mid if first(x)] + [x for x in mid if not first(x)] + part[z + 1:], p, pick[p]
 
-    def kept_first(x):
-        return x
+        nothing, own = [{q: 0.0 for q in eng} for c in cases], [[[tail[i]] * len(alts[0][i]) for i in range(n)] for c in cases]
+        best = None
+        for turn in range(TURNS + 1):
+            t = run(order, nothing, own, nothing)[0]
+            if best is None or t < best[0]:
+                best = (t, list(order), list(pick))
+            order.sort(key=lambda x: ends[0][x] - alts[0][x][pick[x]][1])
+            rest = [[0.0] * n for c in cases]
+            for c in cases:
+                rests(order, c, rest[c], own[c], nothing[c])
+            at = -rnd(WIDTH // 2)
+            while at < n - WIDTH // 4 and turn < TURNS:
+                lo, hi = max(at, 0), min(at + WIDTH, n)
+                part, inside = order[lo:hi], set(order[lo:hi])
+                before, behind = [dict(x) for x in nothing], [dict(x) for x in nothing]
+                for c in cases:
+                    for i in order[:lo]:
+                        before[c][que[i]] = ends[c][i]
+                    for i in reversed(order[hi:]):
+                        behind[c][que[i]] = rest[c][i]
+                beyond = [{i: [max([tail[i]] + [rest[c][y] + (0 if soft and que[y] == q else lag) for y, soft, lag in gives[c][i]
+                                                if y not in inside]) for q, d in alts[c][i]] for i in part} for c in cases]
+                now, tops = run(part, before, beyond, behind)
+                fresh = {}
+                for _ in range(MOVES):
+                    new = move(part, tops, inside, before, beyond, behind, rest, fresh)
+                    if new is None:
+                        continue
+                    other, x, k = new
+                    old, kept = pick[x], [([ends[c][i] for i in part], [why[c][i] for i in part]) for c in cases]
+                    pick[x], que[x] = k, alts[0][x][k][0]
+                    t, t2 = run(other, before, beyond, behind)
+                    if t <= now + SLACK * (1 - turn / TURNS) ** 2 * rnd(16) / 16:
+                        now, tops, fresh = t, t2, {}
+                        part = sorted(other, key=lambda y: ends[0][y] - alts[0][y][pick[y]][1])
+                    else:
+                        pick[x], que[x] = old, alts[0][x][old][0]
+                        for c in cases:
+                            for i, e, w in zip(part, *kept[c]):
+                                ends[c][i], why[c][i] = e, w
+                order[lo:hi] = part
+                at += WIDTH // 2
+        NOTE.append(best[0])
+        return [(i, best[2][i]) for i in best[1]]
 
     def flush():
         if not ORDER:
             ORDER.extend(order())
         for i, k in ORDER:
-            (ops[i][6] if k else ops[i])[5]()
+            (ops[i][5 + k] if k else ops[i])[5]()
 
     def fin(q, ins):
         sem = "s" + q
@@ -384,8 +452,8 @@ def make(g, T):
         kw = dict(allow_small_or_imprecise_dtypes=True) if fl else {}
         call("G", out, [], lambda: g.iota(ap(out), pattern, base, cm, **kw))
 
-    def sel(out, a, pattern, op, base, cm):
-        call("G", out, [a], lambda: g.affine_select(ap(out), ap(a), pattern, op, 0.0, base, cm))
+    def sel(out, a, pattern, op, base, cm, fill=0.0):
+        call("G", out, [a], lambda: g.affine_select(ap(out), ap(a), pattern, op, fill, base, cm))
 
     def mm(*lst):
         r, w = [x[1] for x in lst] + [x[2] for x in lst], [x[0] for x in lst]
@@ -447,6 +515,22 @@ def rank_program(g, core, T, topo):
     def ind(w, hi, o, lo=0, oh=None):
         return ("@", b(w, 0, hi), b(o, lo, oh))
 
+    def total(out, *terms, start=True, stop=True):
+        mm(*[(out, b(w), x, start and i == 0, stop and i == len(terms) - 1) for i, (w, x) in enumerate(terms)])
+
+    def turn(name):
+        op = K["ops"][-1]
+        K["ops"][-1] = op[:2] + (list(op[2]) + [(name, 0, 1, None, True)],) + op[3:]
+
+    def put(out, x):
+        either(lambda: act(out, x, F.Silu), lambda: cp(out, x))
+
+    def fill(out, c):
+        either(lambda: ms(out, c), lambda: iota(out, [[0, out[2] - out[1]]], int(c), 0))
+
+    def copy(out, x):
+        either(lambda: lin(out, x), lambda: sel(out, x, [[0, out[2] - out[1]]], A.is_ge, 0, 0))
+
     def rev(n, at=0):
         return b(n, 1 + at, LL + at, -1)
 
@@ -463,263 +547,208 @@ def rank_program(g, core, T, topo):
         scan(b(out), b(kd), src, 0.0, A.mult, A.max)
         return b(out, 15, 128, 16)
 
-    def lower(out, eq, row, width, own):
-        part = lambda c, lo, hi: nd(eq, width * c + lo, width * c + hi, c, slice(lo, hi))
-        for c in range(8):
-            n = width - 16 * c
-            own(part(c, 0, n), b(row, 16 * c, width), c)
-            if width > 128 or c < 7:
-                mm(*([(b("pa", out, out + 128), b("BO"), part(c, n - 128, n), False, False)] if width > 128 else []),
-                   *([(b("pa", out + 16 * c + 16, out + 128), b("BA"), part(c, 16, 128 - 16 * c), False, False)] if c < 7 else []))
-        mm((b("pa", out, out + 128), b("TA"), nd(eq, 0, 8 * width, al, slice(0, 16)), False, True))
-
     def seg(c):
-        return (144 * c if c < 4 else 144 * (7 - c) + 16 * (8 - c)), 16 * c + 16
+        return (146 * c + 1 if c < 4 else 162 * (7 - c) + 18), 16 * c + 16
 
-    def least(out, res, row, own):
-        for c in range(8):
-            o, n = seg(c)
-            either(lambda: act(b(out, o, o + n), b(row, 0, n), F.Abs, bias=b(own, c, c + 1), scale=-1.0),
-                   lambda: ts(b(out, o, o + n), b(row, 0, n), b(own, c, c + 1), A.not_equal, 4096.0, A.mult))
-        scan(b(res), b(out), b("KA"), 2 * FRZ, A.min, A.add)
-        return b(res, 14, 576, 160), b(res, 142, 575, -144)
+    def picked(n):
+        return b(n, 15, 584, 162), b(n, 144, 583, -146)
 
-    CS = col(4)
-    DT = b("LC", 24, 32)
-    pe = b("pa", 256, 384) if AOLD else b("ps", 128, 256)
+    CS, DT = col(4), b("LC", 24, 32)
 
     dma("Y", T.Qi[:], T.req[:], w=[b("Qi")])
     dma("Y", T.Ci[:], T.child[:], w=[b("Ci")])
-    dma("Y", T.X[:, 0:2048], T.desc[:], w=[b("X", 0, 2048)])
+    dma("Y", T.X[:, 0:2032], T.desc[:, 0:2032], w=[b("X", 0, 2032)])
     dma("Y", T.Ei[:], T.edge[:], w=[b("Ei")])
+    dma("Y", T.XT[:], T.desc[:, 2032:2048], w=[b("XT")])
 
     iota(b("IP", 0, 1), [[1, 1]], 0, 1, False)
     iota(b("ZH"), [[1, 17], [0, 16]], 0, 0)
     iota(b("ZL"), [[0, 17], [1, 16]], 0, 0)
-    for lo, hi in ((0, 144), (144, 704), (704, 1400), (1400, 2064)):
+    for lo, hi in ((0, 144), (144, 704), (704, 1400), (1400, 2200)):
         iota(b("IOT", lo, hi), [[1, hi - lo]], lo, 0)
-    if not TOLD:
-        ms(b("IOT", 2048, 2049), 4000.0)
-    if not AOLD:
-        lin(b("CODE", 0, 128), b("IOT", 0, 128), 1.0, 128.0)
-        for n in (128, 256, 512, 1024):
-            lin(b("CODE", n, min(2 * n, 1920)), b("CODE", 0, min(n, 896)), 2.0 ** (n // 128))
-    else:
-        for lo in range(0, KIDS[1][2], 272):
-            either(lambda: act(b("STD", lo, lo + 272), b("ZH"), scale=0.0), lambda: ms(b("STD", lo, lo + 272), 0.0))
-        iota(b("THR"), [[256, 6]], 192, 0)
+    iota(b("THR"), [[256, 6]], 192, 0)
     lin(b("RMQ"), b("IOT", 0, 144))
     for lo in [SB[0]] + LB[0] + LB[1][:1]:
         iota(b("C", lo, lo + 128), [[0, 128]], CO, 0)
-    iota(DT, [[32, 8]], TDUMP + (0 if TOLD else 4096), 2)
-    iota(b("LC", 0, 16), [[0, 2], [16, 8]], NDUMP, 1)
-    iota(b("K3", 1, LL), [[0, 8], [16, 17]], 0, 0)
-    iota(b("JC"), [[16, 8]], BLANK + 16, 1)
-    iota(b("dd"), [[256, 8]], 0, 16)
+    iota(b("LC", 0, 24), [[0, 3], [16, 8]], NDUMP, 1)
+    iota(b("K3", 1, LL), [[0, 8], [16, 17]], 2064, 0)
     ts(b("IC", 0, 1), b("IP", 0, 1), 4, A.arith_shift_right)
     ts(b("IC", 1, 2), b("IP", 0, 1), 15, A.bitwise_and)
     cp(col(0), b("IP", 0, 1))
     cp(b("cols", 1, 3), b("IC"))
-    ms(b("C", Z, NEW), float(Z))
-    for x in (REST[0][2], REST[1][1], REST[1][2]):
-        ms(b("C", x, x + 1), float(Z))
-    act(b("L", Z, NEW), b("C", Z, NEW), F.Silu, scale=0.0)
+    fill(b("C", TOP, TOP + 8), float(CO))
+    ms(b("M16"), -16.0)
+    act(b("STD", 0, 136), b("M16", 0, 136), F.Silu, scale=0.0)
     K["ops"][-1] = K["ops"][-1][:3] + (K["ops"][-1][3] + 1600,) + K["ops"][-1][4:]
-    lin(b("L", BLANK, BLANK + 8), b("L", Z, NEW))
+    turn("#s")
+    for lo in (136, 280):
+        either(lambda: act(b("STD", lo, lo + 144), b("ZH", 0, 144), scale=0.0), lambda: fill(b("STD", lo, lo + 144), 0.0))
+    lin(b("L", BLANK, BLANK + 8), b("STD", 0, 8))
     lin(col(3), col(2), 1.0, 1.0)
     ts(col(5), col(2), 0.0, A.is_equal)
     ts(col(6), col(2), 0.0, A.is_gt)
     ts(col(11), col(2), 14.5, A.is_gt)
     lin(col(7), col(11), 4095.0, 1.0)
     lin(col(4), col(11), 1.0 - 2.0 ** -12, 2.0 ** -12)
-    if not AOLD:
-        lin(col(14), col(11), -4095.0 * 271.5, 4096.0 * 271.5)
-        lin(col(15), col(7), 2048.0)
-        lin(b("c24", 0, 1), col(11), 1.0 - 2.0 ** 24, 2.0 ** 24)
     lin(col(16), col(11), 63.0, 1.0)
-    for j, c, d in ((8, -16.0, 0.0), (9, -32.0, 0.0), (10, -256.0, 0.0)):
-        lin(col(j), col(1), c, d)
+    lin(col(8), col(1), -16.0)
+    lin(col(9), col(4), -1.0)
+    lin(col(10), col(2), 1.0, 16.0 * 2047)
     ts(b("BO"), b("ZH", 0, 128), col(1), A.is_equal)
     lin(b("B0"), b("BO"), col(5))
-    if not AOLD:
-        lin(b("BA"), b("BO"), 256.0)
-        sel(b("TA"), b("BA"), [[1, 128]], A.is_gt, 0, -1)
-        ms(b("ONE"), 1.0)
+    turn("#s")
+    lin(b("B1"), b("B0"), 16.0)
     sel(b("SHD"), b("BO"), [[1, 128]], A.is_equal, -1, -1)
     ts(b("KD"), b("ZL", 0, 128), col(2), A.is_gt)
-    ts(b("KT"), b("ZL", 0, 128), col(3), A.is_equal, 4095.0, A.mult)
-    tt(b("KD"), b("KD"), b("KT"), A.add)
+    ts(b("KD6"), b("ZL", 0, 128), col(3), A.is_equal, 4095.0, A.mult)
+    tt(b("KD"), b("KD"), b("KD6"), A.add)
     ts(b("OHZ"), b("ZL"), col(2), A.is_equal)
     ts(b("IDZ"), b("ZH"), col(2), A.is_equal)
     ts(b("TRZ"), b("ZH"), col(2), A.is_le)
-    if not AOLD:
-        act(b("KD2"), b("KD"), F.Square)
+    lin(b("ID4", 0, 17), b("IDZ", 0, 272, 16), 4096.0)
     ts(b("KD6"), b("KD"), 64.0, A.min)
     lin(b("B6"), b("BO"), 1.0 / 64)
     ts(col(17), col(2), 7.5, A.is_gt, -16.0, A.mult)
     ts(col(17), col(17), col(2), A.add, 8.0, A.add)
     lin(col(13), col(17), -1.0, 15.0)
+    ts(b("I"), b("IOT", 0, 128), col(0), A.is_equal)
     ts(b("OHC"), b("ZL"), col(13), A.is_equal, 17.0, A.mult)
     ts(b("OHB"), b("ZH"), col(17), A.is_equal, 16.0, A.mult)
-    tt(b("OHB"), b("OHB"), b("OHC"), A.max)
-    for s in range(S_):
-        lin(b("OH%d" % s), b("OHB"), 272.0 * (s + 1), -16 * 272.0 * (s + 1))
-    ts(b("I"), b("IOT", 0, 128), col(0), A.is_equal)
-    for n, c in (("IH", HH / 2), ("IR", 2.0 ** 37), ("I2", 2.0), ("Im", -1.0), ("I4", 4096.0), ("Im4", -4096.0),
-                 ("I32", 1.0), ("I12", 2.0 ** -12) if AOLD else ("I7", col(7)), ("IC6", col(16)), ("ICS", CS), ("I16", 16.0), ("I6", 1.0 / 16)):
+    total(b("ps", 0, 272), ("I", b("OHB")), ("I", b("OHC")))
+    act(b("OHB"), b("ps", 0, 272), F.Relu, bias=17.0, scale=-1.0)
+    lin(b("OH2", 0, 256), b("OHB", 0, 256), -816.0, 816.0)
+    lin(b("OH2", 256, 528), b("OHB"), -816.0, 816.0)
+    lin(b("WW", 0, 272), b("OHZ"), 4096.0, -4096.0)
+    for s in range(2):
+        lin(b("WW", 272 * s + 272, 272 * s + 544), b("OHB"), -272.0 * (s + 1), -136.0)
+    for j, (r, s) in enumerate(((0, 0), (0, 1), (1, 0))):
+        fill(b("KP", 8 * j, 8 * j + 8), 17 * 2048.0 + 136 + 272 * (s + 1) - (BLANK + 16 - LB[r][s] - 136) - 32768)
+    fill(b("KP", 24, 32), 32768.0)
+    ms(b("ZR"), 0.0)
+    for n, c in (("IH", HH / 2), ("IR", 2.0 ** 37), ("I2", 0.5), ("Im", -1.0), ("I4", 4096.0), ("Im4", -4096.0),
+                 ("I16", 16.0), ("IG", 65536.0), ("I6", 1.0 / 16), ("I32", 1.0), ("Ia", -256.0), ("Ib", 257.0)):
+        either(lambda: lin(b(n), b("I"), c),
+               lambda: sel(b(n), b("STD", 0, 128) if SCRATCH[n][2] == F32 else b("ZR"), [[-1, 128]], A.not_equal, 0, 1, c))
+    for n, c in (("IC6", col(16)), ("ICS", col(7))):
         lin(b(n), b("I"), c)
     lin(col(12), col(1), 16.0, 15.0)
     ts(b("CZ"), b("IOT", 0, 144), col(12), A.is_equal, -HH, A.mult)
-    ts(col(17), col(11), -4095.0, A.mult, 4096.0, A.add)
-    if TOLD:
-        lin(DT, DT, 1.0, col(9))
-    else:
-        ts(DT, DT, col(9), A.add, col(17), A.mult)
-    if AOLD:
-        lin(b("THR"), b("THR"), col(17))
-        lin(b("THS"), b("THR"), -32768.0)
-    if TSCAN:
-        ms(b("KF"), 0.0)
-        lin(b("KG", 0, 16), b("OHZ", 0, 16), 4096.0)
-        ms(b("KG", 16, 17), -8192.0)
-        lin(b("KG", 15, 16), b("KG", 15, 16), 1.0, -4096.0)
-        for c in range(8):
-            o = 162 * c if c < 4 else 146 * (7 - c) + 129
-            lin(b("KF", o, o + 17), b("KG", 0, 17))
-    if AOLD:
-        ms(b("KA"), 0.0)
-        lin(b("KB", 0, 16), b("OHZ", 0, 16), -FRZ)
-        ms(b("KB", 16, 17), 2 * FRZ)
-        lin(b("KB", 15, 16), b("KB", 15, 16), 1.0, FRZ)
-        for c in range(8):
-            o, n = seg(c)
-            lin(b("KA", o + n - 16 - (c > 0), o + n), b("KB", 1 - (c > 0), 17))
-    lin(b("LC", 0, 16), b("LC", 0, 16), 1.0, col(8))
-    lin(b("JC"), b("JC"), 1.0, col(8))
-    lin(b("JP"), b("dd"), 1.0, col(10))
-    if not AOLD:
-        ms(b("KC", 0, 24), -65536.0)
-    ms(b("KC", 0 if AOLD else 24, 40), 0.0)
-    ms(b("KC", 8, 16), 4096.0)
-    ms(b("KC", 80, 88), -256.0 * HH)
-    lin(b("Ia"), b("I"), -256.0)
-    lin(b("Ib"), b("I"), 257.0)
-    ms(b("LC", 16, 24), 256.0)
-    ms(b("M16"), -16.0)
-    ms(b("RD"), 0.0)
-    ms(b("DF", 2048, 2064), 0.0)
+    ts(col(14), col(11), -4095.0, A.mult, 4096.0, A.add)
+    lin(col(15), col(14), 256.5)
+    lin(b("THR"), b("THR"), col(14))
+    lin(b("THS"), b("THR"), -32768.0)
+    fill(b("KF"), 0.0)
+    lin(b("KG", 0, 16), b("OHZ", 0, 16), 4096.0)
+    ms(b("KG", 16, 17), -8192.0)
+    lin(b("KG", 15, 16), b("KG", 15, 16), 1.0, -4096.0)
+    for c in range(8):
+        copy(b("KF", sum(seg(c)) - 17, sum(seg(c))), b("KG", 0, 17))
+    lin(b("KA"), b("KF"), -4096.0)
+    ms(b("AD", 0, 584, 146), FRZ / 2)
+    ms(b("AD", 17, 504, 162), FRZ / 2)
+    lin(b("LC", 0, 24), b("LC", 0, 24), 1.0, col(8))
+    fill(b("LC", 8, 16), 256.0)
+    copy(b("U0", 24, 40), b("LC", 8, 24))
+    copy(b("U1", 24, 40), b("LC", 8, 24))
+    lin(b("JC"), b("LC", 0, 8), 1.0, BLANK + 16.0 - NDUMP)
+    lin(b("JP"), b("LC", 0, 8), 16.0, -16.0 * NDUMP)
+    lin(DT, b("LC", 0, 8), 2.0, TDUMP - 2.0 * NDUMP)
+    fill(b("KC", 8, 32), 0.0)
+    fill(b("KC", 0, 8), 4096.0)
+    ms(b("KC", 32, 40), -256.0 * HH)
+    ms(b("KR", 0, 128), -0.25)
+    fill(b("KR", 128, 256), 3072.0)
+    fill(b("RD"), 0.0)
+    fill(b("DF", 2048, 2064), 0.0)
     ms(nd("AB", 0, 2176, al, slice(16, 17)), NONE)
     ts(b("B620"), b("M16"), 0.0, A.mult, 1241.0, A.add)
 
-    def roots(r, src):
-        vz = "vz%d" % r
+    def roots(src):
         ts(b("Q1"), src, 1.0, A.add)
-        mm((b("pw", 0, 128), b("B0"), b("Q1"), True, True))
+        total(b("pw", 0, 128), ("B0", b("Q1")))
         ts(b("qi"), diag("SQ", b("pw", 0, 128)), CS, A.mult, 16.0 * CO - 1, A.add)
         ts(b("qj", 0, 8), b("qi"), 4, A.arith_shift_right)
         ts(b("qj", 8, 16), b("qi"), 15, A.bitwise_and)
-        cp(b(vz), b("qj"))
-        cp(b("v%d" % r, 0, 8), b("qj", 0, 8))
+        cp(b("vz1"), b("qj"))
+        cp(b("v1"), b("qj", 0, 8))
         ts(zs_(0), b("qj", 8, 16), 4096.0, A.mult)
-        if AOLD:
-            ts(b("x5%d" % r), b("qj", 0, 8), 4096.0, A.mult)
+        ts(b("x51"), b("qj", 0, 8), 4096.0, A.mult)
 
     def roots_first():
-        ts(b("HP"), b("Qi"), 4, A.arith_shift_right)
-        ts(b("HI"), b("Qi"), 15, A.bitwise_and)
-        ts(b("Q1"), b("HP"), 1.0, A.add)
-        ts(b("Hf"), b("HI"), 1.0, A.add)
-        mm((b("pw", 0, 128), b("B0"), b("Q1"), True, True))
-        mm((pe, b("B0"), b("Hf"), True, True))
-        ts(b("vz0", 0, 8), diag("SQ", b("pw", 0, 128)), CS, A.mult, CO - 1.0, A.add)
-        ts(b("OH"), pe, col(3), A.is_equal)
-        ts(b("v0", 0, 8), b("SQ", 15, 128, 16), CS, A.mult, CO - 1.0, A.add)
-        lin(zs_(0), diag("SE", pe), col(7), -4096.0)
-        if AOLD:
-            lin(b("x50"), b("SQ", 15, 128, 16), col(7), 4096.0 * (CO - 1))
+        pe = b("pa", 256, 384)
+        ts(b("Q1"), b("Qi"), -1.0 / 16, A.mult, 2047.47, A.add)
+        cp(b("Q16"), b("Qi"))
+        total(b("pw", 0, 128), ("B0", b("Q1")))
+        total(pe, ("B0", b("Q16")), ("B1", b("Q1")))
+        ts(b("vz0", 0, 8), diag("SQ", b("pw", 0, 128)), col(9), A.mult, CO + 2047.0, A.add)
+        ts(b("OH"), pe, col(10), A.is_equal)
+        ts(b("v0"), b("SQ", 15, 128, 16), col(9), A.mult, CO + 2047.0, A.add)
+        lin(zs_(0), diag("SE", pe), col(7), -65536.0 * 2047)
+        ts(b("x50"), b("v0"), 4096.0, A.mult)
 
-    def child(r, s, row=True):
-        vz, n, last = "vz%d" % r, LB[r][s], (r, s) == (RO_ - 1, S_ - 1)
-        if row:
+    def child(r, s):
+        n, rows = LB[r][s], ind("C", TOP + 1 if s else OLD, "vz%d" % r, 0, 8)
+        if r or s:
             lin(b("OH"), ("@", b("OHZ"), zl_(r, s)))
-        if last:
-            tt(b("M1"), ind("C", REST[r][s] + 1, vz, 0, 8), b("OH"), A.mult)
-        else:
+        tt(b("M1"), rows, b("OH"), A.mult)
+        if r + s < 3:
+            lin(b("CG"), rows)
+        if s and not r:
+            lin(b("C", LB[r][s - 1] + 136, LB[r][s - 1] + 264), ind("C", KIDS[r][s - 1], "cl"))
+        if s == 0:
             iota(b("CN"), [[0, 128]], n - n % 16 - 4096, 0)
-            if MDIR:
-                tt(b("M1"), ind("C", REST[r][s] + 1, vz, 0, 8), b("OH"), A.mult)
-            else:
-                mm((b("ph", 128, 256), b("I"), b("OH"), True, True))
-            lin(b("CG"), ind("C", REST[r][s] + 1, vz, 0, 8))
-            if not MDIR:
-                tt(b("M1"), b("CG"), b("ph", 128, 256), A.mult)
-            mm((b("ph", 256, 384), b("I"), b("RMQ", n % 16, n % 16 + 128), True, False), (b("ph", 256, 384), b("I"), b("CN"), False, False),
-               (b("ph", 256, 384), b("I4"), b("OH"), False, True))
+            total(b("ph", 256, 384), ("I", b("RMQ", n % 16, n % 16 + 128)), ("I", b("CN")), ("I4", b("OH")))
             tt(b("CV"), b("CG"), b("ph", 256, 384), A.max)
-        mm((b("pm", 0, 128), b("B6"), b("M1"), True, True))
+        total(b("pm", 0, 128), ("B6", b("M1")))
         ts(b("cl"), diag("SC", b("pm", 0, 128), "KD6"), col(16), A.mult, float(CO), A.max)
 
     def edge(r, s):
         lin(b("uE"), ind("L", KIDS[r][s], "cl"))
-        ts(b("El"), ind("L", KIDS[r][s], "cl") if DIRECT else b("uE"), -1.0, A.mult, 2047.0, A.add)
-
-    def made(r, out, zl, steps):
-        pz, pn = b("pw", 256, 264), b("pw", 264, 272)
-        mm((pn, b("I32"), b("JC"), True, False), *[(pn, b("I"), b("mk%d" % r, 8 * i, 8 * i + 8), False, False) for i in range(2 * steps - 2)])
-        mm(*[(pn, b("I"), b("mk%d" % r, 8 * i, 8 * i + 8), False, i % 2 == 1) for i in (2 * steps - 2, 2 * steps - 1)])
-        ts(b(out), pn, float(BLANK), A.min)
-        if zl:
-            mm(*[(pz, b("I32"), b("U%d" % i, 16, 24), i == 0, i == steps - 1) for i in range(steps)])
-            ts(b(zl), pz, 256.0 - 256 * steps, A.add)
+        ts(b("El"), ind("L", KIDS[r][s], "cl"), -1.0, A.mult, 2047.0, A.add)
 
     def acts(r, s):
-        if AOLD:
-            j, pa = 3 * r + s, b("pa", 0, 8)
-            lin(b("vcol"), ind("IOT", REST[r][s] + 1, "vz%d" % r, 0, 8), 4096.0)
-            mm((pa, b("I12"), b("x5%d" % r), True, False))
-            for h, e in enumerate(least("AD", "RA", "vcol", "x5%d" % r)):
-                out = b("athr", 4 * h, 4 * h + 4)
-                either(lambda: act(out, e, F.Relu, bias=BIG, scale=-BIG / 2048), lambda: ts(out, e, 0.5, A.is_lt, BIG, A.mult))
-            mm((pa, b("I"), b("athr"), False, True))
-            tt(b("x2"), pa, b("LC", 0, 8), A.min)
-            cp(b("sl"), b("x2"))
-            act(ind("STD", TOP, "sl"), b("IOT", 256 * j + 256, 256 * j + 384), F.Silu)
-            lin(b("SG"), ind("STD", KIDS[r][s], "cl"))
-            e = diag("SA", b("SG"))
-            either(lambda: act(b("nf"), e, F.Relu, bias=b("THS", j, j + 1), scale=32768.0),
-                   lambda: ts(b("nf"), e, b("THR", j, j + 1), A.is_gt, BIG, A.mult))
-            return b("nf")
-        lin(b("VC", 0, 128), ind("CODE", REST[r][s] + 1, "vz%d" % r, 0, 8))
-        lin(b("VC", 128, 256), ind("CODE", KIDS[r][s], "cl"))
-        diag("SV", b("VC", 0, 128), "KD2")
-        mm((b("pa", 0, 128), b("BO"), b("ONE"), True, False))
-        lower(0, "EQ", "VC", 256, lambda o, x, c: ts(o, x, b("c24", 0, 1), A.mult, b("SV", 16 * c + 15, 16 * c + 16), A.is_equal))
-        e = diag("SA", b("pa", 0, 128))
-        either(lambda: act(b("athr"), e, F.Relu, bias=-271.5 * 2 ** 23, scale=col(15)),
-               lambda: ts(b("athr"), e, col(14), A.is_gt, BIG, A.mult))
-        return e
+        j, pa = 3 * r + s, b("pa", 0, 8)
+        lin(b("vcol"), ind("IOT", TOP + 1 if s else OLD, "vz%d" % r, 0, 8), 4096.0)
+        for c in range(8):
+            o, n = seg(c)
+            either(lambda: act(b("AD", o, o + n), b("vcol", 0, n), F.Abs, bias=b("x5%d" % r, c, c + 1), scale=-1.0),
+                   lambda: ts(b("AD", o, o + n), b("vcol", 0, n), b("x5%d" % r, c, c + 1), A.not_equal, 4096.0, A.mult))
+        scan(b("RA"), b("AD"), b("KA"), 2 * FRZ, A.min, A.add)
+        for h, e in enumerate(picked("RA")):
+            out = b("athr", 4 * h, 4 * h + 4)
+            either(lambda: act(out, e, F.Relu, bias=BIG, scale=-BIG / 2048), lambda: ts(out, e, 0.5, A.is_lt, BIG, A.mult))
+        total(pa, ("I", b("v%d" % r)), ("I", b("athr")))
+        tt(b("x2"), pa, b("LC", 0, 8), A.min)
+        cp(b("sl"), b("x2"))
+        (cp if j in STDV else put)(ind("STD", TOP, "sl"), b("IOT", 256 * j + 256, 256 * j + 384))
+        lin(b("SG"), ind("STD", KIDS[r][s], "cl"))
+        if j < 5:
+            lo, hi = (KIDS[0] + KIDS[1])[j:j + 2]
+            iota(b("STD", lo, hi), [[0, hi - lo]], 0, 0)
+        e = diag("SA", b("SG"))
+        either(lambda: act(b("nf"), e, F.Relu, bias=b("THS", j, j + 1), scale=32768.0),
+               lambda: ts(b("nf"), e, b("THR", j, j + 1), A.is_gt, BIG, A.mult))
 
     def payload():
         for x in range(8):
             ts(nd("QX", 128 * x, 128 * x + 128, al, x, al), b("Q16"), b("BO", 16 * x, 16 * x + 1), A.mult)
         mm(*[(b("pq", 1 + 17 * c, 18 + 17 * c), nd("QX", 0, 1024, c, al, al), b("IDZ", 0, 272, 16), True, True) for c in range(8)])
-        cp(b("QI", 1, LL), b("pq", 1, LL))
-        ts(b("QA", 1, LL), b("QI", 1, LL), 15, A.bitwise_and)
-        tt(b("W3n", 1, LL), b("QA", 1, LL), b("K3", 1, LL), A.add)
-        lin(b("W3", 1, LL), b("W3n", 1, LL), 4096.0)
-        lin(b("W2", 1, LL), b("W3n", 1, LL), 4096.0, -4096.0 * HH)
+        mm((b("pq", 140, 276), b("I4"), b("K3", 1, LL), True, False),
+           *[(b("pq", 140 + 17 * c, 157 + 17 * c), nd("QX", 0, 1024, c, al, al), b("ID4", 0, 17), False, False) for c in range(8)])
+        lin(b("FL", 1, LL), b("pq", 1, LL), 1.0, 2056.5)
+        total(b("pq", 140, 276), ("Im4", b("FL", 1, LL)), start=False)
+        lin(b("W3", 1, LL), b("pq", 140, 276))
+        lin(b("W2", 1, LL), b("pq", 140, 276), 1.0, -4096.0 * HH)
         tt(b("W1", 1, LL), b("pq", 1, LL), b("W3", 1, LL), A.add)
 
-    def hashes(r):
-        src = b("QF" if r else "LQ")
-        if r == 0:
-            cp(b("Q16"), src)
-        mm((b("pq", 256, 384), b("SHD"), b("Q16"), True, True))
-        tt(b("HP"), b("pq", 256, 384), src, A.mult)
+    def hashes():
+        total(b("pq", 256, 384), ("SHD", b("Q16")))
+        tt(b("HP"), b("pq", 256, 384), b("QF"), A.mult)
         ts(b("HI"), b("HP"), 5, A.arith_shift_right, 2047, A.bitwise_and)
-        cp(b("Hf"), b("HI"))
-        ts(b("Hm"), b("HI"), 2046.5, A.is_gt, -2047.0, A.mult)
-        mm(*[(b("pq", 384, 512), b(w), b(x), x == "Hf", x == "Q16") for w, x in (("I", "Hf"), ("I", "Hm"), ("Im", "Q16"))])
+        cp(b("X6"), b("HI"))
+        either(lambda: act(b("Hm"), b("X6"), F.Relu, bias=-1023.0, scale=0.5), lambda: ts(b("Hm"), b("X6"), 2046.5, A.is_gt, 0.5, A.mult))
+        total(b("pq", 384, 512), ("I32", b("X6")), ("Im", b("Q16")), stop=False)
+        total(b("pq", 384, 512), ("Im4", b("Hm")), ("I", b("Hm")), ("I", b("Hm")), start=False)
         lin(b("HMQ"), b("pq", 384, 512), col(6))
 
     def distances(r, s):
@@ -727,138 +756,124 @@ def rank_program(g, core, T, topo):
         if s:
             act(at0("RD"), zs_(s), F.Relu, bias=-15.0, scale=2.0 ** -12)
             scan(b("RMP", 1, LL), b("M16", 1, LL), b("RD", 1, LL), 0.0, A.add, A.max)
-        mm((pd, b("IH"), b("B620", 1, LL), True, False), *([(pd, b("IR"), b("RMP", 1, LL), False, False)] if s else []))
+        total(pd, ("IH", b("B620", 1, LL)), *([("IR", b("RMP", 1, LL))] if s else []), stop=False)
         for lo, hi in zip(CHUNKS, CHUNKS[1:]):
-            lin(b("XQ", 16 * lo, 16 * hi), ind("X", 2064, "Ql", lo, hi))
+            lin(b("XQ", 16 * lo, 16 * hi), ind("X", 2064, "Ql%d" % r, lo, hi))
             tt(b("DF", 16 * lo, 16 * hi), ind("X", 2064, "El", lo, hi), b("XQ", 16 * lo, 16 * hi), A.subtract)
-            act(nd("AB", 17 * lo, 17 * hi, slice(lo, hi), slice(0, 16)), b("DF", 16 * lo, 16 * hi), F.Abs)
-        for h in range(2):
+            for x, y in ((lo, hi - 8), (hi - 8, hi)) if SPLIT and hi == 128 else ((lo, hi),):
+                act(nd("AB", 17 * x, 17 * y, slice(x, y), slice(0, 16)), b("DF", 16 * x, 16 * y), F.Abs)
+        for h, lo, hi in ((0, 0, 16), (1, 0, 8), (1, 8, 16)):
             mm(*[(b("pd", 1 + 68 * h, 69 + 68 * h), b("CZ", 15 - p, 143 - p),
-                  nd("AB", 1088 * h, 1088 * h + 1088, slice(64 * h + p, 64 * h + 64, 16), al), False, h == 1 and p == 15) for p in range(16)])
+                  nd("AB", 1088 * h, 1088 * h + 1088, slice(64 * h + p, 64 * h + 64, 16), al), False, h == 1 and p == 15) for p in range(lo, hi)])
 
     def cut_rows(r, s):
-        uu, n1 = "UU%d" % (s % 2), SB[r]
-        px = b(pe[0], 384, 392)
-        tt(b("EL"), ind("IDZ", 272, uu, 16, 24), b("X6" if s == S_ - 1 else "WN"), A.mult)
-        mm((pe, b("BO"), b("EL"), True, True))
+        uu, end = "UU%d" % (s % 2), s == S_ - 1
+        pe, px, py, po = b("pq", 0, 128) if end else b("ps", 128, 256), b("ps", 384, 392), b("ps", 392, 400), b("ps", 256, 384)
+        tt(b("EL"), ind("IDZ", 272, uu, 8, 16), b("X6" if end else "WN"), A.mult)
+        total(pe, ("BO", b("EL")))
         e = diag("SE", pe)
-        if s == S_ - 1:
+        if end:
             ts(b(uu, 24, 32), e, CS, A.mult, -1.0, A.add)
-        else:
-            lin(b("fz"), b("zcf"), -1.0, -2048.5)
-            lin(b("fu"), e, CS, 2048.5)
-            mm((px, b("I16"), b("zcf"), True, False), (px, b("I16"), b("fz"), False, False), (px, b("ICS"), e, False, False))
-            mm((px, b("Im"), b("fu"), False, True))
-            ts(b(uu, 24, 32), px, 17 * 2048.0 + 136, A.add)
-        tt(b("OHM"), ind("OH%d" % s, 272, uu, 24, 32), b("IOT", n1, n1 + 128), A.add)
-        act(ind("C", TOP, uu, 0, 8), b("OHM"), F.Silu)
+            ts(b("fl", 16, 24), e, col(15), A.is_gt, 256.0, A.mult)
+            tt(b("OHM"), ind("OH2", 528, uu, 24, 32), b("IOT", SB[r], SB[r] + 128), A.add)
+            put(ind("C", TOP, uu, 16, 24), b("OHM"))
+            return
+        j, cut = 2 * r + s, b("mk%d" % r, 16 * s, 16 * s + 8)
+        lin(b("fz"), b("zcf"), -1.0, -2048.5)
+        lin(b("fu"), e, CS, 2048.5)
+        total(px, ("I4", b("KP", 24, 32)), ("I4", b("KP", 8 * j, 8 * j + 8)), ("Im4", cut), ("IG", b("zcf")), ("IG", b("fz")), ("ICS", e),
+              stop=False)
+        total(px, ("Im4", b("fu")), start=False)
+        total(py, ("Im4", cut), ("I4", b("zcf")), ("I4", b("fz")), ("ICS", e), ("Im4", b("fu")))
+        ts(b("fl", 8 * s, 8 * s + 8), py, (BLANK + 16 - LB[r][s] - 136 - 4097.0) * 4096, A.is_equal, 256.0, A.mult)
+        tt(b("x3"), px, zs_(s + 1), A.max)
+        ts(b(uu, 24, 32), b("x3"), 2.0 ** -12, A.mult)
+        lin(b("Wg"), ind("WW", 816, uu, 24, 32))
+        iota(b("CN"), [[0, 128]], LB[r][s + 1], 0)
+        total(po, ("I", b("RMQ", 0, 128)), ("I", b("CN")), ("I", b("Wg")))
+        tt(b("CV"), b("CG"), po, A.max)
 
-    def second(r, lst):
-        tt(b("L", SB[r], SB[r] + 128), ("@", b("TRZ"), lst), b("uQ%d" % r), A.mult)
+    def travel(src, land, tag):
+        (lin if tag == "1" else cp)(b(land, 0, 16), b(src, 0, 16))
+        K["ops"].append(("G", [b(src)], [b(land, 16)], 7500 if tag == "E" else 1400, FLY, lambda: send(src, land, tag)))
 
-    def unlike(out, x):
-        ts(b("X6"), x, 1.5 * 2 ** 27, A.add, -1.5 * 2 ** 27, A.add)
-        tt(out, x, b("X6"), A.not_equal)
-
-    def at_cut(r, src, lst):
-        tt(b("Y"), src, b("uQ%d" % r), A.subtract)
-        tt(b("EL"), ("@", b("IDZ"), lst), b("Y"), A.mult)
-        mm((b("pq", 0, 128), b("BO"), b("EL"), True, True))
-        unlike(b("X5"), b("pq", 0, 128))
-        tt(b("L", SB[r], SB[r] + 128), b("L", SB[r], SB[r] + 128), b("X5"), A.mult)
-
-    def travel(src, land, tag, n=16, at=16, first=0, st=16):
-        (cp if tag == "E" else lin)(b(land, 0, n), b(src, first, first + n))
-        K["ops"].append(("G", [b(src, first, first + 8 * st)], [b(land, at)], 7500 if tag == "E" else 1400, FLY,
-                         lambda: send(src, land, tag, n, at, first, st)))
-
-    def send(src, land, tag, w, at, first, st):
+    def send(src, land, tag):
         sent = [0]
-        part = lambda x: T[x[0]][x[3]]
-        whole = b(src, first, first + 8 * st)
-        deps("G", [whole], [], "loc" + tag, 0)
+        deps("G", [b(src)], [], "loc" + tag, 0)
         for calls in plan(core, T.cores, topo):
             tr = []
             for d, en in calls:
                 e = (T.rank_of(d) - rank) % 8
                 rid, pid = topo.addr(d, core)
                 tr.append(RemoteDMATransfer(dst_ids=[DstId(rid=rid, pnc=pid)], dma_engine_mask=sum(1 << x for x in en),
-                                            remote_sem=T.sem["arr" + tag], src=part(b(src, first + st * e, first + st * e + w)),
-                                            dst=part(b(land, at * e, at * e + w))))
+                                            remote_sem=T.sem["arr" + tag], src=T[src][:, 16 * e:16 * e + 16], dst=T[land][:, 16 * e:16 * e + 16]))
                 sent[0] += len(en)
             g.remote_dma_fused(tr, local_sem=T.sem["loc" + tag])
         n = sum(len(en) for s in T.cores if s != core for calls in plan(s, T.cores, topo) for d, en in calls if d == core)
-        K["acc"].setdefault(land, []).append((at, 8 * at, 1, "R", "arr" + tag, n, True, b(land, at, 8 * at)))
-        K["acc"].setdefault(whole[0], []).append((whole[1], whole[2], 0, "R", "loc" + tag, sent[0], True, whole))
+        K["acc"].setdefault(land, []).append((16, 128, 1, "R", "arr" + tag, n, True, b(land, 16)))
+        K["acc"].setdefault(src, []).append((0, 128, 0, "R", "loc" + tag, sent[0], True, b(src)))
         K["final"]["arr" + tag] = n
         K["final"]["loc" + tag] = sent[0]
 
     def step(r, s):
         end, last = s == S_ - 1, (r, s) == (RO_ - 1, S_ - 1)
-        v, zs, vz, uu, sz = b("v%d" % r, 0, 8), zs_(s), "vz%d" % r, "UU%d" % (s % 2), "SZ%d" % s
-        lb, cb, mk = LB[r][s], LB[r][s] + 136, "mk%d" % r
+        v, zs, vz, uu, sz, uQ = b("v%d" % r), zs_(s), "vz%d" % r, "UU%d" % (s % 2), "SZ%d" % s, b("uQ%d" % r)
+        lb, cb, mk, old = LB[r][s], LB[r][s] + 136, "mk%d" % r, b("CV" if r else "SND")
         low = b("L", cb, cb + 128) if last else b("WN")
         distances(r, s)
-        sa = acts(r, s)
+        acts(r, s)
         if last:
-            cp(b("X", 2047, 2048), b("xsave", 0, 1))
+            cp(b("X", 2047, 2048), b("XT", 15, 16))
         if s == 0:
             payload()
-            lin(b("uQ%d" % r), b("QF"), -1.0, 2047.0)
+            lin(uQ, b("QF"), -1.0, 2047.0)
             lin(b("L", lb, lb + 128), b("QF"), -1.0, 2047.0)
         else:
-            tt(b("L", lb, lb + 128), ("@", b("TRZ"), zl_(r, s)), b("uQ%d" % r), A.mult)
+            tt(b("L", lb, lb + 128), ("@", b("TRZ"), zl_(r, s)), uQ, A.mult)
+        if end:
+            tt(old, ("@", b("TRZ"), zl_(r, s)), b("HMQ"), A.mult)
         if s and (r == 0 or s == 1):
             cut_rows(r, s - 1)
         if s == 1:
-            second(r, b("UU0", 16, 24))
-            hashes(r)
-        if (r, s) == (1, 0):
-            at_cut(0, ind("L", BLANK + 1, "id0"), b("za"))
-        if last:
-            made(r, "ido", "zo", s)
-            second(r, b("zo"))
-            at_cut(r, ind("L", BLANK + 1, "ido"), b("zo"))
-            tt(b("X5"), b("uE"), b("uQ1"), A.subtract)
-            unlike(b("Y"), b("X5"))
-        if (r, s) == (0, 1):
-            roots(1, b("LQ"))
-        if (r, s) == (0, 2):
-            lin(b("XA"), b("uE"), 1.0, 2048.5)
-            mm((b("pq", 0, 128), b("I32"), b("uE"), True, False), (b("pq", 0, 128), b("Im"), b("XA"), False, False),
-               (b("pq", 0, 128), b("I16"), b("XB"), False, True))
-            lin(b("X6"), b("pq", 0, 128), 1.0, 2048.0 + 9)
-        if (r, s) == (0, 1):
+            total(b("ps", 400, 408), ("I32", b("U0", 8, 16)), ("I", b("fl", 0, 8)))
+            ts(b("za"), b("ps", 400, 408), 256.0, A.min)
+            tt(b("L", SB[r], SB[r] + 128), ind("TRZ", 272, "za"), uQ, A.mult)
+            hashes()
             lin(b("XA"), b("QF"), 1.0, 2048.5)
-            mm((b("pq", 0, 128), b("I32"), b("QF"), True, False), (b("pq", 0, 128), b("Im"), b("XA"), False, True))
+            total(b("pq", 0, 128), ("I32", b("QF")), ("Im", b("XA")))
             lin(b("XB"), b("pq", 0, 128), 1.0, 2048.0 + 8)
-        if r == 0:
-            lin(b("C", cb, cb + 128), ind("C", KIDS[r][s], "cl"))
-        s3, E1, A1 = at0(sz, 1), b("EA", 0, 8), b("EA", 8, 16)
-        M, tk, pp, U = [b("ph", 8 * i, 8 * i + 8) for i in range(3)], b("pt", 0, 8), b("pt", 8, 16), "U%d" % s
+        if (r, s) == (0, 1):
+            roots(b("LQ"))
+        if s + r > 1:
+            lin(b("XA"), b("uE"), 1.0, 2048.5)
+            total(b("pq", 128, 256), ("I32", b("uE")), ("Im", b("XA")), ("I", b("XB")))
+            if r:
+                ts(b("Y"), b("pq", 128, 256), -2041.0, A.not_equal)
+            else:
+                ts(b("XC"), b("pq", 128, 256), -2041.0, A.is_equal, 256.0, A.mult)
+                total(b("pq", 0, 128), ("I32", b("uE")), ("Im", b("XA")), ("I16", b("XB")), ("I", b("XC")))
+                lin(b("X6"), b("pq", 0, 128), 1.0, 2048.0 + 9)
+        s3, E1, A1, cf = at0(sz, 1), b("EA", 0, 8), b("EA", 8, 16), b("SC", 15, 128, 16)
+        M, tk, pp, U = [b("ph", 8 * i, 8 * i + 8) for i in (2, 0, 1)], b("pt", 0, 8), b("pt", 8, 16), "U%d" % s
         pz, pc = b("pw", 288, 296), b("pm", 272, 280)
-        cf = b("SC", 15, 128, 16)
         mm((b("ph", 0, 24), b("I"), b("KC", 0, 24), True, False), (M[0], b("IC6"), cf, False, False), (M[1], b("I"), v, False, False))
-        i7 = b("I" if AOLD else "I7")
-        mm(*[(x, b("I"), b("athr"), False, False) for x in (M if AOLD else M[1:2])])
-        mm((M[0], i7, sa, False, False), (M[2], i7, sa, False, False))
+        mm(*[(x, b("I"), b("athr"), False, False) for x in M])
+        mm((M[0], b("I"), b("nf"), False, False), (M[2], b("I"), b("nf"), False, False))
         mm((b("pt", 0, 16), b("I"), b("KC", 16, 32), True, False), (pp, b("I"), b("JP"), False, False))
-        if AOLD:
-            mm((tk, b("I"), b("athr"), False, False))
-        mm((tk, i7, sa, False, False))
-        mm((pz, b("I4"), b("KC", 80, 88), True, False), (pz, b("Im"), b("athr"), False, False))
+        mm((tk, b("I"), b("athr"), False, False))
+        mm((tk, b("I"), b("nf"), False, False))
+        total(pz, ("I4", b("KC", 32, 40)), ("Im", b("athr")), stop=False)
         if not end:
-            mm((pc, b("IC6"), cf, True, False), (pc, b("Im"), v, False, True))
+            total(pc, ("IC6", cf), ("Im", v))
         scan(rev("S2"), rev("pd"), rev("W2"), 0.0, A.min, A.max)
         scan(rev(sz, 136), rev("pd"), rev("W3"), 0.0, A.min, A.max)
-        mm((pz, b("Ia"), at0("S2"), False, False))
-        mm((pz, b("Ib"), s3, False, True))
+        total(pz, ("Ia", at0("S2")), start=False, stop=False)
+        total(pz, ("Ib", s3), start=False)
         if not end:
-            zn = zs_(3 * r + s + 1)
-            tt(zn, zs, pz, A.max)
+            tt(zs_(s + 1), zs, pz, A.max)
             ts(b("dn"), pz, -0.5, A.is_ge)
             either(lambda: act(b("y3"), pz, F.Relu, bias=-4096.0 * 255), lambda: ts(b("y3"), pz, -4096.0 * 255, A.add, 0.0, A.max))
-            ts(b("zl%d" % ((s + 1) % 2)), zn, 2.0 ** -12, A.mult)
+            ts(zl_(r, s + 1), zs_(s + 1), 2.0 ** -12, A.mult)
             tt(b("y2"), b("dn"), pc, A.mult)
         scan(rev("S1"), rev("pd"), rev("W1"), 0.0, A.min, A.max)
         lin(at0(sz, 2), at0("S2"), 1.0, 4096.0 * HH)
@@ -868,124 +883,120 @@ def rank_program(g, core, T, topo):
         mm((tk, b("Im4"), b("zcf"), False, False), (pp, b("I6"), b("zcf"), False, False), (tk, b("I4"), E1, False, False),
            (tk, b("I4"), A1, False, True))
         ts(b("tp"), b("pt", 0, 16), -7.5 / 16, A.add, 2048.0, A.min)
-        if TOLD and not TSCAN:
-            lin(b("TS"), tk, 4096.0)
-            tt(b("TU"), tk, DT, A.min)
         mm((M[2], b("I"), b("zcf"), False, False), *[(M[i], b("Im4" if i == 1 else "I4"), E1, False, False) for i in range(3)],
            *[(M[i], b("I4"), A1, False, i == 2) for i in range(3)])
-        tt(b(U), b("ph", 0, 24), b("LC", 0, 24), A.min)
+        tt(b(U, 0, 24), b("ph", 0, 24), b("U%d" % (s - 1), 16, 40) if s and not last else b("LC", 0, 24), A.min)
         for i, x in enumerate((cb, lb)):
             ts(b(mk, 16 * s + 8 * i, 16 * s + 8 * i + 8), M[i], NDUMP - 0.5, A.is_lt, x - BLANK - 16.0, A.mult)
-        cp(b(uu, 0, 24), b(U))
-        if last:
-            tt(b("CV"), ("@", b("TRZ"), zl_(r, s)), b("HMQ"), A.mult)
+        cp(b(uu, 0, 24), b(U, 0, 24))
+        if end:
+            total(b("pm", 128, 256), ("I", b("Q16")), stop=False)
             ts(b("lz"), pz, 2.0 ** -12, A.mult)
-            tt(b("HK"), ind("TRZ", 272, "lz"), b("CV"), A.mult)
-            tt(b("SND"), b("HK"), b("QF"), A.add)
-            travel("SND", "LAND1", "1")
-        elif end:
-            tt(b("zt"), zs, pz, A.max)
-            travel("zt", "LK", "0", 1, 4, 0, 1)
+            tt(b("HK"), ind("TRZ", 272, "lz"), old, A.mult)
+            total(b("pm", 128, 256), ("I", b("HK")), start=False)
+            (lin if r else cp)(b("SND" if r else "SQl"), b("pm", 128, 256))
+            travel(*(("SND", "LAND1", "1") if r else ("SQl", "Ql1", "0")))
         lin(b("DFg"), ind("DF", 2064, "tp", 8, 16))
         lin(b("XQg"), ind("X", XW, "tp", 0, 8))
-        mm((b("ps", 0, 128), b("I"), b("DFg"), True, False), (b("ps", 0, 128), b("I2"), b("XQg"), False, True))
-        lin(b("DS"), b("ps", 0, 128), 0.5 - 2.0 ** -12, 2.0 ** 23)
-        lin(b("DH"), b("DS"), 1.0, -2.0 ** 23)
-        if TSCAN:
-            (cp if ROW16 else lin)(b("VT" if ROW16 else "tcol"), ind("IOT", 2064, "tp", 0, 8))
-            tt(b("NF", 0, 584, 146), b("pt", 0, 4), b("LC", 24, 28), A.min)
-            tt(b("NF", 17, 504, -162), b("pt", 4, 8), b("LC", 28, 32), A.min)
-            for c in range(8):
-                o = 146 * c + 1 if c < 4 else 162 * (7 - c) + 18
-                ts(b("NF", o, o + 16 * c + 16), b("VT" if ROW16 else "tcol", 0, 16 * c + 16), b("pt", c, c + 1), A.is_equal,
-                   b("LC", 24 + c, 25 + c), A.mult)
+        total(b("ps", 0, 128), ("I", b("KR", 0, 128)), ("I2", b("DFg")), ("I", b("XQg")), ("I4", b("KR", 128, 256)), ("Im4", b("KR", 128, 256)))
+        lin(b("DH"), b("ps", 0, 128))
+        cp(b("VT"), ind("IOT", 2064, "tp", 0, 8))
+        tt(b("NF", 0, 584, 146), b("pt", 0, 4), b("LC", 24, 28), A.min)
+        tt(b("NF", 17, 504, -162), b("pt", 4, 8), b("LC", 28, 32), A.min)
+        for c in range(8):
+            o, n = seg(c)
+            ts(b("NF", o, o + n), b("VT", 0, n), b("pt", c, c + 1), A.is_equal, b("LC", 24 + c, 25 + c), A.mult)
+
+        def descriptors():
             scan(b("RF"), b("NF"), b("KF"), 0.0, A.max, A.add)
-            cp(b("didx", 0, 4), b("RF", 15, 584, 162))
-            cp(b("didx", 4, 8), b("RF", 144, 583, -146))
-        elif TOLD:
-            lin(b("tcol"), ind("IOT", 2064, "tp", 0, 8), 4096.0)
-            for h, e in enumerate(least("NE", "RE", "tcol", "TS")):
-                tt(b("d0", 4 * h, 4 * h + 4), b("LC", 24 + 4 * h, 28 + 4 * h), e, A.subtract)
-            tt(b("dd"), b("d0"), b("TU"), A.max)
-            cp(b("didx"), b("dd"))
-        else:
-            cp(b("VT"), ind("IOT", 2064, "tp", 0, 8))
-            mm((b("pa", 128, 256), b("BA"), b("ONE"), True, False))
-            mm((b("pa", 128, 256), b("I"), b("VT"), False, False))
-            lower(128, "EN", "VT", 128, lambda o, x, c: ts(o, x, b("pt", c, c + 1), A.is_equal, 16.0, A.mult))
-            tt(b("dd"), diag("SN", b("pa", 128, 256)), DT, A.min)
-            ts(b("didx"), b("dd"), CS, A.mult, -4096.0, A.add)
-        cp(ind("X", XW, "didx"), b("DH"))
-        if last:
-            dma("Y", T.yd[:], T.X[:, 0:2048], r=[b("X", 0, 2048)])
-        tt(low, ind("TRZ", 272, uu, 16, 24), b("uE"), A.mult)
+            if last:
+                turn("#a")
+            for h, e in enumerate(picked("RF")):
+                cp(b("didx", 4 * h, 4 * h + 4), e)
+            cp(ind("X", XW, "didx"), b("DH"))
         if not last:
-            act(ind("C", TOP, uu, 8, 16), b("CV"), F.Silu)
+            descriptors()
+        tt(low, ind("TRZ", 272, uu, 8, 16), b("uE"), A.mult)
+        if not last:
+            put(ind("C", TOP, uu, 0, 8), b("CV"))
         if not end:
             pv = b("pw", 272, 280)
-            mm((pv, b("I"), v, True, False), (pv, b("I"), b("y3"), False, False), (pv, b("I"), b("y2"), False, False))
-            mm((pv, b("Im4"), b(mk, 16 * s, 16 * s + 8), False, False), (pv, b("Im4"), b(mk, 16 * s + 8, 16 * s + 16), False, True))
-            ts(b(vz, 0, 8), pv, float(REST[r][s + 1]), A.min)
-            ts(v, pv, float(REST[r][s + 1]), A.min)
-            if AOLD:
-                lin(b("x5%d" % r), pv, 4096.0)
+            total(pv, ("I", v), ("I", b("y3")), ("I", b("y2")), stop=False)
+            total(pv, ("Im4", b(mk, 16 * s, 16 * s + 8)), ("Im4", b(mk, 16 * s + 8, 16 * s + 16)), start=False)
+            ts(b(vz, 0, 8), pv, float(TOP), A.min)
+            ts(v, pv, float(TOP), A.min)
+            lin(b("x5%d" % r), pv, 4096.0)
             child(r, s + 1)
-        if end:
-            if r == 0:
-                cut_rows(0, 2)
-            if r == 0:
-                mm((b("pw", 272, 280), b("I32"), b("U1", 16, 24), True, False))
-                mm((b("pw", 272, 280), b("I32"), b("U2", 16, 24), False, True))
-                ts(b("zo"), b("pw", 272, 280), -256.0, A.add)
-                tt(b("X5"), ind("TRZ", 272, "zo"), b("uQ0"), A.mult)
-            made(r, "id%d" % r, None if r else "za", S_)
-        tt(ind("L", TOP, uu, 0, 8), b("uE"), low, A.subtract)
         if end and r == 0:
-            tt(b("L", SB[0], SB[0] + 128), b("L", SB[0], SB[0] + 128), b("X5"), A.add)
+            lin(b("C", cb, cb + 128), ind("C", KIDS[r][s], "cl"))
+            cut_rows(0, 2)
+            total(b("pw", 272, 280), ("I32", b("U1", 8, 16)), ("I", b("fl", 8, 16)), stop=False)
+            total(b("pw", 272, 280), ("I32", b("U2", 8, 16)), start=False, stop=False)
+            total(b("pw", 272, 280), ("I", b("fl", 16, 24)), start=False)
+            ts(b("zo"), b("pw", 272, 280), -256.0, A.add, 256.0, A.min)
+            tt(b("X5"), ind("TRZ", 272, "zo"), uQ, A.mult)
+        if end:
+            pn = b("pw", 264, 272)
+            total(pn, ("I32", b("JC")), *[("I", b(mk, 8 * i, 8 * i + 8)) for i in range(4)], stop=False)
+            total(pn, ("I", b(mk, 32, 40)), ("I", b(mk, 40, 48)), start=False)
+            ts(b("id%d" % r), pn, float(BLANK), A.min)
+            if last:
+                turn("#b")
+        tt(ind("L", TOP, uu, 16, 24), b("uE"), low, A.subtract)
         if last:
-            tt(b("EL"), ind("IDZ", 272, uu, 16, 24), b("Y"), A.mult)
-            tt(b("WN"), ind("TRZ", 272, uu, 16, 24), b("uQ1"), A.mult)
-            mm((b("pq", 0, 128), b("BO"), b("EL"), True, True))
-            tt(b("LN"), b("WN"), b("pq", 0, 128), A.mult)
+            turn("#a")
+        if end and r == 0:
+            total(b("ps", 256, 384), ("I32", b("X5")), ("I32", b("L", SB[0], SB[0] + 128)))
+            lin(b("L", SB[0], SB[0] + 128), b("ps", 256, 384))
+        if r and s:
+            tt(b("EL"), ind("IDZ", 272, uu, 8, 16), b("Y"), A.mult)
+            tt(b("OHM"), ind("TRZ", 272, uu, 8, 16), uQ, A.mult)
+            total(b("pq", 0, 128), ("BO", b("EL")))
+            tt(b("LN" if last else "X5"), b("OHM"), b("pq", 0, 128), A.mult)
+        if last:
+            turn("#b")
+            descriptors()
+            turn("#b")
+            dma("Y", T.yd[:], T.X[:, 0:2048], r=[b("X", 0, 2048)])
         elif end:
             lin(b("L", cb, cb + 128), low)
         else:
             dma("Y", T.L[:, cb:cb + 128], T.WN[:], r=[low], w=[b("L", cb, cb + 128)])
-        if not end:
             edge(r, s + 1)
 
     roots_first()
-    cp(b("Ql"), b("Qi"))
-    ts(b("C", CO, Z), b("Ci"), float(CO), A.add)
-    ts(b("L", CO, Z), b("Ei"), -1.0, A.mult, 2047.0, A.add)
+    cp(b("Ql0"), b("Qi"))
+    if HINT:
+        turn("#q")
+    ts(b("C", CO, OLD), b("Ci"), float(CO), A.add)
+    if HINT:
+        turn("#q")
+    ts(b("L", CO, OLD), b("Ei"), -1.0, A.mult, 2047.0, A.add)
     lin(b("lsave", 0, 1), b("L", CO, CO + 1))
     ms(b("L", CO, CO + 1), -1.0)
-    child(0, 0, False)
+    child(0, 0)
     cp(b("QF"), b("Qi"))
-    ms(b("X", 2048, XW), FAR)
-    cp(b("xsave", 0, 1), b("X", 2047, 2048))
+    fill(b("X", 2048, XW), FAR)
+    cp(b("X", 2032, 2047), b("XT", 0, 15))
     ms(b("X", 2047, 2048), NONE)
     edge(0, 0)
     travel("Qi", "LQ", "E")
-    cp(b("Q16"), b("Qi"))
     for s in range(S_):
         step(0, s)
     child(1, 0)
     edge(1, 0)
-    ts(b("lz"), b("LK", 0, 32, 4), 2.0 ** -12, A.mult)
-    tt(b("HK"), ind("TRZ", 272, "lz"), b("HMQ"), A.mult)
-    tt(b("QF"), b("HK"), b("LQ"), A.add)
-    cp(b("Ql"), b("QF"))
+    cp(b("QF"), b("Ql1"))
     cp(b("Q16"), b("QF"))
     for s in range(S_):
         step(1, s)
-    lin(b("YE", 0, 384), b("L", CO, Z), -1.0, 2047.0)
+    lin(b("YE", 0, 384), b("L", CO, OLD), -1.0, 2047.0)
     lin(b("YE", 0, 1), b("lsave", 0, 1), -1.0, 2047.0)
     for r in range(RO_):
-        n1 = 384 + 256 * r
-        lin(b("YE", n1, n1 + 256, 2), ind("L", BLANK + 1, "id%d" % r), -1.0, 2047.0)
-        lin(b("X6") if r else b("YE", n1 + 1, n1 + 256, 2), b("L", SB[r], SB[r] + 128), -1.0, 2047.0)
-    tt(b("YE", 641, 896, 2), b("X6"), b("LN"), A.subtract)
+        lin(b("YE", 384 + 256 * r, 640 + 256 * r, 2), ind("L", BLANK + 1, "id%d" % r), -1.0, 2047.0)
+    lin(b("YE", 385, 640, 2), b("L", SB[0], SB[0] + 128), -1.0, 2047.0)
+    for i, x in enumerate((b("X5"), b("L", SB[1], SB[1] + 128), b("LN"))):
+        total(b("ph", 128, 256), ("I32", x), start=i == 0, stop=i == 2)
+    lin(b("YE", 641, 896, 2), b("ph", 128, 256), -1.0, 2047.0)
     dma("Y", T.ye[:, 0:640], T.YE[:, 0:640], r=[b("YE", 0, 640)])
     dma("Y", T.ye[:, 640:896], T.YE[:, 640:896], r=[b("YE", 640, 896)])
     dma("Y", T.yr[:], T.LAND1[:], r=[b("LAND1")])

from concourse.bass import DstId, RemoteDMATransfer
from concourse.mybir import AluOpType as A, ActivationFunctionType as F

S_, RO_ = 3, 2
F32, BF, H16, I32, U16 = "float32", "bfloat16", "float16", "int32", "uint16"
SCRATCH = {}
PLACE = {}


def _b(name, n, d, where="sbuf", own=False):
    pool = {F32: "poolf", U16: "poolu", I32: "pooli", BF: "poolb", H16: "poolh"}[d]
    if isinstance(n, list):
        SCRATCH[name] = (where, [128] + n, d)
    elif n > (88 if d == BF else 40) or where != "sbuf" or own:
        SCRATCH[name] = (where, [128, n], d)
        PLACE[name] = (name, 0, n)
    else:
        at = SCRATCH[pool][1][1] if pool in SCRATCH else 0
        SCRATCH[pool] = ("sbuf", [128, at + n + n % 2], d)
        PLACE[name] = (pool, at, n)


XW, LL = 2320, 137
for _d, _l in (
    (BF, "X:2320 XQ:2048 DF:2064 BO:128 B0:128 B1:128 B6:128 SHD:128 I:128 I2:128 Im:128 IH:128 IR:128 I4:128 Im4:128 I16:128 I6:128 "
         "IG:128 IC6:128 ZR:128 CZ:144 ZH:272 ZL:272 OHZ:272 TRZ:272 IDZ:272 ID4:18 OHB:272 OHC:272 OH2:528 WW:816 KD:128 KD6:128 "
         "K3:137 M16:137 RD:137 RMP:137 FL:137 KA:584 KF:584 KG:18 KC:40 KP:32 KR:256 AD:584 RA:584 OH:128 SG:128 SA:128 XQg:128 "
         "DFg:128 DH:128 CN:128 RMQ:144 Wg:128 XA:128 XB:128 XC:128 Hm:128 athr:8 nf:8 EA:16 zcf:8 mk0:48 mk1:48 fl:24 fz:8 fu:8 JP:8 dn:8 y3:8"),
    (F32, "L:2464 C:2200 STD:2192 IOT:2200 W1:137 W2:137 W3:137 S1:137 S2:137 SZ0:409 SZ1:409 SZ2:409 QF:128 uQ0:128 uQ1:128 "
          "LAND1:128 SND:128 HMQ:128 uE:128 CV:128 CG:128 SE:128 SQ:128 WN:128 OHM:128 LN:128 X5:128 X6:128 YE:896 vcol:128 "
          "I32:128 ICS:128 Ia:128 Ib:128 cols:18 LC:32 lsave:2 JC:8 U0:40 U1:40 U2:24 THR:6 THS:6 x50:8 x51:8 x2:8 x3:8"),
    (H16, "Q16:128 Q1:128 B620:137 M1:128 EL:128 HK:128 Y:128 VT:128 SC:128 NF:584 RF:584 v0:8 v1:8 y2:8"),
    (I32, "Qi:128 LQ:128 Ci:384 Ei:384 HP:128 HI:128 IP:2 IC:2 qi:8 qj:16"),
    (U16, "Ql0:128 Ql1:128 SQl:128 El:128 vz0:16 vz1:16 cl:8 tp:16 lz:8 zo:8 za:8 UU0:32 UU1:32 id0:8 id1:8 didx:8 sl:8 zl0:8 zl1:8"),
):
    for _x in _l.split():
        _b(_x.split(":")[0], int(_x.split(":")[1]), _d)
_b("AB", [128, 17], BF); _b("QX", [8, 8, 16], H16); _b("XT", 16, BF, own=True)
PS = ["pd", "pm", "pt", "ps", "pq", "pa", "pw", "ph"]
for _n in PS:
    _b(_n, 512, F32, "psum")
SEMAPHORES = ["sV", "sT", "sS", "sG", "locE", "loc0", "loc1", "arrE", "arr0", "arr1"] + ["d%d" % _i for _i in range(16)]
TDUMP, BIG, HH, FRZ, CO = 2050, float(2 ** 22), float(2 ** 22), float(2 ** 24), 32
FAR, NONE = 294.0, 560.0
OLD, NEW = CO + 384, CO + 392
NDUMP, TOP, BLANK = NEW + 136 * 12, NEW + 136 * 13, NEW + 136 * 14 + 128
SB = [NEW, NEW + 136 * 7]
LB = [[NEW + 136 * _j for _j in _l] for _l in ((1, 3, 5), (8, 10, 13))]
KIDS = [[NEW, LB[0][0] + 128, LB[0][1] + 128], [LB[0][2] + 264, LB[1][0] + 128, LB[1][1] + 128]]
CHUNKS = (0, 24, 64, 100, 128)
SPLIT, STDV = True, (1, 3, 4, 5)
HOP, FLY = 240, 3000
PLANS, PASSES = [(_h, _l) for _h in (280, 300, 320, 350) for _l in (100, 300, 600)], 4
CASES = [(250, 1, 0.65, 1.56, 3.8), (330, 1, 0.6, 1.3, 2.8), (220, 1.3, 0.8, 1.7, 4.4)]
TURNS, WIDTH, MOVES, SLACK, EARLY, SEED = 55, 160, 150, 300, 0.1, 12345
CELLS, NOTE, HINT = {}, [], True
ORDER = []


def make(g, T):
    eng = {"V": g.vector, "S": g.scalar, "T": g.tensor, "G": g, "Y": g.sync}
    tick = {"V": 0, "S": 0, "T": 0, "G": 0}
    known = {q: {} for q in eng}
    snap, acc, final, ndma, ops, indirect = {}, {}, {}, [0], [], {}

    def ap(x):
        if not isinstance(x, tuple):
            return x
        if x[0] == "@":
            return ap(x[1]).indirect(ap(x[2]))
        return T[x[0]][x[3]]

    def flat(xs):
        out = []
        for x in xs:
            if isinstance(x, tuple):
                out += [x[1], x[2]] if x[0] == "@" else [x]
        return out

    def wait(q, sem, val):
        k = known[q]
        if k.get(sem, 0) >= val:
            return
        eng[q].wait_ge(T.sem[sem], val)
        k[sem] = val
        for s, v in snap.get((sem, val), {}).items():
            if k.get(s, 0) < v:
                k[s] = v

    def deps(q, reads, writes, sem, val, dma=False):
        need = {}
        for isw, xs in ((0, reads), (1, writes)):
            for x in xs:
                n, lo, hi = x[0], x[1], x[2]
                ps = n in PS
                for e in acc.get(n, []):
                    elo, ehi, ew, eq, es, ev, ed, ex = e
                    if ps:
                        if eq == q and (q == "T" or not (isw or ew) or ehi <= lo or hi <= elo):
                            continue
                    elif ehi <= lo or hi <= elo or not (isw or ew) or (not dma and not ed and apart(x, ex)):
                        continue
                    need[es] = max(need.get(es, 0), ev)
        for s in sorted(need, key=lambda z: z == "s" + q):
            wait(q, s, need[s])
        for isw, xs in ((0, reads), (1, writes)):
            for x in xs:
                n, lo, hi = x[0], x[1], x[2]
                l = acc.setdefault(n, [])
                if isw and x[4] and n not in PS:
                    l[:] = [e for e in l if not (lo <= e[0] and e[1] <= hi)]
                else:
                    l[:] = [e for e in l if not (e[3] == q and not e[6] and not dma and e[7][3] == x[3] and e[2] == isw)]
                l.append((lo, hi, isw, q, sem, val, dma, x))

    def cells(x):
        key = (x[0], repr(x[3]))
        if key not in CELLS:
            at = [0]
            for i, d in zip(x[3][1:], SCRATCH[x[0]][1][1:]):
                at = [a * d + k for a in at for k in ([i] if isinstance(i, int) else range(*i.indices(d)))]
            CELLS[key] = frozenset(at)
        return CELLS[key]

    def apart(x, y):
        return not (x[4] and y[4]) and cells(x).isdisjoint(cells(y))

    def size(x):
        if x[0] == "@":
            return 16 * size(x[2])
        n = 1
        for i, d in zip(x[3][1:], SCRATCH[x[0]][1][1:]):
            n *= 1 if isinstance(i, int) else len(range(*i.indices(d)))
        return n

    def cycles(q, out, ins, both):
        full = [x for x in ins if isinstance(x, tuple) and size(x) == size(out)]
        if out[0] == "@" or any(x[0] == "@" for x in full):
            return 70 + size(out) * (3.8 if out[0] == "@" else 1.56)
        if q == "G":
            return 180 + 2 * size(out)
        f = 2 if both and all(x[0] not in PS for x in full) else 1
        if q == "V" and not both and all(SCRATCH[x[0]][2] in (BF, H16, U16) for x in full + [out]):
            f = 0.5
        return max(64, f * size(out))

    def call(q, out, ins, f, both=False):
        w, r = ([out[1]], [out[2]]) if out[0] == "@" else ([out], [])
        r = flat(ins) + r

        def emit():
            deps(q, r, w, "s" + q, tick[q] + 1)
            fin(q, f())
        if out[0] == "@" or any(isinstance(x, tuple) and x[0] == "@" for x in ins):
            indirect[emit] = ("s" if out[0] == "@" else "g", size(out))
        ops.append((q, r, w, cycles(q, out, ins, both), HOP, emit))

    def either(*fs):
        n = len(ops)
        for f in fs:
            f()
        ways = [x for op in ops[n:] for x in [op[:6]] + list(op[6:])]
        del ops[n:]
        s = ways[0]
        ops.append((s[0], [x for op in ways for x in op[1]], s[2], s[3], s[4], s[5], *ways[1:]))

    def order():
        seen, pred = {}, []
        for i, op in enumerate(ops):
            p = {}
            for isw, xs in ((0, op[1]), (1, op[2])):
                for x in xs:
                    for lo, hi, ew, j, y in seen.get(x[0], []):
                        hit = lo < x[2] and x[1] < hi and (isw or ew) and (op[4] != HOP or ops[j][4] != HOP or not apart(x, y))
                        alike = len(op) == 6 == len(ops[j]) and ops[j][0] == op[0] != "T"
                        if hit or (x[0] in PS and not alike):
                            p[j] = p.get(j, False) or (hit and x[0][0] != "#")
            for isw, xs in ((0, op[1]), (1, op[2])):
                for x in xs:
                    l = seen.setdefault(x[0], [])
                    if isw and x[4]:
                        l[:] = [e for e in l if not (x[1] <= e[0] and e[1] <= x[2])]
                    l.append((x[1], x[2], isw, i, x))
            p.pop(i, None)
            pred.append(p)
        every = range(len(ops))
        succ = [[] for op in ops]
        for i in every:
            for j in pred[i]:
                succ[j].append(i)

        def gap(j, i, qj, qi, hop):
            return 0 if qj == qi and (qi == "T" or not pred[i][j]) else hop if ops[j][4] == HOP else ops[j][4]

        def sweep(seq, back, hop, lean):
            place, busy = {}, {q: [] for q in eng}
            for i in seq:
                best = None
                for k, op in enumerate([ops[i]] + list(ops[i][6:])):
                    if back:
                        t = max([place[j][1] + gap(i, j, op[0], place[j][2], hop) for j in succ[i]] + [op[4]])
                    else:
                        t = max([place[j][1] + gap(j, i, place[j][2], op[0], hop) for j in pred[i]] + [0])
                    l, at = busy[op[0]], 0
                    while at < len(l) and l[at][0] < t + op[3]:
                        t = max(t, l[at][1])
                        at += 1
                    if best is None or t + op[3] + lean < best[1]:
                        best = (t, t + op[3], op[0], k, at)
                busy[best[2]].insert(best[4], best[:2])
                place[i] = best
            return place

        def span(seq, hop, slow):
            end, free = {}, {q: 0 for q in eng}
            for i, k in seq:
                op = ops[i][5 + k] if k else ops[i]
                t = max([end[j][0] + gap(j, i, end[j][1], op[0], hop) for j in pred[i]] + [free[op[0]]])
                free[op[0]] = t + op[3] * (slow if op[0] in "VS" else 1)
                end[i] = (free[op[0]], op[0])
            return max(end[i][0] + ops[i][4] for i in every)

        kept = None
        for hop, lean in PLANS:
            level = [op[3] + op[4] for op in ops]
            for i in reversed(every):
                for j in pred[i]:
                    level[j] = max(level[j], ops[j][3] + gap(j, i, ops[j][0], ops[i][0], hop) + level[i] + 1)
            place = sweep(sorted(every, key=lambda i: -level[i]), False, hop, lean)
            for _ in range(PASSES):
                place = sweep(sorted(every, key=lambda i: (-place[i][1], level[i])), True, hop, lean)
                place = sweep(sorted(every, key=lambda i: (-place[i][1], -level[i])), False, hop, lean)
                seq = [(i, place[i][3]) for i in sorted(every, key=lambda i: (place[i][0], -level[i]))]
                t = span(seq, HOP, 1) + span(seq, 1.25 * HOP, 1.4) / 1.4
                if kept is None or t < kept[0]:
                    kept = (t, seq)
        return polish(kept[1], pred, succ)

    def polish(seq, pred, succ):
        n, cases = len(ops), range(len(CASES))
        below = [0] * n
        for j in reversed(range(n)):
            for i in succ[j]:
                below[j] |= below[i] | 1 << i
        need = [[] for _ in range(n)]
        for j in range(n):
            hard = 0
            for k in succ[j]:
                if ops[j][0] != "T" or ops[k][0] != "T":
                    hard |= below[k] if pred[k][j] or "T" in (ops[j][0], ops[k][0]) else 0
            for i in succ[j]:
                both = ops[j][0] == ops[i][0] == "T"
                if not (below[j] & ~(1 << i) and both and any(below[k] >> i & 1 for k in succ[j])) and not hard >> i & 1:
                    need[i].append((j, both or not pred[i][j], ops[j][4]))
        tail = [op[4] for op in ops]

        def held(o, slow, pe, gather, scatter):
            kind, m = indirect.get(o[5], ("", 0))
            d = o[3] + m * (gather - 1.56 if kind == "g" else scatter - 3.8)
            return o[0], d * (pe if o[0] == "T" else 1 if o[0] == "Y" or o[4] != HOP else slow)
        alts = [[[held(o, *x[1:]) for o in [op] + list(op[6:])] for op in ops] for x in CASES]
        needs = [[[(j, soft, x[0] if lag == HOP else lag) for j, soft, lag in l] for l in need] for x in CASES]
        gives = [[[] for _ in ops] for c in cases]
        for c in cases:
            for i in range(n):
                for j, soft, lag in needs[c][i]:
                    gives[c][j].append((i, soft, lag))
        order, pick = [i for i, k in seq], [0] * n
        for i, k in seq:
            pick[i] = k
        ends, why, que = [[0.0] * n for c in cases], [[None] * n for c in cases], [alts[0][i][pick[i]][0] for i in range(n)]
        state = [SEED]

        def rnd(m):
            state[0] = (state[0] * 1103515245 + 12345) % 2 ** 31
            return (state[0] >> 8) % m

        def rests(part, c, rest, beyond, behind):
            nxt = dict(behind)
            for x in reversed(part):
                q = que[x]
                t = max(beyond[x][pick[x]], nxt[q])
                for y, soft, lag in gives[c][x]:
                    e = rest[y] if soft and que[y] == q else rest[y] + lag
                    if e > t:
                        t = e
                rest[x] = nxt[q] = t + alts[c][x][pick[x]][1]

        def run(part, before, beyond, behind):
            total, tops = 0.0, []
            for c in cases:
                end, wh, alt, need, out = ends[c], why[c], alts[c], needs[c], beyond[c]
                free, last = dict(before[c]), {q: None for q in eng}
                top, at, early = 0.0, None, 0.0
                for i in part:
                    k = pick[i]
                    q, d = alt[i][k]
                    t, w = free[q], last[q]
                    for j, soft, lag in need[i]:
                        e = end[j] if soft and que[j] == q else end[j] + lag
                        if e >= t:
                            t, w = e, ~j
                    t += d
                    end[i], wh[i], free[q], last[q] = t, w, t, i
                    early += t
                    if t + out[i][k] > top:
                        top, at = t + out[i][k], i
                for q in eng:
                    if last[q] is not None and free[q] + behind[c][q] > top:
                        top, at = free[q] + behind[c][q], last[q]
                total += (top + EARLY * early / len(part)) / CASES[c][1]
                tops.append(at)
            return total, tops

        def move(part, tops, inside, before, beyond, behind, rest, fresh):
            c = rnd(len(CASES))
            i, pairs = tops[c], []
            while i is not None and i in inside:
                w = why[c][i]
                if w is not None and w >= 0 and not below[w] >> i & 1:
                    pairs.append((w, i))
                i = w if w is None or w >= 0 else ~w
            if not pairs:
                return None
            p, i = pairs[rnd(len(pairs))]
            kind, m, end = rnd(12), len(part), ends[c]
            if kind < 7:
                if c not in fresh:
                    rests(part, c, rest[c], beyond[c], behind[c])
                    fresh[c] = {x: k for k, x in enumerate(part)}
                pos, rs, x = fresh[c], rest[c], p if kind % 3 else i
                lo = max([pos.get(j, -1) for j in pred[x]] + [-1])
                hi = min([pos.get(j, m) for j in succ[x]] + [m])
                found = None
                for k, (q, d) in enumerate(alts[c][x]):
                    ready = max([end[j] + (0 if soft and que[j] == q else lag) for j, soft, lag in needs[c][x]] + [0])
                    after = max([rs[y] + (0 if soft and que[y] == q else lag) for y, soft, lag in gives[c][x]] + [tail[x]])
                    z = lo
                    while z >= 0 and (que[part[z]] != q or part[z] == x):
                        z -= 1
                    u, at = end[part[z]] if z >= 0 else before[c][q], lo + 1
                    for z in range(lo + 1, m + 1):
                        w = part[z] if z < m else None
                        if w is not None and (que[w] != q or w == x):
                            continue
                        t = max(ready, u) + d + max(after, rs[w] if w is not None else behind[c][q]) + rnd(128)
                        if (found is None or t < found[0]) and (k != pick[x] or not at <= pos[x] <= z):
                            found = (t, k, at)
                        if z >= hi:
                            break
                        u, at = end[w], z + 1
                if found is None:
                    return None
                a, z = pos[x], found[2]
                return (part[:z] + [x] + part[z:a] + part[a + 1:] if z <= a else part[:a] + part[a + 1:z] + [x] + part[z:]), x, found[1]
            if kind < 9 and len(alts[0][(p, i)[kind % 2]]) > 1:
                x = (p, i)[kind % 2]
                return part, x, (pick[x] + 1 + rnd(len(alts[0][x]) - 1)) % len(alts[0][x])
            a, z = part.index(p), part.index(i)
            if kind % 2:
                first = lambda x: x == i or below[x] >> i & 1
            else:
                first = lambda x: not (x == p or below[p] >> x & 1)
            mid = part[a:z + 1]
            return part[:a] + [x for x in mid if first(x)] + [x for x in mid if not first(x)] + part[z + 1:], p, pick[p]

        nothing, own = [{q: 0.0 for q in eng} for c in cases], [[[tail[i]] * len(alts[0][i]) for i in range(n)] for c in cases]
        best = None
        for turn in range(TURNS + 1):
            t = run(order, nothing, own, nothing)[0]
            if best is None or t < best[0]:
                best = (t, list(order), list(pick))
            order.sort(key=lambda x: ends[0][x] - alts[0][x][pick[x]][1])
            rest = [[0.0] * n for c in cases]
            for c in cases:
                rests(order, c, rest[c], own[c], nothing[c])
            at = -rnd(WIDTH // 2)
            while at < n - WIDTH // 4 and turn < TURNS:
                lo, hi = max(at, 0), min(at + WIDTH, n)
                part, inside = order[lo:hi], set(order[lo:hi])
                before, behind = [dict(x) for x in nothing], [dict(x) for x in nothing]
                for c in cases:
                    for i in order[:lo]:
                        before[c][que[i]] = ends[c][i]
                    for i in reversed(order[hi:]):
                        behind[c][que[i]] = rest[c][i]
                beyond = [{i: [max([tail[i]] + [rest[c][y] + (0 if soft and que[y] == q else lag) for y, soft, lag in gives[c][i]
                                                if y not in inside]) for q, d in alts[c][i]] for i in part} for c in cases]
                now, tops = run(part, before, beyond, behind)
                fresh = {}
                for _ in range(MOVES):
                    new = move(part, tops, inside, before, beyond, behind, rest, fresh)
                    if new is None:
                        continue
                    other, x, k = new
                    old, kept = pick[x], [([ends[c][i] for i in part], [why[c][i] for i in part]) for c in cases]
                    pick[x], que[x] = k, alts[0][x][k][0]
                    t, t2 = run(other, before, beyond, behind)
                    if t <= now + SLACK * (1 - turn / TURNS) ** 2 * rnd(16) / 16:
                        now, tops, fresh = t, t2, {}
                        part = sorted(other, key=lambda y: ends[0][y] - alts[0][y][pick[y]][1])
                    else:
                        pick[x], que[x] = old, alts[0][x][old][0]
                        for c in cases:
                            for i, e, w in zip(part, *kept[c]):
                                ends[c][i], why[c][i] = e, w
                order[lo:hi] = part
                at += WIDTH // 2
        NOTE.append(best[0])
        return [(i, best[2][i]) for i in best[1]]

    def flush():
        if not ORDER:
            ORDER.extend(order())
        for i, k in ORDER:
            (ops[i][5 + k] if k else ops[i])[5]()

    def fin(q, ins):
        sem = "s" + q
        tick[q] += 1
        snap[(sem, tick[q])] = dict(known[q])
        final[sem] = tick[q]
        ins.then_inc(T.sem[sem], 1)

    def tt(out, a, b, op):
        call("V", out, [a, b], lambda: g.vector.tensor_tensor(ap(out), ap(a), ap(b), op), True)

    def ts(out, a, s1, op0, s2=None, op1=None):
        more = () if op1 is None else (op1,)
        call("V", out, [a, s1, s2], lambda: g.vector.tensor_scalar(ap(out), ap(a), ap(s1), ap(s2), op0, *more))

    def cp(out, a):
        call("V", out, [a], lambda: g.vector.tensor_copy(ap(out), ap(a)))

    def ms(out, c):
        call("V", out, [], lambda: g.vector.memset(ap(out), c))

    def scan(out, d0, d1, init, op0, op1):
        call("V", out, [d0, d1], lambda: g.vector.tensor_tensor_scan(ap(out), ap(d0), ap(d1), init, op0, op1))

    def act(out, a, func=F.Copy, bias=0.0, scale=1.0):
        if out[0] == "@":
            call("S", out, [a], lambda: g.scalar.activation(ap(out), ap(a), func))
        else:
            call("S", out, [a, bias, scale], lambda: g.scalar.activation(ap(out), ap(a), func, bias=ap(bias), scale=ap(scale)))

    def lin(out, a, scale=1.0, bias=0.0):
        either(lambda: act(out, a, F.Identity if isinstance(bias, tuple) else F.Copy, bias, scale),
               lambda: ts(out, a, scale, A.mult, bias, A.add))

    def iota(out, pattern, base, cm, fl=True):
        kw = dict(allow_small_or_imprecise_dtypes=True) if fl else {}
        call("G", out, [], lambda: g.iota(ap(out), pattern, base, cm, **kw))

    def sel(out, a, pattern, op, base, cm, fill=0.0):
        call("G", out, [a], lambda: g.affine_select(ap(out), ap(a), pattern, op, fill, base, cm))

    def mm(*lst):
        r, w = [x[1] for x in lst] + [x[2] for x in lst], [x[0] for x in lst]

        def emit():
            deps("T", r, w, "sT", tick["T"] + 1)
            for o, lt, rh, st, sp in lst:
                ins = g.tensor.matmul(ap(o), ap(lt), ap(rh), st, sp)
            fin("T", ins)
        ops.append(("T", r, w, sum(max(64, size(x[0])) * (3.2 if SCRATCH[x[1][0]][2] == F32 else 0.8) for x in lst), HOP, emit))

    def dma(q, out, in_, r=(), w=()):
        sem = "d%d" % ndma[0]
        ndma[0] += 1

        def emit():
            deps(q, list(r), list(w), sem, 16, True)
            snap[(sem, 16)] = dict(known[q])
            final[sem] = 16
            eng[q].dma_start(out, in_).then_inc(T.sem[sem], 16)
        x = (list(r) + list(w))[0]
        ops.append((q, list(r), list(w), 120 + size(x) * (0.8 if SCRATCH[x[0]][2] == BF else 1.6), FLY - 600, emit))

    return dict(tt=tt, ts=ts, cp=cp, ms=ms, scan=scan, act=act, iota=iota, sel=sel, mm=mm, dma=dma, wait=wait, deps=deps,
                known=known, final=final, acc=acc, ops=ops, flush=flush, lin=lin, either=either)


def plan(src, cores, topo):
    far = [d for d in cores if d != src and d not in topo.cores_of(src)]
    near = [d for d in cores if d != src and d in topo.cores_of(src)]
    eng = topo.engines(src, far[0])
    rest = [e for e in topo.engines(src, near[0]) if e not in eng]
    h = len(eng) // 2
    a = [(d, eng[2 * i:2 * i + 2]) for i, d in enumerate(far[:h])]
    b = [(d, eng[h * i:h * i + h]) for i, d in enumerate(far[h:])] + [(d, rest) for d in near]
    return [a, b]


def rank_program(g, core, T, topo):
    rank = T.rank_of(core)
    if rank is None:
        return
    K = make(g, T)
    tt, ts, cp, ms, scan, act, iota, sel, mm, dma, wait, deps, lin, either = (
        K[x] for x in ("tt", "ts", "cp", "ms", "scan", "act", "iota", "sel", "mm", "dma", "wait", "deps", "lin", "either"))
    al = slice(None)

    def b(n, lo=0, hi=None, st=1):
        n, at, size = PLACE[n]
        lo, hi = at + lo, at + (size if hi is None else hi)
        return (n, lo, hi, (al, slice(lo, hi, st) if st > 0 else slice(hi - 1, lo - 1, st)), abs(st) == 1)

    def nd(n, lo, hi, *idx):
        return (n, lo, hi, (al,) + idx, False)

    def col(j):
        return b("cols", j, j + 1)

    def ind(w, hi, o, lo=0, oh=None):
        return ("@", b(w, 0, hi), b(o, lo, oh))

    def total(out, *terms, start=True, stop=True):
        mm(*[(out, b(w), x, start and i == 0, stop and i == len(terms) - 1) for i, (w, x) in enumerate(terms)])

    def turn(name):
        op = K["ops"][-1]
        K["ops"][-1] = op[:2] + (list(op[2]) + [(name, 0, 1, None, True)],) + op[3:]

    def put(out, x):
        either(lambda: act(out, x, F.Silu), lambda: cp(out, x))

    def fill(out, c):
        either(lambda: ms(out, c), lambda: iota(out, [[0, out[2] - out[1]]], int(c), 0))

    def copy(out, x):
        either(lambda: lin(out, x), lambda: sel(out, x, [[0, out[2] - out[1]]], A.is_ge, 0, 0))

    def rev(n, at=0):
        return b(n, 1 + at, LL + at, -1)

    def at0(n, k=0, m=1):
        return b(n, 1 + 136 * k, 1 + 136 * (k + m), 17)

    def zs_(s):
        return at0("SZ%d" % (s % 3))

    def zl_(r, s):
        return b("zl%d" % (s % 2)) if s else b("vz%d" % r, 8, 16)

    def diag(out, src, kd="KD"):
        scan(b(out), b(kd), src, 0.0, A.mult, A.max)
        return b(out, 15, 128, 16)

    def seg(c):
        return (146 * c + 1 if c < 4 else 162 * (7 - c) + 18), 16 * c + 16

    def picked(n):
        return b(n, 15, 584, 162), b(n, 144, 583, -146)

    CS, DT = col(4), b("LC", 24, 32)

    dma("Y", T.Qi[:], T.req[:], w=[b("Qi")])
    dma("Y", T.Ci[:], T.child[:], w=[b("Ci")])
    dma("Y", T.X[:, 0:2032], T.desc[:, 0:2032], w=[b("X", 0, 2032)])
    dma("Y", T.Ei[:], T.edge[:], w=[b("Ei")])
    dma("Y", T.XT[:], T.desc[:, 2032:2048], w=[b("XT")])

    iota(b("IP", 0, 1), [[1, 1]], 0, 1, False)
    iota(b("ZH"), [[1, 17], [0, 16]], 0, 0)
    iota(b("ZL"), [[0, 17], [1, 16]], 0, 0)
    for lo, hi in ((0, 144), (144, 704), (704, 1400), (1400, 2200)):
        iota(b("IOT", lo, hi), [[1, hi - lo]], lo, 0)
    iota(b("THR"), [[256, 6]], 192, 0)
    lin(b("RMQ"), b("IOT", 0, 144))
    for lo in [SB[0]] + LB[0] + LB[1][:1]:
        iota(b("C", lo, lo + 128), [[0, 128]], CO, 0)
    iota(b("LC", 0, 24), [[0, 3], [16, 8]], NDUMP, 1)
    iota(b("K3", 1, LL), [[0, 8], [16, 17]], 2064, 0)
    ts(b("IC", 0, 1), b("IP", 0, 1), 4, A.arith_shift_right)
    ts(b("IC", 1, 2), b("IP", 0, 1), 15, A.bitwise_and)
    cp(col(0), b("IP", 0, 1))
    cp(b("cols", 1, 3), b("IC"))
    fill(b("C", TOP, TOP + 8), float(CO))
    ms(b("M16"), -16.0)
    act(b("STD", 0, 136), b("M16", 0, 136), F.Silu, scale=0.0)
    K["ops"][-1] = K["ops"][-1][:3] + (K["ops"][-1][3] + 1600,) + K["ops"][-1][4:]
    turn("#s")
    for lo in (136, 280):
        either(lambda: act(b("STD", lo, lo + 144), b("ZH", 0, 144), scale=0.0), lambda: fill(b("STD", lo, lo + 144), 0.0))
    lin(b("L", BLANK, BLANK + 8), b("STD", 0, 8))
    lin(col(3), col(2), 1.0, 1.0)
    ts(col(5), col(2), 0.0, A.is_equal)
    ts(col(6), col(2), 0.0, A.is_gt)
    ts(col(11), col(2), 14.5, A.is_gt)
    lin(col(7), col(11), 4095.0, 1.0)
    lin(col(4), col(11), 1.0 - 2.0 ** -12, 2.0 ** -12)
    lin(col(16), col(11), 63.0, 1.0)
    lin(col(8), col(1), -16.0)
    lin(col(9), col(4), -1.0)
    lin(col(10), col(2), 1.0, 16.0 * 2047)
    ts(b("BO"), b("ZH", 0, 128), col(1), A.is_equal)
    lin(b("B0"), b("BO"), col(5))
    turn("#s")
    lin(b("B1"), b("B0"), 16.0)
    sel(b("SHD"), b("BO"), [[1, 128]], A.is_equal, -1, -1)
    ts(b("KD"), b("ZL", 0, 128), col(2), A.is_gt)
    ts(b("KD6"), b("ZL", 0, 128), col(3), A.is_equal, 4095.0, A.mult)
    tt(b("KD"), b("KD"), b("KD6"), A.add)
    ts(b("OHZ"), b("ZL"), col(2), A.is_equal)
    ts(b("IDZ"), b("ZH"), col(2), A.is_equal)
    ts(b("TRZ"), b("ZH"), col(2), A.is_le)
    lin(b("ID4", 0, 17), b("IDZ", 0, 272, 16), 4096.0)
    ts(b("KD6"), b("KD"), 64.0, A.min)
    lin(b("B6"), b("BO"), 1.0 / 64)
    ts(col(17), col(2), 7.5, A.is_gt, -16.0, A.mult)
    ts(col(17), col(17), col(2), A.add, 8.0, A.add)
    lin(col(13), col(17), -1.0, 15.0)
    ts(b("I"), b("IOT", 0, 128), col(0), A.is_equal)
    ts(b("OHC"), b("ZL"), col(13), A.is_equal, 17.0, A.mult)
    ts(b("OHB"), b("ZH"), col(17), A.is_equal, 16.0, A.mult)
    total(b("ps", 0, 272), ("I", b("OHB")), ("I", b("OHC")))
    act(b("OHB"), b("ps", 0, 272), F.Relu, bias=17.0, scale=-1.0)
    lin(b("OH2", 0, 256), b("OHB", 0, 256), -816.0, 816.0)
    lin(b("OH2", 256, 528), b("OHB"), -816.0, 816.0)
    lin(b("WW", 0, 272), b("OHZ"), 4096.0, -4096.0)
    for s in range(2):
        lin(b("WW", 272 * s + 272, 272 * s + 544), b("OHB"), -272.0 * (s + 1), -136.0)
    for j, (r, s) in enumerate(((0, 0), (0, 1), (1, 0))):
        fill(b("KP", 8 * j, 8 * j + 8), 17 * 2048.0 + 136 + 272 * (s + 1) - (BLANK + 16 - LB[r][s] - 136) - 32768)
    fill(b("KP", 24, 32), 32768.0)
    ms(b("ZR"), 0.0)
    for n, c in (("IH", HH / 2), ("IR", 2.0 ** 37), ("I2", 0.5), ("Im", -1.0), ("I4", 4096.0), ("Im4", -4096.0),
                 ("I16", 16.0), ("IG", 65536.0), ("I6", 1.0 / 16), ("I32", 1.0), ("Ia", -256.0), ("Ib", 257.0)):
        either(lambda: lin(b(n), b("I"), c),
               lambda: sel(b(n), b("STD", 0, 128) if SCRATCH[n][2] == F32 else b("ZR"), [[-1, 128]], A.not_equal, 0, 1, c))
    for n, c in (("IC6", col(16)), ("ICS", col(7))):
        lin(b(n), b("I"), c)
    lin(col(12), col(1), 16.0, 15.0)
    ts(b("CZ"), b("IOT", 0, 144), col(12), A.is_equal, -HH, A.mult)
    ts(col(14), col(11), -4095.0, A.mult, 4096.0, A.add)
    lin(col(15), col(14), 256.5)
    lin(b("THR"), b("THR"), col(14))
    lin(b("THS"), b("THR"), -32768.0)
    fill(b("KF"), 0.0)
    lin(b("KG", 0, 16), b("OHZ", 0, 16), 4096.0)
    ms(b("KG", 16, 17), -8192.0)
    lin(b("KG", 15, 16), b("KG", 15, 16), 1.0, -4096.0)
    for c in range(8):
        copy(b("KF", sum(seg(c)) - 17, sum(seg(c))), b("KG", 0, 17))
    lin(b("KA"), b("KF"), -4096.0)
    ms(b("AD", 0, 584, 146), FRZ / 2)
    ms(b("AD", 17, 504, 162), FRZ / 2)
    lin(b("LC", 0, 24), b("LC", 0, 24), 1.0, col(8))
    fill(b("LC", 8, 16), 256.0)
    copy(b("U0", 24, 40), b("LC", 8, 24))
    copy(b("U1", 24, 40), b("LC", 8, 24))
    lin(b("JC"), b("LC", 0, 8), 1.0, BLANK + 16.0 - NDUMP)
    lin(b("JP"), b("LC", 0, 8), 16.0, -16.0 * NDUMP)
    lin(DT, b("LC", 0, 8), 2.0, TDUMP - 2.0 * NDUMP)
    fill(b("KC", 8, 32), 0.0)
    fill(b("KC", 0, 8), 4096.0)
    ms(b("KC", 32, 40), -256.0 * HH)
    ms(b("KR", 0, 128), -0.25)
    fill(b("KR", 128, 256), 3072.0)
    fill(b("RD"), 0.0)
    fill(b("DF", 2048, 2064), 0.0)
    ms(nd("AB", 0, 2176, al, slice(16, 17)), NONE)
    ts(b("B620"), b("M16"), 0.0, A.mult, 1241.0, A.add)

    def roots(src):
        ts(b("Q1"), src, 1.0, A.add)
        total(b("pw", 0, 128), ("B0", b("Q1")))
        ts(b("qi"), diag("SQ", b("pw", 0, 128)), CS, A.mult, 16.0 * CO - 1, A.add)
        ts(b("qj", 0, 8), b("qi"), 4, A.arith_shift_right)
        ts(b("qj", 8, 16), b("qi"), 15, A.bitwise_and)
        cp(b("vz1"), b("qj"))
        cp(b("v1"), b("qj", 0, 8))
        ts(zs_(0), b("qj", 8, 16), 4096.0, A.mult)
        ts(b("x51"), b("qj", 0, 8), 4096.0, A.mult)

    def roots_first():
        pe = b("pa", 256, 384)
        ts(b("Q1"), b("Qi"), -1.0 / 16, A.mult, 2047.47, A.add)
        cp(b("Q16"), b("Qi"))
        total(b("pw", 0, 128), ("B0", b("Q1")))
        total(pe, ("B0", b("Q16")), ("B1", b("Q1")))
        ts(b("vz0", 0, 8), diag("SQ", b("pw", 0, 128)), col(9), A.mult, CO + 2047.0, A.add)
        ts(b("OH"), pe, col(10), A.is_equal)
        ts(b("v0"), b("SQ", 15, 128, 16), col(9), A.mult, CO + 2047.0, A.add)
        lin(zs_(0), diag("SE", pe), col(7), -65536.0 * 2047)
        ts(b("x50"), b("v0"), 4096.0, A.mult)

    def child(r, s):
        n, rows = LB[r][s], ind("C", TOP + 1 if s else OLD, "vz%d" % r, 0, 8)
        if r or s:
            lin(b("OH"), ("@", b("OHZ"), zl_(r, s)))
        tt(b("M1"), rows, b("OH"), A.mult)
        if r + s < 3:
            lin(b("CG"), rows)
        if s and not r:
            lin(b("C", LB[r][s - 1] + 136, LB[r][s - 1] + 264), ind("C", KIDS[r][s - 1], "cl"))
        if s == 0:
            iota(b("CN"), [[0, 128]], n - n % 16 - 4096, 0)
            total(b("ph", 256, 384), ("I", b("RMQ", n % 16, n % 16 + 128)), ("I", b("CN")), ("I4", b("OH")))
            tt(b("CV"), b("CG"), b("ph", 256, 384), A.max)
        total(b("pm", 0, 128), ("B6", b("M1")))
        ts(b("cl"), diag("SC", b("pm", 0, 128), "KD6"), col(16), A.mult, float(CO), A.max)

    def edge(r, s):
        lin(b("uE"), ind("L", KIDS[r][s], "cl"))
        ts(b("El"), ind("L", KIDS[r][s], "cl"), -1.0, A.mult, 2047.0, A.add)

    def acts(r, s):
        j, pa = 3 * r + s, b("pa", 0, 8)
        lin(b("vcol"), ind("IOT", TOP + 1 if s else OLD, "vz%d" % r, 0, 8), 4096.0)
        for c in range(8):
            o, n = seg(c)
            either(lambda: act(b("AD", o, o + n), b("vcol", 0, n), F.Abs, bias=b("x5%d" % r, c, c + 1), scale=-1.0),
                   lambda: ts(b("AD", o, o + n), b("vcol", 0, n), b("x5%d" % r, c, c + 1), A.not_equal, 4096.0, A.mult))
        scan(b("RA"), b("AD"), b("KA"), 2 * FRZ, A.min, A.add)
        for h, e in enumerate(picked("RA")):
            out = b("athr", 4 * h, 4 * h + 4)
            either(lambda: act(out, e, F.Relu, bias=BIG, scale=-BIG / 2048), lambda: ts(out, e, 0.5, A.is_lt, BIG, A.mult))
        total(pa, ("I", b("v%d" % r)), ("I", b("athr")))
        tt(b("x2"), pa, b("LC", 0, 8), A.min)
        cp(b("sl"), b("x2"))
        (cp if j in STDV else put)(ind("STD", TOP, "sl"), b("IOT", 256 * j + 256, 256 * j + 384))
        lin(b("SG"), ind("STD", KIDS[r][s], "cl"))
        if j < 5:
            lo, hi = (KIDS[0] + KIDS[1])[j:j + 2]
            iota(b("STD", lo, hi), [[0, hi - lo]], 0, 0)
        e = diag("SA", b("SG"))
        either(lambda: act(b("nf"), e, F.Relu, bias=b("THS", j, j + 1), scale=32768.0),
               lambda: ts(b("nf"), e, b("THR", j, j + 1), A.is_gt, BIG, A.mult))

    def payload():
        for x in range(8):
            ts(nd("QX", 128 * x, 128 * x + 128, al, x, al), b("Q16"), b("BO", 16 * x, 16 * x + 1), A.mult)
        mm(*[(b("pq", 1 + 17 * c, 18 + 17 * c), nd("QX", 0, 1024, c, al, al), b("IDZ", 0, 272, 16), True, True) for c in range(8)])
        mm((b("pq", 140, 276), b("I4"), b("K3", 1, LL), True, False),
           *[(b("pq", 140 + 17 * c, 157 + 17 * c), nd("QX", 0, 1024, c, al, al), b("ID4", 0, 17), False, False) for c in range(8)])
        lin(b("FL", 1, LL), b("pq", 1, LL), 1.0, 2056.5)
        total(b("pq", 140, 276), ("Im4", b("FL", 1, LL)), start=False)
        lin(b("W3", 1, LL), b("pq", 140, 276))
        lin(b("W2", 1, LL), b("pq", 140, 276), 1.0, -4096.0 * HH)
        tt(b("W1", 1, LL), b("pq", 1, LL), b("W3", 1, LL), A.add)

    def hashes():
        total(b("pq", 256, 384), ("SHD", b("Q16")))
        tt(b("HP"), b("pq", 256, 384), b("QF"), A.mult)
        ts(b("HI"), b("HP"), 5, A.arith_shift_right, 2047, A.bitwise_and)
        cp(b("X6"), b("HI"))
        either(lambda: act(b("Hm"), b("X6"), F.Relu, bias=-1023.0, scale=0.5), lambda: ts(b("Hm"), b("X6"), 2046.5, A.is_gt, 0.5, A.mult))
        total(b("pq", 384, 512), ("I32", b("X6")), ("Im", b("Q16")), stop=False)
        total(b("pq", 384, 512), ("Im4", b("Hm")), ("I", b("Hm")), ("I", b("Hm")), start=False)
        lin(b("HMQ"), b("pq", 384, 512), col(6))

    def distances(r, s):
        pd = b("pd", 1, LL)
        if s:
            act(at0("RD"), zs_(s), F.Relu, bias=-15.0, scale=2.0 ** -12)
            scan(b("RMP", 1, LL), b("M16", 1, LL), b("RD", 1, LL), 0.0, A.add, A.max)
        total(pd, ("IH", b("B620", 1, LL)), *([("IR", b("RMP", 1, LL))] if s else []), stop=False)
        for lo, hi in zip(CHUNKS, CHUNKS[1:]):
            lin(b("XQ", 16 * lo, 16 * hi), ind("X", 2064, "Ql%d" % r, lo, hi))
            tt(b("DF", 16 * lo, 16 * hi), ind("X", 2064, "El", lo, hi), b("XQ", 16 * lo, 16 * hi), A.subtract)
            for x, y in ((lo, hi - 8), (hi - 8, hi)) if SPLIT and hi == 128 else ((lo, hi),):
                act(nd("AB", 17 * x, 17 * y, slice(x, y), slice(0, 16)), b("DF", 16 * x, 16 * y), F.Abs)
        for h, lo, hi in ((0, 0, 16), (1, 0, 8), (1, 8, 16)):
            mm(*[(b("pd", 1 + 68 * h, 69 + 68 * h), b("CZ", 15 - p, 143 - p),
                  nd("AB", 1088 * h, 1088 * h + 1088, slice(64 * h + p, 64 * h + 64, 16), al), False, h == 1 and p == 15) for p in range(lo, hi)])

    def cut_rows(r, s):
        uu, end = "UU%d" % (s % 2), s == S_ - 1
        pe, px, py, po = b("pq", 0, 128) if end else b("ps", 128, 256), b("ps", 384, 392), b("ps", 392, 400), b("ps", 256, 384)
        tt(b("EL"), ind("IDZ", 272, uu, 8, 16), b("X6" if end else "WN"), A.mult)
        total(pe, ("BO", b("EL")))
        e = diag("SE", pe)
        if end:
            ts(b(uu, 24, 32), e, CS, A.mult, -1.0, A.add)
            ts(b("fl", 16, 24), e, col(15), A.is_gt, 256.0, A.mult)
            tt(b("OHM"), ind("OH2", 528, uu, 24, 32), b("IOT", SB[r], SB[r] + 128), A.add)
            put(ind("C", TOP, uu, 16, 24), b("OHM"))
            return
        j, cut = 2 * r + s, b("mk%d" % r, 16 * s, 16 * s + 8)
        lin(b("fz"), b("zcf"), -1.0, -2048.5)
        lin(b("fu"), e, CS, 2048.5)
        total(px, ("I4", b("KP", 24, 32)), ("I4", b("KP", 8 * j, 8 * j + 8)), ("Im4", cut), ("IG", b("zcf")), ("IG", b("fz")), ("ICS", e),
              stop=False)
        total(px, ("Im4", b("fu")), start=False)
        total(py, ("Im4", cut), ("I4", b("zcf")), ("I4", b("fz")), ("ICS", e), ("Im4", b("fu")))
        ts(b("fl", 8 * s, 8 * s + 8), py, (BLANK + 16 - LB[r][s] - 136 - 4097.0) * 4096, A.is_equal, 256.0, A.mult)
        tt(b("x3"), px, zs_(s + 1), A.max)
        ts(b(uu, 24, 32), b("x3"), 2.0 ** -12, A.mult)
        lin(b("Wg"), ind("WW", 816, uu, 24, 32))
        iota(b("CN"), [[0, 128]], LB[r][s + 1], 0)
        total(po, ("I", b("RMQ", 0, 128)), ("I", b("CN")), ("I", b("Wg")))
        tt(b("CV"), b("CG"), po, A.max)

    def travel(src, land, tag):
        (lin if tag == "1" else cp)(b(land, 0, 16), b(src, 0, 16))
        K["ops"].append(("G", [b(src)], [b(land, 16)], 7500 if tag == "E" else 1400, FLY, lambda: send(src, land, tag)))

    def send(src, land, tag):
        sent = [0]
        deps("G", [b(src)], [], "loc" + tag, 0)
        for calls in plan(core, T.cores, topo):
            tr = []
            for d, en in calls:
                e = (T.rank_of(d) - rank) % 8
                rid, pid = topo.addr(d, core)
                tr.append(RemoteDMATransfer(dst_ids=[DstId(rid=rid, pnc=pid)], dma_engine_mask=sum(1 << x for x in en),
                                            remote_sem=T.sem["arr" + tag], src=T[src][:, 16 * e:16 * e + 16], dst=T[land][:, 16 * e:16 * e + 16]))
                sent[0] += len(en)
            g.remote_dma_fused(tr, local_sem=T.sem["loc" + tag])
        n = sum(len(en) for s in T.cores if s != core for calls in plan(s, T.cores, topo) for d, en in calls if d == core)
        K["acc"].setdefault(land, []).append((16, 128, 1, "R", "arr" + tag, n, True, b(land, 16)))
        K["acc"].setdefault(src, []).append((0, 128, 0, "R", "loc" + tag, sent[0], True, b(src)))
        K["final"]["arr" + tag] = n
        K["final"]["loc" + tag] = sent[0]

    def step(r, s):
        end, last = s == S_ - 1, (r, s) == (RO_ - 1, S_ - 1)
        v, zs, vz, uu, sz, uQ = b("v%d" % r), zs_(s), "vz%d" % r, "UU%d" % (s % 2), "SZ%d" % s, b("uQ%d" % r)
        lb, cb, mk, old = LB[r][s], LB[r][s] + 136, "mk%d" % r, b("CV" if r else "SND")
        low = b("L", cb, cb + 128) if last else b("WN")
        distances(r, s)
        acts(r, s)
        if last:
            cp(b("X", 2047, 2048), b("XT", 15, 16))
        if s == 0:
            payload()
            lin(uQ, b("QF"), -1.0, 2047.0)
            lin(b("L", lb, lb + 128), b("QF"), -1.0, 2047.0)
        else:
            tt(b("L", lb, lb + 128), ("@", b("TRZ"), zl_(r, s)), uQ, A.mult)
        if end:
            tt(old, ("@", b("TRZ"), zl_(r, s)), b("HMQ"), A.mult)
        if s and (r == 0 or s == 1):
            cut_rows(r, s - 1)
        if s == 1:
            total(b("ps", 400, 408), ("I32", b("U0", 8, 16)), ("I", b("fl", 0, 8)))
            ts(b("za"), b("ps", 400, 408), 256.0, A.min)
            tt(b("L", SB[r], SB[r] + 128), ind("TRZ", 272, "za"), uQ, A.mult)
            hashes()
            lin(b("XA"), b("QF"), 1.0, 2048.5)
            total(b("pq", 0, 128), ("I32", b("QF")), ("Im", b("XA")))
            lin(b("XB"), b("pq", 0, 128), 1.0, 2048.0 + 8)
        if (r, s) == (0, 1):
            roots(b("LQ"))
        if s + r > 1:
            lin(b("XA"), b("uE"), 1.0, 2048.5)
            total(b("pq", 128, 256), ("I32", b("uE")), ("Im", b("XA")), ("I", b("XB")))
            if r:
                ts(b("Y"), b("pq", 128, 256), -2041.0, A.not_equal)
            else:
                ts(b("XC"), b("pq", 128, 256), -2041.0, A.is_equal, 256.0, A.mult)
                total(b("pq", 0, 128), ("I32", b("uE")), ("Im", b("XA")), ("I16", b("XB")), ("I", b("XC")))
                lin(b("X6"), b("pq", 0, 128), 1.0, 2048.0 + 9)
        s3, E1, A1, cf = at0(sz, 1), b("EA", 0, 8), b("EA", 8, 16), b("SC", 15, 128, 16)
        M, tk, pp, U = [b("ph", 8 * i, 8 * i + 8) for i in (2, 0, 1)], b("pt", 0, 8), b("pt", 8, 16), "U%d" % s
        pz, pc = b("pw", 288, 296), b("pm", 272, 280)
        mm((b("ph", 0, 24), b("I"), b("KC", 0, 24), True, False), (M[0], b("IC6"), cf, False, False), (M[1], b("I"), v, False, False))
        mm(*[(x, b("I"), b("athr"), False, False) for x in M])
        mm((M[0], b("I"), b("nf"), False, False), (M[2], b("I"), b("nf"), False, False))
        mm((b("pt", 0, 16), b("I"), b("KC", 16, 32), True, False), (pp, b("I"), b("JP"), False, False))
        mm((tk, b("I"), b("athr"), False, False))
        mm((tk, b("I"), b("nf"), False, False))
        total(pz, ("I4", b("KC", 32, 40)), ("Im", b("athr")), stop=False)
        if not end:
            total(pc, ("IC6", cf), ("Im", v))
        scan(rev("S2"), rev("pd"), rev("W2"), 0.0, A.min, A.max)
        scan(rev(sz, 136), rev("pd"), rev("W3"), 0.0, A.min, A.max)
        total(pz, ("Ia", at0("S2")), start=False, stop=False)
        total(pz, ("Ib", s3), start=False)
        if not end:
            tt(zs_(s + 1), zs, pz, A.max)
            ts(b("dn"), pz, -0.5, A.is_ge)
            either(lambda: act(b("y3"), pz, F.Relu, bias=-4096.0 * 255), lambda: ts(b("y3"), pz, -4096.0 * 255, A.add, 0.0, A.max))
            ts(zl_(r, s + 1), zs_(s + 1), 2.0 ** -12, A.mult)
            tt(b("y2"), b("dn"), pc, A.mult)
        scan(rev("S1"), rev("pd"), rev("W1"), 0.0, A.min, A.max)
        lin(at0(sz, 2), at0("S2"), 1.0, 4096.0 * HH)
        lin(b("zcf"), s3, 2.0 ** -12)
        tt(b("EA"), at0(sz, 0, 2), at0(sz, 1, 2), A.is_ge)
        mm((tk, b("I32"), at0("S1"), False, False))
        mm((tk, b("Im4"), b("zcf"), False, False), (pp, b("I6"), b("zcf"), False, False), (tk, b("I4"), E1, False, False),
           (tk, b("I4"), A1, False, True))
        ts(b("tp"), b("pt", 0, 16), -7.5 / 16, A.add, 2048.0, A.min)
        mm((M[2], b("I"), b("zcf"), False, False), *[(M[i], b("Im4" if i == 1 else "I4"), E1, False, False) for i in range(3)],
           *[(M[i], b("I4"), A1, False, i == 2) for i in range(3)])
        tt(b(U, 0, 24), b("ph", 0, 24), b("U%d" % (s - 1), 16, 40) if s and not last else b("LC", 0, 24), A.min)
        for i, x in enumerate((cb, lb)):
            ts(b(mk, 16 * s + 8 * i, 16 * s + 8 * i + 8), M[i], NDUMP - 0.5, A.is_lt, x - BLANK - 16.0, A.mult)
        cp(b(uu, 0, 24), b(U, 0, 24))
        if end:
            total(b("pm", 128, 256), ("I", b("Q16")), stop=False)
            ts(b("lz"), pz, 2.0 ** -12, A.mult)
            tt(b("HK"), ind("TRZ", 272, "lz"), old, A.mult)
            total(b("pm", 128, 256), ("I", b("HK")), start=False)
            (lin if r else cp)(b("SND" if r else "SQl"), b("pm", 128, 256))
            travel(*(("SND", "LAND1", "1") if r else ("SQl", "Ql1", "0")))
        lin(b("DFg"), ind("DF", 2064, "tp", 8, 16))
        lin(b("XQg"), ind("X", XW, "tp", 0, 8))
        total(b("ps", 0, 128), ("I", b("KR", 0, 128)), ("I2", b("DFg")), ("I", b("XQg")), ("I4", b("KR", 128, 256)), ("Im4", b("KR", 128, 256)))
        lin(b("DH"), b("ps", 0, 128))
        cp(b("VT"), ind("IOT", 2064, "tp", 0, 8))
        tt(b("NF", 0, 584, 146), b("pt", 0, 4), b("LC", 24, 28), A.min)
        tt(b("NF", 17, 504, -162), b("pt", 4, 8), b("LC", 28, 32), A.min)
        for c in range(8):
            o, n = seg(c)
            ts(b("NF", o, o + n), b("VT", 0, n), b("pt", c, c + 1), A.is_equal, b("LC", 24 + c, 25 + c), A.mult)

        def descriptors():
            scan(b("RF"), b("NF"), b("KF"), 0.0, A.max, A.add)
            if last:
                turn("#a")
            for h, e in enumerate(picked("RF")):
                cp(b("didx", 4 * h, 4 * h + 4), e)
            cp(ind("X", XW, "didx"), b("DH"))
        if not last:
            descriptors()
        tt(low, ind("TRZ", 272, uu, 8, 16), b("uE"), A.mult)
        if not last:
            put(ind("C", TOP, uu, 0, 8), b("CV"))
        if not end:
            pv = b("pw", 272, 280)
            total(pv, ("I", v), ("I", b("y3")), ("I", b("y2")), stop=False)
            total(pv, ("Im4", b(mk, 16 * s, 16 * s + 8)), ("Im4", b(mk, 16 * s + 8, 16 * s + 16)), start=False)
            ts(b(vz, 0, 8), pv, float(TOP), A.min)
            ts(v, pv, float(TOP), A.min)
            lin(b("x5%d" % r), pv, 4096.0)
            child(r, s + 1)
        if end and r == 0:
            lin(b("C", cb, cb + 128), ind("C", KIDS[r][s], "cl"))
            cut_rows(0, 2)
            total(b("pw", 272, 280), ("I32", b("U1", 8, 16)), ("I", b("fl", 8, 16)), stop=False)
            total(b("pw", 272, 280), ("I32", b("U2", 8, 16)), start=False, stop=False)
            total(b("pw", 272, 280), ("I", b("fl", 16, 24)), start=False)
            ts(b("zo"), b("pw", 272, 280), -256.0, A.add, 256.0, A.min)
            tt(b("X5"), ind("TRZ", 272, "zo"), uQ, A.mult)
        if end:
            pn = b("pw", 264, 272)
            total(pn, ("I32", b("JC")), *[("I", b(mk, 8 * i, 8 * i + 8)) for i in range(4)], stop=False)
            total(pn, ("I", b(mk, 32, 40)), ("I", b(mk, 40, 48)), start=False)
            ts(b("id%d" % r), pn, float(BLANK), A.min)
            if last:
                turn("#b")
        tt(ind("L", TOP, uu, 16, 24), b("uE"), low, A.subtract)
        if last:
            turn("#a")
        if end and r == 0:
            total(b("ps", 256, 384), ("I32", b("X5")), ("I32", b("L", SB[0], SB[0] + 128)))
            lin(b("L", SB[0], SB[0] + 128), b("ps", 256, 384))
        if r and s:
            tt(b("EL"), ind("IDZ", 272, uu, 8, 16), b("Y"), A.mult)
            tt(b("OHM"), ind("TRZ", 272, uu, 8, 16), uQ, A.mult)
            total(b("pq", 0, 128), ("BO", b("EL")))
            tt(b("LN" if last else "X5"), b("OHM"), b("pq", 0, 128), A.mult)
        if last:
            turn("#b")
            descriptors()
            turn("#b")
            dma("Y", T.yd[:], T.X[:, 0:2048], r=[b("X", 0, 2048)])
        elif end:
            lin(b("L", cb, cb + 128), low)
        else:
            dma("Y", T.L[:, cb:cb + 128], T.WN[:], r=[low], w=[b("L", cb, cb + 128)])
            edge(r, s + 1)

    roots_first()
    cp(b("Ql0"), b("Qi"))
    if HINT:
        turn("#q")
    ts(b("C", CO, OLD), b("Ci"), float(CO), A.add)
    if HINT:
        turn("#q")
    ts(b("L", CO, OLD), b("Ei"), -1.0, A.mult, 2047.0, A.add)
    lin(b("lsave", 0, 1), b("L", CO, CO + 1))
    ms(b("L", CO, CO + 1), -1.0)
    child(0, 0)
    cp(b("QF"), b("Qi"))
    fill(b("X", 2048, XW), FAR)
    cp(b("X", 2032, 2047), b("XT", 0, 15))
    ms(b("X", 2047, 2048), NONE)
    edge(0, 0)
    travel("Qi", "LQ", "E")
    for s in range(S_):
        step(0, s)
    child(1, 0)
    edge(1, 0)
    cp(b("QF"), b("Ql1"))
    cp(b("Q16"), b("QF"))
    for s in range(S_):
        step(1, s)
    lin(b("YE", 0, 384), b("L", CO, OLD), -1.0, 2047.0)
    lin(b("YE", 0, 1), b("lsave", 0, 1), -1.0, 2047.0)
    for r in range(RO_):
        lin(b("YE", 384 + 256 * r, 640 + 256 * r, 2), ind("L", BLANK + 1, "id%d" % r), -1.0, 2047.0)
    lin(b("YE", 385, 640, 2), b("L", SB[0], SB[0] + 128), -1.0, 2047.0)
    for i, x in enumerate((b("X5"), b("L", SB[1], SB[1] + 128), b("LN"))):
        total(b("ph", 128, 256), ("I32", x), start=i == 0, stop=i == 2)
    lin(b("YE", 641, 896, 2), b("ph", 128, 256), -1.0, 2047.0)
    dma("Y", T.ye[:, 0:640], T.YE[:, 0:640], r=[b("YE", 0, 640)])
    dma("Y", T.ye[:, 640:896], T.YE[:, 640:896], r=[b("YE", 640, 896)])
    dma("Y", T.yr[:], T.LAND1[:], r=[b("LAND1")])
    K["flush"]()
    for s, n in K["final"].items():
        K["known"]["G"].pop(s, None)
        wait("G", s, n)
